import numpy as np, ml_dtypes
CORES = [40,41,42,43,44,45,46,47]
N = 8
BF = ml_dtypes.bfloat16
def gentries(a):
    return np.ascontiguousarray(a.reshape(8, 16, -1).transpose(0, 2, 1)).reshape(8, -1)
def gtable(e):
    e = np.asarray(e); return np.ascontiguousarray(e.reshape(8, -1, 16).transpose(0, 2, 1)).reshape(128, -1).astype(np.int32)
M, NC, R, L, S, D = 4096, 1024, 32, 192, 2, 3
def mag(rng, shape, lo, hi):
    return lo + (hi - lo) * rng.random(shape)
def thin(rng, y):
    k = rng.integers(0, 16, y.shape); low = mag(rng, y.shape, 1.0, 2.0) * np.exp2(rng.choice(np.array([-20.0, -12.0, -10.0, -8.0, -7.0, -6.0, -5.0]), y.shape))
    return np.where(k == 0, 0.0, np.where(k < 4, low, y))
def parts(rng):
    return {"X": rng.integers(-7, 8, (N, 8, 16, M)), "E": mag(rng, (N, 8, 16, M), 0.5, 2.0), "XR": rng.integers(-7, 8, (N, 8, 16, R)), "ER": mag(rng, (N, 8, 16, R), 0.5, 1.0),
            "HC": rng.integers(0, M, (N, 8, 16, NC)), "TC": rng.integers(0, M, (N, 8, 16, NC)), "NH": rng.integers(0, M, (N, 8, 16, S, L)), "NT": rng.integers(0, M, (N, 8, 16, S, L)),
            "h": rng.integers(0, M, (N, 8, L)), "p": rng.integers(0, R, (N, 8, L)), "t": rng.integers(0, M, (N, 8, L))}
def pack(d):
    b = lambda v: np.ascontiguousarray(v.reshape(N, 128, -1)).astype(np.float32).astype(BF)
    i = lambda v: np.ascontiguousarray(v.reshape(N, 128, -1)).astype(np.int32)
    l = lambda v: np.stack([gtable(a) for a in v])
    return {"xe": b(d["X"]), "ee": b(d["E"]), "xr": b(d["XR"]), "er": b(d["ER"]), "hc": i(d["HC"]), "tc": i(d["TC"]), "nh": i(d["NH"]), "nt": i(d["NT"]), "hl": l(d["h"]), "rl": l(d["p"]), "tl": l(d["t"])}
def setup_inputs(rng):
    return pack(parts(rng))
def setup_inputs_spread(rng):
    d = parts(rng)
    full = mag(rng, (N, 8, 16, M), 0.25, 1.0) * np.exp2(rng.choice(np.array([-1.0, -1.0, -1.0, -1.0, -1.0, -1.0, 0.0, 1.0]), (N, 8, 1, M)))
    d["E"] = thin(rng, full); d["E"][:, :, 0] = full[:, :, 0]; d["ER"] = thin(rng, d["ER"])
    amp = rng.choice(np.array([1, 2, 4, 7]), (N, 8, 1, M)); d["X"] = rng.integers(0, 2 ** 20, (N, 8, 16, M)) % (2 * amp + 1) - amp
    low = lambda n, shape: np.minimum((n * rng.random(shape) ** 2).astype(np.int64), n - 1)
    for k in ("HC", "TC", "NH", "NT", "h", "t"): d[k] = low(M, d[k].shape)
    d["p"] = low(R, d["p"].shape)
    g = int(rng.integers(0, 8)); o = rng.permutation(M)
    cold = np.zeros(M, bool); cold[o[:2 * NC]] = True
    d["E"][:, g] = np.where(cold, mag(rng, (N, 16, M), 0.1875, 0.3125), mag(rng, (N, 16, M), 1.75, 2.0)); d["ER"][:, g] = mag(rng, (N, 16, R), 0.875, 1.0)
    h = o[rng.integers(2 * NC, M, (N, L))]; t = o[rng.integers(2 * NC, M, (N, L))]; p = rng.integers(0, R, (N, L))
    d["h"][:, g] = h; d["t"][:, g] = t; d["p"][:, g] = p
    d["HC"][:, g] = o[:NC]; d["TC"][:, g] = o[NC:2 * NC]
    d["NH"][:, g] = o[(37 * p + t) & (NC - 1)][:, None, None, :]
    d["NT"][:, g] = np.roll(o[NC + ((37 * h + p) & (NC - 1))], D, axis=0)[:, None, None, :]
    return pack(d)
def setup_inputs_ends(rng):
    d = parts(rng); sign = lambda shape: 2 * rng.integers(0, 2, shape) - 1
    v = 7 * sign((2, 8, 16)); X = 7 * sign((N, 8, 16, M)); z = rng.integers(0, 8, (N, 8, 1, M))
    for j in range(4): X = np.where(z == j, (1 - 2 * (j & 1)) * v[j >> 1][None, :, :, None], X)
    for c, w in ((0, v[0]), (1, v[1]), (2, v[1]), (3, v[0]), (4, -v[0]), (5, -v[1]), (M - 4, v[0]), (M - 3, v[1]), (M - 2, v[0]), (M - 1, v[1])): X[..., c] = w
    both = np.sign(v[0] * v[1]) * 7; XR = 7 * sign((N, 8, 16, R)); XR[..., 0] = both; XR[..., R - 1] = -both
    twin = np.array([1, 2, 3, 4, 5, M - 2, M - 3, M // 2])
    ent = lambda shape: np.where(rng.random(shape) < 0.8, (M - 1) * rng.integers(0, 2, shape), twin[rng.integers(0, 8, shape)])
    for k in ("HC", "TC", "NH", "NT", "h", "t"): d[k] = ent(d[k].shape)
    p = np.where(rng.random((N, 8, L)) < 0.8, (R - 1) * rng.integers(0, 2, (N, 8, L)), rng.integers(0, R, (N, 8, L)))
    d["h"][..., L - 2:] = 0; d["t"][..., L - 2:] = M - 1; p[..., L - 1] = 0; p[..., L - 2] = R - 1
    kh = (37 * (R - 1) + M - 1) & (NC - 1); kt = (R - 1) & (NC - 1); kx = (M - 1) & (NC - 1)
    d["HC"][:, ::7, :, kh] = M - 4; d["NH"][:, ::7, :, 0, L - 2] = M - 4; d["TC"][:, ::7, :, kt] = M - 1; d["NT"][:, ::7, :, 0, L - 2] = M - 1
    d["HC"][:, 7, :14, kx] = 4; d["HC"][:, 7, 14, kx] = 3; d["HC"][:, 7, 15, kx] = 0; d["NH"][:, 7, :, 0, L - 1] = 4
    g = int(rng.integers(1, 7))
    d["E"][:, g] = mag(rng, (N, 16, M), 1.5, 2.0); d["E"][:, g, :, M - 1] = 2.0; d["ER"][:, g] = mag(rng, (N, 16, R), 0.75, 1.0); d["ER"][:, g, :, R - 1] = 1.0
    d["X"], d["XR"], d["p"] = X, XR, p
    return pack(d)
def setup_inputs_crowd(rng):
    d = parts(rng); o = rng.permutation(8); h, p, t = d["h"], d["p"], d["t"]; one = int(rng.integers(0, L))
    for g in (o[0], o[1]):
        for a in (h, p, t): a[:, g] = a[:, g, :1].copy()
    h[:, o[1], one] = (h[:, o[1], one] + 1 + rng.integers(0, M - 1, N)) % M; t[:, o[1], one] = (t[:, o[1], one] + 1 + rng.integers(0, NC - 1, N)) % M; p[:, o[1], one] = rng.integers(0, R, N)
    p[:, o[2]] = p[:, o[2], :1].copy(); t[:, o[2]] = t[:, o[2], :1] % NC + NC * rng.integers(0, M // NC, (N, L))
    for g in (o[3], o[4]):
        c = rng.choice(np.array([0, M - 1, M // 2, 17]), N)
        for k in ("HC", "TC"): d[k][:, g] = c[:, None, None]
        for k in ("NH", "NT"):
            keep = d[k][:, g, :, :, one].copy(); d[k][:, g] = c[:, None, None, None]
            if g == o[4]: d[k][:, g, :, :, one] = keep
    j = np.arange(L) & 1
    for a in (h, p, t): a[:, o[5]] = a[:, o[5]][:, j].copy()
    b = rng.integers(0, NC, (2, N, 1)); inv = pow(37, -1, NC)
    t[:, o[6]] = (b[0] - 37 * p[:, o[6]]) & (NC - 1); h[:, o[6]] = ((b[1] - p[:, o[6]]) * inv) & (NC - 1)
    return pack(d)
def setup_inputs_ties(rng):
    d = parts(rng); o = rng.permutation(8); X, XR = d["X"], d["XR"]
    X[:, o[:2]] = rng.integers(-1, 2, (N, 2, 16, M)); XR[:, o[:2]] = rng.integers(-1, 2, (N, 2, 16, R))
    XR[:, o[2]] = XR[:, o[2]] * (rng.random((N, 1, R)) < 0.5)
    g = o[3]; H = M // 2; X[:, g, :, H:] = X[:, g, :, :H].copy()
    for r in range(N):
        q = (r + D) % N; kh = (37 * d["p"][r, g] + d["t"][r, g]) & (NC - 1); kt = (37 * d["h"][r, g] + d["p"][r, g]) & (NC - 1)
        d["NH"][r, g, ::2, 0] = (d["HC"][r, g][:, kh][::2] + H) % M; d["NT"][q, g, ::2, 0] = (d["TC"][q, g][:, kt][::2] + H) % M
    for g in (o[4], o[5]):
        v = 2 * rng.integers(0, 2, (15, 1)) - 1
        X[:, g, :15] = 7 * v; XR[:, g, :15] = 7; XR[:, g, 15] = 2 * rng.integers(0, 2, (N, R)) - 1
    for k in ("HC", "TC"): d[k][:, o[6]] = d[k][:, o[6], :1].copy()
    return pack(d)
def setup_inputs_full(rng):
    d = parts(rng); kind = rng.permutation(8); sign = lambda shape: 2 * rng.integers(0, 2, shape) - 1; take = lambda a, i: np.take_along_axis(a, i, 2)
    w = 1 - 2 * (kind & 1); run = (kind >> 2) == 1; head = ((np.arange(N)[:, None] + ((kind >> 1) & 1)) & 1) == 0
    F = M - NC; dp = F + np.argsort(rng.random((N, 8, NC)), axis=-1); fp = np.argsort(rng.random((N, 8, F)), axis=-1)
    sg = np.ones((N, 8, M), np.int64); np.put_along_axis(sg, dp[..., NC // 2:], -1, 2); np.put_along_axis(sg, fp[..., F // 2:], -1, 2)
    v = sign((N, 8, 16)); X = 7 * v[..., None] * sg[:, :, None, :]; dent = np.arange(16)[:, None] == rng.integers(0, 16, (N, 8, 1, NC))
    X[..., F:] = np.where(dent, 6 * v[..., None] * sg[:, :, None, F:], X[..., F:])
    sp = sign((N, 8, R)); XR = 7 * (v * np.roll(v, -D, axis=0))[..., None] * sp[:, :, None, :]
    p = d["p"]; keys = np.argsort(rng.random((2, N, 8, NC)), axis=-1)[..., :L]; block = NC * rng.integers(0, M // NC - 1, (2, N, 8, L)); inv = pow(37, -1, NC)
    t = ((keys[0] - 37 * p) & (NC - 1)) + block[0]; h = (((keys[1] - p) * inv) & (NC - 1)) + block[1]
    cut = rng.random((N, 8, L)) < 0.3; cut[..., 0] = True
    first = np.maximum.accumulate(np.where(cut, np.arange(L), 0), axis=-1); own = np.where(run[None, :, None], first, np.arange(L)); up = (w > 0)[None, :, None]
    for tail in (0, 1):
        need = w[None, :, None] * take(sp, p) * take(np.roll(sg, -D * (1 - tail), axis=0), h if tail else t); neg = (need < 0).astype(np.int64); slot = own + L * tail
        dented = take(np.roll(dp, -D * tail, axis=0), slot + (NC // 2) * neg)
        whole = [take(np.roll(fp, -D * tail, axis=0), slot + 2 * L * e + (F // 2) * neg) for e in (0, 1)]
        good = [np.where(up, y, dented)[:, :, None, :] for y in whole]; poor = [np.where(up, dented, y)[:, :, None, :] for y in whole]
        star = np.arange(16)[:, None] == rng.integers(1, 16, (N, 8, 1, L)); m = rng.random((2, N, 8, 16, L)) < 0.2
        m[:, :, :, 0] = False; m[0] &= ~star; m[1] |= star; m &= (head == (tail == 0))[None, :, :, None, None]
        z = rng.integers(0, 2, (2, N, 8, 16, L)) == 1
        c = np.roll(np.where(m, np.where(z, good[1], good[0]), np.where(z, poor[1], poor[0])), D * tail, axis=1)
        k = np.roll(keys[tail], D * tail, axis=0)
        np.put_along_axis(d["TC" if tail else "HC"], np.broadcast_to(k[:, :, None, :], (N, 8, 16, L)), c[0], 3)
        d["NT" if tail else "NH"][:, :, :, 0] = c[1]
    d["X"], d["XR"], d["h"], d["t"] = X, XR, h, t
    return pack(d)
def check_ranges(d):
    bad = []
    for k, lo, hi in (("xe", -7, 7), ("xr", -7, 7), ("hc", 0, M - 1), ("tc", 0, M - 1), ("nh", 0, M - 1), ("nt", 0, M - 1), ("hl", 0, M - 1), ("rl", 0, R - 1), ("tl", 0, M - 1)):
        v = np.asarray(d[k]).astype(np.float64)
        if not np.all((v >= lo) & (v <= hi) & (v == np.rint(v))): bad.append("range of " + k)
    for k, hi in (("ee", 2.0), ("er", 1.0)):
        v = np.asarray(d[k]).astype(np.float64)
        if not np.all((v == 0) | ((v >= 2.0 ** -20) & (v <= hi))): bad.append("range of " + k)
        if k == "ee" and not np.all(v[:, ::16] >= 0.125): bad.append("least value of feature 0 in ee")
    return bad
def pick(tab, ix):
    return np.take_along_axis(tab, ix.reshape(8, 1, -1), 2)
def side(x, e, c, key, n, u, v):
    a = pick(c, key)
    score = lambda m: np.add.reduce(pick(x, m).reshape(8, 16, 16, L) * u[:, :, None, :], axis=1)
    sa, sn = score(a), score(n); won = sn > sa; a = np.where(won, n, a); s = np.where(won, sn, sa)
    ea = pick(e, a).reshape(8, 16, 16, L)
    w = np.reciprocal(1.0 + np.exp(-0.0625 * np.add.reduce(ea * v[:, :, None, :], axis=1))); G = np.add.reduce(w[:, None] * ea, axis=2)
    k = np.argmax(s, axis=1)[:, None, :]; best = lambda y: np.take_along_axis(y, k, 1)[:, 0]
    b = best(a); nx = np.clip(pick(x, b) - np.sign(u), -7, 7); ne = 0.875 * pick(e, b) + 0.125 * best(w)[:, None] * v
    return a, G, best(s), b, nx, ne
def put(tab, key, live, new):
    for g in range(8):
        lanes = np.nonzero(live[g])[0]; names, i = np.unique(key[g][lanes], return_index=True)
        tab[g][:, names] = new[g][:, lanes[i]]
def reference(xe, ee, xr, er, hc, tc, nh, nt, hl, rl, tl):
    whole = lambda y: y.astype(np.float32).astype(np.int64).reshape(N, 8, 16, -1)
    X, XR = whole(xe), whole(xr); E = ee.astype(np.float64).reshape(N, 8, 16, M); ER = er.astype(np.float64).reshape(N, 8, 16, R)
    HC = hc.astype(np.int64).reshape(N, 8, 16, NC); TC = tc.astype(np.int64).reshape(N, 8, 16, NC)
    NH = nh.astype(np.int64).reshape(N, 8, 16, S, L); NT = nt.astype(np.int64).reshape(N, 8, 16, S, L)
    h, p, t = [np.stack([gentries(a) for a in y]).astype(np.int64) for y in (hl, rl, tl)]
    yh = np.zeros((N, 8, 16, L)); yt = np.zeros((N, 8, 16, L)); every = np.ones((8, L), bool)
    for s in range(S):
        kh = (37 * p + t) & (NC - 1); kt = (37 * h + p) & (NC - 1); hs, ts = [], []
        for r in range(N):
            q = (r + D) % N
            xp, ep = pick(XR[r], p[r]), pick(ER[r], p[r])
            hs.append(side(X[r], E[r], HC[r], kh[r], NH[r][:, :, s], xp * pick(X[q], t[r]), ep * pick(E[q], t[r])))
            ts.append(side(X[q], E[q], TC[q], kt[r], NT[q][:, :, s], pick(X[r], h[r]) * xp, pick(E[r], h[r]) * ep))
            yh[r] += hs[r][1]; yt[q] += ts[r][1]
        if s == S - 1: break
        head = [hs[r][2] >= ts[r][2] for r in range(N)]
        for r in range(N):
            put(HC[r], kh[r], every, hs[r][0]); put(X[r], hs[r][3], head[r], hs[r][4]); put(E[r], hs[r][3], head[r], hs[r][5])
        for r in range(N):
            q = (r + D) % N
            put(TC[q], kt[r], every, ts[r][0]); put(X[q], ts[r][3], ~head[r], ts[r][4]); put(E[q], ts[r][3], ~head[r], ts[r][5])
            h[r] = np.where(head[r], hs[r][3], h[r]); t[r] = np.where(head[r], t[r], ts[r][3])
    return {"yh": yh.reshape(N, 128, L).astype(np.float32), "yt": yt.reshape(N, 128, L).astype(np.float32)}

def check_inputs(d):
    bad = list(check_ranges(d))
    if not bad:
        for name, y in reference(**d).items():
            for q in range(N):
                v = np.abs(np.asarray(y[q], np.float64)); s = np.sqrt(np.mean(v * v))
                if v.max() > 4 * s or s < 2.0 ** 2: bad.append('%s of rank %d is uneven or too small' % (name, q))
    return bad

@@ -1,0 +1,557 @@
+import math
+import numpy as np
+from concourse.bass import DstId, RemoteDMATransfer
+from concourse.mybir import AluOpType as ALU, ActivationFunctionType as ACT
+
+M, NK, L, D, NR = 4096, 1024, 192, 3, 8
+B, F, I, U = "bfloat16", "float32", "int32", "uint16"
+XCH = 32
+HILO = True
+SCRATCH, PLACE = {}, {}
+
+
+def _buf(names, cols, dtype, where="sbuf"):
+    for n in names.split():
+        if cols in (1, 24):
+            home = "SMALL_" + dtype
+            at = SCRATCH[home][1][1] if home in SCRATCH else 0
+            PLACE[n] = (home, at, cols); SCRATCH[home] = (where, [128, at + (16 if cols == 1 else 32)], dtype)
+        else:
+            SCRATCH[n] = (where, [128] + (list(cols) if isinstance(cols, tuple) else [cols]), dtype)
+
+
+_buf("X", M + L, B); _buf("E", M, B); _buf("E32", M + L, F); _buf("HC TC", NK + L, I); _buf("NN", 4 * L, I)
+_buf("XR XP", 72, B); _buf("LS LP", 36, I); _buf("MO MP", 2 * L, B)
+_buf("IP I1 I2 I3 I4", 1, I); _buf("JC GC K15 C1 C2 G192", 1, F)
+_buf("ID32 BO32", 128, F); _buf("IDB BO IOA IOB", 128, B); _buf("THR", 2 * L, F); _buf("RS16 RS32 MD IOC", 2 * L, B)
+_buf("RD RD0 RD1 IOD", 64, F); _buf("MK IOE THM IOF", 512, B); _buf("HALF WROW WD WS", L, F)
+_buf("AM", 1024, B); _buf("SEL IOG", 240, B); _buf("W64 A64", 128, F)
+_buf("SC24 SC12 SC48 PARI", 24, I); _buf("DUM0 DUMX DUMC C37 PARF", 24, F)
+_buf("CEXP CPERM CSIG CT8 CTR CBLK OP OQ OHT0 OHT1 OKEY0 OKEY1 OB OSX OSC", 24, U)
+_buf("KEY0 KT Q MI EXS INS EXK INK KK Z2", 24, I)
+_buf("HTF Z1 LV BS0 BS D0 D1 F1 F2 G1 G2 G3 KF", 24, F)
+_buf("UO0 UO1 U0 U1 SU E1 NX0 NX FLG FLS FLGK FLSK", 2 * L, B)
+_buf("VO0 VO1 V0 V1 V8 CF CS DD WDD AF OAA BD BSC PV WV EB SCS RM", 2 * L, F)
+_buf("VHL", 4 * L, B); _buf("BR16 KR16", 2 * L, U); _buf("OFF", 4 * L, U); _buf("OA OFN", 2 * L, U)
+_buf("UB", 16 * L, B); _buf("VB0 VB1", (2, 8 * L), B)
+_buf("XG", 64 * L, B); _buf("EA0", 32 * L, B)
+if HILO:
+    _buf("VC0 VC1", (2, 8 * L), B); _buf("EA1 EAL", 16 * L, B); _buf("EL", M + L, B); _buf("EN", 2 * L, F); _buf("ENH ENL", 2 * L, B); _buf("VHM", 4 * L, B)
+else:
+    _buf("VF", 16 * L, F); _buf("EA1", 32 * L, F)
+_buf("WN", 448, B); _buf("TT", 832, B); _buf("EQ", 2496, B)
+_buf("W", 1024, F); _buf("ET", 2048, F); _buf("GS0 GS1", (64, 24), F)
+_buf("PSC PL2 PMS PZ PE0 PE1 PE2 PG", 512, F, "psum")
+NDMA = 40
+SEMAPHORES = ["cv", "ca", "ct", "cg", "loc"] + ["d%d" % i for i in range(NDMA)] + ["r%d" % i for i in range(16)]
+
+
+def A(n, a=None, b=None, st=1, p=None):
+    n, at, w = PLACE[n] if n in PLACE else (n, 0, SCRATCH[n][1][1])
+    a = at + (0 if a is None else a)
+    b = at + (w if b is None else b)
+    ps = slice(0, 128) if p is None else slice(p[0], p[1])
+    return {"n": n, "ix": (ps, slice(a, b, st)), "lo": a, "hi": b, "cnt": len(range(a, b, st))}
+
+
+def A3(n, ix, cnt):
+    return {"n": n, "ix": ix, "lo": 0, "hi": 1 << 20, "cnt": cnt}
+
+
+def IND(win, off):
+    return {"n": win["n"], "ix": win["ix"], "lo": win["lo"], "hi": win["hi"], "off": off, "cnt": 16 * off["cnt"]}
+
+
+def two(*aps):
+    return all(SCRATCH[a["n"]][2] in (B, U) for a in aps)
+
+
+def psum(a):
+    return SCRATCH[a["n"]][0] == "psum"
+
+
+CASES = [(1.0, 0.5, 1.45, 3.4, 6, 120, 2000), (0.9, 0.45, 1.1, 2.2, 4, 80, 1600), (1.15, 0.75, 1.9, 4.5, 10, 200, 2600)]
+USCAT = {(0, 0): True, (0, 1): True, (1, 0): False, (1, 1): False}
+
+
+def build(case):
+    CY, PECY, GAT, SCA, MMI, WAKE, DML = case
+    ops = []
+
+    def add(eng, kind, args, rd, wr, cost, lat=0.0):
+        r = []
+        for a in rd:
+            if isinstance(a, dict):
+                r.append(a)
+                if "off" in a: r.append(a["off"])
+        for a in wr:
+            if "off" in a: r.append(a["off"])
+        ops.append({"eng": eng, "kind": kind, "args": args, "rd": r, "wr": list(wr), "cost": cost, "lat": lat})
+
+    def vc(out, ins, c):
+        n = out["cnt"]
+        if "off" in out: return 60 + n * SCA
+        if "off" in ins[0]: return 60 + n * GAT
+        return 30 + max(64, n * c) * CY
+
+    def cp(out, a, eng="v", scale=None, bias=None):
+        c = {"v": vc(out, [a], 0.5 if two(out, a) else 1)}
+        if eng == "va": c["a"] = 70 + out["cnt"] * (GAT if "off" in a else CY)
+        add(eng, "cp", (out, a, scale, bias), [a, bias], [out], c)
+
+    def ts(out, a, s1, op0, s2=None, op1=None):
+        add("v", "ts", (out, a, s1, s2, op0, op1), [a, s1, s2], [out], {"v": vc(out, [a], 0.5 if two(out, a) else 1)})
+
+    def tt(out, a, b, op):
+        add("v", "tt", (out, a, b, op), [a, b], [out], {"v": vc(out, [a], 1 if psum(a) or psum(b) else 2)})
+
+    def scan(out, d0, d1, init, op0, op1):
+        add("v", "scan", (out, d0, d1, init, op0, op1), [d0, d1], [out], {"v": vc(out, [d0], 0.5 if two(out, d0, d1) else 1)})
+
+    def tr(out, a):
+        add("v", "tr", (out, a), [a], [out], {"v": vc(out, [a], 0.5)})
+
+    def ms(out, val):
+        add("v", "ms", (out, val), [], [out], {"v": vc(out, [out], 0.5 if two(out) else 1)})
+
+    def act(out, a, func, scale=1.0):
+        add("a", "act", (out, a, func, scale), [a], [out], {"a": 70 + out["cnt"] * CY})
+
+    def iota(out, pat, base=0, chm=0):
+        add("g", "iota", (out, pat, base, chm), [], [out], {"g": 160 + 2 * out["cnt"] * CY})
+
+    def mm(lst):
+        c = sum(max(min(64, x[1]["cnt"]), x[2]["cnt"]) * (4 if SCRATCH[x[1]["n"]][2] == F else 1) * PECY + MMI for x in lst)
+        add("t", "mm", lst, [x[1] for x in lst] + [x[2] for x in lst], [x[0] for x in lst], {"t": c}, 60)
+
+    def dma(q, pairs, kb):
+        add(q, "dma", pairs, [x[1] for x in pairs], [x[0] for x in pairs if isinstance(x[0], dict)], {q: (700 if q == "g" else 70) * len(pairs)}, DML + 215 * kb)
+
+    def send(pairs, kb):
+        add("g", "send", pairs, [x[1] for x in pairs], [x[0] for x in pairs], {"g": 400}, DML + 215 * kb)
+
+    H = lambda n, d, w=L: A(n, d * w, d * w + w)
+    full = (slice(0, 128), slice(None))
+    dma("s", [(A("LS", 0, 12), ("hl", full)), (A("LS", 12, 24), ("rl", full)), (A("LS", 24, 36), ("tl", full))], 0)
+    dma("a", [(A("X", 0, M), ("xe", full))], 9)
+    dma("s", [(A("XR", 0, 32), ("xr", full)), (A("XR", 32, 64), ("er", full))], 0)
+    dma("s", [(A("TC", 0, NK), ("tc", full)), (A("NN", 2 * L, 4 * L), ("nt", full))], 12)
+    dma("s", [(A("HC", 0, NK), ("hc", full)), (A("NN", 0, 2 * L), ("nh", full))], 16)
+    dma("s", [(A("E"), ("ee", full))], 20)
+    ms(A("XR", 64, 72), 0.0)
+    send([(A("LP"), A("LS"), 1), (A("XP"), A("XR"), 1)], 4)
+    iota(A("IP"), [[0, 1]], 0, 1)
+    ts(A("I1"), A("IP"), 15, ALU.bitwise_and); cp(A("JC"), A("I1")); ts(A("K15"), A("JC"), -1.0, ALU.mult, 15.0, ALU.add)
+    ts(A("I2"), A("IP"), 4, ALU.arith_shift_right); cp(A("GC"), A("I2"))
+    iota(A("SC24"), [[1, 24]]); cp(A("CEXP"), A("SC24"))
+    iota(A("IOC"), [[0, 24], [1, 16]]); ts(A("MD"), A("IOC"), A("JC"), ALU.is_equal)
+    iota(A("IOA"), [[1, 128]], 0, -1); ts(A("ID32"), A("IOA"), 0.0, ALU.is_equal); ts(A("IDB"), A("IOA"), 0.0, ALU.is_equal)
+    iota(A("IOB"), [[1, 8], [0, 16]]); ts(A("BO32"), A("IOB"), A("GC"), ALU.is_equal); ts(A("BO"), A("IOB"), A("GC"), ALU.is_equal)
+    iota(A("IOD"), [[-32, 4], [-1, 16]], 0, 1)
+    ts(A("RD0"), A("IOD"), 0.0, ALU.is_equal); ts(A("RD1"), A("IOD"), 16.0, ALU.is_equal); tt(A("RD"), A("RD1"), A("RD0"), ALU.subtract)
+    iota(A("IOE"), [[0, 64], [1, 8]]); ts(A("MK"), A("IOE"), A("GC"), ALU.not_equal, -256.0, ALU.mult)
+    iota(A("IOF"), [[0, 8], [1, 8], [0, 8]]); ts(A("THM"), A("IOF"), A("GC"), ALU.not_equal, 32768.0, ALU.mult)
+    iota(A("IOG"), [[1, 240]], -112); ts(A("SEL"), A("IOG"), A("JC"), ALU.is_equal)
+    ms(A("UB", 0, 768), 0.0)
+    for j in (1, 2, 3): cp(H("UB", j, 768), A("UB", 0, 768), "va")
+    ms(A("WN"), 0.0)
+    ms(A("RS32"), 0.0); ms(A("RS32", 0, None, 32), -1e6); ms(A("RS16"), 1.0); ms(A("RS16", 0, None, 16), 0.0)
+    ms(A("HALF"), 0.70710678); scan(A("WROW"), A("HALF"), A("HALF"), 2.0 ** 96, ALU.mult, ALU.mult)
+    tt(A("WD"), A("WROW"), A("MD", 0, L), ALU.mult); scan(A("WS"), A("RS16", 0, L), A("WD"), 0.0, ALU.mult, ALU.add)
+    for d in (0, 1): cp(H("THR", d), A("WD"), "va", 2.5)
+    iota(A("SC12"), [[0, 2], [16, 12]]); ts(A("DUM0"), A("SC12"), A("JC"), ALU.add)
+    ts(A("DUMX"), A("DUM0"), float(M), ALU.add); ts(A("DUMC"), A("DUM0"), float(NK), ALU.add)
+    ts(A("PARI"), A("SC24"), A("GC"), ALU.add); ts(A("PARI"), A("PARI"), 1, ALU.bitwise_and); ts(A("PARF"), A("PARI"), 208.0, ALU.mult)
+    tt(A("PARF"), A("PARF"), A("DUM0"), ALU.add); cp(A("CTR"), A("PARF"))
+    ts(A("I3"), A("IP"), 7, ALU.bitwise_and); ts(A("I4"), A("IP"), 3, ALU.arith_shift_right, 1, ALU.bitwise_and)
+    ts(A("C1"), A("I3"), 24.0, ALU.mult); tt(A("C1"), A("C1"), A("I4"), ALU.add); ts(A("CPERM"), A("SC24"), 2.0, ALU.mult, A("C1"), ALU.add)
+    ts(A("C2"), A("I4"), 24.0, ALU.mult); tt(A("C2"), A("C2"), A("I3"), ALU.add)
+    iota(A("SC48", 0, 12), [[8, 3], [48, 4]]); ts(A("CSIG", 0, 12), A("SC48", 0, 12), A("C2"), ALU.add)
+    ts(A("C2"), A("I3"), 8.0, ALU.mult); tt(A("C2"), A("C2"), A("I4"), ALU.add); ts(A("CT8"), A("SC24"), 2.0, ALU.mult, A("C2"), ALU.add)
+    ts(A("G192"), A("GC"), float(L), ALU.mult); ts(A("CBLK"), A("DUM0"), A("G192"), ALU.add)
+    ms(A("C37", 0, 12), 37.0); ms(A("C37", 12, 24), 1.0)
+    cp(A("OP", 0, 12), A("LS", 12, 24)); ts(A("OP", 12, 24), A("LS", 12, 24), 32.0, ALU.add)
+    cp(A("OQ", 0, 12), A("LP", 12, 24)); ts(A("OQ", 12, 24), A("LP", 12, 24), 32.0, ALU.add)
+    cp(A("MO"), IND(A("XR", 0, 64), A("OP")), "va"); cp(A("MP"), IND(A("XP", 0, 64), A("OQ")), "va")
+    ts(A("KT", 0, 12), A("LS", 12, 24), 37.0, ALU.mult); tt(A("KT", 0, 12), A("KT", 0, 12), A("LS", 24, 36), ALU.add)
+    ts(A("KT", 12, 24), A("LP", 0, 12), 37.0, ALU.mult); tt(A("KT", 12, 24), A("KT", 12, 24), A("LP", 12, 24), ALU.add)
+    for d in (0, 1):
+        ts(H("KEY0", d, 12), H("KT", d, 12), NK - 1, ALU.bitwise_and); cp(H("OKEY0", d, 12), H("KEY0", d, 12))
+    cp(A("OHT0", 0, 12), A("LS", 0, 12)); cp(A("OHT0", 12, 24), A("LP", 24, 36))
+    cp(A("HTF", 0, 12), A("LS", 0, 12)); cp(A("HTF", 12, 24), A("LP", 24, 36))
+    cp(A("Q", 0, 12), A("LS", 12, 24)); ts(A("Q", 12, 24), A("LP", 12, 24), 37.0, ALU.mult)
+
+    def uv(s):
+        o = "OHT%d" % s
+        for d in (0, 1): tt(H("UO%d" % s, d), IND(A("X", 0, M), H(o, d, 12)), A(("MO", "MP")[d], 0, L), ALU.mult)
+        pair = [(H("U%d" % s, 1), H("UO%d" % s, 0), 1), (H("U%d" % s, 0), H("UO%d" % s, 1), -1)]
+        if s == 0: send(pair[:1], 0.5); send(pair[1:], 0.5)
+        else: send(pair, 1)
+        for d in (0, 1): tt(H("VO%d" % s, d), IND(A(("E", "E32")[s], 0, M), H(o, d, 12)), A(("MO", "MP")[d], L, 2 * L), ALU.mult)
+        send([(H("V%d" % s, 1), H("VO%d" % s, 0), 1), (H("V%d" % s, 0), H("VO%d" % s, 1), -1)], 2)
+
+    def ublock(s, d):
+        if USCAT[s, d]:
+            return cp(IND(H("UB", d, 8 * L), A("CBLK", 0, 12)), H("U%d" % s, d))
+        dma("s", [(A("UB", (8 * d + g) * L, (8 * d + g + 1) * L, 1, (16 * g, 16 * g + 16)), A("U%d" % s, d * L, d * L + L, 1, (16 * g, 16 * g + 16))) for g in range(8)], 0.5)
+
+    def vblock(s, d):
+        if s == 0 or HILO:
+            hl, v = ("VHL", "VHM")[s], H("V%d" % s, d)
+            cp(A(hl, 2 * d * L, 2 * d * L + L), v, "va")
+            tt(A(hl, 2 * d * L + L, 2 * d * L + 2 * L), v, A(hl, 2 * d * L, 2 * d * L + L), ALU.subtract)
+            dma("s", [(A3("V%s%d" % ("BC"[s], d), (slice(16 * g, 16 * g + 16), slice(None), slice(g * L, g * L + L)), 2 * L), A(hl, 2 * d * L, 2 * d * L + 2 * L, 1, (16 * g, 16 * g + 16))) for g in range(8)], 1)
+        else:
+            dma("s", [(A("VF", (8 * d + g) * L, (8 * d + g + 1) * L, 1, (16 * g, 16 * g + 16)), A("V1", d * L, d * L + L, 1, (16 * g, 16 * g + 16))) for g in range(8)], 1)
+
+    def lists(s, d):
+        ent = A("NN", (2 * d + s) * L, (2 * d + s + 1) * L)
+        cp(H("CF", d), IND(A(("HC", "TC")[d], 0, NK), H("OKEY%d" % s, d, 12)))
+        if s == 0:
+            cp(A("OFF", 2 * d * L + 1, 2 * d * L + 2 * L, 2), ent)
+            cp(A("OFF", 2 * d * L, 2 * d * L + 2 * L, 2), H("CF", d))
+            tt(H("DD", d), ent, H("CF", d), ALU.subtract)
+        else:
+            cp(H("OFN", d), IND(ent, A("CPERM", 0, 12)))
+            cp(H("OFF", d), IND(H("CF", d), A("CPERM", 0, 12)))
+            cp(H("CS", d), IND(H("CF", d), A("CSIG", 0, 12)), "va")
+            tt(H("DD", d), IND(ent, A("CSIG", 0, 12)), H("CS", d), ALU.subtract)
+
+    def contest(s, d):
+        sc = "PSC"
+        for l0 in range(0, L, XCH):
+            x0 = 32 * (d * L + l0)
+            cp(A("XG", x0, x0 + 32 * XCH), IND(A("X", 0, M), A("OFF", 2 * (d * L + l0), 2 * (d * L + l0 + XCH))), "va")
+            lst = []
+            for l in range(l0, l0 + XCH):
+                c, j16 = divmod(l, 16); j, q = divmod(c, 4)
+                lst.append((A(sc, 128 * j + j16, 128 * j + 128, 16, (32 * q, 32 * q + 32)), A("XG", 32 * (d * L + l), 32 * (d * L + l) + 32),
+                            A("UB", 8 * d * L + l, 8 * d * L + 8 * L, L), True, True))
+            mm(lst)
+        cp(A("SCS"), A(sc, 0, 384), "va", 16.0, A("K15"))
+        mm([(A("PMS", 64 * j, 64 * j + 64), A("SCS", 128 * j, 128 * j + 128), A("RD"), True, True) for j in range(3)])
+        if s == 0: mm([(A("PL2", 128 * j, 128 * j + 128), A("SCS", 128 * j, 128 * j + 128), A("ID32"), True, True) for j in range(3)])
+        w0, t0 = 224 * d, 416 * d
+        ts(A("WN", w0 + 16, w0 + 208), A("PMS", 0, L), 0.0, ALU.is_gt)
+        if s == 0:
+            scan(A("RM"), A("RS32"), A("PL2", 0, 384), 0.0, ALU.add, ALU.max); cp(H("MI", d, 12), A("RM", 31, None, 32))
+        tr(A("TT", t0, t0 + L), A("WN", w0 + 16, w0 + 208)); tr(A("TT", t0 + L, t0 + 416), A("WN", w0, w0 + 224))
+        tt(H("WDD", d), IND(A("TT", t0, t0 + 416), A("CTR", 0, 12)), H("DD", d), ALU.mult)
+        tt(H("AF", d), H("WDD", d), H("CF", d), ALU.add)
+        cp(H("OA", d), IND(H("AF", d), A("CPERM", 0, 12)))
+
+    ring = [0, 0, 0]
+
+    def duel(d, ch):
+        xc = 32 * d * L + 1024 * ch; xn = xc + 16 * L; o0 = d * L + 64 * ch; b = ring[2] % 2; ring[2] += 1; bank = ("PSC", "PL2")[b]
+        cp(A("XG", xn, xn + 1024), IND(A("X", 0, M), A("OFN", o0, o0 + 64)), "va")
+        cp(A("XG", xc, xc + 1024), IND(A("X", 0, M), A("OFF", o0, o0 + 64)), "va", -1.0)
+        lst = []
+        for t8 in range(8):
+            for n, x0 in enumerate((xn, xc)):
+                lst.append((A(bank, t8, 512, 8), A("XG", x0 + 128 * t8, x0 + 128 * t8 + 128), A("UB", 8 * d * L + 8 * ch + t8, 8 * d * L + 8 * L, 24), n == 0, n == 1))
+        mm(lst)
+        tt(H("AM", b, 512), A(bank), A("THM"), ALU.is_gt)
+        mm([(A("PMS", 0, 64), A("SEL", 112 - 16 * g, 240 - 16 * g), A("AM", 512 * b + 64 * g, 512 * b + 64 * g + 64), g == 0, g == 7) for g in range(8)])
+        tt(H("W64", b, 64), A("PMS", 0, 64), A("DD", o0, o0 + 64), ALU.mult)
+        tt(H("A64", b, 64), H("W64", b, 64), A("CS", o0, o0 + 64), ALU.add)
+        cp(A("OA", o0, o0 + 64), IND(H("A64", b, 64), A("CT8", 0, 4)))
+
+    def output(s, d):
+        ea, src, gs = "EA%d" % s, ("E", "E32")[s], "GS%d" % d
+        for ch in range(3):
+            if s == 1: duel(d, ch)
+            e0 = (0 if s == 1 and HILO else 16 * d * L) + 1024 * ch; wb = ring[1] % 2; ring[1] += 1
+            cp(A(ea, e0, e0 + 1024), IND(A(src, 0, M), A("OA", d * L + 64 * ch, d * L + 64 * ch + 64)), "va")
+            low = s == 1 and HILO
+            if low: cp(A("EAL", e0, e0 + 1024), IND(A("EL", 0, M), A("OA", d * L + 64 * ch, d * L + 64 * ch + 64)), "va")
+            lst = [(A("PZ"), A("BO"), A("MK"), True, False)]
+            for t8 in range(8):
+                t = 8 * ch + t8; lhs = A(ea, e0 + 128 * t8, e0 + 128 * t8 + 128)
+                if s == 0 or HILO:
+                    vb = lambda part: A3("V%s%d" % ("BC"[s], d), (slice(0, 128), part, slice(t, 8 * L, 24)), 64)
+                    if low: lst.append((A("PZ", 64 * t8, 64 * t8 + 64), A("EAL", e0 + 128 * t8, e0 + 128 * t8 + 128), vb(0), False, False))
+                    for part in (0, 1): lst.append((A("PZ", 64 * t8, 64 * t8 + 64), lhs, vb(part), False, t8 == 7 and part == 1))
+                else:
+                    lst.append((A("PZ", 64 * t8, 64 * t8 + 64), lhs, A("VF", 8 * d * L + t, 8 * d * L + 8 * L, 24), False, t8 == 7))
+            mm(lst)
+            act(A("W", 512 * wb, 512 * wb + 512), A("PZ"), ACT.Sigmoid, 0.0625)
+            for hf in (0, 1):
+                pe = "PE%d" % (ring[0] % 3); ring[0] += 1
+                parts = (ea, "EAL") if low else (ea,)
+                mm([(A(pe, 128 * i, 128 * i + 128), A(x, e0 + 512 * hf + 128 * i, e0 + 512 * hf + 128 * i + 128), A("IDB" if s == 0 or HILO else "ID32"), x == ea, x == parts[-1])
+                    for i in range(4) for x in parts])
+                cp(A("ET", 1024 * wb + 512 * hf, 1024 * wb + 512 * hf + 512), A(pe), "va")
+            mm([(A("PG", t8, 512, 8), A("ET", 1024 * wb + 128 * t8, 1024 * wb + 128 * t8 + 128), A("W", 512 * wb + 64 * t8, 512 * wb + 64 * t8 + 64), True, True) for t8 in range(8)])
+            o = {"n": gs, "ix": (slice(0, 128), slice(None), slice(8 * ch, 8 * ch + 8)), "lo": ch, "hi": ch + 1, "cnt": 512}
+            if s == 0: cp(o, A("PG"), "va")
+            else: tt(o, A("PG"), o, ALU.add)
+        if s == 1:
+            y = ("yh", "yt")[d]
+            for q in (0, 1):
+                dma("sa"[q], [((y, (slice(16 * g, 16 * g + 16), slice(None))), A3(gs, (slice(16 * g, 16 * g + 16), slice(8 * g, 8 * g + 8), slice(None)), L)) for g in range(4 * q, 4 * q + 4)], 0.5)
+
+    def first(rep, col, bank, tag):
+        for d in (0, 1):
+            lst, e0 = [], 1248 * d
+            for c in range(12):
+                n = L - 16 * c
+                ts(A("EQ", e0, e0 + n), A(rep, d * L + 16 * c, d * L + L), A(col, 12 * d + c, 12 * d + c + 1), ALU.is_equal, A("WS", 16 * c + 15, 16 * c + 16), ALU.mult)
+                lst.append((A(bank, d * L + 16 * c, d * L + L), A("BO"), A("EQ", e0, e0 + n), c == 0, c == 11)); e0 += n
+            mm(lst[:6]); mm(lst[6:])
+        tt(A("FLG" + tag), A(bank, 0, 2 * L), A("THR"), ALU.is_lt)
+        scan(A("FLS" + tag), A("RS16"), A("FLG" + tag), 0.0, ALU.mult, ALU.add)
+
+    uv(0)
+    for d in (0, 1): lists(0, d); ublock(0, d)
+    dma("g", [(A("E32", 0, M), ("ee", full))], 24)
+    whole = lambda n: A3(n, (slice(0, 128), slice(None), slice(None)), 16 * L)
+    if HILO:
+        for part in (0, 1): iota(A3("VC1", (slice(0, 128), part, slice(None)), 8 * L), [[0, 8 * L]])
+        for n in ("VB0", "VB1", "VC0"): dma("s", [(whole(n), whole("VC1"))], 6)
+        dma("s", [(A("EL", 0, 16 * L), whole("VC1")), (A("EL", 16 * L, M), A3("VC1", (slice(0, 128), 0, slice(0, M - 16 * L)), M - 16 * L))], 8)
+    else:
+        for d in (0, 1):
+            for part in (0, 1): iota(A3("VB%d" % d, (slice(0, 128), part, slice(None)), 8 * L), [[0, 8 * L]])
+        for d in (0, 1): iota(H("VF", d, 8 * L), [[0, 8 * L]])
+    cp(A("KF"), A("KEY0")); tt(A("BD"), IND(A("KF"), A("CEXP")), A("MD"), ALU.mult)
+    mm([(A("PG", 0, 2 * L), A("BO32"), A("BD"), True, True)]); cp(A("KR16"), A("PG", 0, 2 * L))
+    first("KR16", "KF", "PZ", "K")
+    tt(A("G3"), A("KF"), A("DUMC"), ALU.subtract); tt(A("G3"), A("G3"), A("FLSK", 15, None, 16), ALU.mult)
+    tt(A("G3"), A("G3"), A("DUMC"), ALU.add); cp(A("OSC"), A("G3"))
+    for d in (1, 0): contest(0, d); vblock(0, d)
+    ts(A("EXS"), A("MI"), 4, ALU.arith_shift_right)
+    send([(H("INS", 1, 12), H("EXS", 0, 12), 1), (H("INS", 0, 12), H("EXS", 1, 12), -1)], 0)
+    ts(A("KK"), A("MI"), 15, ALU.bitwise_and); tt(A("E1"), IND(A("KK"), A("CEXP")), A("MD"), ALU.mult)
+    mm([(A("PL2", 0, 2 * L), A("BO"), A("E1"), True, True)]); ts(A("PSC", 0, 2 * L), A("PL2", 0, 2 * L), A("K15"), ALU.is_equal)
+    tt(A("OAA"), A("PSC", 0, 2 * L), A("AF"), ALU.mult); mm([(A("PMS", 0, 2 * L), A("BO32"), A("OAA"), True, True)])
+    tt(A("BD"), A("PMS", 0, 2 * L), A("MD"), ALU.mult); cp(A("BR16"), A("PMS", 0, 2 * L))
+    scan(A("BSC"), A("RS16"), A("BD"), 0.0, ALU.mult, ALU.add)
+    BL = A("BSC", 15, None, 16)
+    cp(A("OB"), BL)
+    tt(A("Z1"), BL, A("C37"), ALU.mult); tt(A("Z2"), A("Z1"), A("Q"), ALU.add); ts(A("EXK"), A("Z2"), NK - 1, ALU.bitwise_and)
+    send([(H("INK", 1, 12), H("EXK", 0, 12), 1), (H("INK", 0, 12), H("EXK", 1, 12), -1)], 0)
+    for d in (0, 1): cp(IND(A(("HC", "TC")[d]), H("OSC", d, 12)), H("AF", d))
+    act(A("SU"), A("U0"), ACT.Sign); cp(A("V8"), A("V0"), "va", 0.125)
+    tt(A("NX0"), IND(A("X", 0, M), A("OB")), A("SU"), ALU.subtract); ts(A("NX"), A("NX0"), -7.0, ALU.max, 7.0, ALU.min)
+    tt(A("PV"), IND(A("E"), A("OB")), A("V0"), ALU.mult); mm([(A("PL2", 0, 2 * L), A("BO32"), A("PV"), True, True)])
+    act(A("PSC", 0, 2 * L), A("PL2", 0, 2 * L), ACT.Sigmoid, 0.0625); tt(A("WV"), A("PSC", 0, 2 * L), A("V8"), ALU.mult)
+    cp(A("EB"), IND(A("E"), A("OB")), "va", 0.875)
+    tt(A("LV", 0, 12), A("EXS", 0, 12), A("INS", 0, 12), ALU.is_ge); tt(A("LV", 12, 24), A("EXS", 12, 24), A("INS", 12, 24), ALU.is_gt)
+    ts(A("BS0"), A("LV"), -8192.0, ALU.mult, 8192.0, ALU.add); tt(A("BS"), A("BS0"), BL, ALU.add)
+    tt(A("D0"), BL, A("DUMX"), ALU.subtract); tt(A("D1"), A("D0"), A("LV"), ALU.mult)
+    first("BR16", "BS", "PMS", "")
+    tt(A("F1"), A("D1"), A("FLS", 15, None, 16), ALU.mult); tt(A("F2"), A("F1"), A("DUMX"), ALU.add); cp(A("OSX"), A("F2"))
+    tt(A("G1"), BL, A("HTF"), ALU.subtract); tt(A("G1"), A("G1"), A("LV"), ALU.mult); tt(A("G1"), A("G1"), A("HTF"), ALU.add); cp(A("OHT1"), A("G1"))
+    tt(A("G2"), A("KEY0"), A("INK"), ALU.subtract); tt(A("G2"), A("G2"), A("LV"), ALU.mult); tt(A("G2"), A("G2"), A("INK"), ALU.add); cp(A("OKEY1"), A("G2"))
+    for d in (1, 0): output(0, d)
+    for d in (0, 1): cp(IND(A("X"), H("OSX", d, 12)), H("NX", d))
+    for d in (0, 1): tt(IND(A("E32"), H("OSX", d, 12)), H("EB", d), H("WV", d), ALU.add)
+    if HILO:
+        tt(A("EN"), A("EB"), A("WV"), ALU.add); cp(A("ENH"), A("EN"), "va"); tt(A("ENL"), A("EN"), A("ENH"), ALU.subtract)
+        for d in (0, 1): cp(IND(A("EL"), H("OSX", d, 12)), H("ENL", d))
+    uv(1)
+    for d in (0, 1): lists(1, d); ublock(1, d); vblock(1, d)
+    for d in (0, 1): output(1, d)
+    return ops
+
+
+def hazards(ops):
+    hist = {}
+    for i, o in enumerate(ops):
+        deps = {}
+        acc = [(a, False) for a in o["rd"]] + [(a, True) for a in o["wr"]]
+        for a, w in acc:
+            ps = psum(a)
+            for j, lo, hi, w2 in hist.get(a["n"], []):
+                if ps or ((w or w2) and lo < a["hi"] and a["lo"] < hi):
+                    deps[j] = deps.get(j, False) or w or w2
+        for a, w in acc:
+            h = hist.setdefault(a["n"], [])
+            if psum(a): h[:] = [x for x in h if x[0] == i or (x[3] and not w)]
+            elif w: h[:] = [x for x in h if x[0] == i or not (a["lo"] <= x[1] and x[2] <= a["hi"] and a["cnt"] == a["hi"] - a["lo"] and "off" not in a and a["ix"][0] == slice(0, 128))]
+            if (i, a["lo"], a["hi"], w) not in h: h.append((i, a["lo"], a["hi"], w))
+        deps.pop(i, None)
+        o["deps"] = deps
+
+
+def replay(ops, deps, seq, eng, wake):
+    free = {q: 0.0 for q in "vatgs"}; done = [0.0] * len(ops)
+    for i in seq:
+        q = eng[i]; t = free[q]
+        for j in deps[i]:
+            if done[j] + wake > t and not (q == "t" and eng[j] == "t"): t = done[j] + wake
+        free[q] = t + ops[i]["cost"][q]; done[i] = free[q] + ops[i]["lat"]
+    return max(done)
+
+
+def schedule(ops, succ, bias, lean, WAKE):
+    n = len(ops)
+    pr = [0.0] * n
+    for i in range(n - 1, -1, -1):
+        o = ops[i]; pr[i] = min(o["cost"].values()) + o["lat"] + WAKE + max([pr[k] for k in succ[i]] or [0.0]) + bias[i]
+    busy = {q: [] for q in "vatgs"}; done = [0.0] * n; start = [0.0] * n; eng = [None] * n
+    for i in sorted(range(n), key=lambda i: -pr[i]):
+        pe = ops[i]["eng"] == "t"
+        rt = max([done[j] + (-60.0 if pe and eng[j] == "t" else WAKE) for j in ops[i]["deps"]] or [0.0]); best = None
+        for q, c in ops[i]["cost"].items():
+            t = rt
+            for a, b in busy[q]:
+                if t + c <= a: break
+                if b > t: t = b
+            f = t + c + (lean[i] if q == "v" else 0.0)
+            if best is None or f < best[0]: best = (f, t, q)
+        t, q = best[1], best[2]
+        start[i] = t; eng[i] = q; done[i] = t + ops[i]["cost"][q] + ops[i]["lat"]
+        busy[q].append((t, t + ops[i]["cost"][q])); busy[q].sort()
+    order = {q: sorted([i for i in range(n) if eng[i] == q], key=lambda i: start[i]) for q in busy}
+    return order, max(done), start, eng
+
+
+PLAN = {}
+
+
+ROUNDS, MOVES = 2500, 40000
+
+
+def plan():
+    if not PLAN:
+        all_ops = [build(c) for c in CASES]; ops = all_ops[0]; hazards(ops); n = len(ops)
+        deps = [list(o["deps"]) for o in ops]; succ = [[] for _ in ops]
+        for i in range(n):
+            for j in deps[i]: succ[j].append(i)
+        rng = np.random.default_rng(7); flex = [i for i in range(n) if ops[i]["eng"] == "va"]
+
+        def judge(bias, lean):
+            r = schedule(ops, succ, bias, lean, CASES[0][5]); seq = sorted(range(n), key=lambda i: (r[2][i], i))
+            ends = [replay(o, deps, seq, r[3], c[5]) for o, c in zip(all_ops, CASES)]
+            return sum(ends), r, ends
+
+        bias, lean = [0.0] * n, [1000.0] * n; best = judge(bias, lean)
+        for _ in range(ROUNDS):
+            b2, l2 = list(bias), list(lean)
+            for _k in range(int(rng.integers(1, 4))):
+                if rng.random() < 0.6: b2[int(rng.integers(0, n))] = float(rng.choice([0.0, 200.0, 1000.0, 3000.0, 8000.0]))
+                else: l2[flex[int(rng.integers(0, len(flex)))]] = float(rng.choice([-3000.0, 0.0, 500.0, 1500.0, 6000.0]))
+            r = judge(b2, l2)
+            if r[0] <= best[0]: best, bias, lean = r, b2, l2
+        seq = sorted(range(n), key=lambda i: (best[1][2][i], i)); eng = list(best[1][3])
+        tabs = [([o["cost"] for o in oo], [o["lat"] for o in oo], c[5]) for oo, c in zip(all_ops, CASES)]
+        dp = [[j for j in deps[i] if not (ops[i]["eng"] == "t" and ops[j]["eng"] == "t")] for i in range(n)]
+
+        def ends(seq, eng):
+            out = 0.0
+            for cost, lat, wake in tabs:
+                free = {"v": 0.0, "a": 0.0, "t": 0.0, "g": 0.0, "s": 0.0}; done = [0.0] * n
+                for i in seq:
+                    q = eng[i]; t = free[q]
+                    for j in dp[i]:
+                        if done[j] > t: t = done[j]
+                    t += cost[i][q]; free[q] = t; done[i] = t + lat[i] + wake
+                out += max(done)
+            return out
+
+        cur = top = ends(seq, eng); keep = (list(seq), list(eng)); draws = rng.random((MOVES, 4)).tolist()
+        for it, (r0, r1, r2, r3) in enumerate(draws):
+            s2, e2 = list(seq), eng
+            if r0 < 0.2:
+                i = flex[int(r1 * len(flex))]; e2 = list(eng); e2[i] = "a" if eng[i] == "v" else "v"
+            else:
+                p = int(r1 * n); i = s2.pop(p); lo, hi = p, p
+                while lo > 0 and p - lo < 60 and s2[lo - 1] not in ops[i]["deps"]: lo -= 1
+                while hi < n - 1 and hi - p < 60 and i not in ops[s2[hi]]["deps"]: hi += 1
+                s2.insert(lo + int(r2 * (hi - lo + 1)), i)
+            v = ends(s2, e2)
+            if v <= cur - 250.0 * (1.0 - it / MOVES) * math.log(r3 + 1e-12):
+                cur, seq, eng = v, s2, e2
+                if v < top: top, keep = v, (list(s2), list(e2))
+        seq, eng = keep
+        free = {q: 0.0 for q in "vatgs"}; done = [0.0] * n; start = [0.0] * n
+        for i in seq:
+            start[i] = max([free[eng[i]]] + [done[j] for j in dp[i]]); free[eng[i]] = start[i] + ops[i]["cost"][eng[i]]
+            done[i] = free[eng[i]] + ops[i]["lat"] + CASES[0][5]
+        PLAN.update(ops=ops, seq=seq, order={q: [i for i in seq if eng[i] == q] for q in free}, start=start, eng=eng,
+                    end=[replay(o, deps, seq, eng, c[5]) for o, c in zip(all_ops, CASES)])
+    return PLAN
+
+
+def rank_program(g, core, T, topo):
+    rank = T.rank_of(core)
+    if rank is None:
+        return
+    P = plan(); ops, eng, start = P["ops"], P["eng"], P["start"]
+    Q = {"v": g.vector, "a": g.scalar, "t": g.tensor, "g": g, "s": g.sync}
+    peer = {1: T.cores[(rank + D) % NR], -1: T.cores[(rank - D) % NR]}
+    back = {1: peer[-1], -1: peer[1]}
+
+    def ap(a):
+        if isinstance(a, tuple): return T[a[0]][a[1]]
+        if not isinstance(a, dict): return a
+        x = T[a["n"]][a["ix"]]
+        return x.indirect(ap(a["off"])) if "off" in a else x
+
+    def share(src, dst, k, n):
+        e = topo.engines(src, dst); m = len(e) // n
+        return e[k * m:(k + 1) * m]
+
+    seq = P["seq"]
+    count = {q: 0 for q in "vatg"}; nd = [0, 0, 0]; token = {}; known = {q: {} for q in Q}; snap = {}; total = {}
+
+    def wait(q, sem, val, src):
+        if known[q].get(sem, 0) < val:
+            Q[q].wait_ge(T.sem[sem], val); known[q][sem] = val
+        for s2, v2 in snap.get(src, {}).items():
+            if known[q].get(s2, 0) < v2: known[q][s2] = v2
+
+    for i in seq:
+        o, q = ops[i], eng[i]; e = Q[q]; k, x = o["kind"], o["args"]
+        for j in sorted(o["deps"], key=lambda j: -start[j]):
+            if eng[j] == q and ops[j]["kind"] not in ("dma", "send") and (q == "t" or not o["deps"][j]): continue
+            if ops[j]["kind"] == "send":
+                for land, sem, val in token[j]:
+                    if any(a["n"] == land["n"] and a["lo"] < land["hi"] and land["lo"] < a["hi"] for a in o["rd"]): wait(q, sem, val, None)
+            else:
+                wait(q, token[j][0], token[j][1], j)
+        snap[i] = dict(known[q])
+        if k == "send":
+            trs, token[i] = [], []
+            for n, (land, src, way) in enumerate(x):
+                sem = "r%d" % nd[1]; nd[1] += 1
+                mine = share(core, peer[way], n, len(x)); rid, pid = topo.addr(peer[way])[:2]
+                trs.append(RemoteDMATransfer(dst_ids=[DstId(rid=rid, pnc=pid)], dma_engine_mask=sum(1 << b for b in mine), remote_sem=T.sem[sem], src=ap(src), dst=ap(land)))
+                nd[2] += len(mine); val = len(share(back[way], core, n, len(x))); token[i].append((land, sem, val)); total[sem] = val
+            g.remote_dma_fused(trs, local_sem=T.sem.loc)
+            continue
+        if k == "dma":
+            sem = "d%d" % nd[0]; nd[0] += 1
+            for out, src in x: e.dma_start(ap(out), ap(src)).then_inc(T.sem[sem], 16)
+            token[i] = (sem, 16 * len(x)); total[sem] = 16 * len(x)
+            continue
+        if k == "cp":
+            out, a, sc, bi = x
+            if q == "a":
+                if bi is None: r = e.activation(ap(out), ap(a), ACT.Copy, scale=1.0 if sc is None else sc)
+                else: r = e.activation(ap(out), ap(a), ACT.Identity, bias=ap(bi), scale=sc)
+            elif sc is None: r = e.tensor_copy(ap(out), ap(a))
+            elif bi is None: r = e.tensor_scalar(ap(out), ap(a), sc, None, ALU.mult)
+            else: r = e.tensor_scalar(ap(out), ap(a), sc, ap(bi), ALU.mult, ALU.add)
+        elif k == "ts":
+            if x[5] is None: r = e.tensor_scalar(ap(x[0]), ap(x[1]), ap(x[2]), None, x[4])
+            else: r = e.tensor_scalar(ap(x[0]), ap(x[1]), ap(x[2]), ap(x[3]), x[4], x[5])
+        elif k == "tt": r = e.tensor_tensor(ap(x[0]), ap(x[1]), ap(x[2]), x[3])
+        elif k == "scan": r = e.tensor_tensor_scan(ap(x[0]), ap(x[1]), ap(x[2]), x[3], x[4], x[5])
+        elif k == "tr": r = e.transpose(ap(x[0]), ap(x[1]))
+        elif k == "ms": r = e.memset(ap(x[0]), x[1])
+        elif k == "act": r = e.activation(ap(x[0]), ap(x[1]), x[2], scale=x[3])
+        elif k == "iota":
+            if SCRATCH[x[0]["n"]][2] == I: r = e.iota(ap(x[0]), x[1], x[2], x[3])
+            else: r = e.iota(ap(x[0]), x[1], x[2], x[3], allow_small_or_imprecise_dtypes=True)
+        else:
+            for out, a, b, s0, s1 in x: r = e.matmul(ap(out), ap(a), ap(b), s0, s1)
+        count[q] += 1; r.then_inc(T.sem["c" + q], 1); token[i] = ("c" + q, count[q]); total["c" + q] = count[q]
+    total["loc"] = nd[2]
+    seen = {}
+    for q in Q:
+        for s2, v2 in known[q].items(): seen[s2] = max(seen.get(s2, 0), v2)
+    for s2, v2 in total.items():
+        if seen.get(s2, 0) < v2: g.sync.wait_ge(T.sem[s2], v2)

@@ -5,8 +5,10 @@ from concourse.mybir import AluOpType as ALU, ActivationFunctionType as ACT
 
 M, NK, L, D, NR = 4096, 1024, 192, 3, 8
 B, F, I, U = "bfloat16", "float32", "int32", "uint16"
-XCH = 32
-HILO = True
+WIDE = (0, 1, 2, 3, 4)
+LAST = (4, 2, 2)
+QUICK = 2
+ONV = ((2, 6, 8, 10), (2,))
 SCRATCH, PLACE = {}, {}
 
 
@@ -21,45 +23,45 @@ def _buf(names, cols, dtype, where="sbuf"):
 
 
 _buf("X", M + L, B); _buf("E", M, B); _buf("E32", M + L, F); _buf("HC TC", NK + L, I); _buf("NN", 4 * L, I)
-_buf("XR XP", 72, B); _buf("LS LP", 36, I); _buf("MO MP", 2 * L, B)
-_buf("IP I1 I2 I3 I4", 1, I); _buf("JC GC K15 C1 C2 G192", 1, F)
-_buf("ID32 BO32", 128, F); _buf("IDB BO IOA IOB", 128, B); _buf("THR", 2 * L, F); _buf("RS16 RS32 MD IOC", 2 * L, B)
-_buf("RD RD0 RD1 IOD", 64, F); _buf("MK IOE THM IOF", 512, B); _buf("HALF WROW WD WS", L, F)
-_buf("AM", 1024, B); _buf("SEL IOG", 240, B); _buf("W64 A64", 128, F)
-_buf("SC24 SC12 SC48 PARI", 24, I); _buf("DUM0 DUMX DUMC C37 PARF", 24, F)
-_buf("CEXP CPERM CSIG CT8 CTR CBLK OP OQ OHT0 OHT1 OKEY0 OKEY1 OB OSX OSC", 24, U)
+_buf("XR XP", 72, B); _buf("LL", 72, I); _buf("MX ME", 2 * L, B)
+_buf("IP IN I1 I2 I3", 1, I); _buf("K15 KB0 KB1 G2 C1 C2", 1, F)
+_buf("ID32 BO32", 128, F); _buf("IDB BO TRI ONE HALF", 128, B); _buf("MK", 512, B); _buf("ZERO", 768, B); _buf("W32", 256, F); _buf("RD", 64, F)
+for _j, _n in enumerate(LAST): _buf("WQ%d" % _j, (16, 8 * _n), B)
+_buf("RS32 RSB MD NMD IOC", 2 * L, B); _buf("THM AM", 512, B); _buf("SEL IOG", 240, B); _buf("A64", 128, F)
+_buf("SC24 SC12 SCP SCC", 24, I); _buf("DUM0 DUMX DUMC C37 PARF", 24, F)
+_buf("CEXP CPERM CTR OP OQ OHT0 OHT1 OKEY0 OKEY1 OB OSX OSC", 24, U)
 _buf("KEY0 KT Q MI EXS INS EXK INK KK Z2", 24, I)
-_buf("HTF Z1 LV BS0 BS D0 D1 F1 F2 G1 G2 G3 KF", 24, F)
-_buf("UO0 UO1 U0 U1 SU E1 NX0 NX FLG FLS FLGK FLSK", 2 * L, B)
-_buf("VO0 VO1 V0 V1 V8 CF CS DD WDD AF OAA BD BSC PV WV EB SCS RM", 2 * L, F)
-_buf("VHL", 4 * L, B); _buf("BR16 KR16", 2 * L, U); _buf("OFF", 4 * L, U); _buf("OA OFN", 2 * L, U)
-_buf("UB", 16 * L, B); _buf("VB0 VB1", (2, 8 * L), B)
-_buf("XG", 64 * L, B); _buf("EA0", 32 * L, B)
-if HILO:
-    _buf("VC0 VC1", (2, 8 * L), B); _buf("EA1 EAL", 16 * L, B); _buf("EL", M + L, B); _buf("EN", 2 * L, F); _buf("ENH ENL", 2 * L, B); _buf("VHM", 4 * L, B)
-else:
-    _buf("VF", 16 * L, F); _buf("EA1", 32 * L, F)
-_buf("WN", 448, B); _buf("TT", 832, B); _buf("EQ", 2496, B)
-_buf("W", 1024, F); _buf("ET", 2048, F); _buf("GS0 GS1", (64, 24), F)
-_buf("PSC PL2 PMS PZ PE0 PE1 PE2 PG", 512, F, "psum")
+_buf("Z1 LV BS0 BS F1 F2 G1 G3 G4 KF", 24, F)
+_buf("UO0 UO1 U0 U1 SU E1 NX0 NX", 2 * L, B)
+_buf("VO0 VO1 V0 V1 DD WDD AF OAA BD BSC FS FSK PV WV EB SCS0 SCS1 RM0 RM1", 2 * L, F)
+_buf("VH0 VH1", 4 * L, B); _buf("BR16 KR16", 2 * L, U); _buf("OFN OFC", 4 * L, U); _buf("OA", 2 * L, U)
+_buf("UB", (16, L), B); _buf("VB0 VB1", (8, 2 * L), B); _buf("WB0 WB1", (48, 64), B); _buf("WC", (6, 256), B); _buf("WP", 256, B)
+_buf("XG", 64 * L, B); _buf("EA EL ET EU", 32 * L, B)
+_buf("WN", 448, B); _buf("TT", 832, B); _buf("EQ", (24, L), B); _buf("GS0 GS1", (2, L), F)
+_buf("S0 PZ", (8, 64), F, "psum"); _buf("S1 PG0 PG1", 512, F, "psum"); _buf("PG2", (4, 128), F, "psum"); _buf("PT0 PT1", 1024, B, "psum")
 NDMA = 40
 SEMAPHORES = ["cv", "ca", "ct", "cg", "loc"] + ["d%d" % i for i in range(NDMA)] + ["r%d" % i for i in range(16)]
 
 
-def A(n, a=None, b=None, st=1, p=None):
+def A(n, a=None, b=None, st=1, p=(0, 128)):
     n, at, w = PLACE[n] if n in PLACE else (n, 0, SCRATCH[n][1][1])
     a = at + (0 if a is None else a)
     b = at + (w if b is None else b)
-    ps = slice(0, 128) if p is None else slice(p[0], p[1])
-    return {"n": n, "ix": (ps, slice(a, b, st)), "lo": a, "hi": b, "cnt": len(range(a, b, st))}
+    return {"n": n, "ix": (slice(*p), slice(a, b, st)), "lo": a, "hi": b, "cnt": len(range(a, b, st)), "p": p, "st": st}
 
 
-def A3(n, ix, cnt):
-    return {"n": n, "ix": ix, "lo": 0, "hi": 1 << 20, "cnt": cnt}
+def A3(n, rows=None, cols=None, p=(0, 128)):
+    nr, w = SCRATCH[n][1][1:]
+    rows = (0, nr) if rows is None else rows
+    cols = (0, w) if cols is None else cols
+    r = range(rows, rows + 1) if isinstance(rows, int) else range(*rows)
+    c = range(cols, cols + 1) if isinstance(cols, int) else range(*cols)
+    ix = lambda x: x if isinstance(x, int) else slice(*x)
+    return {"n": n, "ix": (slice(*p), ix(rows), ix(cols)), "lo": r[0] * w + c[0], "hi": r[-1] * w + c[-1] + 1, "cnt": len(r) * len(c), "p": p}
 
 
 def IND(win, off):
-    return {"n": win["n"], "ix": win["ix"], "lo": win["lo"], "hi": win["hi"], "off": off, "cnt": 16 * off["cnt"]}
+    return dict(win, off=off, cnt=16 * off["cnt"])
 
 
 def two(*aps):
@@ -70,8 +72,7 @@ def psum(a):
     return SCRATCH[a["n"]][0] == "psum"
 
 
-CASES = [(1.0, 0.5, 1.45, 3.4, 6, 120, 2000), (0.9, 0.45, 1.1, 2.2, 4, 80, 1600), (1.15, 0.75, 1.9, 4.5, 10, 200, 2600)]
-USCAT = {(0, 0): True, (0, 1): True, (1, 0): False, (1, 1): False}
+CASES = [(1.0, 0.5, 1.55, 3.8, 4, 120, 2000), (0.87, 0.44, 1.1, 2.4, 2, 80, 1700), (1.2, 0.6, 2.3, 5.5, 5, 180, 2400)]
 
 
 def build(case):
@@ -80,6 +81,7 @@ def build(case):
 
     def add(eng, kind, args, rd, wr, cost, lat=0.0):
         r = []
+        if len(eng) > 1 and wr[0]["n"] not in ("ET", "EU"): eng = "".join(q for q in "gav" if q in eng)
         for a in rd:
             if isinstance(a, dict):
                 r.append(a)
@@ -95,8 +97,10 @@ def build(case):
         return 30 + max(64, n * c) * CY
 
     def cp(out, a, eng="v", scale=None, bias=None):
-        c = {"v": vc(out, [a], 0.5 if two(out, a) else 1)}
-        if eng == "va": c["a"] = 70 + out["cnt"] * (GAT if "off" in a else CY)
+        c = {}
+        if "v" in eng: c["v"] = vc(out, [a], 0.5 if two(out, a) else 1)
+        if "a" in eng: c["a"] = 70 + out["cnt"] * (GAT if "off" in a else CY)
+        if "g" in eng: c["g"] = 200 + 2 * out["cnt"] * CY
         add(eng, "cp", (out, a, scale, bias), [a, bias], [out], c)
 
     def ts(out, a, s1, op0, s2=None, op1=None):
@@ -117,12 +121,18 @@ def build(case):
     def act(out, a, func, scale=1.0):
         add("a", "act", (out, a, func, scale), [a], [out], {"a": 70 + out["cnt"] * CY})
 
+    def step(out, a):
+        add("va", "step", (out, a), [a], [out], {"v": vc(out, [a], 1), "a": 70 + out["cnt"] * CY})
+
     def iota(out, pat, base=0, chm=0):
         add("g", "iota", (out, pat, base, chm), [], [out], {"g": 160 + 2 * out["cnt"] * CY})
 
-    def mm(lst):
+    def sel(out, a, pat, op, fill, base=0, chm=0):
+        add("g", "sel", (out, a, pat, op, fill, base, chm), [a], [out], {"g": 200 + 2 * out["cnt"] * CY})
+
+    def mm(lst, kind="mm"):
         c = sum(max(min(64, x[1]["cnt"]), x[2]["cnt"]) * (4 if SCRATCH[x[1]["n"]][2] == F else 1) * PECY + MMI for x in lst)
-        add("t", "mm", lst, [x[1] for x in lst] + [x[2] for x in lst], [x[0] for x in lst], {"t": c}, 60)
+        add("t", kind, lst, [x[1] for x in lst] + [x[2] for x in lst], [x[0] for x in lst], {"t": c}, 60)
 
     def dma(q, pairs, kb):
         add(q, "dma", pairs, [x[1] for x in pairs], [x[0] for x in pairs if isinstance(x[0], dict)], {q: (700 if q == "g" else 70) * len(pairs)}, DML + 215 * kb)
@@ -130,229 +140,249 @@ def build(case):
     def send(pairs, kb):
         add("g", "send", pairs, [x[1] for x in pairs], [x[0] for x in pairs], {"g": 400}, DML + 215 * kb)
 
+    who = lambda s, j: "va" if j in ONV[s] else "av"
     H = lambda n, d, w=L: A(n, d * w, d * w + w)
     full = (slice(0, 128), slice(None))
-    dma("s", [(A("LS", 0, 12), ("hl", full)), (A("LS", 12, 24), ("rl", full)), (A("LS", 24, 36), ("tl", full))], 0)
-    dma("a", [(A("X", 0, M), ("xe", full))], 9)
+    grp = lambda g: (16 * g, 16 * g + 16)
+    quad = lambda q: (32 * q, 32 * q + 32)
+    S384 = A3("S0", (0, 6))
+    LT, LP, LH, PT, PP, PH = [A("LL", 12 * j, 12 * j + 12) for j in range(6)]
+    HT = A("LL", 24, 48)
+    ent = lambda s, d: H("NN", 2 * s + d)
+    nn = lambda s, d: (ent(s, d), (("nh", "nt")[d], (slice(0, 128), slice(s * L, s * L + L))))
+    dma("s", [(LT, ("tl", full)), (LP, ("rl", full)), (LH, ("hl", full))], 0)
     dma("s", [(A("XR", 0, 32), ("xr", full)), (A("XR", 32, 64), ("er", full))], 0)
-    dma("s", [(A("TC", 0, NK), ("tc", full)), (A("NN", 2 * L, 4 * L), ("nt", full))], 12)
-    dma("s", [(A("HC", 0, NK), ("hc", full)), (A("NN", 0, 2 * L), ("nh", full))], 16)
-    dma("s", [(A("E"), ("ee", full))], 20)
+    dma("s", [nn(0, 0), nn(0, 1)], 2)
+    dma("a", [(A("X", 0, M), ("xe", full))], 10)
+    dma("a", [(A("TC", 0, NK), ("tc", full))], 14)
+    dma("a", [(A("HC", 0, NK), ("hc", full))], 18)
+    dma("a", [nn(1, 0), nn(1, 1)], 20)
+    dma("a", [(A("E"), ("ee", full))], 28)
     ms(A("XR", 64, 72), 0.0)
-    send([(A("LP"), A("LS"), 1), (A("XP"), A("XR"), 1)], 4)
-    iota(A("IP"), [[0, 1]], 0, 1)
-    ts(A("I1"), A("IP"), 15, ALU.bitwise_and); cp(A("JC"), A("I1")); ts(A("K15"), A("JC"), -1.0, ALU.mult, 15.0, ALU.add)
-    ts(A("I2"), A("IP"), 4, ALU.arith_shift_right); cp(A("GC"), A("I2"))
+    send([(A("LL", 36, 72), A("LL", 0, 36), 1), (A("XP"), A("XR"), 1)], 4)
+    iota(A("IN"), [[0, 1]], 127, -1); ts(A("I1"), A("IN"), 15, ALU.bitwise_and); cp(A("K15"), A("I1"))
+    ts(A("I2"), A("IN"), 31, ALU.bitwise_and, 1, ALU.arith_shift_right); cp(A("KB1"), A("I2")); cp(A("KB0"), A("KB1"), "va", 1.0, 16.0)
+    iota(A("IP"), [[0, 1]], 0, 1); ts(A("I3"), A("IP"), 4, ALU.arith_shift_right, 1, ALU.bitwise_and); cp(A("G2"), A("I3"))
     iota(A("SC24"), [[1, 24]]); cp(A("CEXP"), A("SC24"))
-    iota(A("IOC"), [[0, 24], [1, 16]]); ts(A("MD"), A("IOC"), A("JC"), ALU.is_equal)
-    iota(A("IOA"), [[1, 128]], 0, -1); ts(A("ID32"), A("IOA"), 0.0, ALU.is_equal); ts(A("IDB"), A("IOA"), 0.0, ALU.is_equal)
-    iota(A("IOB"), [[1, 8], [0, 16]]); ts(A("BO32"), A("IOB"), A("GC"), ALU.is_equal); ts(A("BO"), A("IOB"), A("GC"), ALU.is_equal)
-    iota(A("IOD"), [[-32, 4], [-1, 16]], 0, 1)
-    ts(A("RD0"), A("IOD"), 0.0, ALU.is_equal); ts(A("RD1"), A("IOD"), 16.0, ALU.is_equal); tt(A("RD"), A("RD1"), A("RD0"), ALU.subtract)
-    iota(A("IOE"), [[0, 64], [1, 8]]); ts(A("MK"), A("IOE"), A("GC"), ALU.not_equal, -256.0, ALU.mult)
-    iota(A("IOF"), [[0, 8], [1, 8], [0, 8]]); ts(A("THM"), A("IOF"), A("GC"), ALU.not_equal, 32768.0, ALU.mult)
-    iota(A("IOG"), [[1, 240]], -112); ts(A("SEL"), A("IOG"), A("JC"), ALU.is_equal)
-    ms(A("UB", 0, 768), 0.0)
-    for j in (1, 2, 3): cp(H("UB", j, 768), A("UB", 0, 768), "va")
+    iota(A("IOC"), [[0, 24], [-1, 16]], 15); ts(A("MD"), A("IOC"), A("K15"), ALU.is_equal); ts(A("NMD"), A("IOC"), A("K15"), ALU.not_equal, 8192.0, ALU.mult)
+    iota(A("ONE"), [[0, 128]], 1)
+    sel(A("IDB"), A("ONE"), [[-1, 128]], ALU.is_equal, 0.0, 0, 1); cp(A("ID32"), A("IDB"), "ag")
+    sel(A("BO"), A("ONE"), [[-16, 8], [0, 16]], ALU.is_ge, 0.0, 0, 1); sel(A("BO"), A("BO"), [[16, 8], [0, 16]], ALU.is_ge, 0.0, 15, -1); cp(A("BO32"), A("BO"), "ag")
+    sel(A("TRI"), A("BO"), [[1, 128]], ALU.is_gt, 0.0, 0, -1)
+    sel(A("RD"), A("ONE", 0, 64), [[-32, 4], [-2, 16]], ALU.is_equal, 0.0, -1, 1); sel(A("RD"), A("RD"), [[-32, 4], [-2, 16]], ALU.not_equal, -1.0, 0, 1)
+    sel(A("HALF"), A("ONE"), [[0, 4], [1, 2], [0, 16]], ALU.is_equal, 0.0, 0, -1)
+    iota(A("MK"), [[0, 512]], -1024); sel(A("MK"), A("MK"), [[0, 32], [1, 2], [0, 8]], ALU.not_equal, 0.0, 0, -1)
+    iota(A("IOG"), [[-1, 240]], 127); ts(A("SEL"), A("IOG"), A("K15"), ALU.is_equal)
+    ms(A3("UB", (0, 4)), 0.0)
+    for j in (1, 2, 3): cp(A3("UB", (4 * j, 4 * j + 4)), A3("UB", (0, 4)), "va")
     ms(A("WN"), 0.0)
-    ms(A("RS32"), 0.0); ms(A("RS32", 0, None, 32), -1e6); ms(A("RS16"), 1.0); ms(A("RS16", 0, None, 16), 0.0)
-    ms(A("HALF"), 0.70710678); scan(A("WROW"), A("HALF"), A("HALF"), 2.0 ** 96, ALU.mult, ALU.mult)
-    tt(A("WD"), A("WROW"), A("MD", 0, L), ALU.mult); scan(A("WS"), A("RS16", 0, L), A("WD"), 0.0, ALU.mult, ALU.add)
-    for d in (0, 1): cp(H("THR", d), A("WD"), "va", 2.5)
-    iota(A("SC12"), [[0, 2], [16, 12]]); ts(A("DUM0"), A("SC12"), A("JC"), ALU.add)
-    ts(A("DUMX"), A("DUM0"), float(M), ALU.add); ts(A("DUMC"), A("DUM0"), float(NK), ALU.add)
-    ts(A("PARI"), A("SC24"), A("GC"), ALU.add); ts(A("PARI"), A("PARI"), 1, ALU.bitwise_and); ts(A("PARF"), A("PARI"), 208.0, ALU.mult)
-    tt(A("PARF"), A("PARF"), A("DUM0"), ALU.add); cp(A("CTR"), A("PARF"))
-    ts(A("I3"), A("IP"), 7, ALU.bitwise_and); ts(A("I4"), A("IP"), 3, ALU.arith_shift_right, 1, ALU.bitwise_and)
-    ts(A("C1"), A("I3"), 24.0, ALU.mult); tt(A("C1"), A("C1"), A("I4"), ALU.add); ts(A("CPERM"), A("SC24"), 2.0, ALU.mult, A("C1"), ALU.add)
-    ts(A("C2"), A("I4"), 24.0, ALU.mult); tt(A("C2"), A("C2"), A("I3"), ALU.add)
-    iota(A("SC48", 0, 12), [[8, 3], [48, 4]]); ts(A("CSIG", 0, 12), A("SC48", 0, 12), A("C2"), ALU.add)
-    ts(A("C2"), A("I3"), 8.0, ALU.mult); tt(A("C2"), A("C2"), A("I4"), ALU.add); ts(A("CT8"), A("SC24"), 2.0, ALU.mult, A("C2"), ALU.add)
-    ts(A("G192"), A("GC"), float(L), ALU.mult); ts(A("CBLK"), A("DUM0"), A("G192"), ALU.add)
-    ms(A("C37", 0, 12), 37.0); ms(A("C37", 12, 24), 1.0)
-    cp(A("OP", 0, 12), A("LS", 12, 24)); ts(A("OP", 12, 24), A("LS", 12, 24), 32.0, ALU.add)
-    cp(A("OQ", 0, 12), A("LP", 12, 24)); ts(A("OQ", 12, 24), A("LP", 12, 24), 32.0, ALU.add)
-    cp(A("MO"), IND(A("XR", 0, 64), A("OP")), "va"); cp(A("MP"), IND(A("XP", 0, 64), A("OQ")), "va")
-    ts(A("KT", 0, 12), A("LS", 12, 24), 37.0, ALU.mult); tt(A("KT", 0, 12), A("KT", 0, 12), A("LS", 24, 36), ALU.add)
-    ts(A("KT", 12, 24), A("LP", 0, 12), 37.0, ALU.mult); tt(A("KT", 12, 24), A("KT", 12, 24), A("LP", 12, 24), ALU.add)
+    sel(A("RS32"), A("WN", 0, 2 * L), [[0, 12], [1, 32]], ALU.not_equal, -1e6); sel(A("RSB"), A("WN", 0, 2 * L), [[0, 24], [1, 16]], ALU.not_equal, 16384.0)
+    iota(A("SC12"), [[0, 2], [16, 12]], 15); ts(A("DUM0"), A("SC12"), A("K15"), ALU.subtract)
+    cp(A("DUMX"), A("DUM0"), "va", 1.0, float(M)); cp(A("DUMC"), A("DUM0"), "va", 1.0, float(NK))
+    iota(A("SCP", 0, 12), [[0, 6], [1, 2]]); ts(A("PARF", 0, 12), A("SCP", 0, 12), A("G2"), ALU.not_equal, 208.0, ALU.mult)
+    tt(A("PARF", 0, 12), A("PARF", 0, 12), A("DUM0", 0, 12), ALU.add); cp(A("CTR", 0, 12), A("PARF", 0, 12))
+    ts(A("C1"), A("K15"), 7.5, ALU.is_lt, -63.0, ALU.mult); ts(A("C2"), A("K15"), -8.0, ALU.mult, A("C1"), ALU.add)
+    iota(A("SCC", 0, 12), [[64, 3], [2, 4]], 120); ts(A("CPERM", 0, 12), A("SCC", 0, 12), A("C2"), ALU.add)
+    iota(A("C37"), [[-36, 2], [0, 12]], 37)
+    cp(A("OP", 0, 12), LP); cp(A("OQ", 0, 12), PP)
+    for d in (0, 1):
+        cp(H("MX", d), IND(A(("XR", "XP")[d], 0, 32), A(("OP", "OQ")[d], 0, 12)), "va")
+        cp(H("ME", d), IND(A(("XR", "XP")[d], 32, 64), A(("OP", "OQ")[d], 0, 12)), "va", 0.125)
+    ts(A("KT", 0, 12), LP, 37.0, ALU.mult); tt(A("KT", 0, 12), A("KT", 0, 12), LT, ALU.add)
+    ts(A("KT", 12, 24), PH, 37.0, ALU.mult); tt(A("KT", 12, 24), A("KT", 12, 24), PP, ALU.add)
     for d in (0, 1):
         ts(H("KEY0", d, 12), H("KT", d, 12), NK - 1, ALU.bitwise_and); cp(H("OKEY0", d, 12), H("KEY0", d, 12))
-    cp(A("OHT0", 0, 12), A("LS", 0, 12)); cp(A("OHT0", 12, 24), A("LP", 24, 36))
-    cp(A("HTF", 0, 12), A("LS", 0, 12)); cp(A("HTF", 12, 24), A("LP", 24, 36))
-    cp(A("Q", 0, 12), A("LS", 12, 24)); ts(A("Q", 12, 24), A("LP", 12, 24), 37.0, ALU.mult)
+    cp(A("OHT0", 0, 12), LH); cp(A("OHT0", 12, 24), PT)
+    cp(A("Q", 0, 12), LP); ts(A("Q", 12, 24), PP, 37.0, ALU.mult)
+    swap = lambda land, src, w: [(H(land, 1, w), H(src, 0, w), 1), (H(land, 0, w), H(src, 1, w), -1)]
 
     def uv(s):
-        o = "OHT%d" % s
-        for d in (0, 1): tt(H("UO%d" % s, d), IND(A("X", 0, M), H(o, d, 12)), A(("MO", "MP")[d], 0, L), ALU.mult)
-        pair = [(H("U%d" % s, 1), H("UO%d" % s, 0), 1), (H("U%d" % s, 0), H("UO%d" % s, 1), -1)]
-        if s == 0: send(pair[:1], 0.5); send(pair[1:], 0.5)
-        else: send(pair, 1)
-        for d in (0, 1): tt(H("VO%d" % s, d), IND(A(("E", "E32")[s], 0, M), H(o, d, 12)), A(("MO", "MP")[d], L, 2 * L), ALU.mult)
-        send([(H("V%d" % s, 1), H("VO%d" % s, 0), 1), (H("V%d" % s, 0), H("VO%d" % s, 1), -1)], 2)
-
-    def ublock(s, d):
-        if USCAT[s, d]:
-            return cp(IND(H("UB", d, 8 * L), A("CBLK", 0, 12)), H("U%d" % s, d))
-        dma("s", [(A("UB", (8 * d + g) * L, (8 * d + g + 1) * L, 1, (16 * g, 16 * g + 16)), A("U%d" % s, d * L, d * L + L, 1, (16 * g, 16 * g + 16))) for g in range(8)], 0.5)
+        o = "OHT%d" % s; pair = swap("U%d" % s, "UO%d" % s, L)
+        if s == 0:
+            for d in (0, 1):
+                tt(H("UO0", d), IND(A("X", 0, M), H(o, d, 12)), H("MX", d), ALU.mult); send(pair[d:d + 1], 0.5)
+        else:
+            tt(A("UO1"), IND(A("X", 0, M), A(o)), A("MX"), ALU.mult); send(pair, 1)
+        tt(A("VO%d" % s), IND(A(("E", "E32")[s], 0, M), A(o)), A("ME"), ALU.mult)
+        send(swap("V%d" % s, "VO%d" % s, L), 2)
 
     def vblock(s, d):
-        if s == 0 or HILO:
-            hl, v = ("VHL", "VHM")[s], H("V%d" % s, d)
-            cp(A(hl, 2 * d * L, 2 * d * L + L), v, "va")
-            tt(A(hl, 2 * d * L + L, 2 * d * L + 2 * L), v, A(hl, 2 * d * L, 2 * d * L + L), ALU.subtract)
-            dma("s", [(A3("V%s%d" % ("BC"[s], d), (slice(16 * g, 16 * g + 16), slice(None), slice(g * L, g * L + L)), 2 * L), A(hl, 2 * d * L, 2 * d * L + 2 * L, 1, (16 * g, 16 * g + 16))) for g in range(8)], 1)
-        else:
-            dma("s", [(A("VF", (8 * d + g) * L, (8 * d + g + 1) * L, 1, (16 * g, 16 * g + 16)), A("V1", d * L, d * L + L, 1, (16 * g, 16 * g + 16))) for g in range(8)], 1)
+        hl, v = "VH%d" % s, H("V%d" % s, d)
+        cp(H(hl, 2 * d), v, "vag"); tt(H(hl, 2 * d + 1), v, H(hl, 2 * d), ALU.subtract)
+        dma("s", [(A3("VB%d" % d, 4 * (g % 2) + g // 2, None, grp(g)), A(hl, 2 * d * L, 2 * d * L + 2 * L, 1, grp(g))) for g in range(8)], 1)
 
     def lists(s, d):
-        ent = A("NN", (2 * d + s) * L, (2 * d + s + 1) * L)
-        cp(H("CF", d), IND(A(("HC", "TC")[d], 0, NK), H("OKEY%d" % s, d, 12)))
-        if s == 0:
-            cp(A("OFF", 2 * d * L + 1, 2 * d * L + 2 * L, 2), ent)
-            cp(A("OFF", 2 * d * L, 2 * d * L + 2 * L, 2), H("CF", d))
-            tt(H("DD", d), ent, H("CF", d), ALU.subtract)
-        else:
-            cp(H("OFN", d), IND(ent, A("CPERM", 0, 12)))
-            cp(H("OFF", d), IND(H("CF", d), A("CPERM", 0, 12)))
-            cp(H("CS", d), IND(H("CF", d), A("CSIG", 0, 12)), "va")
-            tt(H("DD", d), IND(ent, A("CSIG", 0, 12)), H("CS", d), ALU.subtract)
+        cand = IND(A(("HC", "TC")[d], 0, NK), H("OKEY%d" % s, d, 12))
+        cp(H("OFN", 2 * s + d), ent(s, d), "vg" if s else "v"); cp(H("OFC", 2 * s + d), cand)
+        tt(H("DD", d), cand, ent(s, d), ALU.subtract)
 
-    def contest(s, d):
-        sc = "PSC"
-        for l0 in range(0, L, XCH):
+    def contest(d):
+        sc, scs = "PG%d" % d, "SCS%d" % d
+        for l0 in range(0, L, 64):
             x0 = 32 * (d * L + l0)
-            cp(A("XG", x0, x0 + 32 * XCH), IND(A("X", 0, M), A("OFF", 2 * (d * L + l0), 2 * (d * L + l0 + XCH))), "va")
+            for part in (1, 0): cp(A("XG", x0 + part, x0 + 2048, 2), IND(A("X", 0, M), A(("OFC", "OFN")[part], d * L + l0, d * L + l0 + 64)), who(0, x0 // 1024 + part))
             lst = []
-            for l in range(l0, l0 + XCH):
+            for l in range(l0, l0 + 64):
                 c, j16 = divmod(l, 16); j, q = divmod(c, 4)
-                lst.append((A(sc, 128 * j + j16, 128 * j + 128, 16, (32 * q, 32 * q + 32)), A("XG", 32 * (d * L + l), 32 * (d * L + l) + 32),
-                            A("UB", 8 * d * L + l, 8 * d * L + 8 * L, L), True, True))
+                lst.append((A(sc, 128 * j + j16, 128 * j + 128, 16, quad(q)), A("XG", 32 * (d * L + l), 32 * (d * L + l) + 32),
+                            A3("UB", (8 * d, 8 * d + 8), l), True, True))
             mm(lst)
-        cp(A("SCS"), A(sc, 0, 384), "va", 16.0, A("K15"))
-        mm([(A("PMS", 64 * j, 64 * j + 64), A("SCS", 128 * j, 128 * j + 128), A("RD"), True, True) for j in range(3)])
-        if s == 0: mm([(A("PL2", 128 * j, 128 * j + 128), A("SCS", 128 * j, 128 * j + 128), A("ID32"), True, True) for j in range(3)])
+        cp(A(scs), A(sc, 0, 384), "va", 32.0, A("KB%d" % d))
+        mm([(H(sc, j, 128), A(scs, 128 * j, 128 * j + 128), A("ID32"), True, True) for j in range(3)])
+        mm([(A3("PZ", 3 * d + j), A(scs, 128 * j, 128 * j + 128), A("RD"), True, True) for j in range(3)])
         w0, t0 = 224 * d, 416 * d
-        ts(A("WN", w0 + 16, w0 + 208), A("PMS", 0, L), 0.0, ALU.is_gt)
-        if s == 0:
-            scan(A("RM"), A("RS32"), A("PL2", 0, 384), 0.0, ALU.add, ALU.max); cp(H("MI", d, 12), A("RM", 31, None, 32))
+        scan(A("RM%d" % d), A("RS32"), A(sc, 0, 384), 0.0, ALU.add, ALU.max); cp(H("MI", d, 12), A("RM%d" % d, 31, None, 32))
+        step(A("WN", w0 + 16, w0 + 208), A3("PZ", (3 * d, 3 * d + 3)))
         tr(A("TT", t0, t0 + L), A("WN", w0 + 16, w0 + 208)); tr(A("TT", t0 + L, t0 + 416), A("WN", w0, w0 + 224))
         tt(H("WDD", d), IND(A("TT", t0, t0 + 416), A("CTR", 0, 12)), H("DD", d), ALU.mult)
-        tt(H("AF", d), H("WDD", d), H("CF", d), ALU.add)
+        tt(H("AF", d), H("WDD", d), ent(0, d), ALU.add)
         cp(H("OA", d), IND(H("AF", d), A("CPERM", 0, 12)))
-
-    ring = [0, 0, 0]
+        p0, p1 = H(sc, 0), H(sc, 1)
+        ts(H("KK", d, 12), H("MI", d, 12), 15, ALU.bitwise_and); tt(H("E1", d), IND(A("KK"), H("CEXP", d, 12)), H("MD", d), ALU.mult)
+        mm([(p0, A("BO"), H("E1", d), True, True)]); ts(p0, p0, A("K15"), ALU.is_equal)
+        tt(H("OAA", d), p0, H("AF", d), ALU.mult); mm([(p1, A("BO32"), H("OAA", d), True, True)])
+        mm([(p0, A("IDB"), H("NMD", d), True, False), (p0, A("BO32"), H("OAA", d), False, True)])
+        cp(H("BR16", d), p1); scan(H("BSC", d), H("RSB", d), p0, 0.0, ALU.add, ALU.min)
 
     def duel(d, ch):
-        xc = 32 * d * L + 1024 * ch; xn = xc + 16 * L; o0 = d * L + 64 * ch; b = ring[2] % 2; ring[2] += 1; bank = ("PSC", "PL2")[b]
-        cp(A("XG", xn, xn + 1024), IND(A("X", 0, M), A("OFN", o0, o0 + 64)), "va")
-        cp(A("XG", xc, xc + 1024), IND(A("X", 0, M), A("OFF", o0, o0 + 64)), "va", -1.0)
+        xc = 32 * d * L + 1024 * ch; xn = xc + 16 * L; o0 = d * L + 64 * ch; b = ch % 2
+        cp(A("XG", xn, xn + 1024), IND(A("X", 0, M), A("OFN", 2 * L + o0, 2 * L + o0 + 64)), who(1, o0 // 32 + 1))
+        cp(A("XG", xc, xc + 1024), IND(A("X", 0, M), A("OFC", 2 * L + o0, 2 * L + o0 + 64)), who(1, o0 // 32), -1.0)
         lst = []
-        for t8 in range(8):
+        for t in range(8):
             for n, x0 in enumerate((xn, xc)):
-                lst.append((A(bank, t8, 512, 8), A("XG", x0 + 128 * t8, x0 + 128 * t8 + 128), A("UB", 8 * d * L + 8 * ch + t8, 8 * d * L + 8 * L, 24), n == 0, n == 1))
+                lst.append((A3("S0", None, (8 * t, 8 * t + 8)), A("XG", x0 + 128 * t, x0 + 128 * t + 128),
+                            A3("UB", (8 * d, 8 * d + 8), (64 * ch + 8 * t, 64 * ch + 8 * t + 8)), n == 0, n == 1))
         mm(lst)
-        tt(H("AM", b, 512), A(bank), A("THM"), ALU.is_gt)
-        mm([(A("PMS", 0, 64), A("SEL", 112 - 16 * g, 240 - 16 * g), A("AM", 512 * b + 64 * g, 512 * b + 64 * g + 64), g == 0, g == 7) for g in range(8)])
-        tt(H("W64", b, 64), A("PMS", 0, 64), A("DD", o0, o0 + 64), ALU.mult)
-        tt(H("A64", b, 64), H("W64", b, 64), A("CS", o0, o0 + 64), ALU.add)
-        cp(A("OA", o0, o0 + 64), IND(H("A64", b, 64), A("CT8", 0, 4)))
+        tt(A("AM"), A3("S0"), A("THM"), ALU.is_lt)
+        mm([(A("S1", 0, 64), A("SEL", 112 - 16 * g, 240 - 16 * g), H("AM", g, 64), g == 0, g == 7) for g in range(8)])
+        tt(A("S1", 64, 128), A("S1", 0, 64), A("DD", o0, o0 + 64), ALU.mult)
+        tt(H("A64", b, 64), A("S1", 64, 128), A("NN", 2 * L + o0, 2 * L + o0 + 64), ALU.add)
+        cp(A("OA", o0, o0 + 64), IND(H("A64", b, 64), A("CPERM", 0, 4)))
 
-    def output(s, d):
-        ea, src, gs = "EA%d" % s, ("E", "E32")[s], "GS%d" % d
-        for ch in range(3):
-            if s == 1: duel(d, ch)
-            e0 = (0 if s == 1 and HILO else 16 * d * L) + 1024 * ch; wb = ring[1] % 2; ring[1] += 1
-            cp(A(ea, e0, e0 + 1024), IND(A(src, 0, M), A("OA", d * L + 64 * ch, d * L + 64 * ch + 64)), "va")
-            low = s == 1 and HILO
-            if low: cp(A("EAL", e0, e0 + 1024), IND(A("EL", 0, M), A("OA", d * L + 64 * ch, d * L + 64 * ch + 64)), "va")
-            lst = [(A("PZ"), A("BO"), A("MK"), True, False)]
-            for t8 in range(8):
-                t = 8 * ch + t8; lhs = A(ea, e0 + 128 * t8, e0 + 128 * t8 + 128)
-                if s == 0 or HILO:
-                    vb = lambda part: A3("V%s%d" % ("BC"[s], d), (slice(0, 128), part, slice(t, 8 * L, 24)), 64)
-                    if low: lst.append((A("PZ", 64 * t8, 64 * t8 + 64), A("EAL", e0 + 128 * t8, e0 + 128 * t8 + 128), vb(0), False, False))
-                    for part in (0, 1): lst.append((A("PZ", 64 * t8, 64 * t8 + 64), lhs, vb(part), False, t8 == 7 and part == 1))
-                else:
-                    lst.append((A("PZ", 64 * t8, 64 * t8 + 64), lhs, A("VF", 8 * d * L + t, 8 * d * L + 8 * L, 24), False, t8 == 7))
+    ring = [0]
+
+    def turn(dst, src, e0, n):
+        bank = "PT%d" % (ring[0] % 2); ring[0] += 1
+        mm([(H(bank, t, 128), A(src, e0 + 128 * t, e0 + 128 * t + 128), A("IDB")) for t in range(n)], "trp")
+        cp(A(dst, e0, e0 + 128 * n), A(bank, 0, 128 * n), "va")
+
+    def ublock(s, d):
+        dma("s", [(A3("UB", 8 * d + g, None, grp(g)), A("U%d" % s, d * L, d * L + L, 1, grp(g))) for g in range(8)], 0.5)
+
+    def reals(s, c, wide, t0=0, n=8, j=None):
+        d, ch = divmod(c, 3); off = A("OA", 64 * c + 8 * t0, 64 * c + 8 * (t0 + n)); e0 = 1024 * c + 128 * t0; m = 128 if wide else 32
+        rows, w = ((0, 8) if wide else (2 * ch, 2 * ch + 2), 64) if j is None else ((j, j + 1), 16 * n)
+        ea, el = A("EA", e0, e0 + 128 * n), A("EL", e0, e0 + 128 * n)
+        cp(ea, IND(A(("E", "E32")[s], 0, M), off), "va")
+        if s: tt(el, IND(A("E32", 0, M), off), ea, ALU.subtract)
+        for k, (src, parts) in enumerate((("EA", (0, 1)), ("EL", (0,)))[:s + 1]):
+            lst = [] if k else [(A3("PZ", rows, (0, w)), A("HALF", p=(0, 2)), A("MK", 0, 4 * m, 8 // n, (0, 2)), True, False)]
+            for e in range(0, 128 * n, m):
+                t, p0 = divmod(e, 128)
+                for part in parts:
+                    l0 = part * L + 64 * ch + p0 // 2 + t0 + t
+                    lst.append((A3("PZ", rows, (t, w, n), (p0, p0 + m)), A(src, e0 + e, e0 + e + m), A3("VB%d" % d, None, (l0, l0 + m // 2 - 7, 8)), False,
+                                k == s and t == n - 1 and part == parts[-1]))
             mm(lst)
-            act(A("W", 512 * wb, 512 * wb + 512), A("PZ"), ACT.Sigmoid, 0.0625)
-            for hf in (0, 1):
-                pe = "PE%d" % (ring[0] % 3); ring[0] += 1
-                parts = (ea, "EAL") if low else (ea,)
-                mm([(A(pe, 128 * i, 128 * i + 128), A(x, e0 + 512 * hf + 128 * i, e0 + 512 * hf + 128 * i + 128), A("IDB" if s == 0 or HILO else "ID32"), x == ea, x == parts[-1])
-                    for i in range(4) for x in parts])
-                cp(A("ET", 1024 * wb + 512 * hf, 1024 * wb + 512 * hf + 512), A(pe), "va")
-            mm([(A("PG", t8, 512, 8), A("ET", 1024 * wb + 128 * t8, 1024 * wb + 128 * t8 + 128), A("W", 512 * wb + 64 * t8, 512 * wb + 64 * t8 + 64), True, True) for t8 in range(8)])
-            o = {"n": gs, "ix": (slice(0, 128), slice(None), slice(8 * ch, 8 * ch + 8)), "lo": ch, "hi": ch + 1, "cnt": 512}
-            if s == 0: cp(o, A("PG"), "va")
-            else: tt(o, A("PG"), o, ALU.add)
-        if s == 1:
-            y = ("yh", "yt")[d]
-            for q in (0, 1):
-                dma("sa"[q], [((y, (slice(16 * g, 16 * g + 16), slice(None))), A3(gs, (slice(16 * g, 16 * g + 16), slice(8 * g, 8 * g + 8), slice(None)), L)) for g in range(4 * q, 4 * q + 4)], 0.5)
+        turn("ET", "EA", e0, n)
+        if s: turn("EU", "EL", e0, n)
 
-    def first(rep, col, bank, tag):
+    def weights(c, nc, wide, t0=0, n=8, j=None, quick=False):
+        d, ch = divmod(c, 3)
+        if wide:
+            z = H("W32", c % 2, 128)
+            for q in range(4): act(A("W32", z["lo"], z["hi"], 1, quad(q)), A3("PZ", None, (16 * q, 16 * q + 16), quad(q)), ACT.Sigmoid, 0.5)
+        else:
+            z = A3("PZ", (2 * ch, 2 * (ch + nc))) if j is None else A3("PZ", j, (0, 16 * n)); act(z, z, ACT.Sigmoid, 0.5)
+        if j is None:
+            hi, lo = A3("WC", (c, c + nc), (0, 128)), A3("WC", (c, c + nc), (128, 256))
+            pairs = [(A3("WB%d" % d, (16 * ch + q, 16 * (ch + nc), 4), None, quad(q)), A3("WC", (c, c + nc), None, quad(q))) for q in range(4)]
+        else:
+            hi, lo = A("WP", 32 * t0, 32 * t0 + 16 * n), A("WP", 32 * t0 + 16 * n, 32 * (t0 + n))
+            pairs = [(A3("WQ%d" % j, (q, 16, 4), None, quad(q)), A("WP", 32 * t0, 32 * (t0 + n), 1, quad(q))) for q in range(4)]
+        cp(hi, z, "vag" if wide else "va"); tt(lo, z, hi, ALU.subtract)
+        if quick:
+            for out, src in pairs: cp(out, src, "va")
+        else: dma("s", pairs, 0.5)
+
+    def sums(s, c, t0=0, n=8, j=None):
+        d, ch = divmod(c, 3); bank, h = "PG%d" % (c // 2), c % 2; lst = []
+        if s == 0 and h == 0: mm([(A3(bank) if c == 4 else A(bank), A("IDB"), A("ZERO", 0, 512), True, False)])
+        for src, k in (("ET", 2), ("EU", 1))[:s + 1]:
+            for t in range(t0, t0 + n):
+                for a in range(4):
+                    e0 = 1024 * c + 128 * t + 32 * a
+                    out = A3(bank, (0, 2 * k), (64 * h + t, 64 * h + 64, 8), quad(a)) if c > 3 else A(bank, 256 * h + t, 256 * h + 128 * k, 8, quad(a))
+                    w = A3("WB%d" % d, (16 * ch, 16 * ch + 8 * k), (16 * a + t, 16 * a + 16, 8)) if j is None else A3("WQ%d" % j, (0, 8 * k), (2 * n * a + t - t0, 2 * n * (a + 1), n))
+                    lst.append((out, A(src, e0, e0 + 32), w, False, src == "EU" and h == 1 and t == 7))
+        mm(lst)
+        if s == 1 and h == 1 and t0 + n == 8:
+            if c == 5: parts = [(A3("GS1", None, (64, L)), A3(bank, (0, 2)), A3(bank, (2, 4)))]
+            else: parts = [(A3("GS%d" % (x // 3), None, (64 * (x % 3), 64 * (x % 3) + 64)), H(bank, 2 * (x % 2), 128), H(bank, 2 * (x % 2) + 1, 128)) for x in (c - 1, c)]
+            for out, hi, lo in parts: cp(out, hi, "va"); tt(out, lo, out, ALU.add)
+            if c > 1:
+                y = c // 4
+                for q in (0, 1):
+                    dma("sa"[q], [((("yh", "yt")[y], (slice(*grp(g)), slice(None))), A3("GS%d" % y, g % 2, None, grp(g))) for g in range(4 * q, 4 * q + 4)], 0.5)
+
+    def first(rep, col, bank, out):
+        mm([(A(bank, 0, 2 * L), A("IDB"), A("NMD"), True, False)])
         for d in (0, 1):
-            lst, e0 = [], 1248 * d
+            lst = []
             for c in range(12):
                 n = L - 16 * c
-                ts(A("EQ", e0, e0 + n), A(rep, d * L + 16 * c, d * L + L), A(col, 12 * d + c, 12 * d + c + 1), ALU.is_equal, A("WS", 16 * c + 15, 16 * c + 16), ALU.mult)
-                lst.append((A(bank, d * L + 16 * c, d * L + L), A("BO"), A("EQ", e0, e0 + n), c == 0, c == 11)); e0 += n
-            mm(lst[:6]); mm(lst[6:])
-        tt(A("FLG" + tag), A(bank, 0, 2 * L), A("THR"), ALU.is_lt)
-        scan(A("FLS" + tag), A("RS16"), A("FLG" + tag), 0.0, ALU.mult, ALU.add)
+                ts(A3("EQ", 12 * d + c, (0, n)), A(rep, d * L + 16 * c, d * L + L), A(col, 12 * d + c, 12 * d + c + 1), ALU.is_equal, 8192.0, ALU.mult)
+                if c < 11: lst.append((A(bank, d * L + 16 * c + 16, d * L + L), A("BO"), A3("EQ", 12 * d + c, (16, n)), False, False))
+            lst.append((H(bank, d), A("TRI"), A3("EQ", (12 * d, 12 * d + 12), (0, 16)), False, d == 1))
+            mm(lst[:5]); mm(lst[5:])
+        scan(A(out), A("RSB"), A(bank, 0, 2 * L), 0.0, ALU.add, ALU.min)
 
     uv(0)
     for d in (0, 1): lists(0, d); ublock(0, d)
     dma("g", [(A("E32", 0, M), ("ee", full))], 24)
-    whole = lambda n: A3(n, (slice(0, 128), slice(None), slice(None)), 16 * L)
-    if HILO:
-        for part in (0, 1): iota(A3("VC1", (slice(0, 128), part, slice(None)), 8 * L), [[0, 8 * L]])
-        for n in ("VB0", "VB1", "VC0"): dma("s", [(whole(n), whole("VC1"))], 6)
-        dma("s", [(A("EL", 0, 16 * L), whole("VC1")), (A("EL", 16 * L, M), A3("VC1", (slice(0, 128), 0, slice(0, M - 16 * L)), M - 16 * L))], 8)
-    else:
-        for d in (0, 1):
-            for part in (0, 1): iota(A3("VB%d" % d, (slice(0, 128), part, slice(None)), 8 * L), [[0, 8 * L]])
-        for d in (0, 1): iota(H("VF", d, 8 * L), [[0, 8 * L]])
+    iota(A("ZERO"), [[0, 768]])
+    for n, r in (("VB0", 2), ("VB1", 2), ("WB0", 12), ("WB1", 12)): dma("s", [(A3(n, (r * j, r * j + r)), A("ZERO")) for j in range(4)], 6)
+    dma("s", [(A3("WQ%d" % j), A("ZERO", 0, 128 * n)) for j, n in enumerate(LAST)], 2)
+    iota(A("THM"), [[0, 512]], 1); sel(A("THM"), A("THM"), [[0, 64], [-16, 8]], ALU.is_ge, -32768.0, 0, 1); sel(A("THM"), A("THM"), [[0, 64], [16, 8]], ALU.is_ge, -32768.0, 15, -1)
     cp(A("KF"), A("KEY0")); tt(A("BD"), IND(A("KF"), A("CEXP")), A("MD"), ALU.mult)
-    mm([(A("PG", 0, 2 * L), A("BO32"), A("BD"), True, True)]); cp(A("KR16"), A("PG", 0, 2 * L))
-    first("KR16", "KF", "PZ", "K")
-    tt(A("G3"), A("KF"), A("DUMC"), ALU.subtract); tt(A("G3"), A("G3"), A("FLSK", 15, None, 16), ALU.mult)
-    tt(A("G3"), A("G3"), A("DUMC"), ALU.add); cp(A("OSC"), A("G3"))
-    for d in (1, 0): contest(0, d); vblock(0, d)
+    mm([(S384, A("BO32"), A("BD"), True, True)]); cp(A("KR16"), S384)
+    first("KR16", "KF", "S1", "FSK")
+    tt(A("G3"), A("FSK", 15, None, 16), A("KF"), ALU.add); tt(A("G3"), A("G3"), A("DUMC"), ALU.min); cp(A("OSC"), A("G3"))
+    for d in (0, 1): contest(d); vblock(0, d)
     ts(A("EXS"), A("MI"), 4, ALU.arith_shift_right)
-    send([(H("INS", 1, 12), H("EXS", 0, 12), 1), (H("INS", 0, 12), H("EXS", 1, 12), -1)], 0)
-    ts(A("KK"), A("MI"), 15, ALU.bitwise_and); tt(A("E1"), IND(A("KK"), A("CEXP")), A("MD"), ALU.mult)
-    mm([(A("PL2", 0, 2 * L), A("BO"), A("E1"), True, True)]); ts(A("PSC", 0, 2 * L), A("PL2", 0, 2 * L), A("K15"), ALU.is_equal)
-    tt(A("OAA"), A("PSC", 0, 2 * L), A("AF"), ALU.mult); mm([(A("PMS", 0, 2 * L), A("BO32"), A("OAA"), True, True)])
-    tt(A("BD"), A("PMS", 0, 2 * L), A("MD"), ALU.mult); cp(A("BR16"), A("PMS", 0, 2 * L))
-    scan(A("BSC"), A("RS16"), A("BD"), 0.0, ALU.mult, ALU.add)
+    send(swap("INS", "EXS", 12), 0)
     BL = A("BSC", 15, None, 16)
     cp(A("OB"), BL)
     tt(A("Z1"), BL, A("C37"), ALU.mult); tt(A("Z2"), A("Z1"), A("Q"), ALU.add); ts(A("EXK"), A("Z2"), NK - 1, ALU.bitwise_and)
-    send([(H("INK", 1, 12), H("EXK", 0, 12), 1), (H("INK", 0, 12), H("EXK", 1, 12), -1)], 0)
+    send(swap("INK", "EXK", 12), 0)
     for d in (0, 1): cp(IND(A(("HC", "TC")[d]), H("OSC", d, 12)), H("AF", d))
-    act(A("SU"), A("U0"), ACT.Sign); cp(A("V8"), A("V0"), "va", 0.125)
+    act(A("SU"), A("U0"), ACT.Sign)
     tt(A("NX0"), IND(A("X", 0, M), A("OB")), A("SU"), ALU.subtract); ts(A("NX"), A("NX0"), -7.0, ALU.max, 7.0, ALU.min)
-    tt(A("PV"), IND(A("E"), A("OB")), A("V0"), ALU.mult); mm([(A("PL2", 0, 2 * L), A("BO32"), A("PV"), True, True)])
-    act(A("PSC", 0, 2 * L), A("PL2", 0, 2 * L), ACT.Sigmoid, 0.0625); tt(A("WV"), A("PSC", 0, 2 * L), A("V8"), ALU.mult)
+    tt(A("PV"), IND(A("E"), A("OB")), A("V0"), ALU.mult); mm([(S384, A("BO32"), A("PV"), True, True)])
+    act(S384, S384, ACT.Sigmoid, 0.5); tt(A("WV"), S384, A("V0"), ALU.mult)
     cp(A("EB"), IND(A("E"), A("OB")), "va", 0.875)
-    tt(A("LV", 0, 12), A("EXS", 0, 12), A("INS", 0, 12), ALU.is_ge); tt(A("LV", 12, 24), A("EXS", 12, 24), A("INS", 12, 24), ALU.is_gt)
+    tt(A("LV"), A("EXS"), A("INS"), ALU.is_gt)
     ts(A("BS0"), A("LV"), -8192.0, ALU.mult, 8192.0, ALU.add); tt(A("BS"), A("BS0"), BL, ALU.add)
-    tt(A("D0"), BL, A("DUMX"), ALU.subtract); tt(A("D1"), A("D0"), A("LV"), ALU.mult)
-    first("BR16", "BS", "PMS", "")
-    tt(A("F1"), A("D1"), A("FLS", 15, None, 16), ALU.mult); tt(A("F2"), A("F1"), A("DUMX"), ALU.add); cp(A("OSX"), A("F2"))
-    tt(A("G1"), BL, A("HTF"), ALU.subtract); tt(A("G1"), A("G1"), A("LV"), ALU.mult); tt(A("G1"), A("G1"), A("HTF"), ALU.add); cp(A("OHT1"), A("G1"))
-    tt(A("G2"), A("KEY0"), A("INK"), ALU.subtract); tt(A("G2"), A("G2"), A("LV"), ALU.mult); tt(A("G2"), A("G2"), A("INK"), ALU.add); cp(A("OKEY1"), A("G2"))
-    for d in (1, 0): output(0, d)
+    first("BR16", "BS", "S1", "FS")
+    tt(A("F1"), A("FS", 15, None, 16), A("BS"), ALU.add); tt(A("F2"), A("F1"), A("DUMX"), ALU.min); cp(A("OSX"), A("F2"))
+    tt(A("G1"), BL, HT, ALU.subtract); tt(A("G1"), A("G1"), A("LV"), ALU.mult); tt(A("G1"), A("G1"), HT, ALU.add); cp(A("OHT1"), A("G1"))
+    tt(A("G4"), A("KEY0"), A("INK"), ALU.subtract); tt(A("G4"), A("G4"), A("LV"), ALU.mult); tt(A("G4"), A("G4"), A("INK"), ALU.add); cp(A("OKEY1"), A("G4"))
+    for d in (0, 1):
+        for ch in range(3): reals(0, 3 * d + ch, False)
+        weights(3 * d, 3, False)
+        for ch in range(3): sums(0, 3 * d + ch)
     for d in (0, 1): cp(IND(A("X"), H("OSX", d, 12)), H("NX", d))
     for d in (0, 1): tt(IND(A("E32"), H("OSX", d, 12)), H("EB", d), H("WV", d), ALU.add)
-    if HILO:
-        tt(A("EN"), A("EB"), A("WV"), ALU.add); cp(A("ENH"), A("EN"), "va"); tt(A("ENL"), A("EN"), A("ENH"), ALU.subtract)
-        for d in (0, 1): cp(IND(A("EL"), H("OSX", d, 12)), H("ENL", d))
     uv(1)
-    for d in (0, 1): lists(1, d); ublock(1, d); vblock(1, d)
-    for d in (0, 1): output(1, d)
+    for d in (0, 1):
+        lists(1, d); ublock(1, d); vblock(1, d)
+    for c in range(6):
+        duel(*divmod(c, 3))
+        if c < 5: reals(1, c, c in WIDE); weights(c, 1, c in WIDE); sums(1, c)
+    for j, n in enumerate(LAST):
+        piece = (sum(LAST[:j]), n, j)
+        reals(1, 5, False, *piece); weights(5, 1, False, *piece, quick=j >= len(LAST) - QUICK); sums(1, 5, *piece)
     return ops
 
 
@@ -363,55 +393,44 @@ def hazards(ops):
         acc = [(a, False) for a in o["rd"]] + [(a, True) for a in o["wr"]]
         for a, w in acc:
             ps = psum(a)
-            for j, lo, hi, w2 in hist.get(a["n"], []):
-                if ps or ((w or w2) and lo < a["hi"] and a["lo"] < hi):
+            for j, lo, hi, w2, p, st in hist.get(a["n"], []):
+                apart = st == a.get("st", 1) and (lo - a["lo"]) % st
+                if ps or ((w or w2) and lo < a["hi"] and a["lo"] < hi and p[0] < a["p"][1] and a["p"][0] < p[1] and not apart):
                     deps[j] = deps.get(j, False) or w or w2
         for a, w in acc:
             h = hist.setdefault(a["n"], [])
             if psum(a): h[:] = [x for x in h if x[0] == i or (x[3] and not w)]
-            elif w: h[:] = [x for x in h if x[0] == i or not (a["lo"] <= x[1] and x[2] <= a["hi"] and a["cnt"] == a["hi"] - a["lo"] and "off" not in a and a["ix"][0] == slice(0, 128))]
-            if (i, a["lo"], a["hi"], w) not in h: h.append((i, a["lo"], a["hi"], w))
+            elif w and a["cnt"] == a["hi"] - a["lo"] and "off" not in a:
+                h[:] = [x for x in h if x[0] == i or not (a["lo"] <= x[1] and x[2] <= a["hi"] and a["p"][0] <= x[4][0] and x[4][1] <= a["p"][1])]
+            x = (i, a["lo"], a["hi"], w, a["p"], a.get("st", 1))
+            if x not in h: h.append(x)
         deps.pop(i, None)
         o["deps"] = deps
 
 
-def replay(ops, deps, seq, eng, wake):
-    free = {q: 0.0 for q in "vatgs"}; done = [0.0] * len(ops)
-    for i in seq:
-        q = eng[i]; t = free[q]
-        for j in deps[i]:
-            if done[j] + wake > t and not (q == "t" and eng[j] == "t"): t = done[j] + wake
-        free[q] = t + ops[i]["cost"][q]; done[i] = free[q] + ops[i]["lat"]
-    return max(done)
-
-
-def schedule(ops, succ, bias, lean, WAKE):
+def schedule(ops, succ, bias, lean, WAKE, ahead=0.3):
     n = len(ops)
     pr = [0.0] * n
     for i in range(n - 1, -1, -1):
         o = ops[i]; pr[i] = min(o["cost"].values()) + o["lat"] + WAKE + max([pr[k] for k in succ[i]] or [0.0]) + bias[i]
-    busy = {q: [] for q in "vatgs"}; done = [0.0] * n; start = [0.0] * n; eng = [None] * n
-    for i in sorted(range(n), key=lambda i: -pr[i]):
-        pe = ops[i]["eng"] == "t"
-        rt = max([done[j] + (-60.0 if pe and eng[j] == "t" else WAKE) for j in ops[i]["deps"]] or [0.0]); best = None
-        for q, c in ops[i]["cost"].items():
-            t = rt
-            for a, b in busy[q]:
-                if t + c <= a: break
-                if b > t: t = b
-            f = t + c + (lean[i] if q == "v" else 0.0)
-            if best is None or f < best[0]: best = (f, t, q)
-        t, q = best[1], best[2]
-        start[i] = t; eng[i] = q; done[i] = t + ops[i]["cost"][q] + ops[i]["lat"]
-        busy[q].append((t, t + ops[i]["cost"][q])); busy[q].sort()
-    order = {q: sorted([i for i in range(n) if eng[i] == q], key=lambda i: start[i]) for q in busy}
-    return order, max(done), start, eng
+    free = dict.fromkeys("vatgs", 0.0); ready = [0.0] * n; left = [len(o["deps"]) for o in ops]; eng = [None] * n; seq = []
+    pool = [i for i in range(n) if not left[i]]
+    while pool:
+        t, q = min((max(free[q], ready[i]), q) for i in pool for q in ops[i]["eng"] if q == ops[i]["eng"][0] or free[ops[i]["eng"][0]] > max(free[q], ready[i]) + lean[i])
+        mine = [i for i in pool if q == ops[i]["eng"][0] or q in ops[i]["eng"] and free[ops[i]["eng"][0]] > max(free[q], ready[i]) + lean[i]]
+        rank = lambda i: (q == ops[i]["eng"][0], pr[i])
+        i = max((i for i in mine if ready[i] <= t), key=rank)
+        soon = [j for j in mine if t < ready[j] <= t + ahead * ops[i]["cost"][q] and rank(j) > rank(i)]
+        if soon: i = min(soon, key=lambda j: ready[j]); t = ready[i]
+        pool.remove(i); seq.append(i); eng[i] = q; free[q] = t + ops[i]["cost"][q]
+        for k in succ[i]:
+            ready[k] = max(ready[k], free[q] + (0.0 if q == "t" == ops[k]["eng"] else ops[i]["lat"] + WAKE)); left[k] -= 1
+            if not left[k]: pool.append(k)
+    return seq, eng
 
 
 PLAN = {}
-
-
-ROUNDS, MOVES = 2500, 40000
+ROUNDS, MOVES, HEAT = 2000, 150000, 200.0
 
 
 def plan():
@@ -420,58 +439,101 @@ def plan():
         deps = [list(o["deps"]) for o in ops]; succ = [[] for _ in ops]
         for i in range(n):
             for j in deps[i]: succ[j].append(i)
-        rng = np.random.default_rng(7); flex = [i for i in range(n) if ops[i]["eng"] == "va"]
+        rng = np.random.default_rng(7); flex = [i for i in range(n) if len(ops[i]["cost"]) > 1]
+        tabs = [([o["cost"] for o in oo], [o["lat"] for o in oo], c[5]) for oo, c in zip(all_ops, CASES)]
+        figs = [{q: [x[0][i][q] for x in tabs] + [x[1][i] + x[2] for x in tabs] for q in ops[i]["cost"]} for i in range(n)]
+        above = []
+        for i in range(n):
+            x = 0
+            for j in deps[i]: x |= above[j] | 1 << j
+            above.append(x)
+        direct = lambda i, j: not any(above[k] >> j & 1 for k in deps[i])
+        inline = lambda i, j: ops[i]["eng"] == ops[j]["eng"] and (ops[i]["eng"] == "t" or len(ops[i]["eng"]) == 1 and not ops[i]["deps"][j])
+        dp = [[j for j in deps[i] if direct(i, j) and not inline(i, j)] for i in range(n)]
+
+        def ends(seq, eng):
+            free = dict.fromkeys("vatgs", (0.0, 0.0, 0.0)); d0, d1, d2 = [0.0] * n, [0.0] * n, [0.0] * n
+            for i in seq:
+                q = eng[i]; t0, t1, t2 = free[q]; c0, c1, c2, l0, l1, l2 = figs[i][q]
+                for j in dp[i]:
+                    if d0[j] > t0: t0 = d0[j]
+                    if d1[j] > t1: t1 = d1[j]
+                    if d2[j] > t2: t2 = d2[j]
+                t0 += c0; t1 += c1; t2 += c2; free[q] = (t0, t1, t2); d0[i] = t0 + l0; d1[i] = t1 + l1; d2[i] = t2 + l2
+            return [max(d0), max(d1), max(d2)]
 
         def judge(bias, lean):
-            r = schedule(ops, succ, bias, lean, CASES[0][5]); seq = sorted(range(n), key=lambda i: (r[2][i], i))
-            ends = [replay(o, deps, seq, r[3], c[5]) for o, c in zip(all_ops, CASES)]
-            return sum(ends), r, ends
+            seq, eng = schedule(ops, succ, bias, lean, CASES[0][5])
+            return sum(ends(seq, eng)), seq, eng
 
-        bias, lean = [0.0] * n, [1000.0] * n; best = judge(bias, lean)
+        bias, lean = [0.0] * n, [300.0] * n; best = judge(bias, lean)
         for _ in range(ROUNDS):
             b2, l2 = list(bias), list(lean)
             for _k in range(int(rng.integers(1, 4))):
                 if rng.random() < 0.6: b2[int(rng.integers(0, n))] = float(rng.choice([0.0, 200.0, 1000.0, 3000.0, 8000.0]))
-                else: l2[flex[int(rng.integers(0, len(flex)))]] = float(rng.choice([-3000.0, 0.0, 500.0, 1500.0, 6000.0]))
+                else: l2[flex[int(rng.integers(0, len(flex)))]] = float(rng.choice([0.0, 300.0, 800.0, 1500.0, 6000.0]))
             r = judge(b2, l2)
             if r[0] <= best[0]: best, bias, lean = r, b2, l2
-        seq = sorted(range(n), key=lambda i: (best[1][2][i], i)); eng = list(best[1][3])
-        tabs = [([o["cost"] for o in oo], [o["lat"] for o in oo], c[5]) for oo, c in zip(all_ops, CASES)]
-        dp = [[j for j in deps[i] if not (ops[i]["eng"] == "t" and ops[j]["eng"] == "t")] for i in range(n)]
 
-        def ends(seq, eng):
-            out = 0.0
-            for cost, lat, wake in tabs:
-                free = {"v": 0.0, "a": 0.0, "t": 0.0, "g": 0.0, "s": 0.0}; done = [0.0] * n
-                for i in seq:
-                    q = eng[i]; t = free[q]
-                    for j in dp[i]:
-                        if done[j] > t: t = done[j]
-                    t += cost[i][q]; free[q] = t; done[i] = t + lat[i] + wake
-                out += max(done)
+        def chain(seq, eng, case):
+            cost, lat, wake = tabs[case]; free = {q: (0.0, -1) for q in "vatgs"}; done = [0.0] * n; why = [None] * n
+            for i in seq:
+                t, k = free[eng[i]]; queue = True
+                for j in dp[i]:
+                    if done[j] > t: t, k, queue = done[j], j, False
+                why[i] = (k, queue); t += cost[i][eng[i]]; free[eng[i]] = (t, i); done[i] = t + lat[i] + wake
+            i = done.index(max(done)); out = []
+            while i >= 0:
+                k, queue = why[i]
+                if queue and k >= 0: out.append((i, k))
+                i = k
             return out
 
-        cur = top = ends(seq, eng); keep = (list(seq), list(eng)); draws = rng.random((MOVES, 4)).tolist()
-        for it, (r0, r1, r2, r3) in enumerate(draws):
-            s2, e2 = list(seq), eng
-            if r0 < 0.2:
-                i = flex[int(r1 * len(flex))]; e2 = list(eng); e2[i] = "a" if eng[i] == "v" else "v"
-            else:
-                p = int(r1 * n); i = s2.pop(p); lo, hi = p, p
+        cur, seq, eng = best; top = cur; keep = (list(seq), list(eng)); draws = rng.random((MOVES, 5)).tolist(); arcs = None
+        for it, (r0, r1, r2, r3, r4) in enumerate(draws):
+            if arcs is None: arcs = chain(seq, eng, int(r4 * len(tabs)))
+            s2, e2 = seq, eng
+            i, k = arcs[int(r1 * len(arcs))]
+            if r0 < 0.25:
+                i = (i, k)[r2 < 0.5] if r0 < 0.15 else flex[int(r1 * len(flex))]
+                other = [q for q in ops[i]["cost"] if q != eng[i]]
+                if not other: continue
+                e2 = list(eng); e2[i] = other[int(r4 * len(other))]
+                if r0 > 0.2:
+                    j = flex[min(len(flex) - 1, max(0, flex.index(i) + int(r2 * 13) - 6))]
+                    if j != i and eng[j] == e2[i] and eng[i] in ops[j]["cost"]: e2[j] = eng[i]
+            elif r0 < 0.45:
+                s2 = list(seq); p = int(r1 * n); i = s2.pop(p); lo, hi = p, p
                 while lo > 0 and p - lo < 60 and s2[lo - 1] not in ops[i]["deps"]: lo -= 1
                 while hi < n - 1 and hi - p < 60 and i not in ops[s2[hi]]["deps"]: hi += 1
                 s2.insert(lo + int(r2 * (hi - lo + 1)), i)
-            v = ends(s2, e2)
-            if v <= cur - 250.0 * (1.0 - it / MOVES) * math.log(r3 + 1e-12):
-                cur, seq, eng = v, s2, e2
+            else:
+                hi = seq.index(i); lo = seq.index(k)
+                if r0 < 0.75:
+                    lo = max(0, lo - int(r2 * r2 * 30)); need = set(deps[i]); up, rest = [i], []
+                    for j in reversed(seq[lo:hi]):
+                        if j in need: up.append(j); need.update(deps[j])
+                        else: rest.append(j)
+                    if k in up: continue
+                    s2 = seq[:lo] + up[::-1] + rest[::-1] + seq[hi + 1:]
+                else:
+                    hi = min(n - 1, hi + int(r2 * r2 * 30)); need = set(succ[k]); down, rest = [k], []
+                    for j in seq[lo + 1:hi + 1]:
+                        if j in need: down.append(j); need.update(succ[j])
+                        else: rest.append(j)
+                    if i in down: continue
+                    s2 = seq[:lo] + rest + down + seq[hi + 1:]
+            v = sum(ends(s2, e2))
+            if v <= cur - HEAT * (1.0 - it / MOVES) * math.log(r3 + 1e-12):
+                cur, seq, eng = v, s2, e2; arcs = None
                 if v < top: top, keep = v, (list(s2), list(e2))
+            elif r4 < 0.05: arcs = None
         seq, eng = keep
         free = {q: 0.0 for q in "vatgs"}; done = [0.0] * n; start = [0.0] * n
         for i in seq:
             start[i] = max([free[eng[i]]] + [done[j] for j in dp[i]]); free[eng[i]] = start[i] + ops[i]["cost"][eng[i]]
             done[i] = free[eng[i]] + ops[i]["lat"] + CASES[0][5]
-        PLAN.update(ops=ops, seq=seq, order={q: [i for i in seq if eng[i] == q] for q in free}, start=start, eng=eng,
-                    end=[replay(o, deps, seq, eng, c[5]) for o, c in zip(all_ops, CASES)])
+        PLAN.update(ops=ops, seq=seq, start=start, eng=eng, end=ends(seq, eng))
     return PLAN
 
 
@@ -529,7 +591,8 @@ def rank_program(g, core, T, topo):
             continue
         if k == "cp":
             out, a, sc, bi = x
-            if q == "a":
+            if q == "g": r = e.affine_select(ap(out), ap(a), [[0, out["cnt"]]], ALU.is_ge, 0.0, 0, 0)
+            elif q == "a":
                 if bi is None: r = e.activation(ap(out), ap(a), ACT.Copy, scale=1.0 if sc is None else sc)
                 else: r = e.activation(ap(out), ap(a), ACT.Identity, bias=ap(bi), scale=sc)
             elif sc is None: r = e.tensor_copy(ap(out), ap(a))
@@ -543,9 +606,15 @@ def rank_program(g, core, T, topo):
         elif k == "tr": r = e.transpose(ap(x[0]), ap(x[1]))
         elif k == "ms": r = e.memset(ap(x[0]), x[1])
         elif k == "act": r = e.activation(ap(x[0]), ap(x[1]), x[2], scale=x[3])
+        elif k == "step":
+            if q == "a": r = e.activation(ap(x[0]), ap(x[1]), ACT.Sigmoid, bias=64.0, scale=-4.0)
+            else: r = e.tensor_scalar(ap(x[0]), ap(x[1]), 0.0, None, ALU.is_le)
+        elif k == "sel": r = e.affine_select(ap(x[0]), ap(x[1]), x[2], x[3], x[4], x[5], x[6])
         elif k == "iota":
             if SCRATCH[x[0]["n"]][2] == I: r = e.iota(ap(x[0]), x[1], x[2], x[3])
             else: r = e.iota(ap(x[0]), x[1], x[2], x[3], allow_small_or_imprecise_dtypes=True)
+        elif k == "trp":
+            for out, a, b in x: r = e.transpose(ap(out), ap(a), ap(b))
         else:
             for out, a, b, s0, s1 in x: r = e.matmul(ap(out), ap(a), ap(b), s0, s1)
         count[q] += 1; r.then_inc(T.sem["c" + q], 1); token[i] = ("c" + q, count[q]); total["c" + q] = count[q]

@@ -6,9 +6,12 @@ from concourse.mybir import AluOpType as ALU, ActivationFunctionType as ACT
 M, NK, L, D, NR = 4096, 1024, 192, 3, 8
 B, F, I, U = "bfloat16", "float32", "int32", "uint16"
 WIDE = (0, 1, 2, 3, 4)
+TURN = (0, 1, 2, 3, 4)
+EARLY = (2, 1)
+SPLIT = ()
 LAST = (4, 2, 2)
 QUICK = 2
-ONV = ((2, 6, 8, 10), (2,))
+ONV = ((0, 1, 3, 5, 8), (2, 9))
 SCRATCH, PLACE = {}, {}
 
 
@@ -23,23 +26,23 @@ def _buf(names, cols, dtype, where="sbuf"):
 
 
 _buf("X", M + L, B); _buf("E", M, B); _buf("E32", M + L, F); _buf("HC TC", NK + L, I); _buf("NN", 4 * L, I)
-_buf("XR XP", 72, B); _buf("LL", 72, I); _buf("MX ME", 2 * L, B)
-_buf("IP IN I1 I2 I3", 1, I); _buf("K15 KB0 KB1 G2 C1 C2", 1, F)
-_buf("ID32 BO32", 128, F); _buf("IDB BO TRI ONE HALF", 128, B); _buf("MK", 512, B); _buf("ZERO", 768, B); _buf("W32", 256, F); _buf("RD", 64, F)
+_buf("XR", 64, B); _buf("LL", 72, I); _buf("MX ME", 2 * L, B)
+_buf("IP IN I1 I2 I3 I4", 1, I); _buf("K15 KB0 KB1 G2 C1 C2 C3 C4", 1, F)
+_buf("ID32 BO32", 128, F); _buf("IDB BO TRI ONE HALF OWN", 128, B); _buf("MK", 512, B); _buf("ZERO", 768, B); _buf("W32", 256, F); _buf("RD", 64, F)
 for _j, _n in enumerate(LAST): _buf("WQ%d" % _j, (16, 8 * _n), B)
-_buf("RS32 RSB MD NMD IOC", 2 * L, B); _buf("THM AM", 512, B); _buf("SEL IOG", 240, B); _buf("A64", 128, F)
-_buf("SC24 SC12 SCP SCC", 24, I); _buf("DUM0 DUMX DUMC C37 PARF", 24, F)
-_buf("CEXP CPERM CTR OP OQ OHT0 OHT1 OKEY0 OKEY1 OB OSX OSC", 24, U)
+_buf("RS32", 128, B); _buf("MD", 16, B); _buf("COUNT", NK, I); _buf("RSB NMD IOC", 2 * L, B); _buf("THM AM", 512, B); _buf("SEL IOG", 240, B); _buf("A64", 128, F)
+_buf("SC12 SCP SCB", 24, I); _buf("DUM0 DUMX DUMC C37 PARF", 24, F)
+_buf("OKK CTR CBLK OP OHT0 OHT1 OKEY0 OKEY1 OB OSX OSC", 24, U)
 _buf("KEY0 KT Q MI EXS INS EXK INK KK Z2", 24, I)
-_buf("Z1 LV BS0 BS F1 F2 G1 G3 G4 KF", 24, F)
-_buf("UO0 UO1 U0 U1 SU E1 NX0 NX", 2 * L, B)
-_buf("VO0 VO1 V0 V1 DD WDD AF OAA BD BSC FS FSK PV WV EB SCS0 SCS1 RM0 RM1", 2 * L, F)
-_buf("VH0 VH1", 4 * L, B); _buf("BR16 KR16", 2 * L, U); _buf("OFN OFC", 4 * L, U); _buf("OA", 2 * L, U)
-_buf("UB", (16, L), B); _buf("VB0 VB1", (8, 2 * L), B); _buf("WB0 WB1", (48, 64), B); _buf("WC", (6, 256), B); _buf("WP", 256, B)
-_buf("XG", 64 * L, B); _buf("EA EL ET EU", 32 * L, B)
+_buf("Z1 LV BS0 BS F1 F2 G1 G3 G4 KF HT8", 24, F)
+_buf("UO0 UO1 U0 U1 SU NX0 NX", 2 * L, B)
+_buf("VO0 VO1 V0 V1 DD WDD AF OAA BSC FS FSK PV WV EB SCS0 SCS1 RM0 RM1", 2 * L, F)
+_buf("VH", 6 * L, B); _buf("BR16 KR16", 2 * L, U); _buf("OFN OFC", 4 * L, U); _buf("OA", 2 * L, U)
+_buf("UA", 512 * max(EARLY), B); _buf("UB0 UB1", (8, L), B); _buf("VB0 VB1", (8, 3 * L), B); _buf("WB0 WB1", (48, 64), B); _buf("WC", (6, 256), B); _buf("WP", 256, B)
+_buf("XG", 64 * L, B); _buf("EA ET", 32 * L, B); _buf("EL EU", 4096, B); _buf("EF", 2048 if SPLIT else 8, F)
 _buf("WN", 448, B); _buf("TT", 832, B); _buf("EQ", (24, L), B); _buf("GS0 GS1", (2, L), F)
-_buf("S0 PZ", (8, 64), F, "psum"); _buf("S1 PG0 PG1", 512, F, "psum"); _buf("PG2", (4, 128), F, "psum"); _buf("PT0 PT1", 1024, B, "psum")
-NDMA = 40
+_buf("S0 PZ", (8, 64), F, "psum"); _buf("S1", 512, F, "psum"); _buf("PG0 PG1 PG2", (4, 128), F, "psum"); _buf("PT0 PT1", 1024, B, "psum")
+NDMA = 56
 SEMAPHORES = ["cv", "ca", "ct", "cg", "loc"] + ["d%d" % i for i in range(NDMA)] + ["r%d" % i for i in range(16)]
 
 
@@ -57,7 +60,8 @@ def A3(n, rows=None, cols=None, p=(0, 128)):
     r = range(rows, rows + 1) if isinstance(rows, int) else range(*rows)
     c = range(cols, cols + 1) if isinstance(cols, int) else range(*cols)
     ix = lambda x: x if isinstance(x, int) else slice(*x)
-    return {"n": n, "ix": (slice(*p), ix(rows), ix(cols)), "lo": r[0] * w + c[0], "hi": r[-1] * w + c[-1] + 1, "cnt": len(r) * len(c), "p": p}
+    return {"n": n, "ix": (slice(*p), ix(rows), ix(cols)), "lo": r[0] * w + c[0], "hi": r[-1] * w + c[-1] + 1, "cnt": len(r) * len(c), "p": p,
+            "runs": len(r) if r.step > 1 or len(c) < w else 1}
 
 
 def IND(win, off):
@@ -72,23 +76,32 @@ def psum(a):
     return SCRATCH[a["n"]][0] == "psum"
 
 
-CASES = [(1.0, 0.5, 1.55, 3.8, 4, 120, 2000), (0.87, 0.44, 1.1, 2.4, 2, 80, 1700), (1.2, 0.6, 2.3, 5.5, 5, 180, 2400)]
+CASES = [(1.0, 0.5, 1.55, 4.2, 3, 140, 2000, 2400, 1500, 15), (0.87, 0.44, 1.1, 2.4, 3, 120, 2100, 2600, 2000, 20), (1.2, 0.6, 2.3, 5.5, 4, 170, 2000, 2400, 1500, 15)]
+WEIGHTS, PULL, LOAD, LEAN, BOOST, AHEAD, SEED = (1.0, 0.8, 1.0), 0.2, 0.03, 6000.0, 0.0, 0.0, 1
+END = 75
+KEARLY = True
+DUE = {"XG": [6.5, 11, 8, 12.5, 9.5, 13, 7, 14, 11, 15, 12.5, 16.5, 30.5, 40, 32.2, 41, 33.9, 43, 35.5, 45, 37.2, 48, 38.9, 52],
+       "EA": [19, 20.7, 22.3, 24, 25.7, 27.4, 47, 50, 54, 57.5, 60], "SCS1": [15], "SCS0": [18.5], "OA": [17.5, 22], "X": [0, 28, 28.8],
+       "FSK": [34], "U1": [30], "LL": [0.2, 3], "U0": [5.2, 8.5], "MX": [3.1, 3.8], "ME": [3.4], "UA": [0, 12], "V0": [12],
+       "XR": [0.3], "ONE": [1.8], "WC": [30, 31, 37, 38], "ET": [36, 37, 38, 40, 41, 42], "KR16": [28], "PG1": [0] * 9 + [38, 44], "PG2": [0, 39, 40], "PG0": [0] * 9 + [42, 43], "HC": [0, 36], "TC": [0, 38], "V1": [40]}
+DUE = {}
+SIZE = {B: 2, U: 2, F: 4, I: 4}
 
 
 def build(case):
-    CY, PECY, GAT, SCA, MMI, WAKE, DML = case
+    CY, PECY, GAT, SCA, MMI, WAKE, DML, RML, FIRST, ROW = case
     ops = []
 
     def add(eng, kind, args, rd, wr, cost, lat=0.0):
         r = []
-        if len(eng) > 1 and wr[0]["n"] not in ("ET", "EU"): eng = "".join(q for q in "gav" if q in eng)
+        if len(eng) > 1 and wr[0]["n"] not in KEEP: eng = "".join(q for q in "gav" if q in eng)
         for a in rd:
             if isinstance(a, dict):
                 r.append(a)
                 if "off" in a: r.append(a["off"])
         for a in wr:
             if "off" in a: r.append(a["off"])
-        ops.append({"eng": eng, "kind": kind, "args": args, "rd": r, "wr": list(wr), "cost": cost, "lat": lat})
+        ops.append({"eng": eng, "kind": kind, "args": args, "rd": r, "wr": list(wr), "cost": cost, "lat": lat, "hold": 0.0, "bias": 0.0})
 
     def vc(out, ins, c):
         n = out["cnt"]
@@ -121,8 +134,8 @@ def build(case):
     def act(out, a, func, scale=1.0):
         add("a", "act", (out, a, func, scale), [a], [out], {"a": 70 + out["cnt"] * CY})
 
-    def step(out, a):
-        add("va", "step", (out, a), [a], [out], {"v": vc(out, [a], 1), "a": 70 + out["cnt"] * CY})
+    def step(out, a, eng="va"):
+        add(eng, "step", (out, a), [a], [out], {"v": vc(out, [a], 1), "a": 70 + out["cnt"] * CY} if eng == "va" else {"a": 1400 * CY})
 
     def iota(out, pat, base=0, chm=0):
         add("g", "iota", (out, pat, base, chm), [], [out], {"g": 160 + 2 * out["cnt"] * CY})
@@ -134,13 +147,21 @@ def build(case):
         c = sum(max(min(64, x[1]["cnt"]), x[2]["cnt"]) * (4 if SCRATCH[x[1]["n"]][2] == F else 1) * PECY + MMI for x in lst)
         add("t", kind, lst, [x[1] for x in lst] + [x[2] for x in lst], [x[0] for x in lst], {"t": c}, 60)
 
-    def dma(q, pairs, kb):
-        add(q, "dma", pairs, [x[1] for x in pairs], [x[0] for x in pairs if isinstance(x[0], dict)], {q: (700 if q == "g" else 70) * len(pairs)}, DML + 215 * kb)
+    def hold(pairs):
+        sides = [x[0] if isinstance(x[0], dict) else x[1] for x in pairs]
+        return sum((a["p"][1] - a["p"][0]) * (a["cnt"] * SIZE[SCRATCH[a["n"]][2]] * 0.21 / 128 + a.get("runs", 1) * ROW / 16) for a in sides)
+
+    def dma(q, pairs, kb, after=None):
+        add(q, "dma", pairs, [x[1] for x in pairs] + [after], [x[0] for x in pairs if isinstance(x[0], dict)], {q: (900 if q == "g" else 70) * len(pairs)}, DML)
+        ops[-1]["hold"] = hold(pairs) * (2 if kb == "add" else 1); ops[-1]["add"] = kb == "add"
+        if kb == "add": ops[-1]["rd"] += ops[-1]["wr"]
 
     def send(pairs, kb):
-        add("g", "send", pairs, [x[1] for x in pairs], [x[0] for x in pairs], {"g": 400}, DML + 215 * kb)
+        add("g", "send", pairs, [x[1] for x in pairs], [x[0] for x in pairs], {"g": 400}, RML + (FIRST if kb == 4 else 0))
+        ops[-1]["hold"] = hold(pairs)
 
     who = lambda s, j: "va" if j in ONV[s] else "av"
+    KEEP = ("ET", "EU", "XG", "UA", "MX", "ME", "WN", "OA")
     H = lambda n, d, w=L: A(n, d * w, d * w + w)
     full = (slice(0, 128), slice(None))
     grp = lambda g: (16 * g, 16 * g + 16)
@@ -152,20 +173,15 @@ def build(case):
     nn = lambda s, d: (ent(s, d), (("nh", "nt")[d], (slice(0, 128), slice(s * L, s * L + L))))
     dma("s", [(LT, ("tl", full)), (LP, ("rl", full)), (LH, ("hl", full))], 0)
     dma("s", [(A("XR", 0, 32), ("xr", full)), (A("XR", 32, 64), ("er", full))], 0)
-    dma("s", [nn(0, 0), nn(0, 1)], 2)
-    dma("a", [(A("X", 0, M), ("xe", full))], 10)
-    dma("a", [(A("TC", 0, NK), ("tc", full))], 14)
-    dma("a", [(A("HC", 0, NK), ("hc", full))], 18)
-    dma("a", [nn(1, 0), nn(1, 1)], 20)
-    dma("a", [(A("E"), ("ee", full))], 28)
-    ms(A("XR", 64, 72), 0.0)
-    send([(A("LL", 36, 72), A("LL", 0, 36), 1), (A("XP"), A("XR"), 1)], 4)
+    dma("s", [nn(0, 1)], 2)
+    dma("s", [(A("X", 0, M), ("xe", full))], 10)
+    dma("s", [nn(0, 0)], 2)
+    send([(A("LL", 36, 72), A("LL", 0, 36), 1)], 4)
     iota(A("IN"), [[0, 1]], 127, -1); ts(A("I1"), A("IN"), 15, ALU.bitwise_and); cp(A("K15"), A("I1"))
     ts(A("I2"), A("IN"), 31, ALU.bitwise_and, 1, ALU.arith_shift_right); cp(A("KB1"), A("I2")); cp(A("KB0"), A("KB1"), "va", 1.0, 16.0)
     iota(A("IP"), [[0, 1]], 0, 1); ts(A("I3"), A("IP"), 4, ALU.arith_shift_right, 1, ALU.bitwise_and); cp(A("G2"), A("I3"))
-    iota(A("SC24"), [[1, 24]]); cp(A("CEXP"), A("SC24"))
-    iota(A("IOC"), [[0, 24], [-1, 16]], 15); ts(A("MD"), A("IOC"), A("K15"), ALU.is_equal); ts(A("NMD"), A("IOC"), A("K15"), ALU.not_equal, 8192.0, ALU.mult)
-    iota(A("ONE"), [[0, 128]], 1)
+    iota(A("IOC"), [[0, 24], [-1, 16]], 15); ts(A("MD"), A("IOC", 0, 16), A("K15"), ALU.is_equal); ts(A("NMD"), A("IOC"), A("K15"), ALU.not_equal, 8192.0, ALU.mult)
+    ms(A("WN"), 0.0); step(A("ONE"), A("WN", 0, 128), "a")
     sel(A("IDB"), A("ONE"), [[-1, 128]], ALU.is_equal, 0.0, 0, 1); cp(A("ID32"), A("IDB"), "ag")
     sel(A("BO"), A("ONE"), [[-16, 8], [0, 16]], ALU.is_ge, 0.0, 0, 1); sel(A("BO"), A("BO"), [[16, 8], [0, 16]], ALU.is_ge, 0.0, 15, -1); cp(A("BO32"), A("BO"), "ag")
     sel(A("TRI"), A("BO"), [[1, 128]], ALU.is_gt, 0.0, 0, -1)
@@ -173,27 +189,26 @@ def build(case):
     sel(A("HALF"), A("ONE"), [[0, 4], [1, 2], [0, 16]], ALU.is_equal, 0.0, 0, -1)
     iota(A("MK"), [[0, 512]], -1024); sel(A("MK"), A("MK"), [[0, 32], [1, 2], [0, 8]], ALU.not_equal, 0.0, 0, -1)
     iota(A("IOG"), [[-1, 240]], 127); ts(A("SEL"), A("IOG"), A("K15"), ALU.is_equal)
-    ms(A3("UB", (0, 4)), 0.0)
-    for j in (1, 2, 3): cp(A3("UB", (4 * j, 4 * j + 4)), A3("UB", (0, 4)), "va")
-    ms(A("WN"), 0.0)
-    sel(A("RS32"), A("WN", 0, 2 * L), [[0, 12], [1, 32]], ALU.not_equal, -1e6); sel(A("RSB"), A("WN", 0, 2 * L), [[0, 24], [1, 16]], ALU.not_equal, 16384.0)
+    ms(A3("UB1"), 0.0); cp(A("UA"), A3("UB1", None, (0, 64 * max(EARLY))), "va")
+    sel(A("RS32"), A("WN", 0, 128), [[0, 4], [1, 32]], ALU.not_equal, -1e6); sel(A("RSB"), A("WN", 0, 2 * L), [[0, 24], [1, 16]], ALU.not_equal, 16384.0)
     iota(A("SC12"), [[0, 2], [16, 12]], 15); ts(A("DUM0"), A("SC12"), A("K15"), ALU.subtract)
     cp(A("DUMX"), A("DUM0"), "va", 1.0, float(M)); cp(A("DUMC"), A("DUM0"), "va", 1.0, float(NK))
     iota(A("SCP", 0, 12), [[0, 6], [1, 2]]); ts(A("PARF", 0, 12), A("SCP", 0, 12), A("G2"), ALU.not_equal, 208.0, ALU.mult)
     tt(A("PARF", 0, 12), A("PARF", 0, 12), A("DUM0", 0, 12), ALU.add); cp(A("CTR", 0, 12), A("PARF", 0, 12))
-    ts(A("C1"), A("K15"), 7.5, ALU.is_lt, -63.0, ALU.mult); ts(A("C2"), A("K15"), -8.0, ALU.mult, A("C1"), ALU.add)
-    iota(A("SCC", 0, 12), [[64, 3], [2, 4]], 120); ts(A("CPERM", 0, 12), A("SCC", 0, 12), A("C2"), ALU.add)
     iota(A("C37"), [[-36, 2], [0, 12]], 37)
-    cp(A("OP", 0, 12), LP); cp(A("OQ", 0, 12), PP)
-    for d in (0, 1):
-        cp(H("MX", d), IND(A(("XR", "XP")[d], 0, 32), A(("OP", "OQ")[d], 0, 12)), "va")
-        cp(H("ME", d), IND(A(("XR", "XP")[d], 32, 64), A(("OP", "OQ")[d], 0, 12)), "va", 0.125)
+    ts(A("C1"), A("K15"), 7.5, ALU.is_lt, 56.0, ALU.mult)
+    ts(A("I4"), A("IP"), 4, ALU.arith_shift_right); tt(A("C3"), A("C1"), A("K15"), ALU.subtract); ts(A("C4"), A("I4"), 8.0, ALU.mult, A("C3"), ALU.add)
+    iota(A("SCB", 0, 12), [[128, 12]], 15); ts(A("CBLK", 0, 12), A("SCB", 0, 12), A("C4"), ALU.add)
+    cp(A("OP", 0, 12), LP)
+    cp(H("MX", 0), IND(A("XR", 0, 32), A("OP", 0, 12)), "va"); cp(H("ME", 0), IND(A("XR", 32, 64), A("OP", 0, 12)), "va", 0.125)
+    send([(H("MX", 1), H("MX", 0), 1), (H("ME", 1), H("ME", 0), 1)], 1)
+    dma("s", [(A("TC", 0, NK), ("tc", full))], 14, H("ME", 0))
     ts(A("KT", 0, 12), LP, 37.0, ALU.mult); tt(A("KT", 0, 12), A("KT", 0, 12), LT, ALU.add)
     ts(A("KT", 12, 24), PH, 37.0, ALU.mult); tt(A("KT", 12, 24), A("KT", 12, 24), PP, ALU.add)
     for d in (0, 1):
         ts(H("KEY0", d, 12), H("KT", d, 12), NK - 1, ALU.bitwise_and); cp(H("OKEY0", d, 12), H("KEY0", d, 12))
     cp(A("OHT0", 0, 12), LH); cp(A("OHT0", 12, 24), PT)
-    cp(A("Q", 0, 12), LP); ts(A("Q", 12, 24), PP, 37.0, ALU.mult)
+    ts(A("HT8"), HT, 8192.0, ALU.add); cp(A("Q", 0, 12), LP); ts(A("Q", 12, 24), PP, 37.0, ALU.mult)
     swap = lambda land, src, w: [(H(land, 1, w), H(src, 0, w), 1), (H(land, 0, w), H(src, 1, w), -1)]
 
     def uv(s):
@@ -201,15 +216,17 @@ def build(case):
         if s == 0:
             for d in (0, 1):
                 tt(H("UO0", d), IND(A("X", 0, M), H(o, d, 12)), H("MX", d), ALU.mult); send(pair[d:d + 1], 0.5)
+            dma("s", [(A("HC", 0, NK), ("hc", full))], 18, H("UO0", 0)); dma("s", [(A("E"), ("ee", full))], 28, H("UO0", 1)); dma("s", [nn(1, 0), nn(1, 1)], 20, H("UO0", 1))
         else:
             tt(A("UO1"), IND(A("X", 0, M), A(o)), A("MX"), ALU.mult); send(pair, 1)
         tt(A("VO%d" % s), IND(A(("E", "E32")[s], 0, M), A(o)), A("ME"), ALU.mult)
         send(swap("V%d" % s, "VO%d" % s, L), 2)
 
     def vblock(s, d):
-        hl, v = "VH%d" % s, H("V%d" % s, d)
-        cp(H(hl, 2 * d), v, "vag"); tt(H(hl, 2 * d + 1), v, H(hl, 2 * d), ALU.subtract)
-        dma("s", [(A3("VB%d" % d, 4 * (g % 2) + g // 2, None, grp(g)), A(hl, 2 * d * L, 2 * d * L + 2 * L, 1, grp(g))) for g in range(8)], 1)
+        v = H("V%d" % s, d); n = 3 if s and any(c // 3 == d for c in SPLIT) else 2
+        cp(H("VH", 3 * d), v, "vag"); tt(H("VH", 3 * d + 1), v, H("VH", 3 * d), ALU.subtract)
+        if n == 3: cp(H("VH", 3 * d + 2), H("VH", 3 * d), "va", -1.0)
+        dma("s", [(A3("VB%d" % d, 4 * (g % 2) + g // 2, (0, n * L), grp(g)), A("VH", 3 * d * L, (3 * d + n) * L, 1, grp(g))) for g in range(8)], 1)
 
     def lists(s, d):
         cand = IND(A(("HC", "TC")[d], 0, NK), H("OKEY%d" % s, d, 12))
@@ -224,69 +241,81 @@ def build(case):
             lst = []
             for l in range(l0, l0 + 64):
                 c, j16 = divmod(l, 16); j, q = divmod(c, 4)
-                lst.append((A(sc, 128 * j + j16, 128 * j + 128, 16, quad(q)), A("XG", 32 * (d * L + l), 32 * (d * L + l) + 32),
-                            A3("UB", (8 * d, 8 * d + 8), l), True, True))
+                lst.append((A3(sc, j, (j16, 128, 16), quad(q)), A("XG", 32 * (d * L + l), 32 * (d * L + l) + 32),
+                            A3("UB%d" % d, None, l) if d or l >= 64 * EARLY[0] else A("UA", 64 * (l // 8) + l % 8, 64 * (l // 8) + 64, 8), True, True))
             mm(lst)
-        cp(A(scs), A(sc, 0, 384), "va", 32.0, A("KB%d" % d))
-        mm([(H(sc, j, 128), A(scs, 128 * j, 128 * j + 128), A("ID32"), True, True) for j in range(3)])
+        cp(A(scs), A3(sc, (0, 3)), "va", 32.0, A("KB%d" % d))
+        mm([(A3(sc, j), A(scs, 128 * j, 128 * j + 128), A("ID32"), True, True) for j in range(3)])
         mm([(A3("PZ", 3 * d + j), A(scs, 128 * j, 128 * j + 128), A("RD"), True, True) for j in range(3)])
         w0, t0 = 224 * d, 416 * d
-        scan(A("RM%d" % d), A("RS32"), A(sc, 0, 384), 0.0, ALU.add, ALU.max); cp(H("MI", d, 12), A("RM%d" % d, 31, None, 32))
+        for j in range(3): scan(H("RM%d" % d, j, 128), A("RS32"), A3(sc, j), 0.0, ALU.add, ALU.max)
+        cp(H("MI", d, 12), A("RM%d" % d, 31, None, 32))
         step(A("WN", w0 + 16, w0 + 208), A3("PZ", (3 * d, 3 * d + 3)))
         tr(A("TT", t0, t0 + L), A("WN", w0 + 16, w0 + 208)); tr(A("TT", t0 + L, t0 + 416), A("WN", w0, w0 + 224))
         tt(H("WDD", d), IND(A("TT", t0, t0 + 416), A("CTR", 0, 12)), H("DD", d), ALU.mult)
         tt(H("AF", d), H("WDD", d), ent(0, d), ALU.add)
-        cp(H("OA", d), IND(H("AF", d), A("CPERM", 0, 12)))
-        p0, p1 = H(sc, 0), H(sc, 1)
-        ts(H("KK", d, 12), H("MI", d, 12), 15, ALU.bitwise_and); tt(H("E1", d), IND(A("KK"), H("CEXP", d, 12)), H("MD", d), ALU.mult)
-        mm([(p0, A("BO"), H("E1", d), True, True)]); ts(p0, p0, A("K15"), ALU.is_equal)
-        tt(H("OAA", d), p0, H("AF", d), ALU.mult); mm([(p1, A("BO32"), H("OAA", d), True, True)])
+        cp(H("OA", d), H("AF", d))
+        p0, p1 = A3(sc, (0, 2), (0, 96)), A3(sc, (2, 4), (0, 96))
+        ts(H("KK", d, 12), H("MI", d, 12), 15, ALU.bitwise_and); ts(H("OKK", d, 12), H("KK", d, 12), -1.0, ALU.mult, 15.0, ALU.add)
+        tt(H("OAA", d), IND(A("MD"), H("OKK", d, 12)), H("AF", d), ALU.mult); mm([(p1, A("BO32"), H("OAA", d), True, True)])
         mm([(p0, A("IDB"), H("NMD", d), True, False), (p0, A("BO32"), H("OAA", d), False, True)])
-        cp(H("BR16", d), p1); scan(H("BSC", d), H("RSB", d), p0, 0.0, ALU.add, ALU.min)
+        cp(H("BR16", d), p1)
+        for j in (0, 1): scan(H("BSC", 2 * d + j, 96), A("RSB", 0, 96), A3(sc, j, (0, 96)), 0.0, ALU.add, ALU.min)
 
     def duel(d, ch):
         xc = 32 * d * L + 1024 * ch; xn = xc + 16 * L; o0 = d * L + 64 * ch; b = ch % 2
         cp(A("XG", xn, xn + 1024), IND(A("X", 0, M), A("OFN", 2 * L + o0, 2 * L + o0 + 64)), who(1, o0 // 32 + 1))
         cp(A("XG", xc, xc + 1024), IND(A("X", 0, M), A("OFC", 2 * L + o0, 2 * L + o0 + 64)), who(1, o0 // 32), -1.0)
-        lst = []
+        lst = [(A3("S0"), A("OWN", p=(0, 8)), A("THM", p=(0, 8)), True, False)]
         for t in range(8):
             for n, x0 in enumerate((xn, xc)):
                 lst.append((A3("S0", None, (8 * t, 8 * t + 8)), A("XG", x0 + 128 * t, x0 + 128 * t + 128),
-                            A3("UB", (8 * d, 8 * d + 8), (64 * ch + 8 * t, 64 * ch + 8 * t + 8)), n == 0, n == 1))
+                            A3("UB%d" % d, None, (64 * ch + 8 * t, 64 * ch + 8 * t + 8)) if d or ch >= EARLY[1] else H("UA", 8 * ch + t, 64), False, t == 7 and n == 1))
         mm(lst)
-        tt(A("AM"), A3("S0"), A("THM"), ALU.is_lt)
+        step(A("AM"), A3("S0"))
         mm([(A("S1", 0, 64), A("SEL", 112 - 16 * g, 240 - 16 * g), H("AM", g, 64), g == 0, g == 7) for g in range(8)])
         tt(A("S1", 64, 128), A("S1", 0, 64), A("DD", o0, o0 + 64), ALU.mult)
         tt(H("A64", b, 64), A("S1", 64, 128), A("NN", 2 * L + o0, 2 * L + o0 + 64), ALU.add)
-        cp(A("OA", o0, o0 + 64), IND(H("A64", b, 64), A("CPERM", 0, 4)))
+        cp(A("OA", o0, o0 + 64), H("A64", b, 64))
 
     ring = [0]
 
-    def turn(dst, src, e0, n):
+    def turn(dst, src, e0, n, scale=None):
         bank = "PT%d" % (ring[0] % 2); ring[0] += 1
         mm([(H(bank, t, 128), A(src, e0 + 128 * t, e0 + 128 * t + 128), A("IDB")) for t in range(n)], "trp")
-        cp(A(dst, e0, e0 + 128 * n), A(bank, 0, 128 * n), "va")
+        cp(A(dst, e0, e0 + 128 * n), A(bank, 0, 128 * n), "va", scale)
 
     def ublock(s, d):
-        dma("s", [(A3("UB", 8 * d + g, None, grp(g)), A("U%d" % s, d * L, d * L + L, 1, grp(g))) for g in range(8)], 0.5)
+        l0 = 0 if d else 64 * EARLY[s]
+        if l0: cp(IND(A("UA"), A("CBLK", 0, l0 // 16)), A("U%d" % s, 0, l0))
+        if l0 < L: dma("s", [(A3("UB%d" % d, g, (l0, L), grp(g)), A("U%d" % s, d * L + l0, d * L + L, 1, grp(g))) for g in range(8)], 0.5)
+
+    def fetch(s, c, t0=0, n=8, j=None):
+        off = A("OA", 64 * c + 8 * t0, 64 * c + 8 * (t0 + n)); e0 = 1024 * c + 128 * t0; x0 = e0 % 4096
+        ea, el = A("EA", e0, e0 + 128 * n), A("EL", x0, x0 + 128 * n)
+        if s and c in SPLIT:
+            ef = H("EF", SPLIT.index(c) % 2, 1024)
+            cp(ef, IND(A("E32", 0, M), off), "va", -1.0); cp(ea, ef, "va", -1.0)
+            dma("g", [(ef, ea)], "add"); dma("g", [(el, ef)], 0)
+        else:
+            cp(ea, IND(A(("E", "E32")[s], 0, M), off), "va")
+            if s: tt(el, IND(A("E32", 0, M), off), ea, ALU.subtract)
 
     def reals(s, c, wide, t0=0, n=8, j=None):
-        d, ch = divmod(c, 3); off = A("OA", 64 * c + 8 * t0, 64 * c + 8 * (t0 + n)); e0 = 1024 * c + 128 * t0; m = 128 if wide else 32
+        d, ch = divmod(c, 3); e0 = 1024 * c + 128 * t0; x0 = e0 % 4096; m = 128 if wide else 32; split = s and c in SPLIT
         rows, w = ((0, 8) if wide else (2 * ch, 2 * ch + 2), 64) if j is None else ((j, j + 1), 16 * n)
-        ea, el = A("EA", e0, e0 + 128 * n), A("EL", e0, e0 + 128 * n)
-        cp(ea, IND(A(("E", "E32")[s], 0, M), off), "va")
-        if s: tt(el, IND(A("E32", 0, M), off), ea, ALU.subtract)
-        for k, (src, parts) in enumerate((("EA", (0, 1)), ("EL", (0,)))[:s + 1]):
+        turn("ET", "EA", e0, n)
+        for k, (src, parts) in enumerate((("EA", (0, 1)), ("EL", (2 if split else 0,)))[:s + 1]):
+            if k: e0 = x0
             lst = [] if k else [(A3("PZ", rows, (0, w)), A("HALF", p=(0, 2)), A("MK", 0, 4 * m, 8 // n, (0, 2)), True, False)]
             for e in range(0, 128 * n, m):
                 t, p0 = divmod(e, 128)
                 for part in parts:
-                    l0 = part * L + 64 * ch + p0 // 2 + t0 + t
-                    lst.append((A3("PZ", rows, (t, w, n), (p0, p0 + m)), A(src, e0 + e, e0 + e + m), A3("VB%d" % d, None, (l0, l0 + m // 2 - 7, 8)), False,
+                    l0 = part * L + 64 * ch + 8 * (t0 + t) + p0 // 16
+                    lst.append((A3("PZ", rows, (t, w, n), (p0, p0 + m)), A(src, e0 + e, e0 + e + m), A3("VB%d" % d, None, (l0, l0 + m // 16)), False,
                                 k == s and t == n - 1 and part == parts[-1]))
             mm(lst)
-        turn("ET", "EA", e0, n)
-        if s: turn("EU", "EL", e0, n)
+        if s: turn("EU", "EL", x0, n, -1.0 if split else None)
 
     def weights(c, nc, wide, t0=0, n=8, j=None, quick=False):
         d, ch = divmod(c, 3)
@@ -308,23 +337,22 @@ def build(case):
 
     def sums(s, c, t0=0, n=8, j=None):
         d, ch = divmod(c, 3); bank, h = "PG%d" % (c // 2), c % 2; lst = []
-        if s == 0 and h == 0: mm([(A3(bank) if c == 4 else A(bank), A("IDB"), A("ZERO", 0, 512), True, False)])
         for src, k in (("ET", 2), ("EU", 1))[:s + 1]:
             for t in range(t0, t0 + n):
                 for a in range(4):
-                    e0 = 1024 * c + 128 * t + 32 * a
-                    out = A3(bank, (0, 2 * k), (64 * h + t, 64 * h + 64, 8), quad(a)) if c > 3 else A(bank, 256 * h + t, 256 * h + 128 * k, 8, quad(a))
+                    e0 = (1024 * c + 128 * t + 32 * a) % (4096 if k == 1 else 6144)
+                    out = A3(bank, (0, 2 * k), (64 * h + 8 * t, 64 * h + 8 * t + 8), quad(a))
                     w = A3("WB%d" % d, (16 * ch, 16 * ch + 8 * k), (16 * a + t, 16 * a + 16, 8)) if j is None else A3("WQ%d" % j, (0, 8 * k), (2 * n * a + t - t0, 2 * n * (a + 1), n))
                     lst.append((out, A(src, e0, e0 + 32), w, False, src == "EU" and h == 1 and t == 7))
         mm(lst)
         if s == 1 and h == 1 and t0 + n == 8:
-            if c == 5: parts = [(A3("GS1", None, (64, L)), A3(bank, (0, 2)), A3(bank, (2, 4)))]
-            else: parts = [(A3("GS%d" % (x // 3), None, (64 * (x % 3), 64 * (x % 3) + 64)), H(bank, 2 * (x % 2), 128), H(bank, 2 * (x % 2) + 1, 128)) for x in (c - 1, c)]
+            if c != 3: parts = [(A3("GS%d" % d, None, (64 * ch - 64, 64 * ch + 64)), A3(bank, (0, 2)), A3(bank, (2, 4)))]
+            else: parts = [(A3("GS%d" % x, None, (128 - 128 * x, L - 128 * x)), A3(bank, (0, 2), (64 * x, 64 * x + 64)), A3(bank, (2, 4), (64 * x, 64 * x + 64))) for x in (0, 1)]
             for out, hi, lo in parts: cp(out, hi, "va"); tt(out, lo, out, ALU.add)
             if c > 1:
                 y = c // 4
                 for q in (0, 1):
-                    dma("sa"[q], [((("yh", "yt")[y], (slice(*grp(g)), slice(None))), A3("GS%d" % y, g % 2, None, grp(g))) for g in range(4 * q, 4 * q + 4)], 0.5)
+                    dma("sa"[q * y], [((("yh", "yt")[y], (slice(*grp(g)), slice(None))), A3("GS%d" % y, g % 2, None, grp(g))) for g in range(4 * q, 4 * q + 4)], 0.5)
 
     def first(rep, col, bank, out):
         mm([(A(bank, 0, 2 * L), A("IDB"), A("NMD"), True, False)])
@@ -339,24 +367,32 @@ def build(case):
         scan(A(out), A("RSB"), A(bank, 0, 2 * L), 0.0, ALU.add, ALU.min)
 
     uv(0)
-    for d in (0, 1): lists(0, d); ublock(0, d)
-    dma("g", [(A("E32", 0, M), ("ee", full))], 24)
     iota(A("ZERO"), [[0, 768]])
-    for n, r in (("VB0", 2), ("VB1", 2), ("WB0", 12), ("WB1", 12)): dma("s", [(A3(n, (r * j, r * j + r)), A("ZERO")) for j in range(4)], 6)
-    dma("s", [(A3("WQ%d" % j), A("ZERO", 0, 128 * n)) for j, n in enumerate(LAST)], 2)
-    iota(A("THM"), [[0, 512]], 1); sel(A("THM"), A("THM"), [[0, 64], [-16, 8]], ALU.is_ge, -32768.0, 0, 1); sel(A("THM"), A("THM"), [[0, 64], [16, 8]], ALU.is_ge, -32768.0, 15, -1)
-    cp(A("KF"), A("KEY0")); tt(A("BD"), IND(A("KF"), A("CEXP")), A("MD"), ALU.mult)
-    mm([(S384, A("BO32"), A("BD"), True, True)]); cp(A("KR16"), S384)
-    first("KR16", "KF", "S1", "FSK")
-    tt(A("G3"), A("FSK", 15, None, 16), A("KF"), ALU.add); tt(A("G3"), A("G3"), A("DUMC"), ALU.min); cp(A("OSC"), A("G3"))
-    for d in (0, 1): contest(d); vblock(0, d)
+    dma("s", [(A3("UB0", (4 * j, 4 * j + 4)), A("ZERO")) for j in (0, 1)], 3, H("UO0", 1))
+    for d in (0, 1): lists(0, d); ublock(0, d)
+    dma("g", [(A("E32", 0, M), ("ee", full))], 24, A("V0"))
+    for n in ("VB1", "VB0"): dma("s", [(A3(n, (2 * j, 2 * j + 2), (0, 2 * L)), A("ZERO")) for j in range(4)], 6, H("U0", 0))
+    for n in ("WB1", "WB0"): dma("s", [(A3(n, (12 * j, 12 * j + 12)), A("ZERO")) for j in range(4)], 6, A("V0"))
+    for d in sorted({c // 3 for c in SPLIT}): dma("s", [(A3("VB%d" % d, (4 * j, 4 * j + 4), (2 * L, 3 * L)), A("ZERO")) for j in range(2)], 3)
+    dma("s", [(A3("WQ%d" % j), A("ZERO", 0, 128 * n)) for j, n in enumerate(LAST)], 2, A("V0"))
+    sel(A("OWN"), A("ONE"), [[1, 8], [0, 16]], ALU.is_equal, 0.0, 0, -1)
+    iota(A("THM"), [[0, 512]], 16384); sel(A("THM"), A("THM"), [[0, 64], [1, 8]], ALU.not_equal, 0.0, 0, -1)
+    iota(A("COUNT"), [[1, NK]]); cp(A("KF"), A("KEY0")); cp(A("KR16"), IND(A("COUNT"), A("OKEY0")))
+
+    def keys():
+        first("KR16", "KF", "S1", "FSK")
+        tt(A("G3"), A("FSK", 15, None, 16), A("KF"), ALU.add); tt(A("G3"), A("G3"), A("DUMC"), ALU.min); cp(A("OSC"), A("G3"))
+
+    if KEARLY: keys()
+    for d in (1, 0):
+        k = len(ops); contest(d); vblock(0, d)
+        for o in ops[k:]: o["bias"] = BOOST * d
     ts(A("EXS"), A("MI"), 4, ALU.arith_shift_right)
     send(swap("INS", "EXS", 12), 0)
     BL = A("BSC", 15, None, 16)
     cp(A("OB"), BL)
     tt(A("Z1"), BL, A("C37"), ALU.mult); tt(A("Z2"), A("Z1"), A("Q"), ALU.add); ts(A("EXK"), A("Z2"), NK - 1, ALU.bitwise_and)
     send(swap("INK", "EXK", 12), 0)
-    for d in (0, 1): cp(IND(A(("HC", "TC")[d]), H("OSC", d, 12)), H("AF", d))
     act(A("SU"), A("U0"), ACT.Sign)
     tt(A("NX0"), IND(A("X", 0, M), A("OB")), A("SU"), ALU.subtract); ts(A("NX"), A("NX0"), -7.0, ALU.max, 7.0, ALU.min)
     tt(A("PV"), IND(A("E"), A("OB")), A("V0"), ALU.mult); mm([(S384, A("BO32"), A("PV"), True, True)])
@@ -366,10 +402,13 @@ def build(case):
     ts(A("BS0"), A("LV"), -8192.0, ALU.mult, 8192.0, ALU.add); tt(A("BS"), A("BS0"), BL, ALU.add)
     first("BR16", "BS", "S1", "FS")
     tt(A("F1"), A("FS", 15, None, 16), A("BS"), ALU.add); tt(A("F2"), A("F1"), A("DUMX"), ALU.min); cp(A("OSX"), A("F2"))
-    tt(A("G1"), BL, HT, ALU.subtract); tt(A("G1"), A("G1"), A("LV"), ALU.mult); tt(A("G1"), A("G1"), HT, ALU.add); cp(A("OHT1"), A("G1"))
+    tt(A("G1"), A("HT8"), A("BS0"), ALU.subtract); tt(A("G1"), A("G1"), A("BS"), ALU.min); cp(A("OHT1"), A("G1"))
     tt(A("G4"), A("KEY0"), A("INK"), ALU.subtract); tt(A("G4"), A("G4"), A("LV"), ALU.mult); tt(A("G4"), A("G4"), A("INK"), ALU.add); cp(A("OKEY1"), A("G4"))
-    for d in (0, 1):
-        for ch in range(3): reals(0, 3 * d + ch, False)
+    if not KEARLY: keys()
+    for d in (0, 1): cp(IND(A(("HC", "TC")[d]), H("OSC", d, 12)), H("AF", d))
+    for b in range(3): mm([(A3("PG%d" % b), A("IDB"), A("ZERO", 0, 512), True, False)])
+    for d in (1, 0):
+        for ch in range(3): fetch(0, 3 * d + ch); reals(0, 3 * d + ch, False)
         weights(3 * d, 3, False)
         for ch in range(3): sums(0, 3 * d + ch)
     for d in (0, 1): cp(IND(A("X"), H("OSX", d, 12)), H("NX", d))
@@ -378,11 +417,19 @@ def build(case):
     for d in (0, 1):
         lists(1, d); ublock(1, d); vblock(1, d)
     for c in range(6):
-        duel(*divmod(c, 3))
-        if c < 5: reals(1, c, c in WIDE); weights(c, 1, c in WIDE); sums(1, c)
+        k = len(ops); duel(*divmod(c, 3))
+        for o in ops[k:k + 2]: o["bias"] = AHEAD * c
+        if c < 4: fetch(1, c)
+    for c in TURN:
+        if c == 4: fetch(1, c)
+        reals(1, c, c in WIDE); weights(c, 1, c in WIDE, quick=c - 5 >= len(LAST) - QUICK); sums(1, c)
     for j, n in enumerate(LAST):
         piece = (sum(LAST[:j]), n, j)
-        reals(1, 5, False, *piece); weights(5, 1, False, *piece, quick=j >= len(LAST) - QUICK); sums(1, 5, *piece)
+        fetch(1, 5, *piece); reals(1, 5, False, *piece); weights(5, 1, False, *piece, quick=j >= len(LAST) - QUICK); sums(1, 5, *piece)
+    seen = {}
+    for o in ops:
+        n = o["wr"][0]["n"] if o["wr"] else "y"; k = seen[n] = seen.get(n, -1) + 1; x = DUE.get(n, [])
+        o["due"] = 1000.0 * x[k] if k < len(x) and x[k] else 1000.0 * END
     return ops
 
 
@@ -412,25 +459,26 @@ def schedule(ops, succ, bias, lean, WAKE, ahead=0.3):
     n = len(ops)
     pr = [0.0] * n
     for i in range(n - 1, -1, -1):
-        o = ops[i]; pr[i] = min(o["cost"].values()) + o["lat"] + WAKE + max([pr[k] for k in succ[i]] or [0.0]) + bias[i]
-    free = dict.fromkeys("vatgs", 0.0); ready = [0.0] * n; left = [len(o["deps"]) for o in ops]; eng = [None] * n; seq = []
+        o = ops[i]; pr[i] = o["cost"][o["eng"][0]] + max([o["hold"] + o["lat"] + WAKE + pr[k] for k in succ[i]] + [-o["due"]]) + bias[i]
+    free = dict.fromkeys("vatgsd", 0.0); ready = [0.0] * n; left = [len(o["deps"]) for o in ops]; eng = [None] * n; seq = []
     pool = [i for i in range(n) if not left[i]]
     while pool:
         t, q = min((max(free[q], ready[i]), q) for i in pool for q in ops[i]["eng"] if q == ops[i]["eng"][0] or free[ops[i]["eng"][0]] > max(free[q], ready[i]) + lean[i])
         mine = [i for i in pool if q == ops[i]["eng"][0] or q in ops[i]["eng"] and free[ops[i]["eng"][0]] > max(free[q], ready[i]) + lean[i]]
         rank = lambda i: (q == ops[i]["eng"][0], pr[i])
         i = max((i for i in mine if ready[i] <= t), key=rank)
-        soon = [j for j in mine if t < ready[j] <= t + ahead * ops[i]["cost"][q] and rank(j) > rank(i)]
+        soon = [j for j in mine if t < ready[j] <= t + (1.0 if q == "g" else ahead) * ops[i]["cost"][q] and rank(j) > rank(i)]
         if soon: i = min(soon, key=lambda j: ready[j]); t = ready[i]
-        pool.remove(i); seq.append(i); eng[i] = q; free[q] = t + ops[i]["cost"][q]
+        pool.remove(i); seq.append(i); eng[i] = q; t = free[q] = t + ops[i]["cost"][q]
+        if ops[i]["hold"]: t = free["d"] = max(t, free["d"]) + ops[i]["hold"]
         for k in succ[i]:
-            ready[k] = max(ready[k], free[q] + (0.0 if q == "t" == ops[k]["eng"] else ops[i]["lat"] + WAKE)); left[k] -= 1
+            ready[k] = max(ready[k], t + (0.0 if q == "t" == ops[k]["eng"] else ops[i]["lat"] + WAKE)); left[k] -= 1
             if not left[k]: pool.append(k)
     return seq, eng
 
 
 PLAN = {}
-ROUNDS, MOVES, HEAT = 2000, 150000, 200.0
+ROUNDS, MOVES, STARTS, HEAT, SHOW = 100, 300000, 3, 150.0, 0
 
 
 def plan():
@@ -439,9 +487,10 @@ def plan():
         deps = [list(o["deps"]) for o in ops]; succ = [[] for _ in ops]
         for i in range(n):
             for j in deps[i]: succ[j].append(i)
-        rng = np.random.default_rng(7); flex = [i for i in range(n) if len(ops[i]["cost"]) > 1]
+        rng = np.random.default_rng(SEED); flex = [i for i in range(n) if len(ops[i]["cost"]) > 1]
         tabs = [([o["cost"] for o in oo], [o["lat"] for o in oo], c[5]) for oo, c in zip(all_ops, CASES)]
         figs = [{q: [x[0][i][q] for x in tabs] + [x[1][i] + x[2] for x in tabs] for q in ops[i]["cost"]} for i in range(n)]
+        held = {i: [oo[i]["hold"] for oo in all_ops] for i in range(n) if ops[i]["hold"]}
         above = []
         for i in range(n):
             x = 0
@@ -451,22 +500,35 @@ def plan():
         inline = lambda i, j: ops[i]["eng"] == ops[j]["eng"] and (ops[i]["eng"] == "t" or len(ops[i]["eng"]) == 1 and not ops[i]["deps"][j])
         dp = [[j for j in deps[i] if direct(i, j) and not inline(i, j)] for i in range(n)]
 
-        def ends(seq, eng):
-            free = dict.fromkeys("vatgs", (0.0, 0.0, 0.0)); d0, d1, d2 = [0.0] * n, [0.0] * n, [0.0] * n
-            for i in seq:
-                q = eng[i]; t0, t1, t2 = free[q]; c0, c1, c2, l0, l1, l2 = figs[i][q]
+        kept = {}; load = {i: {q: 0.0 if q == "g" else sum(f[:3]) for q, f in figs[i].items()} for i in flex}
+
+        def ends(seq, eng, p0=0):
+            p0 -= p0 % 16
+            if p0: marks = kept["marks"][:p0 // 16]; free = dict(kept["marks"][p0 // 16]); d0, d1, d2 = [list(x) for x in kept["done"]]
+            else: marks = []; free = dict.fromkeys("vatgsd", (0.0, 0.0, 0.0)); d0, d1, d2 = [0.0] * n, [0.0] * n, [0.0] * n
+            kept["new"] = (marks, (d0, d1, d2))
+            for p in range(p0, n):
+                if not p & 15: marks.append(dict(free))
+                i = seq[p]; q = eng[i]; t0, t1, t2 = free[q]; c0, c1, c2, l0, l1, l2 = figs[i][q]
                 for j in dp[i]:
                     if d0[j] > t0: t0 = d0[j]
                     if d1[j] > t1: t1 = d1[j]
                     if d2[j] > t2: t2 = d2[j]
-                t0 += c0; t1 += c1; t2 += c2; free[q] = (t0, t1, t2); d0[i] = t0 + l0; d1[i] = t1 + l1; d2[i] = t2 + l2
+                t0 += c0; t1 += c1; t2 += c2; free[q] = (t0, t1, t2)
+                if i in held:
+                    h, e = held[i], free["d"]; t0 = max(t0, e[0]) + h[0]; t1 = max(t1, e[1]) + h[1]; t2 = max(t2, e[2]) + h[2]; free["d"] = (t0, t1, t2)
+                d0[i] = t0 + l0; d1[i] = t1 + l1; d2[i] = t2 + l2
             return [max(d0), max(d1), max(d2)]
+
+        def score(seq, eng, p0=0):
+            x = ends(seq, eng, p0)
+            return sum(w * (e + PULL * sum(d) / n) for w, e, d in zip(WEIGHTS, x, kept["new"][1])) + LOAD * sum(load[i][eng[i]] for i in flex)
 
         def judge(bias, lean):
             seq, eng = schedule(ops, succ, bias, lean, CASES[0][5])
-            return sum(ends(seq, eng)), seq, eng
+            return score(seq, eng), seq, eng
 
-        bias, lean = [0.0] * n, [300.0] * n; best = judge(bias, lean)
+        bias, lean = [o["bias"] for o in ops], [LEAN if o["kind"] in ("cp", "step") and o["wr"][0]["cnt"] >= 512 else 300.0 for o in ops]; best = judge(bias, lean)
         for _ in range(ROUNDS):
             b2, l2 = list(bias), list(lean)
             for _k in range(int(rng.integers(1, 4))):
@@ -476,12 +538,16 @@ def plan():
             if r[0] <= best[0]: best, bias, lean = r, b2, l2
 
         def chain(seq, eng, case):
-            cost, lat, wake = tabs[case]; free = {q: (0.0, -1) for q in "vatgs"}; done = [0.0] * n; why = [None] * n
+            cost, lat, wake = tabs[case]; free = {q: (0.0, -1) for q in "vatgsd"}; done = [0.0] * n; why = [None] * n
             for i in seq:
                 t, k = free[eng[i]]; queue = True
                 for j in dp[i]:
                     if done[j] > t: t, k, queue = done[j], j, False
-                why[i] = (k, queue); t += cost[i][eng[i]]; free[eng[i]] = (t, i); done[i] = t + lat[i] + wake
+                t += cost[i][eng[i]]; free[eng[i]] = (t, i)
+                if i in held:
+                    if free["d"][0] > t: (t, k), queue = free["d"], True
+                    t += held[i][case]; free["d"] = (t, i)
+                why[i] = (k, queue); done[i] = t + lat[i] + wake
             i = done.index(max(done)); out = []
             while i >= 0:
                 k, queue = why[i]
@@ -489,8 +555,19 @@ def plan():
                 i = k
             return out
 
-        cur, seq, eng = best; top = cur; keep = (list(seq), list(eng)); draws = rng.random((MOVES, 5)).tolist(); arcs = None
+        runs = []; each = MOVES // (STARTS + 2); draws = rng.random((MOVES, 5)).tolist()
         for it, (r0, r1, r2, r3, r4) in enumerate(draws):
+            if it % each == 0 and it <= STARTS * each:
+                if it: runs.append((top, keep))
+                cur, (seq, eng) = (best[0], best[1:]) if it < STARTS * each else min(runs)
+                top = cur; keep = (list(seq), list(eng)); arcs = None; score(seq, eng); kept["marks"], kept["done"] = kept["new"]
+            heat = HEAT * (1.0 - it % each / each) if it < STARTS * each else 0.6 * HEAT * (MOVES - it) / (MOVES - STARTS * each)
+            if it % 500 == 0:
+                d0 = kept["done"][0]; at = [d0[i] - figs[i][eng[i]][0] - figs[i][eng[i]][3] - held.get(i, (0.0,))[0] for i in range(n)]; last = {}
+                for i in seq:
+                    at[i] = max([at[i], last.get(eng[i], 0.0)] + [at[j] for j in deps[i]]) + 1e-6; last[eng[i]] = at[i]
+                s2 = sorted(seq, key=lambda i: at[i]); v = score(s2, eng)
+                if v <= cur + HEAT: cur, seq = v, s2; kept["marks"], kept["done"] = kept["new"]
             if arcs is None: arcs = chain(seq, eng, int(r4 * len(tabs)))
             s2, e2 = seq, eng
             i, k = arcs[int(r1 * len(arcs))]
@@ -498,10 +575,10 @@ def plan():
                 i = (i, k)[r2 < 0.5] if r0 < 0.15 else flex[int(r1 * len(flex))]
                 other = [q for q in ops[i]["cost"] if q != eng[i]]
                 if not other: continue
-                e2 = list(eng); e2[i] = other[int(r4 * len(other))]
+                e2 = list(eng); e2[i] = other[int(r4 * len(other))]; lo = seq.index(i)
                 if r0 > 0.2:
                     j = flex[min(len(flex) - 1, max(0, flex.index(i) + int(r2 * 13) - 6))]
-                    if j != i and eng[j] == e2[i] and eng[i] in ops[j]["cost"]: e2[j] = eng[i]
+                    if j != i and eng[j] == e2[i] and eng[i] in ops[j]["cost"]: e2[j] = eng[i]; lo = min(lo, seq.index(j))
             elif r0 < 0.45:
                 s2 = list(seq); p = int(r1 * n); i = s2.pop(p); lo, hi = p, p
                 while lo > 0 and p - lo < 60 and s2[lo - 1] not in ops[i]["deps"]: lo -= 1
@@ -509,6 +586,7 @@ def plan():
                 s2.insert(lo + int(r2 * (hi - lo + 1)), i)
             else:
                 hi = seq.index(i); lo = seq.index(k)
+                if hi < lo: continue
                 if r0 < 0.75:
                     lo = max(0, lo - int(r2 * r2 * 30)); need = set(deps[i]); up, rest = [i], []
                     for j in reversed(seq[lo:hi]):
@@ -523,16 +601,17 @@ def plan():
                         else: rest.append(j)
                     if i in down: continue
                     s2 = seq[:lo] + rest + down + seq[hi + 1:]
-            v = sum(ends(s2, e2))
-            if v <= cur - HEAT * (1.0 - it / MOVES) * math.log(r3 + 1e-12):
-                cur, seq, eng = v, s2, e2; arcs = None
+            v = score(s2, e2, lo)
+            if v <= cur - heat * math.log(r3 + 1e-12):
+                cur, seq, eng = v, s2, e2; arcs = None if r4 < 0.3 else arcs; kept["marks"], kept["done"] = kept["new"]
                 if v < top: top, keep = v, (list(s2), list(e2))
             elif r4 < 0.05: arcs = None
         seq, eng = keep
-        free = {q: 0.0 for q in "vatgs"}; done = [0.0] * n; start = [0.0] * n
+        free = {q: 0.0 for q in "vatgsd"}; done = [0.0] * n; start = [0.0] * n; cost, lat, wake = tabs[SHOW]
         for i in seq:
-            start[i] = max([free[eng[i]]] + [done[j] for j in dp[i]]); free[eng[i]] = start[i] + ops[i]["cost"][eng[i]]
-            done[i] = free[eng[i]] + ops[i]["lat"] + CASES[0][5]
+            start[i] = max([free[eng[i]]] + [done[j] for j in dp[i]]); t = free[eng[i]] = start[i] + cost[i][eng[i]]
+            if i in held: t = free["d"] = max(t, free["d"]) + held[i][SHOW]
+            done[i] = t + lat[i] + wake
         PLAN.update(ops=ops, seq=seq, start=start, eng=eng, end=ends(seq, eng))
     return PLAN
 
@@ -586,7 +665,7 @@ def rank_program(g, core, T, topo):
             continue
         if k == "dma":
             sem = "d%d" % nd[0]; nd[0] += 1
-            for out, src in x: e.dma_start(ap(out), ap(src)).then_inc(T.sem[sem], 16)
+            for out, src in x: e.dma_start(ap(out), ap(src), **({"accum_op": ALU.add} if o["add"] else {})).then_inc(T.sem[sem], 16)
             token[i] = (sem, 16 * len(x)); total[sem] = 16 * len(x)
             continue
         if k == "cp":
@@ -607,7 +686,7 @@ def rank_program(g, core, T, topo):
         elif k == "ms": r = e.memset(ap(x[0]), x[1])
         elif k == "act": r = e.activation(ap(x[0]), ap(x[1]), x[2], scale=x[3])
         elif k == "step":
-            if q == "a": r = e.activation(ap(x[0]), ap(x[1]), ACT.Sigmoid, bias=64.0, scale=-4.0)
+            if q == "a": r = e.activation(ap(x[0]), ap(x[1]), ACT.Sigmoid, bias=64.0, scale=-128.0)
             else: r = e.tensor_scalar(ap(x[0]), ap(x[1]), 0.0, None, ALU.is_le)
         elif k == "sel": r = e.affine_select(ap(x[0]), ap(x[1]), x[2], x[3], x[4], x[5], x[6])
         elif k == "iota":

@@ -5,45 +5,52 @@ from concourse.mybir import AluOpType as ALU, ActivationFunctionType as ACT
 
 M, NK, L, D, NR = 4096, 1024, 192, 3, 8
 B, F, I, U = "bfloat16", "float32", "int32", "uint16"
-WIDE = (0, 1, 2, 3, 4)
-TURN = (0, 1, 2, 3, 4)
+WIDE = (0, 1, 2, 3, 4, 5)
+PAIRS = ()
+DIRECT = (4, 5)
 EARLY = (2, 1)
-SPLIT = ()
-LAST = (4, 2, 2)
-QUICK = 2
-ONV = ((0, 1, 3, 5, 8), (2, 9))
+LAST = (2,)
+NEQ, RO, ZB, LAG, AHEAD, APART = 12, "va", (1, 1, 0, 1, 0, 1), 3, 0, 0
+NEF, NET, NEA, NW = 2, 4, 3, 3
+ONV = ((7, 9, 6, 1), (2, 9))
+NL = sum(LAST)
+TH = ()
 SCRATCH, PLACE = {}, {}
 
 
 def _buf(names, cols, dtype, where="sbuf"):
     for n in names.split():
-        if cols in (1, 24):
+        if cols in (1, 12, 24):
             home = "SMALL_" + dtype
             at = SCRATCH[home][1][1] if home in SCRATCH else 0
-            PLACE[n] = (home, at, cols); SCRATCH[home] = (where, [128, at + (16 if cols == 1 else 32)], dtype)
+            PLACE[n] = (home, at, cols); SCRATCH[home] = (where, [128, at + (32 if cols == 24 else 16)], dtype)
         else:
             SCRATCH[n] = (where, [128] + (list(cols) if isinstance(cols, tuple) else [cols]), dtype)
 
 
 _buf("X", M + L, B); _buf("E", M, B); _buf("E32", M + L, F); _buf("HC TC", NK + L, I); _buf("NN", 4 * L, I)
-_buf("XR", 64, B); _buf("LL", 72, I); _buf("MX ME", 2 * L, B)
-_buf("IP IN I1 I2 I3 I4", 1, I); _buf("K15 KB0 KB1 G2 C1 C2 C3 C4", 1, F)
-_buf("ID32 BO32", 128, F); _buf("IDB BO TRI ONE HALF OWN", 128, B); _buf("MK", 512, B); _buf("ZERO", 768, B); _buf("W32", 256, F); _buf("RD", 64, F)
-for _j, _n in enumerate(LAST): _buf("WQ%d" % _j, (16, 8 * _n), B)
-_buf("RS32", 128, B); _buf("MD", 16, B); _buf("COUNT", NK, I); _buf("RSB NMD IOC", 2 * L, B); _buf("THM AM", 512, B); _buf("SEL IOG", 240, B); _buf("A64", 128, F)
-_buf("SC12 SCP SCB", 24, I); _buf("DUM0 DUMX DUMC C37 PARF", 24, F)
-_buf("OKK CTR CBLK OP OHT0 OHT1 OKEY0 OKEY1 OB OSX OSC", 24, U)
-_buf("KEY0 KT Q MI EXS INS EXK INK KK Z2", 24, I)
-_buf("Z1 LV BS0 BS F1 F2 G1 G3 G4 KF HT8", 24, F)
+_buf("XR", 64, B); _buf("LL", 36, I); _buf("S16", 48, U); _buf("RL", 24, I); _buf("OT RKEY", 12, U); _buf("MX ME", 2 * L, B)
+_buf("IP IN I1 I2 I3 I4", 1, I); _buf("K15 KB0 KB1 G2 C1 C3 C4", 1, F)
+_buf("ID32 BO32", 128, F); _buf("IDB BO TRI ONE HALF OWN OWNN" + " HALFP" * bool(PAIRS), 128, B); _buf("COL" + " THR" * bool(TH), 512, B); _buf("IH", 128, I)
+_buf("ZERO", 768, B); _buf("ZERO32", 384, F); _buf("RD", 128, F); _buf("RS32", 2 * L, B); _buf("MD", 16, B); _buf("COUNT", NK, I)
+_buf("RSB NMD NMD2 IOC SELQ", L, B); _buf("DRX DRC", L, F); _buf("AM", 512, B); _buf("SEL IOG", 240, B); _buf("A64", 128, F)
+_buf("SC12 SCP SCB", 12, I); _buf("DUM0 PARF", 12, F); _buf("C37", 24, F); _buf("CTR CBLK ROSC", 12, U)
+_buf("OKK OHT1 OKEY1 OB OSX OSC", 24, U)
+_buf("KA KB KEY KEY0 Q MI INS EXK INK KK Z2", 24, I)
+_buf("Z1 LV BS0 BS F1 G1 G3 G4 KF HT8", 24, F)
 _buf("UO0 UO1 U0 U1 SU NX0 NX", 2 * L, B)
-_buf("VO0 VO1 V0 V1 DD WDD AF OAA BSC FS FSK PV WV EB SCS0 SCS1 RM0 RM1", 2 * L, F)
-_buf("VH", 6 * L, B); _buf("BR16 KR16", 2 * L, U); _buf("OFN OFC", 4 * L, U); _buf("OA", 2 * L, U)
-_buf("UA", 512 * max(EARLY), B); _buf("UB0 UB1", (8, L), B); _buf("VB0 VB1", (8, 3 * L), B); _buf("WB0 WB1", (48, 64), B); _buf("WC", (6, 256), B); _buf("WP", 256, B)
-_buf("XG", 64 * L, B); _buf("EA ET", 32 * L, B); _buf("EL EU", 4096, B); _buf("EF", 2048 if SPLIT else 8, F)
-_buf("WN", 448, B); _buf("TT", 832, B); _buf("EQ", (24, L), B); _buf("GS0 GS1", (2, L), F)
-_buf("S0 PZ", (8, 64), F, "psum"); _buf("S1", 512, F, "psum"); _buf("PG0 PG1 PG2", (4, 128), F, "psum"); _buf("PT0 PT1", 1024, B, "psum")
-NDMA = 56
-SEMAPHORES = ["cv", "ca", "ct", "cg", "loc"] + ["d%d" % i for i in range(NDMA)] + ["r%d" % i for i in range(16)]
+_buf("VO0 VO1 V0 V1 DD AF OAA BSC FS PV WV EB SCS0 SCS1", 2 * L, F)
+_buf("VH", 4 * L, B); _buf("BR16 KR16 OA", 2 * L, U); _buf("OFN OFC", 4 * L, U)
+if max(EARLY): _buf("UA", 512 * max(EARLY), B)
+VEARLY = 1
+_buf("VA", 512 * VEARLY, F)
+_buf("UB0 UB1", (8, L), B); _buf("VB0 VB1", (8, 2 * L), B); _buf("VF0 VF1", (8, L), F)
+_buf("WC", (16, 96), B); _buf("WB0 WB1", (32, 96), B); _buf("WS", 128 * NW, F); _buf("WF", (32 * NW, 16), F); _buf("WL", 64 * NL, F)
+_buf("XG", 64 * L, B); _buf("EA", 1024 * NEA, B); _buf("ET", 32 * L, B); _buf("EF", 1024 * NEF + 128 * NL, F); _buf("EU", 1024 * NET + 128 * NL, F)
+_buf("WN", (24, 16), B); _buf("EQ", (NEQ, L), B); _buf("GY0 GY1", (64, 8), F)
+_buf("PZ0 PZ1 PGA PGB PGC", (64, 8), F, "psum"); _buf("S0", (32, 16), F, "psum"); _buf("S1 PT", 512, F, "psum")
+NDMA = 64
+SEMAPHORES = ["cv", "ca", "ct", "cg", "loc"] + ["d%d" % i for i in range(NDMA)] + ["r%d" % i for i in range(20)]
 
 
 def A(n, a=None, b=None, st=1, p=(0, 128)):
@@ -64,6 +71,12 @@ def A3(n, rows=None, cols=None, p=(0, 128)):
             "runs": len(r) if r.step > 1 or len(c) < w else 1}
 
 
+def PB(n, a, cnt, runs=1, st=0, p=(0, 128)):
+    w = SCRATCH[n][1][2]
+    if runs == 1 and cnt > w: return A3(n, (a // w, (a + cnt) // w), None, p)
+    return A3(n, (a // w, a // w + (runs - 1) * st // w + 1, max(1, st // w)), (a % w, a % w + cnt), p)
+
+
 def IND(win, off):
     return dict(win, off=off, cnt=16 * off["cnt"])
 
@@ -76,16 +89,13 @@ def psum(a):
     return SCRATCH[a["n"]][0] == "psum"
 
 
-CASES = [(1.0, 0.5, 1.55, 4.2, 3, 140, 2000, 2400, 1500, 15), (0.87, 0.44, 1.1, 2.4, 3, 120, 2100, 2600, 2000, 20), (1.2, 0.6, 2.3, 5.5, 4, 170, 2000, 2400, 1500, 15)]
-WEIGHTS, PULL, LOAD, LEAN, BOOST, AHEAD, SEED = (1.0, 0.8, 1.0), 0.2, 0.03, 6000.0, 0.0, 0.0, 1
-END = 75
-KEARLY = True
-DUE = {"XG": [6.5, 11, 8, 12.5, 9.5, 13, 7, 14, 11, 15, 12.5, 16.5, 30.5, 40, 32.2, 41, 33.9, 43, 35.5, 45, 37.2, 48, 38.9, 52],
-       "EA": [19, 20.7, 22.3, 24, 25.7, 27.4, 47, 50, 54, 57.5, 60], "SCS1": [15], "SCS0": [18.5], "OA": [17.5, 22], "X": [0, 28, 28.8],
-       "FSK": [34], "U1": [30], "LL": [0.2, 3], "U0": [5.2, 8.5], "MX": [3.1, 3.8], "ME": [3.4], "UA": [0, 12], "V0": [12],
-       "XR": [0.3], "ONE": [1.8], "WC": [30, 31, 37, 38], "ET": [36, 37, 38, 40, 41, 42], "KR16": [28], "PG1": [0] * 9 + [38, 44], "PG2": [0, 39, 40], "PG0": [0] * 9 + [42, 43], "HC": [0, 36], "TC": [0, 38], "V1": [40]}
-DUE = {}
+CASES = [(0.85, 0.42, 1.25, 3.0, 0, 140, 2000, 2400, 1500, 15), (0.87, 0.43, 0.95, 2.2, 0, 120, 2200, 2700, 2000, 20), (1.15, 0.57, 1.9, 4.5, 0, 150, 1800, 2200, 1500, 15)]
+WEIGHTS, PULL, LOAD, SEED, MILES = (1.0, 1.0, 0.7), 0.1, 0.03, 11, (0.0, 0.0, 0.0, 0.03)
 SIZE = {B: 2, U: 2, F: 4, I: 4}
+END, KH = 62, -1
+SOFT = []
+DUE = {"OA": [17.5, 21], "X": [0, 26, 27], "EA": [20, 22, 24, 26, 28, 30], "U0": [5.2, 8.3], "MX": [0, 3.8], "XG": [12, 14, 13, 15, 14, 15.5, 7, 9.5, 8, 11, 8.5, 12],
+       "EF": [36, 38, 41, 45, 49, 53, 56], "VA": [0, 35], "VO1": [31], "TC": [0, 28], "E32": [0, 29.5, 30.5], "WB1": [0, 32], "WB0": [0, 37]}
 
 
 def build(case):
@@ -102,6 +112,10 @@ def build(case):
         for a in wr:
             if "off" in a: r.append(a["off"])
         ops.append({"eng": eng, "kind": kind, "args": args, "rd": r, "wr": list(wr), "cost": cost, "lat": lat, "hold": 0.0, "bias": 0.0})
+
+    def join(k):
+        x = ops[-k:]; del ops[-k:]
+        ops.append(dict(x[0], kind="many", args=x, rd=[a for o in x for a in o["rd"]], wr=[a for o in x for a in o["wr"]], cost={q: sum(o["cost"][q] for o in x) for q in x[0]["cost"]}))
 
     def vc(out, ins, c):
         n = out["cnt"]
@@ -126,7 +140,7 @@ def build(case):
         add("v", "scan", (out, d0, d1, init, op0, op1), [d0, d1], [out], {"v": vc(out, [d0], 0.5 if two(out, d0, d1) else 1)})
 
     def tr(out, a):
-        add("v", "tr", (out, a), [a], [out], {"v": vc(out, [a], 0.5)})
+        add("v", "tr", (out, a), [a], [out], {"v": vc(out, [a], 0.5 if two(out, a) else 1)})
 
     def ms(out, val):
         add("v", "ms", (out, val), [], [out], {"v": vc(out, [out], 0.5 if two(out) else 1)})
@@ -143,293 +157,333 @@ def build(case):
     def sel(out, a, pat, op, fill, base=0, chm=0):
         add("g", "sel", (out, a, pat, op, fill, base, chm), [a], [out], {"g": 200 + 2 * out["cnt"] * CY})
 
-    def mm(lst, kind="mm"):
+    def mm(lst):
         c = sum(max(min(64, x[1]["cnt"]), x[2]["cnt"]) * (4 if SCRATCH[x[1]["n"]][2] == F else 1) * PECY + MMI for x in lst)
-        add("t", kind, lst, [x[1] for x in lst] + [x[2] for x in lst], [x[0] for x in lst], {"t": c}, 60)
+        add("t", "mm", lst, [x[1] for x in lst] + [x[2] for x in lst], [x[0] for x in lst], {"t": c}, 60)
 
     def hold(pairs):
         sides = [x[0] if isinstance(x[0], dict) else x[1] for x in pairs]
         return sum((a["p"][1] - a["p"][0]) * (a["cnt"] * SIZE[SCRATCH[a["n"]][2]] * 0.21 / 128 + a.get("runs", 1) * ROW / 16) for a in sides)
 
-    def dma(q, pairs, kb, after=None):
+    def dma(q, pairs, after=None):
         add(q, "dma", pairs, [x[1] for x in pairs] + [after], [x[0] for x in pairs if isinstance(x[0], dict)], {q: (900 if q == "g" else 70) * len(pairs)}, DML)
-        ops[-1]["hold"] = hold(pairs) * (2 if kb == "add" else 1); ops[-1]["add"] = kb == "add"
-        if kb == "add": ops[-1]["rd"] += ops[-1]["wr"]
+        ops[-1]["hold"] = hold(pairs)
 
-    def send(pairs, kb):
-        add("g", "send", pairs, [x[1] for x in pairs], [x[0] for x in pairs], {"g": 400}, RML + (FIRST if kb == 4 else 0))
+    def send(pairs, first=False):
+        add("g", "send", pairs, [x[1] for x in pairs], [x[0] for x in pairs], {"g": 400}, RML + (FIRST if first else 0))
         ops[-1]["hold"] = hold(pairs)
 
     who = lambda s, j: "va" if j in ONV[s] else "av"
-    KEEP = ("ET", "EU", "XG", "UA", "MX", "ME", "WN", "OA")
+    KEEP = ("XG", "MX", "ME", "WN", "OA")
     H = lambda n, d, w=L: A(n, d * w, d * w + w)
     full = (slice(0, 128), slice(None))
     grp = lambda g: (16 * g, 16 * g + 16)
     quad = lambda q: (32 * q, 32 * q + 32)
-    S384 = A3("S0", (0, 6))
-    LT, LP, LH, PT, PP, PH = [A("LL", 12 * j, 12 * j + 12) for j in range(6)]
-    HT = A("LL", 24, 48)
+    mask = lambda bank, n, left: (PB(bank, 0, n), A(left, p=(0, 8)), A("COL", 0, n, 1, (0, 8)), True, False)
+    OHT0, OKEY0, OSC = (H("S16", 1, 12), A("OT")), (H("S16", 2, 12), A("RKEY")), (H("OSC", 0, 12), A("ROSC"))
     ent = lambda s, d: H("NN", 2 * s + d)
     nn = lambda s, d: (ent(s, d), (("nh", "nt")[d], (slice(0, 128), slice(s * L, s * L + L))))
-    dma("s", [(LT, ("tl", full)), (LP, ("rl", full)), (LH, ("hl", full))], 0)
-    dma("s", [(A("XR", 0, 32), ("xr", full)), (A("XR", 32, 64), ("er", full))], 0)
-    dma("s", [nn(0, 1)], 2)
-    dma("s", [(A("X", 0, M), ("xe", full))], 10)
-    dma("s", [nn(0, 0)], 2)
-    send([(A("LL", 36, 72), A("LL", 0, 36), 1)], 4)
+    dma("a", [(A("LL", 12 * j, 12 * j + 12), (n, full)) for j, n in enumerate(("tl", "rl", "hl"))])
+    dma("a", [(A("XR", 0, 32), ("xr", full)), (A("XR", 32, 64), ("er", full))])
+    dma("s", [nn(0, 1)])
+    dma("s", [(A("X", 0, M), ("xe", full))])
+    dma("s", [nn(0, 0)])
     iota(A("IN"), [[0, 1]], 127, -1); ts(A("I1"), A("IN"), 15, ALU.bitwise_and); cp(A("K15"), A("I1"))
     ts(A("I2"), A("IN"), 31, ALU.bitwise_and, 1, ALU.arith_shift_right); cp(A("KB1"), A("I2")); cp(A("KB0"), A("KB1"), "va", 1.0, 16.0)
-    iota(A("IP"), [[0, 1]], 0, 1); ts(A("I3"), A("IP"), 4, ALU.arith_shift_right, 1, ALU.bitwise_and); cp(A("G2"), A("I3"))
-    iota(A("IOC"), [[0, 24], [-1, 16]], 15); ts(A("MD"), A("IOC", 0, 16), A("K15"), ALU.is_equal); ts(A("NMD"), A("IOC"), A("K15"), ALU.not_equal, 8192.0, ALU.mult)
-    ms(A("WN"), 0.0); step(A("ONE"), A("WN", 0, 128), "a")
+    iota(A("IP"), [[0, 1]], 0, 1)
+    iota(A("IOC"), [[0, 12], [-1, 16]], 15); ts(A("MD"), A("IOC", 0, 16), A("K15"), ALU.is_equal); ts(A("NMD"), A("IOC"), A("K15"), ALU.not_equal, 8192.0, ALU.mult)
+    ts(A("NMD2"), A("NMD"), 8192.0, ALU.add)
+    ms(A("ZERO", 0, 128), 0.0); ms(A("ZERO", 128, 768), 0.0); step(A("ONE"), A("ZERO", 0, 128), "a")
     sel(A("IDB"), A("ONE"), [[-1, 128]], ALU.is_equal, 0.0, 0, 1); cp(A("ID32"), A("IDB"), "ag")
     sel(A("BO"), A("ONE"), [[-16, 8], [0, 16]], ALU.is_ge, 0.0, 0, 1); sel(A("BO"), A("BO"), [[16, 8], [0, 16]], ALU.is_ge, 0.0, 15, -1); cp(A("BO32"), A("BO"), "ag")
-    sel(A("TRI"), A("BO"), [[1, 128]], ALU.is_gt, 0.0, 0, -1)
-    sel(A("RD"), A("ONE", 0, 64), [[-32, 4], [-2, 16]], ALU.is_equal, 0.0, -1, 1); sel(A("RD"), A("RD"), [[-32, 4], [-2, 16]], ALU.not_equal, -1.0, 0, 1)
-    sel(A("HALF"), A("ONE"), [[0, 4], [1, 2], [0, 16]], ALU.is_equal, 0.0, 0, -1)
-    iota(A("MK"), [[0, 512]], -1024); sel(A("MK"), A("MK"), [[0, 32], [1, 2], [0, 8]], ALU.not_equal, 0.0, 0, -1)
+    sel(A("TRI"), A("BO"), [[1, 128]], ALU.is_gt, 0.0, 0, -1); sel(A("TRI"), A("TRI"), [[1, 128]], ALU.not_equal, -1.0, 0, -1)
+    sel(A("RD"), A("ONE"), [[-32, 4], [-2, 32]], ALU.is_equal, 0.0, -1, 1); sel(A("RD"), A("RD"), [[-32, 4], [-2, 32]], ALU.not_equal, -1.0, 0, 1)
     iota(A("IOG"), [[-1, 240]], 127); ts(A("SEL"), A("IOG"), A("K15"), ALU.is_equal)
-    ms(A3("UB1"), 0.0); cp(A("UA"), A3("UB1", None, (0, 64 * max(EARLY))), "va")
-    sel(A("RS32"), A("WN", 0, 128), [[0, 4], [1, 32]], ALU.not_equal, -1e6); sel(A("RSB"), A("WN", 0, 2 * L), [[0, 24], [1, 16]], ALU.not_equal, 16384.0)
-    iota(A("SC12"), [[0, 2], [16, 12]], 15); ts(A("DUM0"), A("SC12"), A("K15"), ALU.subtract)
-    cp(A("DUMX"), A("DUM0"), "va", 1.0, float(M)); cp(A("DUMC"), A("DUM0"), "va", 1.0, float(NK))
-    iota(A("SCP", 0, 12), [[0, 6], [1, 2]]); ts(A("PARF", 0, 12), A("SCP", 0, 12), A("G2"), ALU.not_equal, 208.0, ALU.mult)
-    tt(A("PARF", 0, 12), A("PARF", 0, 12), A("DUM0", 0, 12), ALU.add); cp(A("CTR", 0, 12), A("PARF", 0, 12))
+    sel(A("SELQ"), A("ZERO", 0, L), [[-32, 4], [-1, 48]], ALU.not_equal, 1.0, 16, 1); sel(A("SELQ"), A("SELQ"), [[0, 4], [1, 3], [0, 16]], ALU.is_equal, 0.0, -1)
+    for r in (0, 4): cp(A3("UB1", (r, r + 4)), A("ZERO"), "va")
+    cp(A("RS32"), A("ZERO", 0, 2 * L), "vag"); ms(A("RS32", 0, None, 32), -1e6); sel(A("RSB"), A("ZERO", 0, L), [[0, 12], [1, 16]], ALU.not_equal, 16384.0)
+    iota(A("SC12"), [[16, 12]], 15)
+    for n, base in (("DRC", NK), ("DRX", M)): cp(A(n), A("ZERO", 0, L), "vag"); ts(A(n, 0, None, 16), A("SC12"), A("K15"), ALU.subtract, float(base), ALU.add)
     iota(A("C37"), [[-36, 2], [0, 12]], 37)
-    ts(A("C1"), A("K15"), 7.5, ALU.is_lt, 56.0, ALU.mult)
-    ts(A("I4"), A("IP"), 4, ALU.arith_shift_right); tt(A("C3"), A("C1"), A("K15"), ALU.subtract); ts(A("C4"), A("I4"), 8.0, ALU.mult, A("C3"), ALU.add)
-    iota(A("SCB", 0, 12), [[128, 12]], 15); ts(A("CBLK", 0, 12), A("SCB", 0, 12), A("C4"), ALU.add)
-    cp(A("OP", 0, 12), LP)
-    cp(H("MX", 0), IND(A("XR", 0, 32), A("OP", 0, 12)), "va"); cp(H("ME", 0), IND(A("XR", 32, 64), A("OP", 0, 12)), "va", 0.125)
-    send([(H("MX", 1), H("MX", 0), 1), (H("ME", 1), H("ME", 0), 1)], 1)
-    dma("s", [(A("TC", 0, NK), ("tc", full))], 14, H("ME", 0))
-    ts(A("KT", 0, 12), LP, 37.0, ALU.mult); tt(A("KT", 0, 12), A("KT", 0, 12), LT, ALU.add)
-    ts(A("KT", 12, 24), PH, 37.0, ALU.mult); tt(A("KT", 12, 24), A("KT", 12, 24), PP, ALU.add)
-    for d in (0, 1):
-        ts(H("KEY0", d, 12), H("KT", d, 12), NK - 1, ALU.bitwise_and); cp(H("OKEY0", d, 12), H("KEY0", d, 12))
-    cp(A("OHT0", 0, 12), LH); cp(A("OHT0", 12, 24), PT)
-    ts(A("HT8"), HT, 8192.0, ALU.add); cp(A("Q", 0, 12), LP); ts(A("Q", 12, 24), PP, 37.0, ALU.mult)
+    if max(EARLY):
+        for r in range(max(EARLY)): cp(H("UA", r, 512), A("ZERO", 0, 512), "va")
+        ts(A("C1"), A("K15"), 7.5, ALU.is_lt, 56.0, ALU.mult)
+        ts(A("I4"), A("IP"), 4, ALU.arith_shift_right); tt(A("C3"), A("C1"), A("K15"), ALU.subtract); ts(A("C4"), A("I4"), 8.0, ALU.mult, A("C3"), ALU.add)
+        iota(A("SCB"), [[128, 12]], 15); ts(A("CBLK"), A("SCB"), A("C4"), ALU.add)
+    send([(A("RL"), A("LL", 0, 24), 1)], True)
+    cp(A("S16", 0, 24), A("LL", 12, 36))
+    cp(H("MX", 0), IND(A("XR", 0, 32), H("S16", 0, 12)), "va"); cp(H("ME", 0), IND(A("XR", 32, 64), H("S16", 0, 12)), "va", 0.125)
+    send([(H("MX", 1), H("MX", 0), 1), (H("ME", 1), H("ME", 0), 1)])
+    ts(A("KA"), A("LL", 12, 36), 37.0, ALU.mult); tt(A("KB"), A("KA"), A("LL", 0, 24), ALU.add); ts(A("KEY"), A("KB"), NK - 1, ALU.bitwise_and)
+    cp(A("S16", 24, 48), A("KEY"))
+    send([(A("RKEY"), H("S16", 3, 12), 1)])
+    cp(OHT0[1], H("RL", 0, 12))
+    dma("s", [(A("TC", 0, NK), ("tc", full))], H("ME", 0))
+    cp(H("KEY0", 0, 12), H("KEY", 0, 12), "vg"); cp(H("KEY0", 1, 12), OKEY0[1], "vg")
+    ts(H("HT8", 0, 12), A("LL", 24, 36), 8192.0, ALU.add); ts(H("HT8", 1, 12), H("RL", 0, 12), 8192.0, ALU.add)
+    cp(H("Q", 0, 12), A("LL", 12, 24), "vg"); ts(H("Q", 1, 12), H("RL", 1, 12), 37.0, ALU.mult)
     swap = lambda land, src, w: [(H(land, 1, w), H(src, 0, w), 1), (H(land, 0, w), H(src, 1, w), -1)]
 
-    def uv(s):
-        o = "OHT%d" % s; pair = swap("U%d" % s, "UO%d" % s, L)
-        if s == 0:
-            for d in (0, 1):
-                tt(H("UO0", d), IND(A("X", 0, M), H(o, d, 12)), H("MX", d), ALU.mult); send(pair[d:d + 1], 0.5)
-            dma("s", [(A("HC", 0, NK), ("hc", full))], 18, H("UO0", 0)); dma("s", [(A("E"), ("ee", full))], 28, H("UO0", 1)); dma("s", [nn(1, 0), nn(1, 1)], 20, H("UO0", 1))
-        else:
-            tt(A("UO1"), IND(A("X", 0, M), A(o)), A("MX"), ALU.mult); send(pair, 1)
-        tt(A("VO%d" % s), IND(A(("E", "E32")[s], 0, M), A(o)), A("ME"), ALU.mult)
-        send(swap("V%d" % s, "VO%d" % s, L), 2)
+    def ublock(s, d):
+        l0 = 64 * EARLY[s] if d == s else 0
+        if l0: cp(IND(A("UA"), A("CBLK", 0, l0 // 16)), A("U%d" % s, d * L, d * L + l0))
+        if l0 == L: return
+        dma("s", [(A3("UB%d" % d, g, (l0, L), grp(g)), A("U%d" % s, d * L + l0, d * L + L, 1, grp(g))) for g in range(8)])
 
     def vblock(s, d):
-        v = H("V%d" % s, d); n = 3 if s and any(c // 3 == d for c in SPLIT) else 2
-        cp(H("VH", 3 * d), v, "vag"); tt(H("VH", 3 * d + 1), v, H("VH", 3 * d), ALU.subtract)
-        if n == 3: cp(H("VH", 3 * d + 2), H("VH", 3 * d), "va", -1.0)
-        dma("s", [(A3("VB%d" % d, 4 * (g % 2) + g // 2, (0, n * L), grp(g)), A("VH", 3 * d * L, (3 * d + n) * L, 1, grp(g))) for g in range(8)], 1)
+        v = H("V%d" % s, d)
+        if s:
+            l0 = 64 * d * VEARLY
+            if l0: cp(IND(A("VA"), A("CBLK", 0, l0 // 16)), A("V1", L, L + l0))
+            dma("s", [(A3("VF%d" % d, g, (l0, L), grp(g)), A("V1", d * L + l0, d * L + L, 1, grp(g))) for g in range(8)])
+        else:
+            cp(H("VH", 2 * d), v, "vag"); tt(H("VH", 2 * d + 1), v, H("VH", 2 * d), ALU.subtract)
+            dma("s", [(A3("VB%d" % d, g, None, grp(g)), A("VH", 2 * d * L, (2 * d + 2) * L, 1, grp(g))) for g in range(8)])
 
     def lists(s, d):
-        cand = IND(A(("HC", "TC")[d], 0, NK), H("OKEY%d" % s, d, 12))
-        cp(H("OFN", 2 * s + d), ent(s, d), "vg" if s else "v"); cp(H("OFC", 2 * s + d), cand)
+        cand = IND(A(("HC", "TC")[d], 0, NK), H("OKEY1", d, 12) if s else OKEY0[d])
+        cp(H("OFN", 2 * s + d), ent(s, d), "vg" if s else "v"); cp(H("OFC", 2 * s + d), cand, "v")
         tt(H("DD", d), cand, ent(s, d), ALU.subtract)
 
     def contest(d):
-        sc, scs = "PG%d" % d, "SCS%d" % d
+        sc, scs, flat = ("PGA", "PGB")[d], "SCS%d" % d, ("S1", "PT")[d]
         for l0 in range(0, L, 64):
             x0 = 32 * (d * L + l0)
             for part in (1, 0): cp(A("XG", x0 + part, x0 + 2048, 2), IND(A("X", 0, M), A(("OFC", "OFN")[part], d * L + l0, d * L + l0 + 64)), who(0, x0 // 1024 + part))
             lst = []
             for l in range(l0, l0 + 64):
                 c, j16 = divmod(l, 16); j, q = divmod(c, 4)
-                lst.append((A3(sc, j, (j16, 128, 16), quad(q)), A("XG", 32 * (d * L + l), 32 * (d * L + l) + 32),
+                lst.append((PB(sc, 128 * j + j16, 1, 8, 16, quad(q)), A("XG", 32 * (d * L + l), 32 * (d * L + l) + 32),
                             A3("UB%d" % d, None, l) if d or l >= 64 * EARLY[0] else A("UA", 64 * (l // 8) + l % 8, 64 * (l // 8) + 64, 8), True, True))
             mm(lst)
-        cp(A(scs), A3(sc, (0, 3)), "va", 32.0, A("KB%d" % d))
-        mm([(A3(sc, j), A(scs, 128 * j, 128 * j + 128), A("ID32"), True, True) for j in range(3)])
-        mm([(A3("PZ", 3 * d + j), A(scs, 128 * j, 128 * j + 128), A("RD"), True, True) for j in range(3)])
-        w0, t0 = 224 * d, 416 * d
-        for j in range(3): scan(H("RM%d" % d, j, 128), A("RS32"), A3(sc, j), 0.0, ALU.add, ALU.max)
-        cp(H("MI", d, 12), A("RM%d" % d, 31, None, 32))
-        step(A("WN", w0 + 16, w0 + 208), A3("PZ", (3 * d, 3 * d + 3)))
-        tr(A("TT", t0, t0 + L), A("WN", w0 + 16, w0 + 208)); tr(A("TT", t0 + L, t0 + 416), A("WN", w0, w0 + 224))
-        tt(H("WDD", d), IND(A("TT", t0, t0 + 416), A("CTR", 0, 12)), H("DD", d), ALU.mult)
-        tt(H("AF", d), H("WDD", d), ent(0, d), ALU.add)
-        cp(H("OA", d), H("AF", d))
-        p0, p1 = A3(sc, (0, 2), (0, 96)), A3(sc, (2, 4), (0, 96))
+        cp(A(scs), PB(sc, 0, 2 * L), "va", 32.0, A("KB%d" % d))
+        mm([(H(flat, j, 128), H(scs, j, 128), A("ID32"), True, True) for j in range(3)])
+        mm([(PB("PZ%d" % d, 0, 2 * L), A("RD"), A(scs), True, True)])
+        scan(A(scs), A("RS32"), A(flat, 0, 2 * L), 0.0, ALU.add, ALU.max)
+        cp(H("MI", d, 12), A(scs, 31, None, 32))
+        send(swap("INS", "MI", 12)[d:d + 1])
+        step(A3("WN"), PB("PZ%d" % d, 0, 2 * L))
+        mm([(PB("S0", L * d + 16 * q, 16, 3, 64, quad(g // 2)), A("SELQ", 48 * q + 16 - 16 * (g % 2), 48 * q + 48 - 16 * (g % 2)), A3("WN", (g, 24, 8)), g % 2 == 0, g % 2 == 1)
+            for q in range(4) for g in range(8)])
+        tt(PB("S0", L * d, L), PB("S0", L * d, L), H("DD", d), ALU.mult)
+        tt(H("AF", d), PB("S0", L * d, L), ent(0, d), ALU.add)
+        cp(H("OA", d), H("AF", d), "vg")
         ts(H("KK", d, 12), H("MI", d, 12), 15, ALU.bitwise_and); ts(H("OKK", d, 12), H("KK", d, 12), -1.0, ALU.mult, 15.0, ALU.add)
-        tt(H("OAA", d), IND(A("MD"), H("OKK", d, 12)), H("AF", d), ALU.mult); mm([(p1, A("BO32"), H("OAA", d), True, True)])
-        mm([(p0, A("IDB"), H("NMD", d), True, False), (p0, A("BO32"), H("OAA", d), False, True)])
-        cp(H("BR16", d), p1)
-        for j in (0, 1): scan(H("BSC", 2 * d + j, 96), A("RSB", 0, 96), A3(sc, j, (0, 96)), 0.0, ALU.add, ALU.min)
+        tt(H("OAA", d), IND(A("MD"), H("OKK", d, 12)), H("AF", d), ALU.mult); mm([(PB(sc, 0, L), A("BO32"), H("OAA", d), True, True)])
+        mm([(A(flat, 0, L), A("IDB"), A("NMD"), True, False), (A(flat, 0, L), A("BO32"), H("OAA", d), False, True)])
+        cp(H("BR16", d), PB(sc, 0, L), "va")
+        scan(H("BSC", d), A("RSB"), A(flat, 0, L), 0.0, ALU.add, ALU.min)
 
-    def duel(d, ch):
-        xc = 32 * d * L + 1024 * ch; xn = xc + 16 * L; o0 = d * L + 64 * ch; b = ch % 2
-        cp(A("XG", xn, xn + 1024), IND(A("X", 0, M), A("OFN", 2 * L + o0, 2 * L + o0 + 64)), who(1, o0 // 32 + 1))
-        cp(A("XG", xc, xc + 1024), IND(A("X", 0, M), A("OFC", 2 * L + o0, 2 * L + o0 + 64)), who(1, o0 // 32), -1.0)
-        lst = [(A3("S0"), A("OWN", p=(0, 8)), A("THM", p=(0, 8)), True, False)]
-        for t in range(8):
+    def duel(c):
+        d, ch = divmod((min(c, 5) + 3) % 6, 3); t0, nt = (0, 8) if c < 5 or not APART else ((0, 8 - NL), (8 - NL, NL))[c - 5]
+        l0 = 64 * ch + 8 * t0; w = 8 * nt; xc = 32 * d * L + 16 * l0; xn = xc + 16 * L; o0 = d * L + l0; b = c % 2; th = c in TH
+        cp(A("XG", xn, xn + 16 * w), IND(A("X", 0, M), A("OFN", 2 * L + o0, 2 * L + o0 + w)), who(1, o0 // 32 + 1))
+        cp(A("XG", xc, xc + 16 * w), IND(A("X", 0, M), A("OFC", 2 * L + o0, 2 * L + o0 + w)), who(1, o0 // 32), -1.0)
+        if c in PAIRS:
             for n, x0 in enumerate((xn, xc)):
-                lst.append((A3("S0", None, (8 * t, 8 * t + 8)), A("XG", x0 + 128 * t, x0 + 128 * t + 128),
-                            A3("UB%d" % d, None, (64 * ch + 8 * t, 64 * ch + 8 * t + 8)) if d or ch >= EARLY[1] else H("UA", 8 * ch + t, 64), False, t == 7 and n == 1))
-        mm(lst)
-        step(A("AM"), A3("S0"))
-        mm([(A("S1", 0, 64), A("SEL", 112 - 16 * g, 240 - 16 * g), H("AM", g, 64), g == 0, g == 7) for g in range(8)])
-        tt(A("S1", 64, 128), A("S1", 0, 64), A("DD", o0, o0 + 64), ALU.mult)
-        tt(H("A64", b, 64), A("S1", 64, 128), A("NN", 2 * L + o0, 2 * L + o0 + 64), ALU.add)
-        cp(A("OA", o0, o0 + 64), H("A64", b, 64))
-
-    ring = [0]
-
-    def turn(dst, src, e0, n, scale=None):
-        bank = "PT%d" % (ring[0] % 2); ring[0] += 1
-        mm([(H(bank, t, 128), A(src, e0 + 128 * t, e0 + 128 * t + 128), A("IDB")) for t in range(n)], "trp")
-        cp(A(dst, e0, e0 + 128 * n), A(bank, 0, 128 * n), "va", scale)
-
-    def ublock(s, d):
-        l0 = 0 if d else 64 * EARLY[s]
-        if l0: cp(IND(A("UA"), A("CBLK", 0, l0 // 16)), A("U%d" % s, 0, l0))
-        if l0 < L: dma("s", [(A3("UB%d" % d, g, (l0, L), grp(g)), A("U%d" % s, d * L + l0, d * L + L, 1, grp(g))) for g in range(8)], 0.5)
-
-    def fetch(s, c, t0=0, n=8, j=None):
-        off = A("OA", 64 * c + 8 * t0, 64 * c + 8 * (t0 + n)); e0 = 1024 * c + 128 * t0; x0 = e0 % 4096
-        ea, el = A("EA", e0, e0 + 128 * n), A("EL", x0, x0 + 128 * n)
-        if s and c in SPLIT:
-            ef = H("EF", SPLIT.index(c) % 2, 1024)
-            cp(ef, IND(A("E32", 0, M), off), "va", -1.0); cp(ea, ef, "va", -1.0)
-            dma("g", [(ef, ea)], "add"); dma("g", [(el, ef)], 0)
+                lst = [] if n else [mask("S0", 128, "HALFP")]
+                for j in range(4):
+                    for t in range(8):
+                        l = 16 * j + 2 * t
+                        lst.append((PB("S0", 2 * t, 2, 8, 16, quad(j)), A("XG", x0 + 16 * l, x0 + 16 * l + 32), A3("UB%d" % d, None, (64 * ch + l, 64 * ch + l + 2)), False, n == 1 and t == 7))
+                mm(lst)
+            step(A("AM", 0, 128), PB("S0", 0, 128))
+            mm([(A("S1", 16 * j, 16 * j + 16, 1, quad(q)), A("SEL", 112 - 16 * h, 144 - 16 * h, 1, quad(j)), A("AM", 32 * q + 16 * h, 32 * q + 16 * h + 16, 1, quad(j)), h == 0, h == 1)
+                for j in range(4) for q in range(4) for h in (0, 1)])
         else:
-            cp(ea, IND(A(("E", "E32")[s], 0, M), off), "va")
-            if s: tt(el, IND(A("E32", 0, M), off), ea, ALU.subtract)
+            for n, x0 in enumerate((xn, xc)):
+                mm(([] if n or th else [mask("S0", 8 * w, "OWN")]) +
+                   [(PB("S0", 8 * t, 8, 8, w), A("XG", x0 + 128 * t, x0 + 128 * t + 128),
+                     A3("UB%d" % d, None, (l0 + 8 * t, l0 + 8 * t + 8)) if not d or ch >= EARLY[1] else H("UA", 8 * ch + t, 64), th and n == t == 0, n == 1 and t == nt - 1) for t in range(nt)])
+            if th: tt(A("AM", 0, 8 * w), PB("S0", 0, 8 * w), A("THR", 0, 8 * w), ALU.is_le)
+            else: step(A("AM", 0, 8 * w), PB("S0", 0, 8 * w))
+            mm([(A("S1", 0, w), A("SEL", 112 - 16 * g, 240 - 16 * g), H("AM", g, w), g == 0, g == 7) for g in range(8)])
+        tt(A("S1", 64, 64 + w), A("S1", 0, w), A("DD", o0, o0 + w), ALU.mult)
+        tt(A("A64", 64 * b, 64 * b + w), A("S1", 64, 64 + w), A("NN", 2 * L + o0, 2 * L + o0 + w), ALU.add)
+        cp(A("OA", o0, o0 + w), A("A64", 64 * b, 64 * b + w), "vg")
 
-    def reals(s, c, wide, t0=0, n=8, j=None):
-        d, ch = divmod(c, 3); e0 = 1024 * c + 128 * t0; x0 = e0 % 4096; m = 128 if wide else 32; split = s and c in SPLIT
-        rows, w = ((0, 8) if wide else (2 * ch, 2 * ch + 2), 64) if j is None else ((j, j + 1), 16 * n)
-        turn("ET", "EA", e0, n)
-        for k, (src, parts) in enumerate((("EA", (0, 1)), ("EL", (2 if split else 0,)))[:s + 1]):
-            if k: e0 = x0
-            lst = [] if k else [(A3("PZ", rows, (0, w)), A("HALF", p=(0, 2)), A("MK", 0, 4 * m, 8 // n, (0, 2)), True, False)]
-            for e in range(0, 128 * n, m):
-                t, p0 = divmod(e, 128)
-                for part in parts:
-                    l0 = part * L + 64 * ch + 8 * (t0 + t) + p0 // 16
-                    lst.append((A3("PZ", rows, (t, w, n), (p0, p0 + m)), A(src, e0 + e, e0 + e + m), A3("VB%d" % d, None, (l0, l0 + m // 16)), False,
-                                k == s and t == n - 1 and part == parts[-1]))
+    sums = lambda c: "PG" + "ABC"[c % 3]
+    gy = lambda c: "GY%d" % (c // 4)
+
+    def readout(c):
+        for j in range(4): cp(A3(gy(c), None, (2 * j, 2 * j + 2), quad(c % 4)), PB(sums(c), 128 * j, 128, p=quad(j)), RO)
+        join(4)
+
+    def store(c):
+        y, c0 = divmod(64 * c, L)
+        pairs = [((("yt", "yh")[y], (slice(*grp(g)), slice(c0, c0 + 64))), A3(gy(c), (8 * g, 8 * g + 8), None, grp(2 * (c % 4) + g % 2))) for g in range(8)]
+        if c == 5: dma("s", pairs[:4]); dma("a", pairs[4:])
+        else: dma("s", pairs)
+
+    def reals0(d):
+        pz = "PZ%d" % d; at = lambda l: (l % 8 // 2, l // 8)
+        for ch in range(3):
+            c = 3 * d + ch; e0 = 1024 * (c % NEA)
+            cp(A("EA", e0, e0 + 1024), IND(A("E"), A("OA", 64 * c, 64 * c + 64)), "va")
+            tr(H("ET", c, 1024), A("EA", e0, e0 + 1024))
+            lst = [] if ch else [mask(pz, 2 * L, "HALF")]
+            for l in range(64 * ch, 64 * ch + 64, 2):
+                j, t = at(l); e = e0 + 16 * (l % 64)
+                for part in (0, 1):
+                    lst.append((PB(pz, 4 * t, 4, 4, 96, quad(j)), A("EA", e, e + 32), A3("VB%d" % d, None, (part * L + l, part * L + l + 2)), False, t == 23 and part == 1))
             mm(lst)
-        if s: turn("EU", "EL", x0, n, -1.0 if split else None)
+        z = PB(pz, 0, 2 * L); hi, lo = A3("WC", (8 * d, 8 * d + 8, 2)), A3("WC", (8 * d + 1, 8 * d + 8, 2))
+        act(z, z, ACT.Sigmoid, 0.5); cp(hi, z, "va"); tt(lo, z, hi, ALU.subtract)
+        dma("s", [(A3("WB%d" % d, (4 * j + q, 32, 16), None, quad(q)), A3("WC", (8 * d + 2 * q, 8 * d + 2 * q + 2), None, quad(j))) for j in range(4) for q in range(4)])
 
-    def weights(c, nc, wide, t0=0, n=8, j=None, quick=False):
-        d, ch = divmod(c, 3)
+    def sums0(c):
+        d, ch = divmod((c + 3) % 6, 3)
+        mm([(PB(sums(c), 2 * t, 2, 32, 16), H("ET", 24 * d + 8 * ch + t, 128), A3("WB%d" % d, (16 * part, 16 * part + 16), (32 * ch + 4 * t, 32 * ch + 4 * t + 4)), t == part == 0, False)
+            for t in range(8) for part in (0, 1)])
+
+    def reals1(c):
+        d, ch = divmod((c + 3) % 6, 3); n = 8 - (NL if c == 5 else 0); wide = c in WIDE; pz = "PZ%d" % ZB[c]; o0 = d * L + 64 * ch
+        e0, u0, r = 1024 * (c % NEF), 1024 * (c % NET), c % NW; vf = "VF%d" % d
+        lane = (lambda j, t: 8 * t + 2 * j) if wide else (lambda j, t: 2 * n * j + 2 * t)
+        cp(A("EF", e0, e0 + 128 * n), IND(A("E32", 0, M), A("OA", o0, o0 + 8 * n)), "va")
+        tr(A("EU", u0, u0 + 128 * n), A("EF", e0, e0 + 128 * n))
         if wide:
-            z = H("W32", c % 2, 128)
-            for q in range(4): act(A("W32", z["lo"], z["hi"], 1, quad(q)), A3("PZ", None, (16 * q, 16 * q + 16), quad(q)), ACT.Sigmoid, 0.5)
+            lst = [mask(pz, 512, "HALF")]
+            lst += [(PB(pz, 8 * t, 8, 8, 64), A("EF", e0 + 128 * t, e0 + 128 * t + 128),
+                     H("VA", 8 * c + t, 64) if c < VEARLY else A3(vf, None, (64 * ch + 8 * t, 64 * ch + 8 * t + 8)), False, t == n - 1) for t in range(n)]
+            mm(lst)
+            zq = lambda j, q0, q1: A3(pz, (16 * q0, 16 * q1), (2 * j, 2 * j + 2), quad(j))
+            if c not in DIRECT:
+                for j in range(4): act(A("WS", 128 * r, 128 * r + 128, 1, quad(j)), zq(j, 0, 4), ACT.Sigmoid, 0.5)
+                join(4)
         else:
-            z = A3("PZ", (2 * ch, 2 * (ch + nc))) if j is None else A3("PZ", j, (0, 16 * n)); act(z, z, ACT.Sigmoid, 0.5)
-        if j is None:
-            hi, lo = A3("WC", (c, c + nc), (0, 128)), A3("WC", (c, c + nc), (128, 256))
-            pairs = [(A3("WB%d" % d, (16 * ch + q, 16 * (ch + nc), 4), None, quad(q)), A3("WC", (c, c + nc), None, quad(q))) for q in range(4)]
-        else:
-            hi, lo = A("WP", 32 * t0, 32 * t0 + 16 * n), A("WP", 32 * t0 + 16 * n, 32 * (t0 + n))
-            pairs = [(A3("WQ%d" % j, (q, 16, 4), None, quad(q)), A("WP", 32 * t0, 32 * (t0 + n), 1, quad(q))) for q in range(4)]
-        cp(hi, z, "vag" if wide else "va"); tt(lo, z, hi, ALU.subtract)
-        if quick:
-            for out, src in pairs: cp(out, src, "va")
-        else: dma("s", pairs, 0.5)
+            lst = [mask(pz, 128, "HALF")]
+            for j in range(4):
+                for t in range(n):
+                    l = lane(j, t)
+                    lst.append((PB(pz, 2 * t, 2, 8, 16, quad(j)), A("EF", e0 + 16 * l, e0 + 16 * l + 32), A3(vf, None, (64 * ch + l, 64 * ch + l + 2)), False, t == n - 1))
+            mm(lst)
+            zq = lambda j, q0, q1: PB(pz, 32 * q0, 32 * (q1 - q0), p=quad(j))
+            if c not in DIRECT: act(H("WS", r, 128), PB(pz, 0, 128), ACT.Sigmoid, 0.5)
+        wf = lambda j, q: A3("WF", (32 * r + 8 * j + 2 * q, 32 * r + 8 * j + 2 * q + 2), None, quad(q))
+        if c in DIRECT:
+            for j in range(4):
+                for q in range(4): act(wf(j, q), zq(j, q, q + 1), ACT.Sigmoid, 0.5)
+                join(4)
+        else: dma("s", [(wf(j, q), A("WS", 128 * r + 32 * q, 128 * r + 32 * q + 32, 1, quad(j))) for j in range(4) for q in range(4)])
+        mm([(PB(sums(c), 2 * t, 2, 32, 16), A("EU", u0 + 128 * t, u0 + 128 * t + 128), A3("WF", (32 * r, 32 * r + 32), (2 * t, 2 * t + 2)), False, t == n - 1) for t in range(n)])
+        ops[-1]["mile"] = MILES[3]
+        readout(c)
 
-    def sums(s, c, t0=0, n=8, j=None):
-        d, ch = divmod(c, 3); bank, h = "PG%d" % (c // 2), c % 2; lst = []
-        for src, k in (("ET", 2), ("EU", 1))[:s + 1]:
-            for t in range(t0, t0 + n):
-                for a in range(4):
-                    e0 = (1024 * c + 128 * t + 32 * a) % (4096 if k == 1 else 6144)
-                    out = A3(bank, (0, 2 * k), (64 * h + 8 * t, 64 * h + 8 * t + 8), quad(a))
-                    w = A3("WB%d" % d, (16 * ch, 16 * ch + 8 * k), (16 * a + t, 16 * a + 16, 8)) if j is None else A3("WQ%d" % j, (0, 8 * k), (2 * n * a + t - t0, 2 * n * (a + 1), n))
-                    lst.append((out, A(src, e0, e0 + 32), w, False, src == "EU" and h == 1 and t == 7))
-        mm(lst)
-        if s == 1 and h == 1 and t0 + n == 8:
-            if c != 3: parts = [(A3("GS%d" % d, None, (64 * ch - 64, 64 * ch + 64)), A3(bank, (0, 2)), A3(bank, (2, 4)))]
-            else: parts = [(A3("GS%d" % x, None, (128 - 128 * x, L - 128 * x)), A3(bank, (0, 2), (64 * x, 64 * x + 64)), A3(bank, (2, 4), (64 * x, 64 * x + 64))) for x in (0, 1)]
-            for out, hi, lo in parts: cp(out, hi, "va"); tt(out, lo, out, ALU.add)
-            if c > 1:
-                y = c // 4
-                for q in (0, 1):
-                    dma("sa"[q * y], [((("yh", "yt")[y], (slice(*grp(g)), slice(None))), A3("GS%d" % y, g % 2, None, grp(g))) for g in range(4 * q, 4 * q + 4)], 0.5)
+    def piece(k):
+        n, t0 = LAST[k], sum(LAST[:k]); l0 = L - 8 * (NL - t0); e0, u0, w0 = 1024 * NEF + 128 * t0, 1024 * NET + 128 * t0, 64 * t0; pz = "PZ%d" % (k % 2)
+        cp(A("EF", e0, e0 + 128 * n), IND(A("E32", 0, M), A("OA", l0, l0 + 8 * n)), "va")
+        tile = lambda t: A("EF", e0 + 128 * t, e0 + 128 * t + 128)
+        mm([mask(pz, 64 * n, "OWNN")] +
+           [(PB(pz, 64 * t, 64), tile(t), A3("VF0", None, (l0 + 8 * t, l0 + 8 * t + 8)), False, t == n - 1) for t in range(n)])
+        mm([(H("PT", t, 128), tile(t), A("ID32"), True, True) for t in range(n)])
+        act(A("WL", w0, w0 + 64 * n), PB(pz, 0, 64 * n), ACT.Sigmoid, 0.5)
+        cp(A("EU", u0, u0 + 128 * n), A("PT", 0, 128 * n), "va")
+        mm([(PB(sums(k), 64 * t + 16 * q, 16, p=quad(1)), A("EU", u0 + 128 * t + 32 * q, u0 + 128 * t + 32 * q + 32), A("WL", w0 + 64 * t + 16 * q, w0 + 64 * t + 16 * q + 16), t == q == 0, t == n - 1 and q == 3)
+            for t in range(n) for q in range(4)])
+        for t in range(n):
+            y = A3(gy(5), (8 - NL + t0 + t, 64, 8), None, quad(1)); tt(y, PB(sums(k), 64 * t, 64, p=quad(1)), y, ALU.add)
+        join(n)
 
-    def first(rep, col, bank, out):
-        mm([(A(bank, 0, 2 * L), A("IDB"), A("NMD"), True, False)])
-        for d in (0, 1):
-            lst = []
-            for c in range(12):
-                n = L - 16 * c
-                ts(A3("EQ", 12 * d + c, (0, n)), A(rep, d * L + 16 * c, d * L + L), A(col, 12 * d + c, 12 * d + c + 1), ALU.is_equal, 8192.0, ALU.mult)
-                if c < 11: lst.append((A(bank, d * L + 16 * c + 16, d * L + L), A("BO"), A3("EQ", 12 * d + c, (16, n)), False, False))
-            lst.append((H(bank, d), A("TRI"), A3("EQ", (12 * d, 12 * d + 12), (0, 16)), False, d == 1))
-            mm(lst[:5]); mm(lst[5:])
-        scan(A(out), A("RSB"), A(bank, 0, 2 * L), 0.0, ALU.add, ALU.min)
+    def first(rep, col, d, bank, spare, num, out):
+        if num: lst = [(H(bank, d), A("IDB"), A("NMD2"), True, False)]
+        else: mm([(H(bank, d), A("IDB"), A("NMD2"), True, False), (H(bank, d), A("BO32"), H("OAA", d), False, False)]); lst = []
+        r0 = 12 * d % NEQ
+        for c in range(12):
+            n = L - 16 * c
+            ts(A3("EQ", r0 + c, (0, n)), A(rep, d * L + 16 * c, d * L + L), A(col, 12 * d + c, 12 * d + c + 1), ALU.is_equal, 8192.0, ALU.mult)
+            if c in (4, 8, 11): join((5, 4, 3)[c // 4 - 1 + (c == 11)])
+            if c < 11: lst.append((A(bank, d * L + 16 * c + 16, d * L + L), A("BO"), A3("EQ", r0 + c, (16, n)), False, False))
+        lst.append((H(bank, d), A("TRI"), A3("EQ", (r0, r0 + 12), (0, 16)), False, True))
+        mm(lst[:-7]); mm(lst[-7:-3]); mm(lst[-3:])
+        scan(H("FS", d), A(spare), H(bank, d), 0.0, ALU.max, ALU.min)
+        fs = A("FS", d * L + 15, d * L + L, 16)
+        if num: tt(H("F1", d, 12), fs, num, ALU.max); cp(out, H("F1", d, 12), "vg")
+        else: cp(out, fs, "vg")
 
-    uv(0)
-    iota(A("ZERO"), [[0, 768]])
-    dma("s", [(A3("UB0", (4 * j, 4 * j + 4)), A("ZERO")) for j in (0, 1)], 3, H("UO0", 1))
+    pair = swap("U0", "UO0", L)
+    for d in (0, 1):
+        tt(H("UO0", d), IND(A("X", 0, M), OHT0[d]), H("MX", d), ALU.mult); send(pair[d:d + 1])
+    dma("s", [(A("HC", 0, NK), ("hc", full))], H("UO0", 0)); dma("s", [(A("E"), ("ee", full))], H("UO0", 1)); dma("s", [nn(1, 0), nn(1, 1)], H("UO0", 1))
+    for d in (0, 1): tt(H("VO0", d), IND(A("E"), OHT0[d]), H("ME", d), ALU.mult)
+    send(swap("V0", "VO0", L))
+    iota(A("ZERO32"), [[0, 384]])
+    fill = lambda n, z, after: dma("s", [(A3(n, (r, r + A(z)["cnt"] // SCRATCH[n][1][2])), A(z)) for r in range(0, SCRATCH[n][1][1], A(z)["cnt"] // SCRATCH[n][1][2])], after)
+    fill("UB0", "ZERO", H("UO0", 1))
     for d in (0, 1): lists(0, d); ublock(0, d)
-    dma("g", [(A("E32", 0, M), ("ee", full))], 24, A("V0"))
-    for n in ("VB1", "VB0"): dma("s", [(A3(n, (2 * j, 2 * j + 2), (0, 2 * L)), A("ZERO")) for j in range(4)], 6, H("U0", 0))
-    for n in ("WB1", "WB0"): dma("s", [(A3(n, (12 * j, 12 * j + 12)), A("ZERO")) for j in range(4)], 6, A("V0"))
-    for d in sorted({c // 3 for c in SPLIT}): dma("s", [(A3("VB%d" % d, (4 * j, 4 * j + 4), (2 * L, 3 * L)), A("ZERO")) for j in range(2)], 3)
-    dma("s", [(A3("WQ%d" % j), A("ZERO", 0, 128 * n)) for j, n in enumerate(LAST)], 2, A("V0"))
-    sel(A("OWN"), A("ONE"), [[1, 8], [0, 16]], ALU.is_equal, 0.0, 0, -1)
-    iota(A("THM"), [[0, 512]], 16384); sel(A("THM"), A("THM"), [[0, 64], [1, 8]], ALU.not_equal, 0.0, 0, -1)
-    iota(A("COUNT"), [[1, NK]]); cp(A("KF"), A("KEY0")); cp(A("KR16"), IND(A("COUNT"), A("OKEY0")))
+    dma("g", [(A("E32", 0, M), ("ee", full))], A("V0"))
+    for n in ("VB1", "VB0"): fill(n, "ZERO", H("U0", 0))
+    for n in ("WB1", "WB0"): fill(n, "ZERO", A("V0"))
+    sel(A("COL"), A("ZERO", 0, 512), [[0, 64], [1, 8]], ALU.not_equal, 1.0, 0, -1)
+    for n, v in (("OWN", 16384.0), ("OWNN", -1024.0)): sel(A(n), A("ZERO", 0, 128), [[1, 8], [0, 16]], ALU.is_equal, v, 0, -1)
+    iota(A("IH"), [[0, 4], [1, 2], [0, 16]], 0, 1); ts(A("IH"), A("IH"), 1, ALU.bitwise_and)
+    for n, v in (("HALF", -1024.0), ("HALFP", 16384.0))[:1 + bool(PAIRS)]: ts(A(n), A("IH"), v, ALU.mult)
+    if TH:
+        mm([mask("S0", 512, "OWN")[:4] + (True,)]); cp(A("THR"), PB("S0", 0, 512), "va", -1.0)
+    iota(A("COUNT"), [[1, NK]]); cp(A("KF"), A("KEY"), "vg")
 
-    def keys():
-        first("KR16", "KF", "S1", "FSK")
-        tt(A("G3"), A("FSK", 15, None, 16), A("KF"), ALU.add); tt(A("G3"), A("G3"), A("DUMC"), ALU.min); cp(A("OSC"), A("G3"))
+    def keys(d):
+        cp(H("KR16", d), IND(A("COUNT"), H("S16", 2 + d, 12)))
+        first("KR16", "KF", d, "S1", "DRC", H("KF", d, 12), H("OSC", d, 12))
 
-    if KEARLY: keys()
+    def cache(d):
+        cp(IND(A(("HC", "TC")[d]), OSC[d]), H("AF", d)); lists(1, d)
+
+    keys(1)
+    if KH < 0: keys(0)
+    send([(A("ROSC"), H("OSC", 1, 12), 1)])
     for d in (1, 0):
-        k = len(ops); contest(d); vblock(0, d)
-        for o in ops[k:]: o["bias"] = BOOST * d
-    ts(A("EXS"), A("MI"), 4, ALU.arith_shift_right)
-    send(swap("INS", "EXS", 12), 0)
+        contest(d); ops[-1]["mile"] = MILES[2]; vblock(0, d)
+    for n in ("VF0", "VF1", "WF"): fill(n, "ZERO32", H("INS", 0, 12))
+    if VEARLY: dma("s", [(H("VA", r, 256), A("ZERO32", 0, 256)) for r in range(2 * VEARLY)], H("INS", 0, 12))
+    reals0(1)
     BL = A("BSC", 15, None, 16)
     cp(A("OB"), BL)
     tt(A("Z1"), BL, A("C37"), ALU.mult); tt(A("Z2"), A("Z1"), A("Q"), ALU.add); ts(A("EXK"), A("Z2"), NK - 1, ALU.bitwise_and)
-    send(swap("INK", "EXK", 12), 0)
+    send(swap("INK", "EXK", 12))
+    S384 = PB("S0", 0, 2 * L)
     act(A("SU"), A("U0"), ACT.Sign)
     tt(A("NX0"), IND(A("X", 0, M), A("OB")), A("SU"), ALU.subtract); ts(A("NX"), A("NX0"), -7.0, ALU.max, 7.0, ALU.min)
     tt(A("PV"), IND(A("E"), A("OB")), A("V0"), ALU.mult); mm([(S384, A("BO32"), A("PV"), True, True)])
     act(S384, S384, ACT.Sigmoid, 0.5); tt(A("WV"), S384, A("V0"), ALU.mult)
     cp(A("EB"), IND(A("E"), A("OB")), "va", 0.875)
-    tt(A("LV"), A("EXS"), A("INS"), ALU.is_gt)
-    ts(A("BS0"), A("LV"), -8192.0, ALU.mult, 8192.0, ALU.add); tt(A("BS"), A("BS0"), BL, ALU.add)
-    first("BR16", "BS", "S1", "FS")
-    tt(A("F1"), A("FS", 15, None, 16), A("BS"), ALU.add); tt(A("F2"), A("F1"), A("DUMX"), ALU.min); cp(A("OSX"), A("F2"))
-    tt(A("G1"), A("HT8"), A("BS0"), ALU.subtract); tt(A("G1"), A("G1"), A("BS"), ALU.min); cp(A("OHT1"), A("G1"))
-    tt(A("G4"), A("KEY0"), A("INK"), ALU.subtract); tt(A("G4"), A("G4"), A("LV"), ALU.mult); tt(A("G4"), A("G4"), A("INK"), ALU.add); cp(A("OKEY1"), A("G4"))
-    if not KEARLY: keys()
-    for d in (0, 1): cp(IND(A(("HC", "TC")[d]), H("OSC", d, 12)), H("AF", d))
-    for b in range(3): mm([(A3("PG%d" % b), A("IDB"), A("ZERO", 0, 512), True, False)])
-    for d in (1, 0):
-        for ch in range(3): fetch(0, 3 * d + ch); reals(0, 3 * d + ch, False)
-        weights(3 * d, 3, False)
-        for ch in range(3): sums(0, 3 * d + ch)
-    for d in (0, 1): cp(IND(A("X"), H("OSX", d, 12)), H("NX", d))
-    for d in (0, 1): tt(IND(A("E32"), H("OSX", d, 12)), H("EB", d), H("WV", d), ALU.add)
-    uv(1)
+    for d in (0, 1): tt(H("LV", d, 12), H("MI", d, 12), H("INS", d, 12), ALU.is_gt)
+    tt(A("G4"), A("KEY0"), A("INK"), ALU.subtract); tt(A("G4"), A("G4"), A("LV"), ALU.mult); tt(A("G4"), A("G4"), A("INK"), ALU.add); cp(A("OKEY1"), A("G4"), "vg")
+    cache(1)
+    if KH < 0: cache(0)
     for d in (0, 1):
-        lists(1, d); ublock(1, d); vblock(1, d)
+        bl = A("BSC", d * L + 15, d * L + L, 16)
+        ts(H("BS0", d, 12), H("LV", d, 12), -8192.0, ALU.mult, 8192.0, ALU.add); tt(H("BS", d, 12), H("BS0", d, 12), bl, ALU.add)
+        first("BR16", "BS", d, ("S1", "PT")[d], "DRX", None, H("OSX", d, 12))
+        cp(IND(A("X"), H("OSX", d, 12)), H("NX", d))
+    ops[-1]["mile"] = MILES[0]
+    tt(A("G1"), A("HT8"), A("BS0"), ALU.subtract); tt(A("G1"), A("G1"), A("BS"), ALU.min); cp(A("OHT1"), A("G1"))
+    reals0(0)
+    for c in range(3): sums0(c)
+    for d in (0, 1): tt(IND(A("E32"), H("OSX", d, 12)), H("EB", d), H("WV", d), ALU.add)
+    tt(A("UO1"), IND(A("X", 0, M), A("OHT1")), A("MX"), ALU.mult); send(swap("U1", "UO1", L))
+    tt(A("VO1"), IND(A("E32", 0, M), A("OHT1")), A("ME"), ALU.mult); send(swap("V1", "VO1", L))
+    for d in (1, 0):
+        ublock(1, d); vblock(1, d)
+    for c in range(LAG):
+        duel(c)
+        if c == KH: keys(0); cache(0)
     for c in range(6):
-        k = len(ops); duel(*divmod(c, 3))
-        for o in ops[k:k + 2]: o["bias"] = AHEAD * c
-        if c < 4: fetch(1, c)
-    for c in TURN:
-        if c == 4: fetch(1, c)
-        reals(1, c, c in WIDE); weights(c, 1, c in WIDE, quick=c - 5 >= len(LAST) - QUICK); sums(1, c)
-    for j, n in enumerate(LAST):
-        piece = (sum(LAST[:j]), n, j)
-        fetch(1, 5, *piece); reals(1, 5, False, *piece); weights(5, 1, False, *piece, quick=j >= len(LAST) - QUICK); sums(1, 5, *piece)
+        if c + LAG < 6 + APART and c < AHEAD: duel(c + LAG)
+        reals1(c)
+        if c + LAG < 6 + APART and c >= AHEAD: duel(c + LAG)
+        if c < 3: sums0(c + 3)
+        if c < 5: store(c)
+    for k in range(len(LAST)): piece(k)
+    store(5)
+    long = [i for i, o in enumerate(ops) if o["kind"] == "cp" and o["wr"][0]["n"] in ("EA", "XG", "EF")][12:]
+    for a, b in zip(long, long[2:]): ops[b]["soft"] = [a]
+    nth = lambda n, k: [i for i, o in enumerate(ops) if o["wr"] and o["wr"][0]["n"] == n][k]
+    for a, j, b, k in SOFT: ops[nth(b, k)].setdefault("soft", []).append(nth(a, j))
     seen = {}
     for o in ops:
         n = o["wr"][0]["n"] if o["wr"] else "y"; k = seen[n] = seen.get(n, -1) + 1; x = DUE.get(n, [])
-        o["due"] = 1000.0 * x[k] if k < len(x) and x[k] else 1000.0 * END
+        o["due"] = 1000.0 * (x[k] if k < len(x) and x[k] else END)
     return ops
 
 
@@ -459,7 +513,7 @@ def schedule(ops, succ, bias, lean, WAKE, ahead=0.3):
     n = len(ops)
     pr = [0.0] * n
     for i in range(n - 1, -1, -1):
-        o = ops[i]; pr[i] = o["cost"][o["eng"][0]] + max([o["hold"] + o["lat"] + WAKE + pr[k] for k in succ[i]] + [-o["due"]]) + bias[i]
+        o = ops[i]; pr[i] = o["cost"][o["eng"][0]] + max([o["hold"] + o["lat"] + WAKE + pr[k] for k in succ[i]] + [0.0]) + bias[i]
     free = dict.fromkeys("vatgsd", 0.0); ready = [0.0] * n; left = [len(o["deps"]) for o in ops]; eng = [None] * n; seq = []
     pool = [i for i in range(n) if not left[i]]
     while pool:
@@ -478,12 +532,15 @@ def schedule(ops, succ, bias, lean, WAKE, ahead=0.3):
 
 
 PLAN = {}
-ROUNDS, MOVES, STARTS, HEAT, SHOW = 100, 300000, 3, 150.0, 0
+PASSES, WARM, SIDE = 1, 300.0, 0.5
+ROUNDS, MOVES, STARTS, HEAT, SHOW, MIX, NOISE = 1000, 170000, 1, 250.0, 0, (0.4, 0.5, 0.1), 2000.0
 
 
 def plan():
     if not PLAN:
         all_ops = [build(c) for c in CASES]; ops = all_ops[0]; hazards(ops); n = len(ops)
+        hard = [o["deps"] for o in ops]
+        for o in ops: o["deps"] = dict({j: True for j in o.get("soft", [])}, **o["deps"]) if False else {**{j: True for j in o.get("soft", [])}, **o["deps"]}
         deps = [list(o["deps"]) for o in ops]; succ = [[] for _ in ops]
         for i in range(n):
             for j in deps[i]: succ[j].append(i)
@@ -500,44 +557,98 @@ def plan():
         inline = lambda i, j: ops[i]["eng"] == ops[j]["eng"] and (ops[i]["eng"] == "t" or len(ops[i]["eng"]) == 1 and not ops[i]["deps"][j])
         dp = [[j for j in deps[i] if direct(i, j) and not inline(i, j)] for i in range(n)]
 
-        kept = {}; load = {i: {q: 0.0 if q == "g" else sum(f[:3]) for q, f in figs[i].items()} for i in flex}
+        miles = [(i, o["mile"]) for i, o in enumerate(ops) if o.get("mile")]
+        fast = [{q: tuple(f) + (dp[i], held.get(i)) for q, f in figs[i].items()} for i in range(n)]; last = [i for i in range(n) if not ops[i]["wr"]]
+        kept = {}; load = {i: {q: sum(f[:3]) * (1.0 if q == "v" else SIDE if q == "a" else 0.0) for q, f in figs[i].items()} for i in flex}
 
         def ends(seq, eng, p0=0):
-            p0 -= p0 % 16
-            if p0: marks = kept["marks"][:p0 // 16]; free = dict(kept["marks"][p0 // 16]); d0, d1, d2 = [list(x) for x in kept["done"]]
+            p0 -= p0 % 32
+            if p0: marks = kept["marks"][:p0 // 32]; free = dict(kept["marks"][p0 // 32]); d0, d1, d2 = [x[:] for x in kept["done"]]
             else: marks = []; free = dict.fromkeys("vatgsd", (0.0, 0.0, 0.0)); d0, d1, d2 = [0.0] * n, [0.0] * n, [0.0] * n
             kept["new"] = (marks, (d0, d1, d2))
-            for p in range(p0, n):
-                if not p & 15: marks.append(dict(free))
-                i = seq[p]; q = eng[i]; t0, t1, t2 = free[q]; c0, c1, c2, l0, l1, l2 = figs[i][q]
-                for j in dp[i]:
-                    if d0[j] > t0: t0 = d0[j]
-                    if d1[j] > t1: t1 = d1[j]
-                    if d2[j] > t2: t2 = d2[j]
-                t0 += c0; t1 += c1; t2 += c2; free[q] = (t0, t1, t2)
-                if i in held:
-                    h, e = held[i], free["d"]; t0 = max(t0, e[0]) + h[0]; t1 = max(t1, e[1]) + h[1]; t2 = max(t2, e[2]) + h[2]; free["d"] = (t0, t1, t2)
-                d0[i] = t0 + l0; d1[i] = t1 + l1; d2[i] = t2 + l2
-            return [max(d0), max(d1), max(d2)]
+            for p in range(p0, n, 32):
+                marks.append(dict(free))
+                for i in seq[p:p + 32]:
+                    q = eng[i]; t0, t1, t2 = free[q]; c0, c1, c2, l0, l1, l2, before, h = fast[i][q]
+                    for j in before:
+                        x = d0[j]
+                        if x > t0: t0 = x
+                        x = d1[j]
+                        if x > t1: t1 = x
+                        x = d2[j]
+                        if x > t2: t2 = x
+                    t0 += c0; t1 += c1; t2 += c2; free[q] = (t0, t1, t2)
+                    if h:
+                        e = free["d"]; t0 = max(t0, e[0]) + h[0]; t1 = max(t1, e[1]) + h[1]; t2 = max(t2, e[2]) + h[2]; free["d"] = (t0, t1, t2)
+                    d0[i] = t0 + l0; d1[i] = t1 + l1; d2[i] = t2 + l2
+            return [max(d0[i] for i in last), max(d1[i] for i in last), max(d2[i] for i in last)]
 
         def score(seq, eng, p0=0):
             x = ends(seq, eng, p0)
-            return sum(w * (e + PULL * sum(d) / n) for w, e, d in zip(WEIGHTS, x, kept["new"][1])) + LOAD * sum(load[i][eng[i]] for i in flex)
+            return sum(w * (e + PULL * sum(d) / n + sum(m * d[i] for i, m in miles)) for w, e, d in zip(WEIGHTS, x, kept["new"][1])) + LOAD * sum(load[i][eng[i]] for i in flex)
 
-        def judge(bias, lean):
-            seq, eng = schedule(ops, succ, bias, lean, CASES[0][5])
-            return score(seq, eng), seq, eng
+        mean = lambda x: sum(w * y for w, y in zip(MIX, x))
+        cost = [{q: mean(f[:3]) for q, f in figs[i].items()} for i in range(n)]
+        way = [mean(list(figs[i].values())[0][3:]) + mean(held.get(i, (0.0, 0.0, 0.0))) for i in range(n)]
+        fwd = [[(j, 0.0 if inline(i, j) else way[j]) for j in deps[i] if direct(i, j)] for i in range(n)]
+        bwd = [[] for _ in range(n)]
+        for i in range(n):
+            for j, w in fwd[i]: bwd[j].append((i, w))
 
-        bias, lean = [o["bias"] for o in ops], [LEAN if o["kind"] in ("cp", "step") and o["wr"][0]["cnt"] >= 512 else 300.0 for o in ops]; best = judge(bias, lean)
-        for _ in range(ROUNDS):
-            b2, l2 = list(bias), list(lean)
-            for _k in range(int(rng.integers(1, 4))):
-                if rng.random() < 0.6: b2[int(rng.integers(0, n))] = float(rng.choice([0.0, 200.0, 1000.0, 3000.0, 8000.0]))
-                else: l2[flex[int(rng.integers(0, len(flex)))]] = float(rng.choice([0.0, 300.0, 800.0, 1500.0, 6000.0]))
-            r = judge(b2, l2)
-            if r[0] <= best[0]: best, bias, lean = r, b2, l2
+        keeps = [mean(held.get(i, (0.0, 0.0, 0.0))) for i in range(n)]
 
-        def chain(seq, eng, case):
+        def gap(line, t, c):
+            p = len(line)
+            while p and line[p - 1][1] > t: p -= 1
+            while p < len(line) and line[p][0] < t + c: t = line[p][1]; p += 1
+            return t, p
+
+        def fill_gaps(key, before, after, eng, tail, lean):
+            busy = {q: [] for q in "vatgsd"}; end = [0.0] * n; at = [0.0] * n
+            for i in sorted(range(n), key=lambda i: key[i]):
+                t = tail[i]
+                for j, w in before[i]:
+                    if end[j] + w > t: t = end[j] + w
+                q = eng[i]; c = cost[i][q]; t, p = gap(busy[q], t, c)
+                if keeps[i]:
+                    off = c if tail is zero else -keeps[i]
+                    while True:
+                        t2, p2 = gap(busy["d"], t + off, keeps[i])
+                        if t2 - off <= t + 1e-6: break
+                        t, p = gap(busy[q], t2 - off, c)
+                    busy["d"].insert(p2, (t + off, t + off + keeps[i]))
+                at[i] = t; end[i] = t + c; busy[q].insert(p, (t, t + c))
+            return at, end, eng
+
+        zero = [0.0] * n; best = None; lean = dict.fromkeys("vatgs", 0.0)
+        big = [i for i in flex if max(cost[i].values()) > 250]
+        pin = [o["eng"][0] for o in ops]; tail = [max(way[i], 1000.0 * END - ops[i]["due"]) for i in range(n)]; now = None
+        for r in range(ROUNDS):
+            p2, t2 = list(pin), list(tail)
+            for _ in range(int(rng.integers(1, 4)) if r else 0):
+                x = rng.random()
+                if x < 0.5:
+                    i = (big if x < 0.4 else flex)[int(rng.integers(0, len(big if x < 0.4 else flex)))]
+                    other = [q for q in cost[i] if q != p2[i]]; q = other[int(rng.integers(0, len(other)))]
+                    mates = [j for j in big if p2[j] == q and p2[i] in cost[j] and abs(j - i) < 60]
+                    if x < 0.2 and mates: p2[mates[int(rng.integers(0, len(mates)))]] = p2[i]
+                    p2[i] = q
+                else:
+                    i = int(rng.integers(0, n)); t2[i] = max(way[i], now[3][i] + NOISE * (2.0 * rng.random() - 0.6))
+            key = [0.0] * n
+            for i in range(n - 1, -1, -1): key[i] = min([key[k] - w for k, w in bwd[i]] + [-t2[i]]) - cost[i][p2[i]]
+            top = None
+            for k in range(PASSES):
+                at, end, eng = fill_gaps(key, fwd, bwd, p2, zero, lean)
+                seq = sorted(range(n), key=lambda i: (at[i], i)); v = score(seq, eng)
+                if top is None or v < top[0]: top = (v, seq, eng, [max(end) - x for x in end])
+                if k + 1 < PASSES:
+                    at, end, _e = fill_gaps([-x for x in end], bwd, fwd, eng, t2, lean)
+                    key = [-x for x in end]
+            if now is None or top[0] <= now[0] + WARM * (1.0 - r / ROUNDS): now, pin, tail = top, p2, t2
+            if best is None or top[0] < best[0]: best = top[:3]
+
+        def chain(seq, eng, case, to=None):
             cost, lat, wake = tabs[case]; free = {q: (0.0, -1) for q in "vatgsd"}; done = [0.0] * n; why = [None] * n
             for i in seq:
                 t, k = free[eng[i]]; queue = True
@@ -548,12 +659,12 @@ def plan():
                     if free["d"][0] > t: (t, k), queue = free["d"], True
                     t += held[i][case]; free["d"] = (t, i)
                 why[i] = (k, queue); done[i] = t + lat[i] + wake
-            i = done.index(max(done)); out = []
+            i = done.index(max(done)) if to is None else to; out = []
             while i >= 0:
                 k, queue = why[i]
                 if queue and k >= 0: out.append((i, k))
                 i = k
-            return out
+            return out or chain(seq, eng, case)
 
         runs = []; each = MOVES // (STARTS + 2); draws = rng.random((MOVES, 5)).tolist()
         for it, (r0, r1, r2, r3, r4) in enumerate(draws):
@@ -563,12 +674,12 @@ def plan():
                 top = cur; keep = (list(seq), list(eng)); arcs = None; score(seq, eng); kept["marks"], kept["done"] = kept["new"]
             heat = HEAT * (1.0 - it % each / each) if it < STARTS * each else 0.6 * HEAT * (MOVES - it) / (MOVES - STARTS * each)
             if it % 500 == 0:
-                d0 = kept["done"][0]; at = [d0[i] - figs[i][eng[i]][0] - figs[i][eng[i]][3] - held.get(i, (0.0,))[0] for i in range(n)]; last = {}
+                d0 = kept["done"][0]; at = [d0[i] - figs[i][eng[i]][0] - figs[i][eng[i]][3] - held.get(i, (0.0,))[0] for i in range(n)]; prev = {}
                 for i in seq:
-                    at[i] = max([at[i], last.get(eng[i], 0.0)] + [at[j] for j in deps[i]]) + 1e-6; last[eng[i]] = at[i]
+                    at[i] = max([at[i], prev.get(eng[i], 0.0)] + [at[j] for j in deps[i]]) + 1e-6; prev[eng[i]] = at[i]
                 s2 = sorted(seq, key=lambda i: at[i]); v = score(s2, eng)
                 if v <= cur + HEAT: cur, seq = v, s2; kept["marks"], kept["done"] = kept["new"]
-            if arcs is None: arcs = chain(seq, eng, int(r4 * len(tabs)))
+            if arcs is None: arcs = chain(seq, eng, int(r4 * len(tabs)), miles[int(r2 * len(miles))][0] if miles and r3 < 0.5 else None)
             s2, e2 = seq, eng
             i, k = arcs[int(r1 * len(arcs))]
             if r0 < 0.25:
@@ -612,6 +723,7 @@ def plan():
             start[i] = max([free[eng[i]]] + [done[j] for j in dp[i]]); t = free[eng[i]] = start[i] + cost[i][eng[i]]
             if i in held: t = free["d"] = max(t, free["d"]) + held[i][SHOW]
             done[i] = t + lat[i] + wake
+        for o, h in zip(ops, hard): o["deps"] = h
         PLAN.update(ops=ops, seq=seq, start=start, eng=eng, end=ends(seq, eng))
     return PLAN
 
@@ -635,7 +747,7 @@ def rank_program(g, core, T, topo):
         e = topo.engines(src, dst); m = len(e) // n
         return e[k * m:(k + 1) * m]
 
-    seq = P["seq"]
+    seq = P["seq"]; issue = caller(ap)
     count = {q: 0 for q in "vatg"}; nd = [0, 0, 0]; token = {}; known = {q: {} for q in Q}; snap = {}; total = {}
 
     def wait(q, sem, val, src):
@@ -665,9 +777,22 @@ def rank_program(g, core, T, topo):
             continue
         if k == "dma":
             sem = "d%d" % nd[0]; nd[0] += 1
-            for out, src in x: e.dma_start(ap(out), ap(src), **({"accum_op": ALU.add} if o["add"] else {})).then_inc(T.sem[sem], 16)
+            for out, src in x: e.dma_start(ap(out), ap(src)).then_inc(T.sem[sem], 16)
             token[i] = (sem, 16 * len(x)); total[sem] = 16 * len(x)
             continue
+        for y in (x if k == "many" else [o]):
+            issue(e, q, y["kind"], y["args"]).then_inc(T.sem["c" + q], 1); count[q] += 1
+        token[i] = ("c" + q, count[q]); total["c" + q] = count[q]
+    total["loc"] = nd[2]
+    seen = {}
+    for q in Q:
+        for s2, v2 in known[q].items(): seen[s2] = max(seen.get(s2, 0), v2)
+    for s2, v2 in total.items():
+        if seen.get(s2, 0) < v2: g.sync.wait_ge(T.sem[s2], v2)
+
+
+def caller(ap):
+    def issue(e, q, k, x):
         if k == "cp":
             out, a, sc, bi = x
             if q == "g": r = e.affine_select(ap(out), ap(a), [[0, out["cnt"]]], ALU.is_ge, 0.0, 0, 0)
@@ -692,14 +817,7 @@ def rank_program(g, core, T, topo):
         elif k == "iota":
             if SCRATCH[x[0]["n"]][2] == I: r = e.iota(ap(x[0]), x[1], x[2], x[3])
             else: r = e.iota(ap(x[0]), x[1], x[2], x[3], allow_small_or_imprecise_dtypes=True)
-        elif k == "trp":
-            for out, a, b in x: r = e.transpose(ap(out), ap(a), ap(b))
         else:
             for out, a, b, s0, s1 in x: r = e.matmul(ap(out), ap(a), ap(b), s0, s1)
-        count[q] += 1; r.then_inc(T.sem["c" + q], 1); token[i] = ("c" + q, count[q]); total["c" + q] = count[q]
-    total["loc"] = nd[2]
-    seen = {}
-    for q in Q:
-        for s2, v2 in known[q].items(): seen[s2] = max(seen.get(s2, 0), v2)
-    for s2, v2 in total.items():
-        if seen.get(s2, 0) < v2: g.sync.wait_ge(T.sem[s2], v2)
+        return r
+    return issue

@@ -5,16 +5,28 @@ from concourse.mybir import AluOpType as ALU, ActivationFunctionType as ACT
 
 M, NK, L, D, NR = 4096, 1024, 192, 3, 8
 B, F, I, U = "bfloat16", "float32", "int32", "uint16"
+DUELS = ((1, 0, 64), (1, 64, 128), (0, 0, 128), (0, 128, 64))
+DB = ("S1", "S1", "S1", "S1")
+BROAD = (3,)
+DIFF = (2, 3, 4, 5)
+ORDER = "D0 D1 R0 D2 R1 D3 R2 R3 R4 R5"
 WIDE = (0, 1, 2, 3, 4, 5)
-PAIRS = ()
 DIRECT = (4, 5)
-EARLY = (2, 1)
-LAST = (2,)
-NEQ, RO, ZB, LAG, AHEAD, APART = 12, "va", (1, 1, 0, 1, 0, 1), 3, 0, 0
-NEF, NET, NEA, NW = 2, 4, 3, 3
-ONV = ((7, 9, 6, 1), (2, 9))
+SHARE = ()
+LOW = ("v0", "w0")
+GB = ("PGC", "PGD", "PGB", "PGA", "S0")
+EARLY = ((3, 2), (0, 1))
+VEARLY = 1
+LAST = ()
+ALL = ("V0", "V1")
+APART = (0, 1, 2, 3, 4, 5)
+KLATE, ZCUT, TWIN, SPLIT = 1, 2, 1, 3
+PARTS = ((2, 3), (3,))
+CUT, AHEAD = (1, 1, 1, 1, 1, 1), 4
+NEQ, RO, ZB = 24, "va", (1, 0, 1, 0, 1, 0)
+NEF, NET, NEA, NW = 3, 4, 6, 3
+ONV = ((9, 8, 0, 4), ())
 NL = sum(LAST)
-TH = ()
 SCRATCH, PLACE = {}, {}
 
 
@@ -28,36 +40,43 @@ def _buf(names, cols, dtype, where="sbuf"):
             SCRATCH[n] = (where, [128] + (list(cols) if isinstance(cols, tuple) else [cols]), dtype)
 
 
-_buf("X", M + L, B); _buf("E", M, B); _buf("E32", M + L, F); _buf("HC TC", NK + L, I); _buf("NN", 4 * L, I)
+_buf("X", M + 2 * L, B); _buf("E", M, B); _buf("E32", M + 2 * L, F); _buf("HC TC", NK + L, I); _buf("NN", 4 * L, I)
 _buf("XR", 64, B); _buf("LL", 36, I); _buf("S16", 48, U); _buf("RL", 24, I); _buf("OT RKEY", 12, U); _buf("MX ME", 2 * L, B)
-_buf("IP IN I1 I2 I3 I4", 1, I); _buf("K15 KB0 KB1 G2 C1 C3 C4", 1, F)
-_buf("ID32 BO32", 128, F); _buf("IDB BO TRI ONE HALF OWN OWNN" + " HALFP" * bool(PAIRS), 128, B); _buf("COL" + " THR" * bool(TH), 512, B); _buf("IH", 128, I)
-_buf("ZERO", 768, B); _buf("ZERO32", 384, F); _buf("RD", 128, F); _buf("RS32", 2 * L, B); _buf("MD", 16, B); _buf("COUNT", NK, I)
-_buf("RSB NMD NMD2 IOC SELQ", L, B); _buf("DRX DRC", L, F); _buf("AM", 512, B); _buf("SEL IOG", 240, B); _buf("A64", 128, F)
-_buf("SC12 SCP SCB", 12, I); _buf("DUM0 PARF", 12, F); _buf("C37", 24, F); _buf("CTR CBLK ROSC", 12, U)
-_buf("OKK OHT1 OKEY1 OB OSX OSC", 24, U)
-_buf("KA KB KEY KEY0 Q MI INS EXK INK KK Z2", 24, I)
-_buf("Z1 LV BS0 BS F1 G1 G3 G4 KF HT8", 24, F)
+_buf("IP IN I1 I2 I3 I4 I5 I6", 1, I); _buf("K15 KB0 KB1 KQ KQ2 C1 C3 C4 C5 C6 C7", 1, F)
+_buf("ID32 BO32", 128, F); _buf("IDB BO TRI ONE HALF OWN", 128, B); _buf("COL", 512, B); _buf("IH", 128, I)
+_buf("ZERO", 768, B); _buf("RD", 128, F); _buf("RS32", 2 * L, B)
+PLACE.update(DRX=("EF", 0, 2 * L), COUNT=("EF", 1024, NK), ZERO32=("EF", 2048, 2 * L), DRC=("EF", 2048 + 2 * L, L))
+_buf("SELW", 240, B); _buf("MR IOR", 16, B)
+_buf("RSB NMD NMD2 IOC SELQ SEL IOG", L, B); _buf("AM", (16, 16), B); _buf("A64", 256, F)
+if BROAD: _buf("AW", (64, 8), B)
+_buf("SCB", 12, I); _buf("SC12", 24, I); _buf("CBLK CBLW ROSC", 12, U)
+_buf("OKK OHT1 OKEY1 OB OSX OSC EXU", 24, U)
+_buf("KA KB KEY MI INS EXK KK Z2", 24, I)
+_buf("F1 KF", 24, F); _buf("TIMES PLUS NEW", 72, F)
 _buf("UO0 UO1 U0 U1 SU NX0 NX", 2 * L, B)
-_buf("VO0 VO1 V0 V1 DD AF OAA BSC FS PV WV EB SCS0 SCS1", 2 * L, F)
+_buf("VO0 VO1 V0 V1 DD AF", 2 * L, F)
+for _k, _n in enumerate("OAA FS PV BSC WV EB SCS1 - SCS0".split()): PLACE[_n] = ("EU", 2 * L * _k, 2 * L)
 _buf("VH", 4 * L, B); _buf("BR16 KR16 OA", 2 * L, U); _buf("OFN OFC", 4 * L, U)
-if max(EARLY): _buf("UA", 512 * max(EARLY), B)
-VEARLY = 1
-_buf("VA", 512 * VEARLY, F)
-_buf("UB0 UB1", (8, L), B); _buf("VB0 VB1", (8, 2 * L), B); _buf("VF0 VF1", (8, L), F)
-_buf("WC", (16, 96), B); _buf("WB0 WB1", (32, 96), B); _buf("WS", 128 * NW, F); _buf("WF", (32 * NW, 16), F); _buf("WL", 64 * NL, F)
+NUA = [max(EARLY[0][_d], EARLY[1][_d]) for _d in (0, 1)]
+for _d in (0, 1):
+    if NUA[_d]: _buf("UA%d" % _d, 512 * NUA[_d], B)
+if VEARLY: _buf("VA", 512 * VEARLY, F)
+_buf("UB0 UB1" if min(EARLY[0][1], EARLY[1][1]) < 3 else "UB0", (8, L), B); _buf("VB0 VB1" if TWIN else "VB1", (8, 2 * L), B); _buf("VF0 VF1", (8, L), F)
+_buf("WC", (16, 96), B); _buf("WB0 WB1" if TWIN else "WB1", (32, 96), B); _buf("WS", 128 * NW, F); _buf("WF", (32 * NW, 16), F); _buf("WL", 64 * max(NL, 1), F)
 _buf("XG", 64 * L, B); _buf("EA", 1024 * NEA, B); _buf("ET", 32 * L, B); _buf("EF", 1024 * NEF + 128 * NL, F); _buf("EU", 1024 * NET + 128 * NL, F)
 _buf("WN", (24, 16), B); _buf("EQ", (NEQ, L), B); _buf("GY0 GY1", (64, 8), F)
-_buf("PZ0 PZ1 PGA PGB PGC", (64, 8), F, "psum"); _buf("S0", (32, 16), F, "psum"); _buf("S1 PT", 512, F, "psum")
+_buf("PZ0 PZ1 PGA PGB PGC PGD", (64, 8), F, "psum"); _buf("S0", (32, 16), F, "psum"); _buf("S1", 512, F, "psum")
+PLACE["MARK"] = ("SELW", 1000, 16)
 NDMA = 64
-SEMAPHORES = ["cv", "ca", "ct", "cg", "loc"] + ["d%d" % i for i in range(NDMA)] + ["r%d" % i for i in range(20)]
+SEMAPHORES = ["cv", "ca", "ct", "cg", "loc", "mark"] + ["d%d" % i for i in range(NDMA)] + ["r%d" % i for i in range(20)]
 
 
 def A(n, a=None, b=None, st=1, p=(0, 128)):
+    name = n
     n, at, w = PLACE[n] if n in PLACE else (n, 0, SCRATCH[n][1][1])
     a = at + (0 if a is None else a)
     b = at + (w if b is None else b)
-    return {"n": n, "ix": (slice(*p), slice(a, b, st)), "lo": a, "hi": b, "cnt": len(range(a, b, st)), "p": p, "st": st}
+    return {"n": n, "as": name, "ix": (slice(*p), slice(a, b, st)), "lo": a, "hi": b, "cnt": len(range(a, b, st)), "p": p, "st": st}
 
 
 def A3(n, rows=None, cols=None, p=(0, 128)):
@@ -67,11 +86,12 @@ def A3(n, rows=None, cols=None, p=(0, 128)):
     r = range(rows, rows + 1) if isinstance(rows, int) else range(*rows)
     c = range(cols, cols + 1) if isinstance(cols, int) else range(*cols)
     ix = lambda x: x if isinstance(x, int) else slice(*x)
-    return {"n": n, "ix": (slice(*p), ix(rows), ix(cols)), "lo": r[0] * w + c[0], "hi": r[-1] * w + c[-1] + 1, "cnt": len(r) * len(c), "p": p,
-            "runs": len(r) if r.step > 1 or len(c) < w else 1}
+    return {"n": n, "as": n, "ix": (slice(*p), ix(rows), ix(cols)), "lo": r[0] * w + c[0], "hi": r[-1] * w + c[-1] + 1, "cnt": len(r) * len(c), "p": p,
+            "runs": len(r) if r.step > 1 or len(c) < w else 1, "st": (c[0], c[-1]) if n[:2] == "GY" else 1}
 
 
 def PB(n, a, cnt, runs=1, st=0, p=(0, 128)):
+    if len(SCRATCH[n][1]) == 2: return A(n, a, a + cnt, 1, p)
     w = SCRATCH[n][1][2]
     if runs == 1 and cnt > w: return A3(n, (a // w, (a + cnt) // w), None, p)
     return A3(n, (a // w, a // w + (runs - 1) * st // w + 1, max(1, st // w)), (a % w, a % w + cnt), p)
@@ -89,29 +109,38 @@ def psum(a):
     return SCRATCH[a["n"]][0] == "psum"
 
 
-CASES = [(0.85, 0.42, 1.25, 3.0, 0, 140, 2000, 2400, 1500, 15), (0.87, 0.43, 0.95, 2.2, 0, 120, 2200, 2700, 2000, 20), (1.15, 0.57, 1.9, 4.5, 0, 150, 1800, 2200, 1500, 15)]
-WEIGHTS, PULL, LOAD, SEED, MILES = (1.0, 1.0, 0.7), 0.1, 0.03, 11, (0.0, 0.0, 0.0, 0.03)
+CASES = [(0.85, 0.42, 1.25, 3.0, 400, 140, 2000, 2400, 1500, 15), (1.05, 0.525, 1.15, 3.0, 550, 150, 2100, 2600, 2000, 20), (1.22, 0.61, 2.4, 6.0, 450, 150, 1900, 2300, 1500, 15)]
+WEIGHTS = (0.36, 0.33, 0.21)
+LATER = [(0.87, 0.43, 1.3, 3.8, 400, 150, 2000, 2400, 1500, 15), (1.08, 0.55, 1.8, 5.5, 450, 160, 2000, 2400, 1600, 16), (1.24, 0.62, 2.55, 7.4, 450, 160, 1900, 2300, 1500, 15)]
+WSECOND, WLATER = (0.36, 0.36, 0.21), (0.36, 0.33, 0.21)
 SIZE = {B: 2, U: 2, F: 4, I: 4}
-END, KH = 62, -1
-SOFT = []
-DUE = {"OA": [17.5, 21], "X": [0, 26, 27], "EA": [20, 22, 24, 26, 28, 30], "U0": [5.2, 8.3], "MX": [0, 3.8], "XG": [12, 14, 13, 15, 14, 15.5, 7, 9.5, 8, 11, 8.5, 12],
-       "EF": [36, 38, 41, 45, 49, 53, 56], "VA": [0, 35], "VO1": [31], "TC": [0, 28], "E32": [0, 29.5, 30.5], "WB1": [0, 32], "WB0": [0, 37]}
+PIN = dict(RS32="a", DRC="a", DRX="g", BO32="a", ID32="g", KF="v", MI="gv", Z2="g", OT="v", OKK="gv", OSX="v", OB="v", EXU="g", UB1="av", MX="a", ME="a", SCS1="a", SCS0="a", WN="va", SU="a", BR16="aa", KB0="v", BO="gga", VH="aggag", WC="aggag", GY0="vvav", GY1="vvvvvvav", AM="avv", AW="a", OFN="gvg", KR16="aa", SELW="g", OSC="g", PLUS="g", EF="vavaaav", EA="a", EU="v", OA="agvgg", OHT1="g", UA0="aav", UA1="vvv")
+END = 57.5
+AFTER = ()
+DUE = dict(ZERO=[0.1,0.4], ONE=[1.6], LL=[0.05,0.05], XR=[0.1], X=[0.4,26.1,26.75], NN=[0.3,4.0,12], IN=[0.1], IP=[0.2], K15=[0.6], CBLK=[2.4], KB0=[2.5], SELQ=[3], ID32=[10.3], BO32=[4.4], BO=[3.4,3.85,4.7], RS32=[2.0,2.6], DRC=[1.7,2.6], DRX=[19.5,22], UB0=[24.6,31], UO0=[5.3,8.0], OFC=[10.9,7.6,28.2,36], OFN=[7.8,3.9,26.5,24], RL=[3.0], HC=[6.05,36.6], MX=[3.3,4.65], ME=[3.6], RKEY=[4.25], KR16=[3.9,17.6], EQ=[4.5,4.9,5.0,22.3,22.6,22.8,23.5,23.9,24.2,32.4,32.8,33.1], U0=[5.85,8.6], E=[6.15], UB1=[2.4,3.1,9.3,31], UA1=[1.0,1.4,9.3,31.5], UA0=[2.2,3.0,12.9], TRI=[6.75,7.2], FS=[10,25.1,33.6], V0=[11.8,14.2], VH=[14.5,15,16,17,17.5,18.5], SCS1=[12.6,14.9,23.5], PZ1=[13.4,20.3,20.7,21.8,22.5,22.8,23.1], WN=[14,17,18.3], S0=[15.1,15.6,19.3,19.7,27,27.5], AF=[15.9,20], SCS0=[16.3,17.2,17.6,18.6,29], MI=[15.2,18.8], INS=[15.7,19.3], OA=[16.3,20.4,34,37.4,37.7,42,42.3,45.3], BR16=[19.5,21.3], BSC=[20.3,21.5], SU=[17.3], EA=[17.7,19.1,20.5,22.5,23.9,25.2], OKEY1=[24.4], TC=[3.2,18.2], PV=[21.8,26], E32=[9.6,15.4,29.2,29.9], VO1=[30.5], UO1=[27.3,30.5], U1=[27.8,31], V1=[31], VF1=[24.8,34.5], VF0=[28.1,35.5], WF=[31.3], XG=[6.4,9.1,6.7,10.4,7.7,10.4,11.8,12.0,13.1,14.5,15.9,15.4,28.1,29.5,30.9,32.2,33.6,34.9,36.3,37.7,37.6,39.8,40.6,42.4], EF=[35.4,38.9,39.1,43.4,44,46.5,47], COUNT=[2.2], VO0=[11.3,13.5], SCB=[2.45], IDB=[5.05], SC12=[5.3], IOC=[2.0], RD=[8.2,9.0], IOG=[2.6], IOR=[11.5], ZERO32=[12.3], COL=[13.4], IH=[13.8,16.5], RSB=[18], NMD=[2.3], NMD2=[2.5], HALF=[18], OWN=[30], SELW=[30,40], SEL=[3.2], OSC=[12,35.2], ROSC=[13], DD=[16.8,14.3,31,37], OAA=[17.5,20.5], OB=[21,22], NX0=[21.4,24.6], NX=[25.35], EB=[26], WV=[28.5], PZ0=[16.8,18.1,28,28.5,29,29.5,30,30.5], TIMES=[1.6,1.7,1.8,21.0,22.9], PLUS=[10.9,12,13.9,14,22.95], ET=[28.9,31.5,32,34.6,36,44], KK=[16.2,19.55], OKK=[16.6,20], NEW=[23.1], Z2=[23.4], EXK=[23.6], EXU=[24], OSX=[25.4], OHT1=[24.7], VA=[22,35.8], MR=[3.5], VB1=[12.3,19], VB0=[16,22], WB1=[20.2,28], WB0=[20.5,33], CBLW=[33])
+DUE.update(VA=[22,35], WS=[39.4,41.5,43.5,46.5], EF=[37.2,39.5,40.5,44,45.5,48], V1=[31.6,34], VO1=[31.2,33.5], E32=[9.6,15.4,30.3,31], U1=[29.2,32.5], UO1=[28.8,32], X=[0.4,27.6,28.3], OA=[16.3,20.4,35.5,38,38.3,42.5,42.8,46], WV=[29.5],
+           PZ0=[16.8,18.1,27.5,28,28.5,29,29.5,30,30.6], WC=[27.5,28,31,31.5], WB1=[20.2,28.2], WB0=[20.5,31.8])
+_OLD = dict(ZERO=[0.1, 0.4], ONE=[1.6], LL=[0.05, 0.05], XR=[0.1], X=[0.4, 27, 27.7], NN=[0.3, 4.2, 11.2], IN=[0.1], IP=[0.2], K15=[0.6], CBLK=[3], KB0=[3], SELQ=[9], ID32=[4.6], BO32=[4.8], BO=[0, 0, 5], RS32=[2.0, 2.6], DRC=[4.2, 5], DRX=[4.4, 9], UB0=[15, 16, 17, 25], UO0=[5.45, 8.2], OFC=[11.5, 7.85], OFN=[9, 4], RL=[3.1], HC=[4.6], MX=[3.4, 4.0], ME=[3.7], RKEY=[4.4], KR16=[4.0], EQ=[4.5, 4.8, 5.1], U0=[5.85, 8.6], E=[5.9], UB1=[2.4, 3.1, 9.3], UA1=[2, 9.2], UA0=[2.5, 12.6], TRI=[7, 7.5], FS=[8.5], V0=[11.2, 15], VH=[14.3, 14.8, 15.3], SCS1=[13.0], PZ1=[13.8], WN=[14.5, 19], S0=[15.1, 15.6], AF=[16.5], SCS0=[17.5, 19.4], MI=[17, 19.7], INS=[17.5, 20.2], OA=[17.5, 21.5, 35, 38.5, 38.5, 44.5, 44.5, 48.5], BR16=[19, 22.3], BSC=[19, 22.3], SU=[17], EA=[19, 20.4, 22, 23.5, 25, 26.5], OKEY1=[25.5], TC=[3.2, 24], PV=[25], E32=[10.2, 29, 29.7], VO1=[30.3], UO1=[28.3], U1=[28.7], V1=[30.7], VB=[11.5, 19.5, 26], WB=[15, 29, 35], VF1=[17.6], VF0=[20.2], WF=[22, 25.6], XG=[6.5, 9.35, 7.1, 10.6, 7.85, 10.7, 12.1, 13.5, 13.4, 14.8, 16.1, 15, 29.2, 30.5, 30.5, 33.5, 32.4, 35, 37.5, 39.5, 39.5, 41.5, 43.5, 45.5], EF=[36.4, 40, 42.5, 46, 49, 51.5, 52.5])
 
 
 def build(case):
     CY, PECY, GAT, SCA, MMI, WAKE, DML, RML, FIRST, ROW = case
-    ops = []
+    ops = []; made = {}
 
     def add(eng, kind, args, rd, wr, cost, lat=0.0):
         r = []
-        if len(eng) > 1 and wr[0]["n"] not in KEEP: eng = "".join(q for q in "gav" if q in eng)
+        name = wr[0]["as"] if wr else "y"; k = made[name] = made.get(name, -1) + 1
+        if len(eng) > 1:
+            q0 = PIN[name][min(k, len(PIN[name]) - 1)] if name in PIN else ""
+            if q0 and q0 in eng: eng = q0 + eng.replace(q0, "")
+            elif name not in ("XG", "OA"): eng = "".join(q for q in "gav" if q in eng)
         for a in rd:
             if isinstance(a, dict):
                 r.append(a)
                 if "off" in a: r.append(a["off"])
         for a in wr:
             if "off" in a: r.append(a["off"])
-        ops.append({"eng": eng, "kind": kind, "args": args, "rd": r, "wr": list(wr), "cost": cost, "lat": lat, "hold": 0.0, "bias": 0.0})
+        ops.append({"eng": eng, "kind": kind, "args": args, "rd": r, "wr": list(wr), "cost": cost, "lat": lat + WAKE, "hold": 0.0, "name": name})
 
     def join(k):
         x = ops[-k:]; del ops[-k:]
@@ -151,6 +180,9 @@ def build(case):
     def step(out, a, eng="va"):
         add(eng, "step", (out, a), [a], [out], {"v": vc(out, [a], 1), "a": 70 + out["cnt"] * CY} if eng == "va" else {"a": 1400 * CY})
 
+    def sign(out, a):
+        add("va", "sign", (out, a), [a], [out], {"v": vc(out, [a], 0.5), "a": 70 + out["cnt"] * CY})
+
     def iota(out, pat, base=0, chm=0):
         add("g", "iota", (out, pat, base, chm), [], [out], {"g": 160 + 2 * out["cnt"] * CY})
 
@@ -158,75 +190,95 @@ def build(case):
         add("g", "sel", (out, a, pat, op, fill, base, chm), [a], [out], {"g": 200 + 2 * out["cnt"] * CY})
 
     def mm(lst):
-        c = sum(max(min(64, x[1]["cnt"]), x[2]["cnt"]) * (4 if SCRATCH[x[1]["n"]][2] == F else 1) * PECY + MMI for x in lst)
+        c = sum(max(min(64, x[1]["cnt"]), x[2]["cnt"]) * (4 if SCRATCH[x[1]["n"]][2] == F else 1) * PECY for x in lst)
         add("t", "mm", lst, [x[1] for x in lst] + [x[2] for x in lst], [x[0] for x in lst], {"t": c}, 60)
 
     def hold(pairs):
         sides = [x[0] if isinstance(x[0], dict) else x[1] for x in pairs]
         return sum((a["p"][1] - a["p"][0]) * (a["cnt"] * SIZE[SCRATCH[a["n"]][2]] * 0.21 / 128 + a.get("runs", 1) * ROW / 16) for a in sides)
 
-    def dma(q, pairs, after=None):
-        add(q, "dma", pairs, [x[1] for x in pairs] + [after], [x[0] for x in pairs if isinstance(x[0], dict)], {q: (900 if q == "g" else 70) * len(pairs)}, DML)
-        ops[-1]["hold"] = hold(pairs)
+    def dma(q, pairs, after=None, kind="dma"):
+        add(q, kind, pairs, [x[1] for x in pairs] + [after], [x[0] for x in pairs if isinstance(x[0], dict)], {q: (2.25 * MMI if q == "g" else 70) * len(pairs)}, DML)
+        ops[-1]["hold"] = hold(pairs) * (2 if kind == "dadd" else 1)
 
     def send(pairs, first=False):
-        add("g", "send", pairs, [x[1] for x in pairs], [x[0] for x in pairs], {"g": 400}, RML + (FIRST if first else 0))
+        add("g", "send", pairs, [x[1] for x in pairs], [x[0] for x in pairs], {"g": MMI}, RML + (FIRST if first else 0))
         ops[-1]["hold"] = hold(pairs)
 
+    def sent():
+        k = made.get("MARK", -1) + 1; add("g", "mark", None, [], [A("MARK", k, k + 1)], {"g": 40}); ops[-1]["soft"] = [len(ops) - 2]
+        return A("MARK", k, k + 1)
+
+    def lower(name, hi, lo, x):
+        if name in LOW: cp(lo, x, "va", -1.0); cp(hi, x, "vag"); dma("g", [(lo, x)], None, "dadd")
+        else: cp(hi, x, "va" if psum(x) else "vag"); tt(lo, x, hi, ALU.subtract)
+
+    def fill(n, z, after, r0=0, rows=None):
+        w = SCRATCH[n][1][2]; rows = rows or SCRATCH[n][1][1]; k = A(z)["cnt"] // w
+        dma("s", [(A3(n, (r, min(rows, r + k))), A(z, 0, w * (min(rows, r + k) - r))) for r in range(r0, rows, k)], after)
+
+    twin = lambda n, d: n + str(d if TWIN else 1)
     who = lambda s, j: "va" if j in ONV[s] else "av"
-    KEEP = ("XG", "MX", "ME", "WN", "OA")
     H = lambda n, d, w=L: A(n, d * w, d * w + w)
     full = (slice(0, 128), slice(None))
     grp = lambda g: (16 * g, 16 * g + 16)
     quad = lambda q: (32 * q, 32 * q + 32)
-    mask = lambda bank, n, left: (PB(bank, 0, n), A(left, p=(0, 8)), A("COL", 0, n, 1, (0, 8)), True, False)
+    mask = lambda bank, n, left, p=(0, 128): (PB(bank, 0, n, p=p), A(left, p[0], p[1], 1, (0, 8)), A("COL", 0, n, 1, (0, 8)), True, False)
     OHT0, OKEY0, OSC = (H("S16", 1, 12), A("OT")), (H("S16", 2, 12), A("RKEY")), (H("OSC", 0, 12), A("ROSC"))
     ent = lambda s, d: H("NN", 2 * s + d)
     nn = lambda s, d: (ent(s, d), (("nh", "nt")[d], (slice(0, 128), slice(s * L, s * L + L))))
-    dma("a", [(A("LL", 12 * j, 12 * j + 12), (n, full)) for j, n in enumerate(("tl", "rl", "hl"))])
+    dma("s", [(A("LL", 12 * j, 12 * j + 12), (n, full)) for j, n in enumerate(("tl", "rl"))])
+    dma("a", [(A("LL", 24, 36), ("hl", full))])
     dma("a", [(A("XR", 0, 32), ("xr", full)), (A("XR", 32, 64), ("er", full))])
     dma("s", [nn(0, 1)])
     dma("s", [(A("X", 0, M), ("xe", full))])
-    dma("s", [nn(0, 0)])
     iota(A("IN"), [[0, 1]], 127, -1); ts(A("I1"), A("IN"), 15, ALU.bitwise_and); cp(A("K15"), A("I1"))
     ts(A("I2"), A("IN"), 31, ALU.bitwise_and, 1, ALU.arith_shift_right); cp(A("KB1"), A("I2")); cp(A("KB0"), A("KB1"), "va", 1.0, 16.0)
     iota(A("IP"), [[0, 1]], 0, 1)
-    iota(A("IOC"), [[0, 12], [-1, 16]], 15); ts(A("MD"), A("IOC", 0, 16), A("K15"), ALU.is_equal); ts(A("NMD"), A("IOC"), A("K15"), ALU.not_equal, 8192.0, ALU.mult)
-    ts(A("NMD2"), A("NMD"), 8192.0, ALU.add)
     ms(A("ZERO", 0, 128), 0.0); ms(A("ZERO", 128, 768), 0.0); step(A("ONE"), A("ZERO", 0, 128), "a")
+    iota(A("IOC"), [[0, 12], [-1, 16]], 15); iota(A("IOR"), [[1, 16]]); ts(A("MR"), A("IOR"), A("K15"), ALU.is_equal)
+    if BROAD: cp(A("SELW"), A("ZERO", 0, 240), "vag"); ts(A("SELW", 112, 128), A("IOC", 0, 16), A("K15"), ALU.is_equal)
+    ts(A("NMD"), A("IOC"), A("K15"), ALU.not_equal, 8192.0, ALU.mult)
+    ts(A("NMD2"), A("NMD"), 8192.0, ALU.add)
     sel(A("IDB"), A("ONE"), [[-1, 128]], ALU.is_equal, 0.0, 0, 1); cp(A("ID32"), A("IDB"), "ag")
     sel(A("BO"), A("ONE"), [[-16, 8], [0, 16]], ALU.is_ge, 0.0, 0, 1); sel(A("BO"), A("BO"), [[16, 8], [0, 16]], ALU.is_ge, 0.0, 15, -1); cp(A("BO32"), A("BO"), "ag")
-    sel(A("TRI"), A("BO"), [[1, 128]], ALU.is_gt, 0.0, 0, -1); sel(A("TRI"), A("TRI"), [[1, 128]], ALU.not_equal, -1.0, 0, -1)
-    sel(A("RD"), A("ONE"), [[-32, 4], [-2, 32]], ALU.is_equal, 0.0, -1, 1); sel(A("RD"), A("RD"), [[-32, 4], [-2, 32]], ALU.not_equal, -1.0, 0, 1)
-    iota(A("IOG"), [[-1, 240]], 127); ts(A("SEL"), A("IOG"), A("K15"), ALU.is_equal)
-    sel(A("SELQ"), A("ZERO", 0, L), [[-32, 4], [-1, 48]], ALU.not_equal, 1.0, 16, 1); sel(A("SELQ"), A("SELQ"), [[0, 4], [1, 3], [0, 16]], ALU.is_equal, 0.0, -1)
-    for r in (0, 4): cp(A3("UB1", (r, r + 4)), A("ZERO"), "va")
+    cp(A("BO"), A("BO32"), "va", 8192.0)
+    sel(A("TRI"), A("BO"), [[1, 128]], ALU.is_gt, 0.0, 0, -1); sel(A("TRI"), A("TRI"), [[1, 128]], ALU.not_equal, -8192.0, 0, -1)
+    sel(A("RD"), A("ONE"), [[-32, 4], [-2, 32]], ALU.is_equal, 0.0, 0, 1); sel(A("RD"), A("RD"), [[-32, 4], [-2, 32]], ALU.not_equal, -1.0, -1, 1)
+    iota(A("IOG"), [[-64, 4], [-1, 48]], 31); ts(A("I5"), A("IP"), 5, ALU.arith_shift_right); ts(A("KQ"), A("I5"), -64.0, ALU.mult, A("K15"), ALU.add)
+    ts(A("I6"), A("IP"), 16, ALU.bitwise_and); ts(A("KQ2"), A("I6"), 64.0, ALU.mult, A("KQ"), ALU.add)
+    ts(A("SEL"), A("IOG"), A("KQ"), ALU.is_equal); ts(A("SELQ"), A("IOG"), A("KQ2"), ALU.is_equal)
+    for r in (0, 4) if min(EARLY[0][1], EARLY[1][1]) < 3 else (): cp(A3("UB1", (r, r + 4)), A("ZERO"), "va")
     cp(A("RS32"), A("ZERO", 0, 2 * L), "vag"); ms(A("RS32", 0, None, 32), -1e6); sel(A("RSB"), A("ZERO", 0, L), [[0, 12], [1, 16]], ALU.not_equal, 16384.0)
-    iota(A("SC12"), [[16, 12]], 15)
-    for n, base in (("DRC", NK), ("DRX", M)): cp(A(n), A("ZERO", 0, L), "vag"); ts(A(n, 0, None, 16), A("SC12"), A("K15"), ALU.subtract, float(base), ALU.add)
-    iota(A("C37"), [[-36, 2], [0, 12]], 37)
-    if max(EARLY):
-        for r in range(max(EARLY)): cp(H("UA", r, 512), A("ZERO", 0, 512), "va")
-        ts(A("C1"), A("K15"), 7.5, ALU.is_lt, 56.0, ALU.mult)
-        ts(A("I4"), A("IP"), 4, ALU.arith_shift_right); tt(A("C3"), A("C1"), A("K15"), ALU.subtract); ts(A("C4"), A("I4"), 8.0, ALU.mult, A("C3"), ALU.add)
-        iota(A("SCB"), [[128, 12]], 15); ts(A("CBLK"), A("SCB"), A("C4"), ALU.add)
-    send([(A("RL"), A("LL", 0, 24), 1)], True)
+    iota(A("SC12"), [[16, 24]], 15)
+    for n, base, k in (("DRC", NK, 12), ("DRX", M, 24)): cp(A(n), A("ZERO", 0, 16 * k), "vag"); ts(A(n, 0, None, 16), A("SC12", 0, k), A("K15"), ALU.subtract, float(base), ALU.add)
+    ms(A("TIMES", 0, 72, 3), 0.0); ms(A("TIMES", 2, 36, 3), 37.0); ms(A("TIMES", 38, 72, 3), 1.0)
+    for d in (1, 0):
+        for c0 in range(0, 512 * NUA[d], 768): w = min(768, 512 * NUA[d] - c0); cp(A("UA%d" % d, c0, c0 + w), A("ZERO", 0, w), "va")
+    ts(A("C1"), A("K15"), -8.0, ALU.mult, 120.0, ALU.add); ts(A("I3"), A("IP"), 1, ALU.bitwise_and); ts(A("C3"), A("I3"), -7.0, ALU.mult, A("C1"), ALU.add)
+    ts(A("I4"), A("IP"), 4, ALU.arith_shift_right); ts(A("C4"), A("I4"), 2.0, ALU.mult, A("C3"), ALU.add)
+    iota(A("SCB"), [[128, 12]], 0); ts(A("CBLK"), A("SCB"), A("C4"), ALU.add)
+    if VEARLY and 0 in WIDE:
+        ts(A("C5"), A("K15"), 7.5, ALU.is_lt, 56.0, ALU.mult); ts(A("C6"), A("K15"), -1.0, ALU.mult, A("C5"), ALU.add); ts(A("C7"), A("I4"), 8.0, ALU.mult, A("C6"), ALU.add)
+        ts(A("CBLW"), A("SCB"), A("C7"), ALU.add, 15.0, ALU.add)
+    send([(A("RL"), A("LL", 0, 24), 1)], True); dma("s", [(A("TC", 0, NK), ("tc", full))], sent())
     cp(A("S16", 0, 24), A("LL", 12, 36))
     cp(H("MX", 0), IND(A("XR", 0, 32), H("S16", 0, 12)), "va"); cp(H("ME", 0), IND(A("XR", 32, 64), H("S16", 0, 12)), "va", 0.125)
     send([(H("MX", 1), H("MX", 0), 1), (H("ME", 1), H("ME", 0), 1)])
     ts(A("KA"), A("LL", 12, 36), 37.0, ALU.mult); tt(A("KB"), A("KA"), A("LL", 0, 24), ALU.add); ts(A("KEY"), A("KB"), NK - 1, ALU.bitwise_and)
     cp(A("S16", 24, 48), A("KEY"))
     send([(A("RKEY"), H("S16", 3, 12), 1)])
-    cp(OHT0[1], H("RL", 0, 12))
-    dma("s", [(A("TC", 0, NK), ("tc", full))], H("ME", 0))
-    cp(H("KEY0", 0, 12), H("KEY", 0, 12), "vg"); cp(H("KEY0", 1, 12), OKEY0[1], "vg")
-    ts(H("HT8", 0, 12), A("LL", 24, 36), 8192.0, ALU.add); ts(H("HT8", 1, 12), H("RL", 0, 12), 8192.0, ALU.add)
-    cp(H("Q", 0, 12), A("LL", 12, 24), "vg"); ts(H("Q", 1, 12), H("RL", 1, 12), 37.0, ALU.mult)
+    cp(OHT0[1], H("RL", 0, 12), "vg")
+    dma("s", [nn(0, 0)], H("ME", 0))
+    side = lambda n, d, c: A(n, 36 * d + c, 36 * d + 36, 3)
+    cp(side("PLUS", 0, 1), A("LL", 24, 36), "vg"); cp(side("PLUS", 1, 1), H("RL", 0, 12), "vg")
+    cp(side("PLUS", 0, 2), A("LL", 12, 24), "vg"); ts(side("PLUS", 1, 2), H("RL", 1, 12), 37.0, ALU.mult)
     swap = lambda land, src, w: [(H(land, 1, w), H(src, 0, w), 1), (H(land, 0, w), H(src, 1, w), -1)]
+    pairs_of = lambda n, l: A(n, 8 * l, 8 * l + 16)
 
     def ublock(s, d):
-        l0 = 64 * EARLY[s] if d == s else 0
-        if l0: cp(IND(A("UA"), A("CBLK", 0, l0 // 16)), A("U%d" % s, d * L, d * L + l0))
+        l0 = 64 * EARLY[s][d]
+        if l0: cp(IND(A("UA%d" % d), A("CBLK", 0, l0 // 16)), A("U%d" % s, d * L, d * L + l0))
         if l0 == L: return
         dma("s", [(A3("UB%d" % d, g, (l0, L), grp(g)), A("U%d" % s, d * L + l0, d * L + L, 1, grp(g))) for g in range(8)])
 
@@ -234,80 +286,94 @@ def build(case):
         v = H("V%d" % s, d)
         if s:
             l0 = 64 * d * VEARLY
-            if l0: cp(IND(A("VA"), A("CBLK", 0, l0 // 16)), A("V1", L, L + l0))
+            if l0: cp(IND(A("VA"), A("CBLW" if 0 in WIDE else "CBLK", 0, l0 // 16)), A("V1", L, L + l0))
             dma("s", [(A3("VF%d" % d, g, (l0, L), grp(g)), A("V1", d * L + l0, d * L + L, 1, grp(g))) for g in range(8)])
         else:
-            cp(H("VH", 2 * d), v, "vag"); tt(H("VH", 2 * d + 1), v, H("VH", 2 * d), ALU.subtract)
-            dma("s", [(A3("VB%d" % d, g, None, grp(g)), A("VH", 2 * d * L, (2 * d + 2) * L, 1, grp(g))) for g in range(8)])
+            lower("v%d" % d, H("VH", 2 * d), H("VH", 2 * d + 1), v)
+            dma("s", [(A3(twin("VB", d), g, None, grp(g)), A("VH", 2 * d * L, (2 * d + 2) * L, 1, grp(g))) for g in range(8)])
 
     def lists(s, d):
         cand = IND(A(("HC", "TC")[d], 0, NK), H("OKEY1", d, 12) if s else OKEY0[d])
-        cp(H("OFN", 2 * s + d), ent(s, d), "vg" if s else "v"); cp(H("OFC", 2 * s + d), cand, "v")
+        cp(H("OFN", 2 * s + d), ent(s, d), "vg"); cp(H("OFC", 2 * s + d), cand, "v")
         tt(H("DD", d), cand, ent(s, d), ALU.subtract)
 
     def contest(d):
-        sc, scs, flat = ("PGA", "PGB")[d], "SCS%d" % d, ("S1", "PT")[d]
+        scs, flat, j0 = "SCS%d" % d, "S1", 0
+        bank = lambda j: (("PGA", "PGC", "PGD"), ("PGB", "PGC", "PGD"))[d][sum(x <= j for x in PARTS[d])]
         for l0 in range(0, L, 64):
             x0 = 32 * (d * L + l0)
             for part in (1, 0): cp(A("XG", x0 + part, x0 + 2048, 2), IND(A("X", 0, M), A(("OFC", "OFN")[part], d * L + l0, d * L + l0 + 64)), who(0, x0 // 1024 + part))
             lst = []
             for l in range(l0, l0 + 64):
                 c, j16 = divmod(l, 16); j, q = divmod(c, 4)
-                lst.append((PB(sc, 128 * j + j16, 1, 8, 16, quad(q)), A("XG", 32 * (d * L + l), 32 * (d * L + l) + 32),
-                            A3("UB%d" % d, None, l) if d or l >= 64 * EARLY[0] else A("UA", 64 * (l // 8) + l % 8, 64 * (l // 8) + 64, 8), True, True))
+                lst.append((PB(bank(j), 128 * j + j16, 1, 8, 16, quad(q)), A("XG", 32 * (d * L + l), 32 * (d * L + l) + 32),
+                            A3("UB%d" % d, None, l) if l >= 64 * EARLY[0][d] else A("UA%d" % d, 16 * (l // 2) + l % 2, 16 * (l // 2) + 16, 2), True, True))
             mm(lst)
-        cp(A(scs), PB(sc, 0, 2 * L), "va", 32.0, A("KB%d" % d))
-        mm([(H(flat, j, 128), H(scs, j, 128), A("ID32"), True, True) for j in range(3)])
-        mm([(PB("PZ%d" % d, 0, 2 * L), A("RD"), A(scs), True, True)])
-        scan(A(scs), A("RS32"), A(flat, 0, 2 * L), 0.0, ALU.add, ALU.max)
-        cp(H("MI", d, 12), A(scs, 31, None, 32))
+            j1 = l0 // 64 + 1
+            if j1 not in PARTS[d]: continue
+            a, b = 128 * j0, 128 * j1
+            cp(A(scs, a, b), PB(bank(j0), a, b - a), "va", 32.0, A("KB%d" % d))
+            mm([(PB(flat, 128 * j, 128), H(scs, j, 128), A("ID32"), True, True) for j in range(j0, j1)])
+            mm([(PB("PZ%d" % d, a, b - a), A("RD"), A(scs, a, b), True, True)])
+            scan(A(scs, a, b), A("RS32", 0, b - a), PB(flat, a, b - a), 0.0, ALU.add, ALU.max)
+            step(A3("WN", (8 * j0, 8 * j1)), PB("PZ%d" % d, a, b - a)); j0 = j1
+        cp(H("MI", d, 12), A(scs, 31, None, 32), "vg")
         send(swap("INS", "MI", 12)[d:d + 1])
-        step(A3("WN"), PB("PZ%d" % d, 0, 2 * L))
+        x = sent()
+        for n in (("WB1", "WB0"), ("VB0",))[d] if TWIN else (("VF1", "VF0"), ("WB1",))[d]: fill(n, "ZERO32" if n[1] == "F" else "ZERO", x)
         mm([(PB("S0", L * d + 16 * q, 16, 3, 64, quad(g // 2)), A("SELQ", 48 * q + 16 - 16 * (g % 2), 48 * q + 48 - 16 * (g % 2)), A3("WN", (g, 24, 8)), g % 2 == 0, g % 2 == 1)
             for q in range(4) for g in range(8)])
         tt(PB("S0", L * d, L), PB("S0", L * d, L), H("DD", d), ALU.mult)
         tt(H("AF", d), PB("S0", L * d, L), ent(0, d), ALU.add)
-        cp(H("OA", d), H("AF", d), "vg")
-        ts(H("KK", d, 12), H("MI", d, 12), 15, ALU.bitwise_and); ts(H("OKK", d, 12), H("KK", d, 12), -1.0, ALU.mult, 15.0, ALU.add)
-        tt(H("OAA", d), IND(A("MD"), H("OKK", d, 12)), H("AF", d), ALU.mult); mm([(PB(sc, 0, L), A("BO32"), H("OAA", d), True, True)])
-        mm([(A(flat, 0, L), A("IDB"), A("NMD"), True, False), (A(flat, 0, L), A("BO32"), H("OAA", d), False, True)])
+        cp(H("OA", d), H("AF", d), "avg")
+
+    def best(d):
+        sc, flat = ("PGA", "PGB")[d], "S1"
+        ts(H("KK", d, 12), H("MI", d, 12), 15, ALU.bitwise_and); cp(H("OKK", d, 12), H("KK", d, 12), "vg")
+        tt(H("OAA", d), IND(A("MR"), H("OKK", d, 12)), H("AF", d), ALU.mult); mm([(PB(sc, 0, L), A("BO32"), H("OAA", d), True, True)])
+        mm([(PB(flat, 0, L), A("IDB"), A("NMD"), True, False), (PB(flat, 0, L), A("BO32"), H("OAA", d), False, True)])
         cp(H("BR16", d), PB(sc, 0, L), "va")
-        scan(H("BSC", d), A("RSB"), A(flat, 0, L), 0.0, ALU.add, ALU.min)
+        scan(H("BSC", d), A("RSB"), PB(flat, 0, L), 0.0, ALU.add, ALU.min)
 
-    def duel(c):
-        d, ch = divmod((min(c, 5) + 3) % 6, 3); t0, nt = (0, 8) if c < 5 or not APART else ((0, 8 - NL), (8 - NL, NL))[c - 5]
-        l0 = 64 * ch + 8 * t0; w = 8 * nt; xc = 32 * d * L + 16 * l0; xn = xc + 16 * L; o0 = d * L + l0; b = c % 2; th = c in TH
-        cp(A("XG", xn, xn + 16 * w), IND(A("X", 0, M), A("OFN", 2 * L + o0, 2 * L + o0 + w)), who(1, o0 // 32 + 1))
-        cp(A("XG", xc, xc + 16 * w), IND(A("X", 0, M), A("OFC", 2 * L + o0, 2 * L + o0 + w)), who(1, o0 // 32), -1.0)
-        if c in PAIRS:
-            for n, x0 in enumerate((xn, xc)):
-                lst = [] if n else [mask("S0", 128, "HALFP")]
-                for j in range(4):
-                    for t in range(8):
-                        l = 16 * j + 2 * t
-                        lst.append((PB("S0", 2 * t, 2, 8, 16, quad(j)), A("XG", x0 + 16 * l, x0 + 16 * l + 32), A3("UB%d" % d, None, (64 * ch + l, 64 * ch + l + 2)), False, n == 1 and t == 7))
+    def duel(k):
+        d, l0, w = DUELS[k]; o0 = d * L + l0; b = k % 2; n = w // 4; m = min(w, 64); f0 = 0 if k in BROAD else 256
+        for l1 in range(l0, l0 + w, m):
+            xc = 32 * d * L + 16 * l1; xn = xc + 16 * L; o1 = 2 * L + d * L + l1; j0 = (l1 - l0) // n; c = (d * 3 + l1 // 64 + 3) % 6
+            cand = IND(A("X", 0, M), A("OFC", o1, o1 + m))
+            cp(A("XG", xn, xn + 16 * m), IND(A("X", 0, M), A("OFN", o1, o1 + m)), who(1, (d * L + l1) // 32 + 1), -1.0)
+            if c in DIFF: tt(A("XG", xc, xc + 16 * m), cand, A("XG", xn, xn + 16 * m), ALU.add)
+            else: cp(A("XG", xc, xc + 16 * m), cand, who(1, (d * L + l1) // 32))
+            for x0 in (xc,) if c in DIFF else (xn, xc):
+                opens = x0 == xn or c in DIFF
+                if k in BROAD:
+                    mm([mask("S1", 8 * w, "OWN")] * opens + [(PB("S1", 64 * t, 64), A("XG", x0 + 128 * t, x0 + 128 * t + 128), A3("UB%d" % d, None, (l0 + 8 * t, l0 + 8 * t + 8)),
+                                                              False, x0 == xc and t == w // 8 - 1) for t in range(w // 8)])
+                    continue
+                lst = [mask(DB[k], 2 * w, "HALF", (32 * j0, 32 * (j0 + m // n)))] * opens
+                for l in range(l1, l1 + m, 2):
+                    j, t = divmod(l - l0, n)
+                    lst.append((PB(DB[k], 8 * t, 16, p=quad(j)), A("XG", x0 + 16 * (l - l1), x0 + 16 * (l - l1) + 32),
+                                A3("UB%d" % d, None, (l, l + 2)) if l >= 64 * EARLY[1][d] else pairs_of("UA%d" % d, l), False, x0 == xc and t == n - 2))
                 mm(lst)
-            step(A("AM", 0, 128), PB("S0", 0, 128))
-            mm([(A("S1", 16 * j, 16 * j + 16, 1, quad(q)), A("SEL", 112 - 16 * h, 144 - 16 * h, 1, quad(j)), A("AM", 32 * q + 16 * h, 32 * q + 16 * h + 16, 1, quad(j)), h == 0, h == 1)
-                for j in range(4) for q in range(4) for h in (0, 1)])
+        if k in BROAD:
+            step(A3("AW", (0, w)), PB("S1", 0, 8 * w))
+            mm([(PB("S1", 0, w), A("SELW", 112 - 16 * g, 240 - 16 * g), A3("AW", (g, w, 8)), g == 0, g == 7) for g in range(8)])
         else:
-            for n, x0 in enumerate((xn, xc)):
-                mm(([] if n or th else [mask("S0", 8 * w, "OWN")]) +
-                   [(PB("S0", 8 * t, 8, 8, w), A("XG", x0 + 128 * t, x0 + 128 * t + 128),
-                     A3("UB%d" % d, None, (l0 + 8 * t, l0 + 8 * t + 8)) if not d or ch >= EARLY[1] else H("UA", 8 * ch + t, 64), th and n == t == 0, n == 1 and t == nt - 1) for t in range(nt)])
-            if th: tt(A("AM", 0, 8 * w), PB("S0", 0, 8 * w), A("THR", 0, 8 * w), ALU.is_le)
-            else: step(A("AM", 0, 8 * w), PB("S0", 0, 8 * w))
-            mm([(A("S1", 0, w), A("SEL", 112 - 16 * g, 240 - 16 * g), H("AM", g, w), g == 0, g == 7) for g in range(8)])
-        tt(A("S1", 64, 64 + w), A("S1", 0, w), A("DD", o0, o0 + w), ALU.mult)
-        tt(A("A64", 64 * b, 64 * b + w), A("S1", 64, 64 + w), A("NN", 2 * L + o0, 2 * L + o0 + w), ALU.add)
-        cp(A("OA", o0, o0 + w), A("A64", 64 * b, 64 * b + w), "vg")
+            step(A3("AM", (0, n // 2)), PB(DB[k], 0, 2 * w))
+            mm([(PB(DB[k], 256 + n * j, n, p=quad(q)), A("SEL", 48 * j + 16 - 16 * h, 48 * j + 48 - 16 * h), A3("AM", (0, n // 2), (4 * q + 2 * h, 4 * q + 2 * h + 2)), h == 0, h == 1)
+                for j in range(4) for q in range(4) for h in (0, 1)])
+        tt(PB(DB[k], f0, w), PB(DB[k], f0, w), A("DD", o0, o0 + w), ALU.mult)
+        tt(A("A64", 128 * b, 128 * b + w), PB(DB[k], f0, w), A("NN", 2 * L + o0, 2 * L + o0 + w), ALU.add)
+        for l1 in range(0, w, m): cp(A("OA", o0 + l1, o0 + l1 + m), A("A64", 128 * b + l1, 128 * b + l1 + m), "gva")
 
-    sums = lambda c: "PG" + "ABC"[c % 3]
+    sums = lambda c: GB[c % len(GB)]
     gy = lambda c: "GY%d" % (c // 4)
 
     def readout(c):
-        for j in range(4): cp(A3(gy(c), None, (2 * j, 2 * j + 2), quad(c % 4)), PB(sums(c), 128 * j, 128, p=quad(j)), RO)
-        join(4)
+        for j in range(4):
+            cp(A3(gy(c), None, (2 * j, 2 * j + 2), quad(c % 4)), PB(sums(c), 128 * j, 128, p=quad(j)), RO)
+            if c < 4 and j == 3: join(4)
+            if c >= 4 and j % 2: join(2)
 
     def store(c):
         y, c0 = divmod(64 * c, L)
@@ -319,170 +385,176 @@ def build(case):
         pz = "PZ%d" % d; at = lambda l: (l % 8 // 2, l // 8)
         for ch in range(3):
             c = 3 * d + ch; e0 = 1024 * (c % NEA)
-            cp(A("EA", e0, e0 + 1024), IND(A("E"), A("OA", 64 * c, 64 * c + 64)), "va")
-            tr(H("ET", c, 1024), A("EA", e0, e0 + 1024))
+            for l in range(0, 64, 64 // CUT[c]): cp(A("EA", e0 + 16 * l, e0 + 16 * l + 1024 // CUT[c]), IND(A("E"), A("OA", 64 * c + l, 64 * c + l + 64 // CUT[c])), "va")
             lst = [] if ch else [mask(pz, 2 * L, "HALF")]
             for l in range(64 * ch, 64 * ch + 64, 2):
                 j, t = at(l); e = e0 + 16 * (l % 64)
                 for part in (0, 1):
-                    lst.append((PB(pz, 4 * t, 4, 4, 96, quad(j)), A("EA", e, e + 32), A3("VB%d" % d, None, (part * L + l, part * L + l + 2)), False, t == 23 and part == 1))
-            mm(lst)
-        z = PB(pz, 0, 2 * L); hi, lo = A3("WC", (8 * d, 8 * d + 8, 2)), A3("WC", (8 * d + 1, 8 * d + 8, 2))
-        act(z, z, ACT.Sigmoid, 0.5); cp(hi, z, "va"); tt(lo, z, hi, ALU.subtract)
-        dma("s", [(A3("WB%d" % d, (4 * j + q, 32, 16), None, quad(q)), A3("WC", (8 * d + 2 * q, 8 * d + 2 * q + 2), None, quad(j))) for j in range(4) for q in range(4)])
+                    lst.append((PB(pz, 4 * t, 4, 4, 96, quad(j)), A("EA", e, e + 32), A3(twin("VB", d), None, (part * L + l, part * L + l + 2)), False, t == 23 and part == 1))
+            for k in range(ZCUT): mm(lst[k * len(lst) // ZCUT:(k + 1) * len(lst) // ZCUT])
+        z = PB(pz, 0, 2 * L); hi, lo = A3("WC", (8 * d, 8 * d + 4)), A3("WC", (8 * d + 4, 8 * d + 8)); w = A("SCS%d" % d) if "w%d" % d in LOW else z
+        act(w, z, ACT.Sigmoid, 0.5); lower("w%d" % d, hi, lo, w)
+        dma("s", [(A3(twin("WB", d), (4 * j + q, 32, 16), None, quad(q)), A3("WC", (8 * d + q, 8 * d + 8, 4), None, quad(j))) for j in range(4) for q in range(4)])
 
     def sums0(c):
         d, ch = divmod((c + 3) % 6, 3)
-        mm([(PB(sums(c), 2 * t, 2, 32, 16), H("ET", 24 * d + 8 * ch + t, 128), A3("WB%d" % d, (16 * part, 16 * part + 16), (32 * ch + 4 * t, 32 * ch + 4 * t + 4)), t == part == 0, False)
+        tr(H("ET", 3 * d + ch, 1024), H("EA", 3 * d + ch, 1024))
+        mm([(PB(sums(c), 2 * t, 2, 32, 16), H("ET", 24 * d + 8 * ch + t, 128), A3(twin("WB", d), (16 * part, 16 * part + 16), (32 * ch + 4 * t, 32 * ch + 4 * t + 4)), t == part == 0, False)
             for t in range(8) for part in (0, 1)])
 
     def reals1(c):
         d, ch = divmod((c + 3) % 6, 3); n = 8 - (NL if c == 5 else 0); wide = c in WIDE; pz = "PZ%d" % ZB[c]; o0 = d * L + 64 * ch
         e0, u0, r = 1024 * (c % NEF), 1024 * (c % NET), c % NW; vf = "VF%d" % d
-        lane = (lambda j, t: 8 * t + 2 * j) if wide else (lambda j, t: 2 * n * j + 2 * t)
         cp(A("EF", e0, e0 + 128 * n), IND(A("E32", 0, M), A("OA", o0, o0 + 8 * n)), "va")
         tr(A("EU", u0, u0 + 128 * n), A("EF", e0, e0 + 128 * n))
+        ws = lambda j, q0, q1: A("WS", 128 * r + 32 * q0, 128 * r + 32 * q1, 1, quad(j))
         if wide:
             lst = [mask(pz, 512, "HALF")]
+            if c in APART: mm(lst); lst = []
             lst += [(PB(pz, 8 * t, 8, 8, 64), A("EF", e0 + 128 * t, e0 + 128 * t + 128),
                      H("VA", 8 * c + t, 64) if c < VEARLY else A3(vf, None, (64 * ch + 8 * t, 64 * ch + 8 * t + 8)), False, t == n - 1) for t in range(n)]
             mm(lst)
             zq = lambda j, q0, q1: A3(pz, (16 * q0, 16 * q1), (2 * j, 2 * j + 2), quad(j))
             if c not in DIRECT:
-                for j in range(4): act(A("WS", 128 * r, 128 * r + 128, 1, quad(j)), zq(j, 0, 4), ACT.Sigmoid, 0.5)
+                for j in range(4): act(ws(j, 0, 4), zq(j, 0, 4), ACT.Sigmoid, 0.5)
                 join(4)
         else:
             lst = [mask(pz, 128, "HALF")]
             for j in range(4):
                 for t in range(n):
-                    l = lane(j, t)
-                    lst.append((PB(pz, 2 * t, 2, 8, 16, quad(j)), A("EF", e0 + 16 * l, e0 + 16 * l + 32), A3(vf, None, (64 * ch + l, 64 * ch + l + 2)), False, t == n - 1))
+                    l = 8 * t + 2 * j
+                    lst.append((PB(pz, 2 * t, 2, 8, 16, quad(j)), A("EF", e0 + 16 * l, e0 + 16 * l + 32),
+                                pairs_of("VA", 64 * ch + l) if c < VEARLY else A3(vf, None, (64 * ch + l, 64 * ch + l + 2)), False, t == n - 1))
             mm(lst)
             zq = lambda j, q0, q1: PB(pz, 32 * q0, 32 * (q1 - q0), p=quad(j))
             if c not in DIRECT: act(H("WS", r, 128), PB(pz, 0, 128), ACT.Sigmoid, 0.5)
         wf = lambda j, q: A3("WF", (32 * r + 8 * j + 2 * q, 32 * r + 8 * j + 2 * q + 2), None, quad(q))
         if c in DIRECT:
-            for j in range(4):
-                for q in range(4): act(wf(j, q), zq(j, q, q + 1), ACT.Sigmoid, 0.5)
+            for j in (3, 2, 1, 0):
+                if (c, j) in SHARE: act(ws(j, 0, 4), zq(j, 0, 4), ACT.Sigmoid, 0.5)
+                for q in range(4):
+                    if (c, j) in SHARE: cp(wf(j, q), ws(j, q, q + 1), "va")
+                    else: act(wf(j, q), zq(j, q, q + 1), ACT.Sigmoid, 0.5)
                 join(4)
-        else: dma("s", [(wf(j, q), A("WS", 128 * r + 32 * q, 128 * r + 32 * q + 32, 1, quad(j))) for j in range(4) for q in range(4)])
+        else: dma("s", [(wf(j, q), ws(j, q, q + 1)) for j in range(4) for q in range(4)])
         mm([(PB(sums(c), 2 * t, 2, 32, 16), A("EU", u0 + 128 * t, u0 + 128 * t + 128), A3("WF", (32 * r, 32 * r + 32), (2 * t, 2 * t + 2)), False, t == n - 1) for t in range(n)])
-        ops[-1]["mile"] = MILES[3]
         readout(c)
 
     def piece(k):
-        n, t0 = LAST[k], sum(LAST[:k]); l0 = L - 8 * (NL - t0); e0, u0, w0 = 1024 * NEF + 128 * t0, 1024 * NET + 128 * t0, 64 * t0; pz = "PZ%d" % (k % 2)
+        n, t0 = LAST[k], sum(LAST[:k]); l0 = L - 8 * (NL - t0); e0, u0, w0 = 1024 * NEF + 128 * t0, 1024 * NET + 128 * t0, 64 * t0; pz = "PZ%d" % ((ZB[5] + 1 + k) % 2)
         cp(A("EF", e0, e0 + 128 * n), IND(A("E32", 0, M), A("OA", l0, l0 + 8 * n)), "va")
         tile = lambda t: A("EF", e0 + 128 * t, e0 + 128 * t + 128)
-        mm([mask(pz, 64 * n, "OWNN")] +
+        mm([mask(pz, 64 * n, "OWN")] +
            [(PB(pz, 64 * t, 64), tile(t), A3("VF0", None, (l0 + 8 * t, l0 + 8 * t + 8)), False, t == n - 1) for t in range(n)])
-        mm([(H("PT", t, 128), tile(t), A("ID32"), True, True) for t in range(n)])
+        mm([(PB("S1", 128 * t, 128), tile(t), A("ID32"), True, True) for t in range(n)])
         act(A("WL", w0, w0 + 64 * n), PB(pz, 0, 64 * n), ACT.Sigmoid, 0.5)
-        cp(A("EU", u0, u0 + 128 * n), A("PT", 0, 128 * n), "va")
-        mm([(PB(sums(k), 64 * t + 16 * q, 16, p=quad(1)), A("EU", u0 + 128 * t + 32 * q, u0 + 128 * t + 32 * q + 32), A("WL", w0 + 64 * t + 16 * q, w0 + 64 * t + 16 * q + 16), t == q == 0, t == n - 1 and q == 3)
+        cp(A("EU", u0, u0 + 128 * n), PB("S1", 0, 128 * n), "va")
+        mm([(PB(sums(k + 6), 64 * t + 16 * q, 16, p=quad(1)), A("EU", u0 + 128 * t + 32 * q, u0 + 128 * t + 32 * q + 32), A("WL", w0 + 64 * t + 16 * q, w0 + 64 * t + 16 * q + 16), t == q == 0, t == n - 1 and q == 3)
             for t in range(n) for q in range(4)])
         for t in range(n):
-            y = A3(gy(5), (8 - NL + t0 + t, 64, 8), None, quad(1)); tt(y, PB(sums(k), 64 * t, 64, p=quad(1)), y, ALU.add)
+            y = A3(gy(5), (8 - NL + t0 + t, 64, 8), None, quad(1)); tt(y, PB(sums(k + 6), 64 * t, 64, p=quad(1)), y, ALU.add)
         join(n)
 
-    def first(rep, col, d, bank, spare, num, out):
-        if num: lst = [(H(bank, d), A("IDB"), A("NMD2"), True, False)]
-        else: mm([(H(bank, d), A("IDB"), A("NMD2"), True, False), (H(bank, d), A("BO32"), H("OAA", d), False, False)]); lst = []
-        r0 = 12 * d % NEQ
-        for c in range(12):
-            n = L - 16 * c
-            ts(A3("EQ", r0 + c, (0, n)), A(rep, d * L + 16 * c, d * L + L), A(col, 12 * d + c, 12 * d + c + 1), ALU.is_equal, 8192.0, ALU.mult)
-            if c in (4, 8, 11): join((5, 4, 3)[c // 4 - 1 + (c == 11)])
-            if c < 11: lst.append((A(bank, d * L + 16 * c + 16, d * L + L), A("BO"), A3("EQ", r0 + c, (16, n)), False, False))
-        lst.append((H(bank, d), A("TRI"), A3("EQ", (r0, r0 + 12), (0, 16)), False, True))
-        mm(lst[:-7]); mm(lst[-7:-3]); mm(lst[-3:])
-        scan(H("FS", d), A(spare), H(bank, d), 0.0, ALU.max, ALU.min)
-        fs = A("FS", d * L + 15, d * L + L, 16)
-        if num: tt(H("F1", d, 12), fs, num, ALU.max); cp(out, H("F1", d, 12), "vg")
-        else: cp(out, fs, "vg")
-
-    pair = swap("U0", "UO0", L)
-    for d in (0, 1):
-        tt(H("UO0", d), IND(A("X", 0, M), OHT0[d]), H("MX", d), ALU.mult); send(pair[d:d + 1])
-    dma("s", [(A("HC", 0, NK), ("hc", full))], H("UO0", 0)); dma("s", [(A("E"), ("ee", full))], H("UO0", 1)); dma("s", [nn(1, 0), nn(1, 1)], H("UO0", 1))
-    for d in (0, 1): tt(H("VO0", d), IND(A("E"), OHT0[d]), H("ME", d), ALU.mult)
-    send(swap("V0", "VO0", L))
-    iota(A("ZERO32"), [[0, 384]])
-    fill = lambda n, z, after: dma("s", [(A3(n, (r, r + A(z)["cnt"] // SCRATCH[n][1][2])), A(z)) for r in range(0, SCRATCH[n][1][1], A(z)["cnt"] // SCRATCH[n][1][2])], after)
-    fill("UB0", "ZERO", H("UO0", 1))
-    for d in (0, 1): lists(0, d); ublock(0, d)
-    dma("g", [(A("E32", 0, M), ("ee", full))], A("V0"))
-    for n in ("VB1", "VB0"): fill(n, "ZERO", H("U0", 0))
-    for n in ("WB1", "WB0"): fill(n, "ZERO", A("V0"))
-    sel(A("COL"), A("ZERO", 0, 512), [[0, 64], [1, 8]], ALU.not_equal, 1.0, 0, -1)
-    for n, v in (("OWN", 16384.0), ("OWNN", -1024.0)): sel(A(n), A("ZERO", 0, 128), [[1, 8], [0, 16]], ALU.is_equal, v, 0, -1)
-    iota(A("IH"), [[0, 4], [1, 2], [0, 16]], 0, 1); ts(A("IH"), A("IH"), 1, ALU.bitwise_and)
-    for n, v in (("HALF", -1024.0), ("HALFP", 16384.0))[:1 + bool(PAIRS)]: ts(A(n), A("IH"), v, ALU.mult)
-    if TH:
-        mm([mask("S0", 512, "OWN")[:4] + (True,)]); cp(A("THR"), PB("S0", 0, 512), "va", -1.0)
-    iota(A("COUNT"), [[1, NK]]); cp(A("KF"), A("KEY"), "vg")
+    def first(rep, col, live, sides, spare, num, out):
+        lo, hi = min(sides), max(sides) + 1
+        mm([(PB("S1", d * L, L), A("IDB"), A("NMD2"), d == sides[0], False) for d in sides] + [(PB("S1", lo * L, (hi - lo) * L), A("BO32"), A("OAA", lo * L, hi * L), False, False)] * (not num))
+        for d in sides:
+            r0 = 12 * d % NEQ; lst = []
+            for c in range(12):
+                n = L - 16 * c
+                ts(A3("EQ", r0 + c, (0, n)), A(rep, d * L + 16 * c, d * L + L), col(12 * d + c), ALU.is_equal, live(12 * d + c), ALU.mult)
+                if c in (4, 8, 11): join((5, 4, 3)[c // 4 - 1 + (c == 11)])
+                if c < 11: lst.append((PB("S1", d * L + 16 * c + 16, n - 16), A("BO"), A3("EQ", r0 + c, (16, n)), False, False))
+            lst.append((PB("S1", d * L, L), A("TRI"), A3("EQ", (r0, r0 + 12), (0, 16)), False, d == sides[-1]))
+            mm(lst[:5]); mm(lst[5:9]); mm(lst[9:])
+        scan(A("FS", lo * L, hi * L), A(spare), PB("S1", lo * L, (hi - lo) * L), 0.0, ALU.max, ALU.min)
+        fs = A("FS", lo * L + 15, hi * L, 16)
+        if num: tt(H("F1", lo, 12), fs, num, ALU.max); cp(out, H("F1", lo, 12), "gva")
+        else: cp(out, fs, "vga")
 
     def keys(d):
-        cp(H("KR16", d), IND(A("COUNT"), H("S16", 2 + d, 12)))
-        first("KR16", "KF", d, "S1", "DRC", H("KF", d, 12), H("OSC", d, 12))
+        cp(H("KR16", d), IND(A("COUNT"), H("S16", 2 + d, 12)), "va")
+        first("KR16", lambda c: A("KF", c, c + 1), lambda c: 1.0, (d,), "DRC", H("KF", d, 12), H("OSC", d, 12))
 
     def cache(d):
         cp(IND(A(("HC", "TC")[d]), OSC[d]), H("AF", d)); lists(1, d)
 
+    pair = swap("U0", "UO0", L)
+    half = lambda k: dma("g", [(A("E32", k * M // 2, (k + 1) * M // 2), ("ee", (slice(0, 128), slice(k * M // 2, (k + 1) * M // 2))))], sent())
+    for d in (0, 1):
+        tt(H("UO0", d), IND(A("X", 0, M), OHT0[d]), H("MX", d), ALU.mult); send(pair[d:d + 1])
+        if d: half(0)
+        else: x = sent(); dma("s", [(A("HC", 0, NK), ("hc", full))], x); dma("s", [(A("E"), ("ee", full))], x)
+    for d in (0, 1):
+        tt(H("VO0", d), IND(A("E"), OHT0[d]), H("ME", d), ALU.mult); send(swap("V0", "VO0", L)[d:d + 1])
+        if d: half(1)
+        else: x = sent(); fill("VB1", "ZERO", x); dma("s", [nn(1, 0), nn(1, 1)], x)
+    iota(A("ZERO32"), [[0, 384]])
+    for d in (0, 1): lists(0, d); ublock(0, d)
+    sel(A("COL"), A("ZERO", 0, 512), [[0, 64], [1, 8]], ALU.not_equal, 1.0, 0, -1)
+    sel(A("OWN"), A("ZERO", 0, 128), [[1, 8], [0, 16]], ALU.is_equal, -16384.0, 0, -1)
+    iota(A("IH"), [[0, 4], [1, 2], [0, 16]], 0, 1); ts(A("IH"), A("IH"), 1, ALU.bitwise_and); ts(A("HALF"), A("IH"), -16384.0, ALU.mult)
+    iota(A("COUNT"), [[1, NK]]); cp(A("KF"), A("KEY"), "vg")
     keys(1)
-    if KH < 0: keys(0)
+    if not KLATE: keys(0)
     send([(A("ROSC"), H("OSC", 1, 12), 1)])
-    for d in (1, 0):
-        contest(d); ops[-1]["mile"] = MILES[2]; vblock(0, d)
-    for n in ("VF0", "VF1", "WF"): fill(n, "ZERO32", H("INS", 0, 12))
-    if VEARLY: dma("s", [(H("VA", r, 256), A("ZERO32", 0, 256)) for r in range(2 * VEARLY)], H("INS", 0, 12))
-    reals0(1)
+    for d in (1, 0): contest(d)
+    for d in (1, 0): best(d)
+    if VEARLY: dma("s", [(H("VA", r, 256), A("ZERO32", 0, 256)) for r in range(2 * VEARLY)], H("AF", 0))
+    vblock(0, 1); reals0(1); vblock(0, 0)
     BL = A("BSC", 15, None, 16)
-    cp(A("OB"), BL)
-    tt(A("Z1"), BL, A("C37"), ALU.mult); tt(A("Z2"), A("Z1"), A("Q"), ALU.add); ts(A("EXK"), A("Z2"), NK - 1, ALU.bitwise_and)
-    send(swap("INK", "EXK", 12))
+    for d0, d1 in ((1, 2), (0, 1)) if SPLIT else ((0, 2),): cp(A("OB", 12 * d0, 12 * d1), A("BSC", d0 * L + 15, d1 * L, 16), "vag")
+    tt(A("PLUS", 0, 72, 3), BL, A("PLUS", 1, 72, 3), ALU.subtract)
+    for d in (0, 1): tt(side("TIMES", d, 1), H("MI", d, 12), H("INS", d, 12), ALU.is_gt)
+    scan(A("NEW"), A("TIMES"), A("PLUS"), 0.0, ALU.mult, ALU.add)
+    cp(A("Z2"), A("NEW", 2, 72, 3), "vg"); ts(A("EXK"), A("Z2"), NK - 1, ALU.bitwise_and); cp(A("EXU"), A("EXK"), "vg")
+    send(swap("OKEY1", "EXU", 12)); x = sent(); fill("UB0", "ZERO", x)
+    if TWIN: fill("VF1", "ZERO32", x)
+    else: fill("WF", "ZERO32", x, 0, 72)
+    cp(A("OHT1"), A("NEW", 1, 72, 3), "gva")
     S384 = PB("S0", 0, 2 * L)
-    act(A("SU"), A("U0"), ACT.Sign)
-    tt(A("NX0"), IND(A("X", 0, M), A("OB")), A("SU"), ALU.subtract); ts(A("NX"), A("NX0"), -7.0, ALU.max, 7.0, ALU.min)
-    tt(A("PV"), IND(A("E"), A("OB")), A("V0"), ALU.mult); mm([(S384, A("BO32"), A("PV"), True, True)])
+    sign(A("SU"), A("U0"))
+    for d0, d1 in ((1, 2), (0, 1)) if SPLIT else ((0, 2),):
+        x = lambda n, w=L: A(n, d0 * w, d1 * w)
+        tt(x("NX0"), IND(A("X", 0, M), x("OB", 12)), x("SU"), ALU.subtract); tt(x("PV"), IND(A("E"), x("OB", 12)), x("V0"), ALU.mult)
+    ts(A("NX"), A("NX0"), -7.0, ALU.max, 7.0, ALU.min)
+    mm([(S384, A("BO32"), A("PV"), True, True)])
     act(S384, S384, ACT.Sigmoid, 0.5); tt(A("WV"), S384, A("V0"), ALU.mult)
     cp(A("EB"), IND(A("E"), A("OB")), "va", 0.875)
-    for d in (0, 1): tt(H("LV", d, 12), H("MI", d, 12), H("INS", d, 12), ALU.is_gt)
-    tt(A("G4"), A("KEY0"), A("INK"), ALU.subtract); tt(A("G4"), A("G4"), A("LV"), ALU.mult); tt(A("G4"), A("G4"), A("INK"), ALU.add); cp(A("OKEY1"), A("G4"), "vg")
     cache(1)
-    if KH < 0: cache(0)
-    for d in (0, 1):
-        bl = A("BSC", d * L + 15, d * L + L, 16)
-        ts(H("BS0", d, 12), H("LV", d, 12), -8192.0, ALU.mult, 8192.0, ALU.add); tt(H("BS", d, 12), H("BS0", d, 12), bl, ALU.add)
-        first("BR16", "BS", d, ("S1", "PT")[d], "DRX", None, H("OSX", d, 12))
-        cp(IND(A("X"), H("OSX", d, 12)), H("NX", d))
-    ops[-1]["mile"] = MILES[0]
-    tt(A("G1"), A("HT8"), A("BS0"), ALU.subtract); tt(A("G1"), A("G1"), A("BS"), ALU.min); cp(A("OHT1"), A("G1"))
-    reals0(0)
+    first("BR16", lambda c: A("BSC", 16 * c + 15, 16 * c + 16), lambda c: A("TIMES", 3 * c + 1, 3 * c + 2), (0, 1), "DRX", None, A("OSX"))
+    for d in (0, 1): cp(IND(A("X"), H("OSX", d, 12)), H("NX", d))
     for c in range(3): sums0(c)
+    reals0(0)
+    for c in range(3, len(GB)): sums0(c)
     for d in (0, 1): tt(IND(A("E32"), H("OSX", d, 12)), H("EB", d), H("WV", d), ALU.add)
-    tt(A("UO1"), IND(A("X", 0, M), A("OHT1")), A("MX"), ALU.mult); send(swap("U1", "UO1", L))
-    tt(A("VO1"), IND(A("E32", 0, M), A("OHT1")), A("ME"), ALU.mult); send(swap("V1", "VO1", L))
+    if SPLIT > 1:
+        for d in (0, 1): tt(H("UO1", d), IND(A("X", 0, M), H("OHT1", d, 12)), H("MX", d), ALU.mult); send(swap("U1", "UO1", L)[d:d + 1])
+    else: tt(A("UO1"), IND(A("X", 0, M), A("OHT1")), A("MX"), ALU.mult); send(swap("U1", "UO1", L))
+    if TWIN: fill("VF0", "ZERO32", sent())
+    if SPLIT > 2:
+        for d in (0, 1): tt(H("VO1", d), IND(A("E32", 0, M), H("OHT1", d, 12)), H("ME", d), ALU.mult); send(swap("V1", "VO1", L)[d:d + 1])
+    else: tt(A("VO1"), IND(A("E32", 0, M), A("OHT1")), A("ME"), ALU.mult); send(swap("V1", "VO1", L))
+    fill("WF", "ZERO32", sent(), 0 if TWIN else 72)
+    if KLATE: keys(0)
+    cache(0)
     for d in (1, 0):
         ublock(1, d); vblock(1, d)
-    for c in range(LAG):
-        duel(c)
-        if c == KH: keys(0); cache(0)
-    for c in range(6):
-        if c + LAG < 6 + APART and c < AHEAD: duel(c + LAG)
+    for x in ORDER.split():
+        c = int(x[1])
+        if x[0] == "D": duel(c); continue
         reals1(c)
-        if c + LAG < 6 + APART and c >= AHEAD: duel(c + LAG)
-        if c < 3: sums0(c + 3)
+        if c + len(GB) < 6: sums0(c + len(GB))
         if c < 5: store(c)
     for k in range(len(LAST)): piece(k)
     store(5)
-    long = [i for i, o in enumerate(ops) if o["kind"] == "cp" and o["wr"][0]["n"] in ("EA", "XG", "EF")][12:]
-    for a, b in zip(long, long[2:]): ops[b]["soft"] = [a]
-    nth = lambda n, k: [i for i, o in enumerate(ops) if o["wr"] and o["wr"][0]["n"] == n][k]
-    for a, j, b, k in SOFT: ops[nth(b, k)].setdefault("soft", []).append(nth(a, j))
+    long = [i for i, o in enumerate(ops) if o["kind"] in ("cp", "tt") and o["name"] in ("EA", "XG", "EF")][12:]
+    for a, b in zip(long, long[AHEAD:]): ops[b]["soft"] = [a]
+    nth = lambda n, k: [i for i, o in enumerate(ops) if o["name"] == n][k]
+    for a, j, b, k in AFTER: ops[nth(a, j)].setdefault("soft", []).append(nth(b, k))
     seen = {}
     for o in ops:
-        n = o["wr"][0]["n"] if o["wr"] else "y"; k = seen[n] = seen.get(n, -1) + 1; x = DUE.get(n, [])
+        n = o["name"]; k = seen[n] = seen.get(n, -1) + 1; x = DUE.get(n, [])
         o["due"] = 1000.0 * (x[k] if k < len(x) and x[k] else END)
     return ops
 
@@ -495,236 +567,196 @@ def hazards(ops):
         for a, w in acc:
             ps = psum(a)
             for j, lo, hi, w2, p, st in hist.get(a["n"], []):
-                apart = st == a.get("st", 1) and (lo - a["lo"]) % st
-                if ps or ((w or w2) and lo < a["hi"] and a["lo"] < hi and p[0] < a["p"][1] and a["p"][0] < p[1] and not apart):
+                apart = st[1] < a["st"][0] or a["st"][1] < st[0] if isinstance(st, tuple) else st == a["st"] and (lo - a["lo"]) % st
+                if p[0] < a["p"][1] and a["p"][0] < p[1] and (ps or (w or w2) and lo < a["hi"] and a["lo"] < hi and not apart):
                     deps[j] = deps.get(j, False) or w or w2
         for a, w in acc:
             h = hist.setdefault(a["n"], [])
-            if psum(a): h[:] = [x for x in h if x[0] == i or (x[3] and not w)]
+            if psum(a): h[:] = [x for x in h if x[0] == i or (x[3] and not w) or x[4][0] < a["p"][0] or a["p"][1] < x[4][1]]
             elif w and a["cnt"] == a["hi"] - a["lo"] and "off" not in a:
                 h[:] = [x for x in h if x[0] == i or not (a["lo"] <= x[1] and x[2] <= a["hi"] and a["p"][0] <= x[4][0] and x[4][1] <= a["p"][1])]
-            x = (i, a["lo"], a["hi"], w, a["p"], a.get("st", 1))
+            x = (i, a["lo"], a["hi"], w, a["p"], a["st"])
             if x not in h: h.append(x)
         deps.pop(i, None)
         o["deps"] = deps
 
 
-def schedule(ops, succ, bias, lean, WAKE, ahead=0.3):
-    n = len(ops)
-    pr = [0.0] * n
-    for i in range(n - 1, -1, -1):
-        o = ops[i]; pr[i] = o["cost"][o["eng"][0]] + max([o["hold"] + o["lat"] + WAKE + pr[k] for k in succ[i]] + [0.0]) + bias[i]
-    free = dict.fromkeys("vatgsd", 0.0); ready = [0.0] * n; left = [len(o["deps"]) for o in ops]; eng = [None] * n; seq = []
-    pool = [i for i in range(n) if not left[i]]
-    while pool:
-        t, q = min((max(free[q], ready[i]), q) for i in pool for q in ops[i]["eng"] if q == ops[i]["eng"][0] or free[ops[i]["eng"][0]] > max(free[q], ready[i]) + lean[i])
-        mine = [i for i in pool if q == ops[i]["eng"][0] or q in ops[i]["eng"] and free[ops[i]["eng"][0]] > max(free[q], ready[i]) + lean[i]]
-        rank = lambda i: (q == ops[i]["eng"][0], pr[i])
-        i = max((i for i in mine if ready[i] <= t), key=rank)
-        soon = [j for j in mine if t < ready[j] <= t + (1.0 if q == "g" else ahead) * ops[i]["cost"][q] and rank(j) > rank(i)]
-        if soon: i = min(soon, key=lambda j: ready[j]); t = ready[i]
-        pool.remove(i); seq.append(i); eng[i] = q; t = free[q] = t + ops[i]["cost"][q]
-        if ops[i]["hold"]: t = free["d"] = max(t, free["d"]) + ops[i]["hold"]
-        for k in succ[i]:
-            ready[k] = max(ready[k], t + (0.0 if q == "t" == ops[k]["eng"] else ops[i]["lat"] + WAKE)); left[k] -= 1
-            if not left[k]: pool.append(k)
-    return seq, eng
-
-
 PLAN = {}
-PASSES, WARM, SIDE = 1, 300.0, 0.5
-ROUNDS, MOVES, STARTS, HEAT, SHOW, MIX, NOISE = 1000, 170000, 1, 250.0, 0, (0.4, 0.5, 0.1), 2000.0
+MOVES, SEED, PULL, LATE, FADE, LOAD, SHOW = 450000, 9, 0.3, 0.04, 1.05, 0.15, 0
+QUEUES, STRIDE, SIDE = "vatgs", 24, dict(v=1.0, a=0.8)
+HINGE = ("U1", "V1", "OKEY1")
+STAGES = ((0.4, 1.0, 0.3, 0, 140.0), (0.85, 1.0, 0.0, 1, 140.0), (1.0, 1.0, 0.0, 0, 30.0), (1.25, 1.0, 0.0, 0, 40.0))
+FAR, BYKEY, DROP = 0.25, 0, 2.5
+MAIN = dict(EF=3.0, U1=5.0, V1=5.0, VA=8.0, WS=8.0, WB0=5.0, WB1=5.0)
 
 
 def plan():
-    if not PLAN:
-        all_ops = [build(c) for c in CASES]; ops = all_ops[0]; hazards(ops); n = len(ops)
-        hard = [o["deps"] for o in ops]
-        for o in ops: o["deps"] = dict({j: True for j in o.get("soft", [])}, **o["deps"]) if False else {**{j: True for j in o.get("soft", [])}, **o["deps"]}
-        deps = [list(o["deps"]) for o in ops]; succ = [[] for _ in ops]
-        for i in range(n):
-            for j in deps[i]: succ[j].append(i)
-        rng = np.random.default_rng(SEED); flex = [i for i in range(n) if len(ops[i]["cost"]) > 1]
-        tabs = [([o["cost"] for o in oo], [o["lat"] for o in oo], c[5]) for oo, c in zip(all_ops, CASES)]
-        figs = [{q: [x[0][i][q] for x in tabs] + [x[1][i] + x[2] for x in tabs] for q in ops[i]["cost"]} for i in range(n)]
-        held = {i: [oo[i]["hold"] for oo in all_ops] for i in range(n) if ops[i]["hold"]}
-        above = []
-        for i in range(n):
-            x = 0
-            for j in deps[i]: x |= above[j] | 1 << j
-            above.append(x)
-        direct = lambda i, j: not any(above[k] >> j & 1 for k in deps[i])
-        inline = lambda i, j: ops[i]["eng"] == ops[j]["eng"] and (ops[i]["eng"] == "t" or len(ops[i]["eng"]) == 1 and not ops[i]["deps"][j])
-        dp = [[j for j in deps[i] if direct(i, j) and not inline(i, j)] for i in range(n)]
+    if "seq" in PLAN: return PLAN
+    three = [build(c) for c in CASES]; ops = three[0]; hazards(ops); n = len(ops)
+    deps = [{**dict.fromkeys(o.get("soft", []), o["kind"] != "mark"), **o["deps"]} for o in ops]; above = []
+    for i in range(n):
+        x = 0
+        for j in deps[i]: x |= above[j] | 1 << j
+        above.append(x)
+    pre = [[j for j in deps[i] if not any(above[k] >> j & 1 for k in deps[i])] for i in range(n)]; suc = [[] for _ in ops]
+    for i in range(n):
+        for j in pre[i]: suc[j].append(i)
+    inline = lambda i, j: ops[i]["eng"] == ops[j]["eng"] and (ops[i]["eng"] == "t" or len(ops[i]["eng"]) == 1 and not deps[i][j])
+    waits = [[j for j in pre[i] if not inline(i, j)] for i in range(n)]
+    way = [o["lat"] + o["hold"] for o in ops]; eng = [o["eng"][0] for o in ops]; own = [o["cost"][o["eng"][0]] for o in ops]
 
-        miles = [(i, o["mile"]) for i, o in enumerate(ops) if o.get("mile")]
-        fast = [{q: tuple(f) + (dp[i], held.get(i)) for q, f in figs[i].items()} for i in range(n)]; last = [i for i in range(n) if not ops[i]["wr"]]
-        kept = {}; load = {i: {q: sum(f[:3]) * (1.0 if q == "v" else SIDE if q == "a" else 0.0) for q, f in figs[i].items()} for i in flex}
+    def gap(line, t, c):
+        p = len(line)
+        while p and line[p - 1][1] > t: p -= 1
+        while p < len(line) and line[p][0] < t + c: t = line[p][1]; p += 1
+        return t, p
 
-        def ends(seq, eng, p0=0):
-            p0 -= p0 % 32
-            if p0: marks = kept["marks"][:p0 // 32]; free = dict(kept["marks"][p0 // 32]); d0, d1, d2 = [x[:] for x in kept["done"]]
-            else: marks = []; free = dict.fromkeys("vatgsd", (0.0, 0.0, 0.0)); d0, d1, d2 = [0.0] * n, [0.0] * n, [0.0] * n
-            kept["new"] = (marks, (d0, d1, d2))
-            for p in range(p0, n, 32):
-                marks.append(dict(free))
-                for i in seq[p:p + 32]:
-                    q = eng[i]; t0, t1, t2 = free[q]; c0, c1, c2, l0, l1, l2, before, h = fast[i][q]
-                    for j in before:
-                        x = d0[j]
-                        if x > t0: t0 = x
-                        x = d1[j]
-                        if x > t1: t1 = x
-                        x = d2[j]
-                        if x > t2: t2 = x
-                    t0 += c0; t1 += c1; t2 += c2; free[q] = (t0, t1, t2)
-                    if h:
-                        e = free["d"]; t0 = max(t0, e[0]) + h[0]; t1 = max(t1, e[1]) + h[1]; t2 = max(t2, e[2]) + h[2]; free["d"] = (t0, t1, t2)
-                    d0[i] = t0 + l0; d1[i] = t1 + l1; d2[i] = t2 + l2
-            return [max(d0[i] for i in last), max(d1[i] for i in last), max(d2[i] for i in last)]
+    key = [0.0] * n
+    for i in range(n - 1, -1, -1): key[i] = min([key[k] - (way[i] if i in waits[k] else 0.0) for k in suc[i]] + [ops[i]["due"], 1000.0 * END - way[i]]) - own[i]
+    for i in range(n): key[i] = max([key[i]] + [key[j] + 1e-3 for j in pre[i]])
+    busy = {q: [] for q in QUEUES + "d"}; at = [0.0] * n
+    for i in sorted(range(n), key=lambda i: key[i]):
+        c, h = own[i], ops[i]["hold"]; t, p = gap(busy[eng[i]], max([0.0] + [at[j] + own[j] + (way[j] if j in waits[i] else 0.0) for j in pre[i]]), c)
+        while h:
+            t2, p2 = gap(busy["d"], t + c, h)
+            if t2 <= t + c + 1e-6: busy["d"].insert(p2, (t + c, t + c + h)); break
+            t, p = gap(busy[eng[i]], t2 - c, c)
+        at[i] = t; busy[eng[i]].insert(p, (t, t + c))
+    seq = sorted(range(n), key=lambda i: ((key if BYKEY else at)[i], i)); PLAN["first"] = (list(at), list(key))
 
-        def score(seq, eng, p0=0):
-            x = ends(seq, eng, p0)
-            return sum(w * (e + PULL * sum(d) / n + sum(m * d[i] for i, m in miles)) for w, e, d in zip(WEIGHTS, x, kept["new"][1])) + LOAD * sum(load[i][eng[i]] for i in flex)
+    figures = lambda three: [{q: (QUEUES.index(q),) + tuple(x[i]["cost"][q] for x in three) + tuple(x[i]["lat"] for x in three) + (waits[i], ops[i]["hold"] and tuple(x[i]["hold"] for x in three))
+                              for q in ops[i]["cost"]} for i in range(n)]
+    figs = figures(three)
+    last = [i for i in range(n) if not ops[i]["wr"]]; flex = [i for i in range(n) if len(figs[i]) > 1]
+    miles = [(i, ops[i]["due"] + way[i], MAIN.get(ops[i]["name"], 1.0)) for i in range(n) if ops[i]["due"] < 1000.0 * END]
+    aims = [x for x in miles for _ in range(int(x[2]))]
+    hinge = [i for i in range(n) if ops[i]["name"] in HINGE]; stage = list(STAGES[0])
+    load = [{q: c * SIDE.get(q, 0.0) for q, c in o["cost"].items()} for o in ops]; W0, W1, W2 = WEIGHTS
 
-        mean = lambda x: sum(w * y for w, y in zip(MIX, x))
-        cost = [{q: mean(f[:3]) for q, f in figs[i].items()} for i in range(n)]
-        way = [mean(list(figs[i].values())[0][3:]) + mean(held.get(i, (0.0, 0.0, 0.0))) for i in range(n)]
-        fwd = [[(j, 0.0 if inline(i, j) else way[j]) for j in deps[i] if direct(i, j)] for i in range(n)]
-        bwd = [[] for _ in range(n)]
-        for i in range(n):
-            for j, w in fwd[i]: bwd[j].append((i, w))
+    def times(seq, fig, p0, marks, done, past=10 ** 6, cut=0.0):
+        p0 -= p0 % STRIDE
+        if p0: m = marks[:p0 // STRIDE]; f0, f1, f2 = map(list, marks[p0 // STRIDE]); d0, d1, d2 = done[0][:], done[1][:], done[2][:]
+        else: m = []; f0, f1, f2 = [0.0] * 6, [0.0] * 6, [0.0] * 6; d0, d1, d2 = [0.0] * n, [0.0] * n, [0.0] * n
+        for p in range(p0, n, STRIDE):
+            if p > past:
+                a, b, c = marks[p // STRIDE]
+                if W0 * (sum(f0[:3]) - sum(a[:3])) + W1 * (sum(f1[:3]) - sum(b[:3])) + W2 * (sum(f2[:3]) - sum(c[:3])) > cut: return None, None
+            m.append((tuple(f0), tuple(f1), tuple(f2)))
+            for i in seq[p:p + STRIDE]:
+                q, c0, c1, c2, l0, l1, l2, before, h = fig[i]; t0 = f0[q]; t1 = f1[q]; t2 = f2[q]
+                for j in before:
+                    if d0[j] > t0: t0 = d0[j]
+                    if d1[j] > t1: t1 = d1[j]
+                    if d2[j] > t2: t2 = d2[j]
+                t0 += c0; t1 += c1; t2 += c2; f0[q] = t0; f1[q] = t1; f2[q] = t2
+                if h: t0 = f0[5] = max(t0, f0[5]) + h[0]; t1 = f1[5] = max(t1, f1[5]) + h[1]; t2 = f2[5] = max(t2, f2[5]) + h[2]
+                d0[i] = t0 + l0; d1[i] = t1 + l1; d2[i] = t2 + l2
+        return m, (d0, d1, d2)
 
-        keeps = [mean(held.get(i, (0.0, 0.0, 0.0))) for i in range(n)]
+    def worth(done, late):
+        d0, d1, d2 = done; e = W0 * max([d0[i] for i in last]) + W1 * max([d1[i] for i in last]) + W2 * max([d2[i] for i in last])
+        v = stage[1] * e + PULL * sum(d0) / n + stage[2] * sum([W0 * d0[i] + W1 * d1[i] + W2 * d2[i] for i in hinge]) / len(hinge)
+        if late:
+            for i, m, w in miles:
+                if d0[i] > m: v += late * w * (d0[i] - m)
+        return v, e
 
-        def gap(line, t, c):
-            p = len(line)
-            while p and line[p - 1][1] > t: p -= 1
-            while p < len(line) and line[p][0] < t + c: t = line[p][1]; p += 1
-            return t, p
-
-        def fill_gaps(key, before, after, eng, tail, lean):
-            busy = {q: [] for q in "vatgsd"}; end = [0.0] * n; at = [0.0] * n
-            for i in sorted(range(n), key=lambda i: key[i]):
-                t = tail[i]
-                for j, w in before[i]:
-                    if end[j] + w > t: t = end[j] + w
-                q = eng[i]; c = cost[i][q]; t, p = gap(busy[q], t, c)
-                if keeps[i]:
-                    off = c if tail is zero else -keeps[i]
-                    while True:
-                        t2, p2 = gap(busy["d"], t + off, keeps[i])
-                        if t2 - off <= t + 1e-6: break
-                        t, p = gap(busy[q], t2 - off, c)
-                    busy["d"].insert(p2, (t + off, t + off + keeps[i]))
-                at[i] = t; end[i] = t + c; busy[q].insert(p, (t, t + c))
-            return at, end, eng
-
-        zero = [0.0] * n; best = None; lean = dict.fromkeys("vatgs", 0.0)
-        big = [i for i in flex if max(cost[i].values()) > 250]
-        pin = [o["eng"][0] for o in ops]; tail = [max(way[i], 1000.0 * END - ops[i]["due"]) for i in range(n)]; now = None
-        for r in range(ROUNDS):
-            p2, t2 = list(pin), list(tail)
-            for _ in range(int(rng.integers(1, 4)) if r else 0):
-                x = rng.random()
-                if x < 0.5:
-                    i = (big if x < 0.4 else flex)[int(rng.integers(0, len(big if x < 0.4 else flex)))]
-                    other = [q for q in cost[i] if q != p2[i]]; q = other[int(rng.integers(0, len(other)))]
-                    mates = [j for j in big if p2[j] == q and p2[i] in cost[j] and abs(j - i) < 60]
-                    if x < 0.2 and mates: p2[mates[int(rng.integers(0, len(mates)))]] = p2[i]
-                    p2[i] = q
-                else:
-                    i = int(rng.integers(0, n)); t2[i] = max(way[i], now[3][i] + NOISE * (2.0 * rng.random() - 0.6))
-            key = [0.0] * n
-            for i in range(n - 1, -1, -1): key[i] = min([key[k] - w for k, w in bwd[i]] + [-t2[i]]) - cost[i][p2[i]]
-            top = None
-            for k in range(PASSES):
-                at, end, eng = fill_gaps(key, fwd, bwd, p2, zero, lean)
-                seq = sorted(range(n), key=lambda i: (at[i], i)); v = score(seq, eng)
-                if top is None or v < top[0]: top = (v, seq, eng, [max(end) - x for x in end])
-                if k + 1 < PASSES:
-                    at, end, _e = fill_gaps([-x for x in end], bwd, fwd, eng, t2, lean)
-                    key = [-x for x in end]
-            if now is None or top[0] <= now[0] + WARM * (1.0 - r / ROUNDS): now, pin, tail = top, p2, t2
-            if best is None or top[0] < best[0]: best = top[:3]
-
-        def chain(seq, eng, case, to=None):
-            cost, lat, wake = tabs[case]; free = {q: (0.0, -1) for q in "vatgsd"}; done = [0.0] * n; why = [None] * n
-            for i in seq:
-                t, k = free[eng[i]]; queue = True
-                for j in dp[i]:
-                    if done[j] > t: t, k, queue = done[j], j, False
-                t += cost[i][eng[i]]; free[eng[i]] = (t, i)
-                if i in held:
-                    if free["d"][0] > t: (t, k), queue = free["d"], True
-                    t += held[i][case]; free["d"] = (t, i)
-                why[i] = (k, queue); done[i] = t + lat[i] + wake
-            i = done.index(max(done)) if to is None else to; out = []
-            while i >= 0:
-                k, queue = why[i]
-                if queue and k >= 0: out.append((i, k))
-                i = k
-            return out or chain(seq, eng, case)
-
-        runs = []; each = MOVES // (STARTS + 2); draws = rng.random((MOVES, 5)).tolist()
-        for it, (r0, r1, r2, r3, r4) in enumerate(draws):
-            if it % each == 0 and it <= STARTS * each:
-                if it: runs.append((top, keep))
-                cur, (seq, eng) = (best[0], best[1:]) if it < STARTS * each else min(runs)
-                top = cur; keep = (list(seq), list(eng)); arcs = None; score(seq, eng); kept["marks"], kept["done"] = kept["new"]
-            heat = HEAT * (1.0 - it % each / each) if it < STARTS * each else 0.6 * HEAT * (MOVES - it) / (MOVES - STARTS * each)
-            if it % 500 == 0:
-                d0 = kept["done"][0]; at = [d0[i] - figs[i][eng[i]][0] - figs[i][eng[i]][3] - held.get(i, (0.0,))[0] for i in range(n)]; prev = {}
-                for i in seq:
-                    at[i] = max([at[i], prev.get(eng[i], 0.0)] + [at[j] for j in deps[i]]) + 1e-6; prev[eng[i]] = at[i]
-                s2 = sorted(seq, key=lambda i: at[i]); v = score(s2, eng)
-                if v <= cur + HEAT: cur, seq = v, s2; kept["marks"], kept["done"] = kept["new"]
-            if arcs is None: arcs = chain(seq, eng, int(r4 * len(tabs)), miles[int(r2 * len(miles))][0] if miles and r3 < 0.5 else None)
-            s2, e2 = seq, eng
-            i, k = arcs[int(r1 * len(arcs))]
-            if r0 < 0.25:
-                i = (i, k)[r2 < 0.5] if r0 < 0.15 else flex[int(r1 * len(flex))]
-                other = [q for q in ops[i]["cost"] if q != eng[i]]
-                if not other: continue
-                e2 = list(eng); e2[i] = other[int(r4 * len(other))]; lo = seq.index(i)
-                if r0 > 0.2:
-                    j = flex[min(len(flex) - 1, max(0, flex.index(i) + int(r2 * 13) - 6))]
-                    if j != i and eng[j] == e2[i] and eng[i] in ops[j]["cost"]: e2[j] = eng[i]; lo = min(lo, seq.index(j))
-            elif r0 < 0.45:
-                s2 = list(seq); p = int(r1 * n); i = s2.pop(p); lo, hi = p, p
-                while lo > 0 and p - lo < 60 and s2[lo - 1] not in ops[i]["deps"]: lo -= 1
-                while hi < n - 1 and hi - p < 60 and i not in ops[s2[hi]]["deps"]: hi += 1
-                s2.insert(lo + int(r2 * (hi - lo + 1)), i)
-            else:
-                hi = seq.index(i); lo = seq.index(k)
-                if hi < lo: continue
-                if r0 < 0.75:
-                    lo = max(0, lo - int(r2 * r2 * 30)); need = set(deps[i]); up, rest = [i], []
-                    for j in reversed(seq[lo:hi]):
-                        if j in need: up.append(j); need.update(deps[j])
-                        else: rest.append(j)
-                    if k in up: continue
-                    s2 = seq[:lo] + up[::-1] + rest[::-1] + seq[hi + 1:]
-                else:
-                    hi = min(n - 1, hi + int(r2 * r2 * 30)); need = set(succ[k]); down, rest = [k], []
-                    for j in seq[lo + 1:hi + 1]:
-                        if j in need: down.append(j); need.update(succ[j])
-                        else: rest.append(j)
-                    if i in down: continue
-                    s2 = seq[:lo] + rest + down + seq[hi + 1:]
-            v = score(s2, e2, lo)
-            if v <= cur - heat * math.log(r3 + 1e-12):
-                cur, seq, eng = v, s2, e2; arcs = None if r4 < 0.3 else arcs; kept["marks"], kept["done"] = kept["new"]
-                if v < top: top, keep = v, (list(s2), list(e2))
-            elif r4 < 0.05: arcs = None
-        seq, eng = keep
-        free = {q: 0.0 for q in "vatgsd"}; done = [0.0] * n; start = [0.0] * n; cost, lat, wake = tabs[SHOW]
+    def chain(seq, fig, case, to):
+        free = [(0.0, -1)] * 6; d = [0.0] * n; why = [None] * n
         for i in seq:
-            start[i] = max([free[eng[i]]] + [done[j] for j in dp[i]]); t = free[eng[i]] = start[i] + cost[i][eng[i]]
-            if i in held: t = free["d"] = max(t, free["d"]) + held[i][SHOW]
-            done[i] = t + lat[i] + wake
-        for o, h in zip(ops, hard): o["deps"] = h
-        PLAN.update(ops=ops, seq=seq, start=start, eng=eng, end=ends(seq, eng))
+            x = fig[i]; t, k = free[x[0]]; queue = True
+            for j in x[7]:
+                if d[j] > t: t, k, queue = d[j], j, False
+            t += x[1 + case]; free[x[0]] = (t, i)
+            if x[8]:
+                if free[5][0] > t: (t, k), queue = free[5], True
+                t += x[8][case]; free[5] = (t, i)
+            why[i] = (k, queue); d[i] = t + x[4 + case]
+        i = d.index(max(d)) if to is None else to; out = []
+        while i >= 0:
+            k, queue = why[i]
+            if queue and k >= 0: out.append((i, k))
+            i = k
+        return out or chain(seq, fig, case, None)
+
+    def in_time(seq, fig, done, case):
+        at = [0.0] * n; free = [0.0] * 5; prev = [0.0] * 5
+        for i in seq:
+            x = fig[i]; t = max([free[x[0]]] + [done[j] for j in x[7]]); free[x[0]] = t + x[1 + case]
+            at[i] = prev[x[0]] = max([free[x[0]] if x[8] else t, prev[x[0]]] + [at[j] for j in pre[i]]) + 1e-6
+        return sorted(seq, key=lambda i: at[i])
+
+    fig = [figs[i][eng[i]] for i in range(n)]; busy = sum(load[i][eng[i]] for i in range(n)); best = arcs = more = None
+    ends = lambda done: sum(w * max([d[i] for i in last]) for w, d in zip(WLATER, done))
+    marks, done = times(seq, fig, 0, None, None); pres, sucs = [set(x) for x in pre], [set(x) for x in suc]
+    for it, (r0, r1, r2, r3, r4) in enumerate(np.random.default_rng(SEED).random((int(MOVES * STAGES[-1][0]), 5)).tolist()):
+        if it % 250 == 0:
+            if it >= MOVES and any(it == int(MOVES * s[0]) // 250 * 250 for s in STAGES):
+                e, seq, eng = best
+                if it == MOVES: more = figures([build(c) for c in LATER]); W0, W1, W2 = WSECOND; best = None
+                fig = [figs[i][eng[i]] for i in range(n)]; busy = sum(load[i][eng[i]] for i in range(n)); marks, done = times(seq, fig, 0, None, None)
+            x = it / MOVES; k = [s[0] > x for s in STAGES].index(True); stage[:] = STAGES[k]; x0 = STAGES[k - 1][0] if k else 0.0
+            late = LATE * max(0.0, 1.0 - FADE * x); heat = stage[4] * (stage[0] - x) / (stage[0] - x0) + 5.0
+            fixed = max(seq.index(i) for i in hinge) + 1 if stage[3] else 0
+            seq = seq[:fixed] + in_time(seq, fig, done[0], 0)[fixed:] if fixed and set(seq[:fixed]) == set(in_time(seq, fig, done[0], 0)[:fixed]) else in_time(seq, fig, done[0], 0); marks, done = times(seq, fig, 0, None, None); cur, e = worth(done, late); cur += LOAD * busy; arcs = None
+            if more: fig2 = [more[i][eng[i]] for i in range(n)]; marks2, done2 = times(seq, fig2, 0, None, None); end2 = ends(done2); e += end2
+            if best is None or e < best[0]: best = (e, seq, eng)
+        if arcs is None:
+            to = aims[int(r2 * len(aims))]
+            if more and r3 < 0.5: arcs = chain(seq, fig2, int(r4 * 3), None)
+            elif r3 < 0.3 and late and done[0][to[0]] > to[1]: arcs = chain(seq, fig, 0, to[0])
+            else: arcs = chain(seq, fig, int(r4 * 3), hinge[int(r2 * len(hinge))] if r1 * (stage[1] + stage[2]) < stage[2] else None)
+        s2, f2, b2, e2 = seq, fig, busy, eng
+        i, k = arcs[int(r1 * len(arcs))]
+        if r0 < 0.25:
+            i = (i, k)[r2 < 0.5] if r0 < 0.15 else flex[int(r1 * len(flex))]
+            other = [q for q in figs[i] if q != eng[i]]
+            if not other: continue
+            q = other[int(r4 * len(other))]; f2 = list(fig); e2 = list(eng); f2[i] = figs[i][q]; e2[i] = q; lo = seq.index(i); hi = lo + 20; b2 += load[i][q] - load[i][eng[i]]
+            if 0.08 < r0 < 0.15 or r0 > 0.2:
+                p = min(n - 1, max(0, lo + int(r2 * 41) - 20)); j = seq[p]
+                if j != i and eng[j] == q and eng[i] in figs[j]: f2[j] = figs[j][eng[i]]; e2[j] = eng[i]; lo = min(lo, p); b2 += load[j][eng[i]] - load[j][q]
+        elif r0 < 0.45:
+            s2 = list(seq); p = int(r1 * n); i = s2.pop(p); lo, hi = p, p
+            while lo > 0 and p - lo < 60 and s2[lo - 1] not in pres[i]: lo -= 1
+            while hi < n - 1 and hi - p < 60 and s2[hi] not in sucs[i]: hi += 1
+            x = lo + int(r2 * (hi - lo + 1)); s2.insert(x, i); lo, hi = min(x, p), max(x, p)
+        else:
+            if r4 > 1.0 - FAR:
+                hi = lo = int(r1 * n); w = int(8 + 80 * r2 * r2)
+                if r0 < 0.75: i = seq[hi]; k = -1; lo = max(0, lo - w)
+                else: k = seq[lo]; i = -1; hi = min(n - 1, hi + w)
+            else: hi = seq.index(i); lo = seq.index(k)
+            if hi < lo: continue
+            if r0 < 0.75:
+                lo = max(0, lo - int(r2 * r2 * 30) * (k >= 0)); need = set(pre[i]); up, rest = [i], []
+                for j in reversed(seq[lo:hi]):
+                    if j in need: up.append(j); need.update(pre[j])
+                    else: rest.append(j)
+                if k in up: continue
+                s2 = seq[:lo] + up[::-1] + rest[::-1] + seq[hi + 1:]
+            else:
+                hi = min(n - 1, hi + int(r2 * r2 * 30) * (i >= 0)); need = set(suc[k]); down, rest = [k], []
+                for j in seq[lo + 1:hi + 1]:
+                    if j in need: down.append(j); need.update(suc[j])
+                    else: rest.append(j)
+                if i in down: continue
+                s2 = seq[:lo] + rest + down + seq[hi + 1:]
+        if lo < fixed: continue
+        m2, d2 = times(s2, f2, lo, marks, done, hi + STRIDE, DROP * (100.0 - heat * math.log(r3 + 1e-12)))
+        if m2 is None: continue
+        v, e = worth(d2, late); v += LOAD * b2
+        if more and v <= cur - heat * math.log(r3 + 1e-12) + 300.0:
+            g2 = fig2 if e2 is eng else [more[j][e2[j]] for j in range(n)]; m3, d3 = times(s2, g2, lo, marks2, done2); e3 = ends(d3); v += e3 - end2
+        if v <= cur - heat * math.log(r3 + 1e-12):
+            if more: v -= e3 - end2; fig2, marks2, done2, end2 = g2, m3, d3, e3
+            cur, seq, fig, marks, done, busy, eng = v, s2, f2, m2, d2, b2, e2
+            if r4 < 0.3: arcs = None
+        elif r4 < 0.05: arcs = None
+    e, seq, eng = best; fig = [figs[i][eng[i]] for i in range(n)]; done = times(seq, fig, 0, None, None)[1]
+    free = [0.0] * 5; start = [0.0] * n
+    for i in seq: start[i] = max([free[fig[i][0]]] + [done[SHOW][j] for j in waits[i]]); free[fig[i][0]] = start[i] + fig[i][1 + SHOW]
+    PLAN.update(waits=waits, ops=ops, seq=seq, start=start, eng=eng, end=[max(d[i] for i in last) for d in done])
     return PLAN
 
 
@@ -743,8 +775,8 @@ def rank_program(g, core, T, topo):
         x = T[a["n"]][a["ix"]]
         return x.indirect(ap(a["off"])) if "off" in a else x
 
-    def share(src, dst, k, n):
-        e = topo.engines(src, dst); m = len(e) // n
+    def share(src, dst, k, n, few):
+        e = topo.engines(src, dst)[::2 if few else 1]; m = len(e) // n
         return e[k * m:(k + 1) * m]
 
     seq = P["seq"]; issue = caller(ap)
@@ -759,7 +791,7 @@ def rank_program(g, core, T, topo):
     for i in seq:
         o, q = ops[i], eng[i]; e = Q[q]; k, x = o["kind"], o["args"]
         for j in sorted(o["deps"], key=lambda j: -start[j]):
-            if eng[j] == q and ops[j]["kind"] not in ("dma", "send") and (q == "t" or not o["deps"][j]): continue
+            if eng[j] == q and ops[j]["kind"] not in ("dma", "dadd", "send") and (q == "t" or not o["deps"][j]): continue
             if ops[j]["kind"] == "send":
                 for land, sem, val in token[j]:
                     if any(a["n"] == land["n"] and a["lo"] < land["hi"] and land["lo"] < a["hi"] for a in o["rd"]): wait(q, sem, val, None)
@@ -770,14 +802,17 @@ def rank_program(g, core, T, topo):
             trs, token[i] = [], []
             for n, (land, src, way) in enumerate(x):
                 sem = "r%d" % nd[1]; nd[1] += 1
-                mine = share(core, peer[way], n, len(x)); rid, pid = topo.addr(peer[way])[:2]
+                few = False; mine = share(core, peer[way], n, len(x), few); rid, pid = topo.addr(peer[way])[:2]
                 trs.append(RemoteDMATransfer(dst_ids=[DstId(rid=rid, pnc=pid)], dma_engine_mask=sum(1 << b for b in mine), remote_sem=T.sem[sem], src=ap(src), dst=ap(land)))
-                nd[2] += len(mine); val = len(share(back[way], core, n, len(x))); token[i].append((land, sem, val)); total[sem] = val
+                nd[2] += len(mine); val = len(share(back[way], core, n, len(x), few)); token[i].append((land, sem, val)); total[sem] = val
             g.remote_dma_fused(trs, local_sem=T.sem.loc)
             continue
-        if k == "dma":
+        if k == "mark":
+            g.sem_inc(T.sem.mark, 1); total["mark"] = total.get("mark", 0) + 1; token[i] = ("mark", total["mark"]); snap[i] = {}
+            continue
+        if k in ("dma", "dadd"):
             sem = "d%d" % nd[0]; nd[0] += 1
-            for out, src in x: e.dma_start(ap(out), ap(src)).then_inc(T.sem[sem], 16)
+            for out, src in x: (e.dma_start(ap(out), ap(src)) if k == "dma" else e.dma_start(ap(out), ap(src), accum_op=ALU.add)).then_inc(T.sem[sem], 16)
             token[i] = (sem, 16 * len(x)); total[sem] = 16 * len(x)
             continue
         for y in (x if k == "many" else [o]):
@@ -811,8 +846,11 @@ def caller(ap):
         elif k == "ms": r = e.memset(ap(x[0]), x[1])
         elif k == "act": r = e.activation(ap(x[0]), ap(x[1]), x[2], scale=x[3])
         elif k == "step":
-            if q == "a": r = e.activation(ap(x[0]), ap(x[1]), ACT.Sigmoid, bias=64.0, scale=-128.0)
-            else: r = e.tensor_scalar(ap(x[0]), ap(x[1]), 0.0, None, ALU.is_le)
+            if q == "a": r = e.activation(ap(x[0]), ap(x[1]), ACT.Sigmoid, bias=64.0, scale=128.0)
+            else: r = e.tensor_scalar(ap(x[0]), ap(x[1]), 0.0, None, ALU.is_ge)
+        elif k == "sign":
+            if q == "a": r = e.activation(ap(x[0]), ap(x[1]), ACT.Sign)
+            else: r = e.tensor_scalar(ap(x[0]), ap(x[1]), -1.0, 1.0, ALU.max, ALU.min)
         elif k == "sel": r = e.affine_select(ap(x[0]), ap(x[1]), x[2], x[3], x[4], x[5], x[6])
         elif k == "iota":
             if SCRATCH[x[0]["n"]][2] == I: r = e.iota(ap(x[0]), x[1], x[2], x[3])

import math
import numpy as np
from concourse.bass import DstId, RemoteDMATransfer
from concourse.mybir import AluOpType as ALU, ActivationFunctionType as ACT

M, NK, L, D, NR = 4096, 1024, 192, 3, 8
B, F, I, U = "bfloat16", "float32", "int32", "uint16"
DUELS = ((1, 0, 64), (1, 64, 128), (0, 0, 128), (0, 128, 64))
DB = ("S1", "S1", "S1", "S1")
BROAD = (3,)
DIFF = (2, 3, 4, 5)
ORDER = "D0 D1 R0 D2 R1 D3 R2 R3 R4 R5"
WIDE = (0, 1, 2, 3, 4, 5)
DIRECT = (4, 5)
SHARE = ()
LOW = ("v0", "w0")
GB = ("PGC", "PGD", "PGB", "PGA", "S0")
EARLY = ((3, 2), (0, 1))
VEARLY = 1
LAST = ()
ALL = ("V0", "V1")
APART = (0, 1, 2, 3, 4, 5)
KLATE, ZCUT, TWIN, SPLIT = 1, 2, 1, 3
PARTS = ((2, 3), (3,))
CUT, AHEAD = (1, 1, 1, 1, 1, 1), 4
NEQ, RO, ZB = 24, "va", (1, 0, 1, 0, 1, 0)
NEF, NET, NEA, NW = 3, 4, 6, 3
ONV = ((9, 8, 0, 4), ())
NL = sum(LAST)
SCRATCH, PLACE = {}, {}


def _buf(names, cols, dtype, where="sbuf"):
    for n in names.split():
        if cols in (1, 12, 24):
            home = "SMALL_" + dtype
            at = SCRATCH[home][1][1] if home in SCRATCH else 0
            PLACE[n] = (home, at, cols); SCRATCH[home] = (where, [128, at + (32 if cols == 24 else 16)], dtype)
        else:
            SCRATCH[n] = (where, [128] + (list(cols) if isinstance(cols, tuple) else [cols]), dtype)


_buf("X", M + 2 * L, B); _buf("E", M, B); _buf("E32", M + 2 * L, F); _buf("HC TC", NK + L, I); _buf("NN", 4 * L, I)
_buf("XR", 64, B); _buf("LL", 36, I); _buf("S16", 48, U); _buf("RL", 24, I); _buf("OT RKEY", 12, U); _buf("MX ME", 2 * L, B)
_buf("IP IN I1 I2 I3 I4 I5 I6", 1, I); _buf("K15 KB0 KB1 KQ KQ2 C1 C3 C4 C5 C6 C7", 1, F)
_buf("ID32 BO32", 128, F); _buf("IDB BO TRI ONE HALF OWN", 128, B); _buf("COL", 512, B); _buf("IH", 128, I)
_buf("ZERO", 768, B); _buf("RD", 128, F); _buf("RS32", 2 * L, B)
PLACE.update(DRX=("EF", 0, 2 * L), COUNT=("EF", 1024, NK), ZERO32=("EF", 2048, 2 * L), DRC=("EF", 2048 + 2 * L, L))
_buf("SELW", 240, B); _buf("MR IOR", 16, B)
_buf("RSB NMD NMD2 IOC SELQ SEL IOG", L, B); _buf("AM", (16, 16), B); _buf("A64", 256, F)
if BROAD: _buf("AW", (64, 8), B)
_buf("SCB", 12, I); _buf("SC12", 24, I); _buf("CBLK CBLW ROSC", 12, U)
_buf("OKK OHT1 OKEY1 OB OSX OSC EXU", 24, U)
_buf("KA KB KEY MI INS EXK KK Z2", 24, I)
_buf("F1 KF", 24, F); _buf("TIMES PLUS NEW", 72, F)
_buf("UO0 UO1 U0 U1 SU NX0 NX", 2 * L, B)
_buf("VO0 VO1 V0 V1 DD AF", 2 * L, F)
for _k, _n in enumerate("OAA FS PV BSC WV EB SCS1 - SCS0".split()): PLACE[_n] = ("EU", 2 * L * _k, 2 * L)
_buf("VH", 4 * L, B); _buf("BR16 KR16 OA", 2 * L, U); _buf("OFN OFC", 4 * L, U)
NUA = [max(EARLY[0][_d], EARLY[1][_d]) for _d in (0, 1)]
for _d in (0, 1):
    if NUA[_d]: _buf("UA%d" % _d, 512 * NUA[_d], B)
if VEARLY: _buf("VA", 512 * VEARLY, F)
_buf("UB0 UB1" if min(EARLY[0][1], EARLY[1][1]) < 3 else "UB0", (8, L), B); _buf("VB0 VB1" if TWIN else "VB1", (8, 2 * L), B); _buf("VF0 VF1", (8, L), F)
_buf("WC", (16, 96), B); _buf("WB0 WB1" if TWIN else "WB1", (32, 96), B); _buf("WS", 128 * NW, F); _buf("WF", (32 * NW, 16), F); _buf("WL", 64 * max(NL, 1), F)
_buf("XG", 64 * L, B); _buf("EA", 1024 * NEA, B); _buf("ET", 32 * L, B); _buf("EF", 1024 * NEF + 128 * NL, F); _buf("EU", 1024 * NET + 128 * NL, F)
_buf("WN", (24, 16), B); _buf("EQ", (NEQ, L), B); _buf("GY0 GY1", (64, 8), F)
_buf("PZ0 PZ1 PGA PGB PGC PGD", (64, 8), F, "psum"); _buf("S0", (32, 16), F, "psum"); _buf("S1", 512, F, "psum")
PLACE["MARK"] = ("SELW", 1000, 16)
NDMA = 64
SEMAPHORES = ["cv", "ca", "ct", "cg", "loc", "mark"] + ["d%d" % i for i in range(NDMA)] + ["r%d" % i for i in range(20)]


def A(n, a=None, b=None, st=1, p=(0, 128)):
    name = n
    n, at, w = PLACE[n] if n in PLACE else (n, 0, SCRATCH[n][1][1])
    a = at + (0 if a is None else a)
    b = at + (w if b is None else b)
    return {"n": n, "as": name, "ix": (slice(*p), slice(a, b, st)), "lo": a, "hi": b, "cnt": len(range(a, b, st)), "p": p, "st": st}


def A3(n, rows=None, cols=None, p=(0, 128)):
    nr, w = SCRATCH[n][1][1:]
    rows = (0, nr) if rows is None else rows
    cols = (0, w) if cols is None else cols
    r = range(rows, rows + 1) if isinstance(rows, int) else range(*rows)
    c = range(cols, cols + 1) if isinstance(cols, int) else range(*cols)
    ix = lambda x: x if isinstance(x, int) else slice(*x)
    return {"n": n, "as": n, "ix": (slice(*p), ix(rows), ix(cols)), "lo": r[0] * w + c[0], "hi": r[-1] * w + c[-1] + 1, "cnt": len(r) * len(c), "p": p,
            "runs": len(r) if r.step > 1 or len(c) < w else 1, "st": (c[0], c[-1]) if n[:2] == "GY" else 1}


def PB(n, a, cnt, runs=1, st=0, p=(0, 128)):
    if len(SCRATCH[n][1]) == 2: return A(n, a, a + cnt, 1, p)
    w = SCRATCH[n][1][2]
    if runs == 1 and cnt > w: return A3(n, (a // w, (a + cnt) // w), None, p)
    return A3(n, (a // w, a // w + (runs - 1) * st // w + 1, max(1, st // w)), (a % w, a % w + cnt), p)


def IND(win, off):
    return dict(win, off=off, cnt=16 * off["cnt"])


def two(*aps):
    return all(SCRATCH[a["n"]][2] in (B, U) for a in aps)


def psum(a):
    return SCRATCH[a["n"]][0] == "psum"


CASES = [(0.85, 0.42, 1.25, 3.0, 400, 140, 2000, 2400, 1500, 15), (1.05, 0.525, 1.15, 3.0, 550, 150, 2100, 2600, 2000, 20), (1.22, 0.61, 2.4, 6.0, 450, 150, 1900, 2300, 1500, 15)]
WEIGHTS = (0.36, 0.33, 0.21)
LATER = [(0.87, 0.43, 1.3, 3.8, 400, 150, 2000, 2400, 1500, 15), (1.08, 0.55, 1.8, 5.5, 450, 160, 2000, 2400, 1600, 16), (1.24, 0.62, 2.55, 7.4, 450, 160, 1900, 2300, 1500, 15)]
WSECOND, WLATER = (0.36, 0.36, 0.21), (0.36, 0.33, 0.21)
SIZE = {B: 2, U: 2, F: 4, I: 4}
PIN = dict(RS32="a", DRC="a", DRX="g", BO32="a", ID32="g", KF="v", MI="gv", Z2="g", OT="v", OKK="gv", OSX="v", OB="v", EXU="g", UB1="av", MX="a", ME="a", SCS1="a", SCS0="a", WN="va", SU="a", BR16="aa", KB0="v", BO="gga", VH="aggag", WC="aggag", GY0="vvav", GY1="vvvvvvav", AM="avv", AW="a", OFN="gvg", KR16="aa", SELW="g", OSC="g", PLUS="g", EF="vavaaav", EA="a", EU="v", OA="agvgg", OHT1="g", UA0="aav", UA1="vvv")
END = 57.5
AFTER = ()
DUE = dict(ZERO=[0.1,0.4], ONE=[1.6], LL=[0.05,0.05], XR=[0.1], X=[0.4,26.1,26.75], NN=[0.3,4.0,12], IN=[0.1], IP=[0.2], K15=[0.6], CBLK=[2.4], KB0=[2.5], SELQ=[3], ID32=[10.3], BO32=[4.4], BO=[3.4,3.85,4.7], RS32=[2.0,2.6], DRC=[1.7,2.6], DRX=[19.5,22], UB0=[24.6,31], UO0=[5.3,8.0], OFC=[10.9,7.6,28.2,36], OFN=[7.8,3.9,26.5,24], RL=[3.0], HC=[6.05,36.6], MX=[3.3,4.65], ME=[3.6], RKEY=[4.25], KR16=[3.9,17.6], EQ=[4.5,4.9,5.0,22.3,22.6,22.8,23.5,23.9,24.2,32.4,32.8,33.1], U0=[5.85,8.6], E=[6.15], UB1=[2.4,3.1,9.3,31], UA1=[1.0,1.4,9.3,31.5], UA0=[2.2,3.0,12.9], TRI=[6.75,7.2], FS=[10,25.1,33.6], V0=[11.8,14.2], VH=[14.5,15,16,17,17.5,18.5], SCS1=[12.6,14.9,23.5], PZ1=[13.4,20.3,20.7,21.8,22.5,22.8,23.1], WN=[14,17,18.3], S0=[15.1,15.6,19.3,19.7,27,27.5], AF=[15.9,20], SCS0=[16.3,17.2,17.6,18.6,29], MI=[15.2,18.8], INS=[15.7,19.3], OA=[16.3,20.4,34,37.4,37.7,42,42.3,45.3], BR16=[19.5,21.3], BSC=[20.3,21.5], SU=[17.3], EA=[17.7,19.1,20.5,22.5,23.9,25.2], OKEY1=[24.4], TC=[3.2,18.2], PV=[21.8,26], E32=[9.6,15.4,29.2,29.9], VO1=[30.5], UO1=[27.3,30.5], U1=[27.8,31], V1=[31], VF1=[24.8,34.5], VF0=[28.1,35.5], WF=[31.3], XG=[6.4,9.1,6.7,10.4,7.7,10.4,11.8,12.0,13.1,14.5,15.9,15.4,28.1,29.5,30.9,32.2,33.6,34.9,36.3,37.7,37.6,39.8,40.6,42.4], EF=[35.4,38.9,39.1,43.4,44,46.5,47], COUNT=[2.2], VO0=[11.3,13.5], SCB=[2.45], IDB=[5.05], SC12=[5.3], IOC=[2.0], RD=[8.2,9.0], IOG=[2.6], IOR=[11.5], ZERO32=[12.3], COL=[13.4], IH=[13.8,16.5], RSB=[18], NMD=[2.3], NMD2=[2.5], HALF=[18], OWN=[30], SELW=[30,40], SEL=[3.2], OSC=[12,35.2], ROSC=[13], DD=[16.8,14.3,31,37], OAA=[17.5,20.5], OB=[21,22], NX0=[21.4,24.6], NX=[25.35], EB=[26], WV=[28.5], PZ0=[16.8,18.1,28,28.5,29,29.5,30,30.5], TIMES=[1.6,1.7,1.8,21.0,22.9], PLUS=[10.9,12,13.9,14,22.95], ET=[28.9,31.5,32,34.6,36,44], KK=[16.2,19.55], OKK=[16.6,20], NEW=[23.1], Z2=[23.4], EXK=[23.6], EXU=[24], OSX=[25.4], OHT1=[24.7], VA=[22,35.8], MR=[3.5], VB1=[12.3,19], VB0=[16,22], WB1=[20.2,28], WB0=[20.5,33], CBLW=[33])
DUE.update(VA=[22,35], WS=[39.4,41.5,43.5,46.5], EF=[37.2,39.5,40.5,44,45.5,48], V1=[31.6,34], VO1=[31.2,33.5], E32=[9.6,15.4,30.3,31], U1=[29.2,32.5], UO1=[28.8,32], X=[0.4,27.6,28.3], OA=[16.3,20.4,35.5,38,38.3,42.5,42.8,46], WV=[29.5],
           PZ0=[16.8,18.1,27.5,28,28.5,29,29.5,30,30.6], WC=[27.5,28,31,31.5], WB1=[20.2,28.2], WB0=[20.5,31.8])
_OLD = dict(ZERO=[0.1, 0.4], ONE=[1.6], LL=[0.05, 0.05], XR=[0.1], X=[0.4, 27, 27.7], NN=[0.3, 4.2, 11.2], IN=[0.1], IP=[0.2], K15=[0.6], CBLK=[3], KB0=[3], SELQ=[9], ID32=[4.6], BO32=[4.8], BO=[0, 0, 5], RS32=[2.0, 2.6], DRC=[4.2, 5], DRX=[4.4, 9], UB0=[15, 16, 17, 25], UO0=[5.45, 8.2], OFC=[11.5, 7.85], OFN=[9, 4], RL=[3.1], HC=[4.6], MX=[3.4, 4.0], ME=[3.7], RKEY=[4.4], KR16=[4.0], EQ=[4.5, 4.8, 5.1], U0=[5.85, 8.6], E=[5.9], UB1=[2.4, 3.1, 9.3], UA1=[2, 9.2], UA0=[2.5, 12.6], TRI=[7, 7.5], FS=[8.5], V0=[11.2, 15], VH=[14.3, 14.8, 15.3], SCS1=[13.0], PZ1=[13.8], WN=[14.5, 19], S0=[15.1, 15.6], AF=[16.5], SCS0=[17.5, 19.4], MI=[17, 19.7], INS=[17.5, 20.2], OA=[17.5, 21.5, 35, 38.5, 38.5, 44.5, 44.5, 48.5], BR16=[19, 22.3], BSC=[19, 22.3], SU=[17], EA=[19, 20.4, 22, 23.5, 25, 26.5], OKEY1=[25.5], TC=[3.2, 24], PV=[25], E32=[10.2, 29, 29.7], VO1=[30.3], UO1=[28.3], U1=[28.7], V1=[30.7], VB=[11.5, 19.5, 26], WB=[15, 29, 35], VF1=[17.6], VF0=[20.2], WF=[22, 25.6], XG=[6.5, 9.35, 7.1, 10.6, 7.85, 10.7, 12.1, 13.5, 13.4, 14.8, 16.1, 15, 29.2, 30.5, 30.5, 33.5, 32.4, 35, 37.5, 39.5, 39.5, 41.5, 43.5, 45.5], EF=[36.4, 40, 42.5, 46, 49, 51.5, 52.5])


def build(case):
    CY, PECY, GAT, SCA, MMI, WAKE, DML, RML, FIRST, ROW = case
    ops = []; made = {}

    def add(eng, kind, args, rd, wr, cost, lat=0.0):
        r = []
        name = wr[0]["as"] if wr else "y"; k = made[name] = made.get(name, -1) + 1
        if len(eng) > 1:
            q0 = PIN[name][min(k, len(PIN[name]) - 1)] if name in PIN else ""
            if q0 and q0 in eng: eng = q0 + eng.replace(q0, "")
            elif name not in ("XG", "OA"): eng = "".join(q for q in "gav" if q in eng)
        for a in rd:
            if isinstance(a, dict):
                r.append(a)
                if "off" in a: r.append(a["off"])
        for a in wr:
            if "off" in a: r.append(a["off"])
        ops.append({"eng": eng, "kind": kind, "args": args, "rd": r, "wr": list(wr), "cost": cost, "lat": lat + WAKE, "hold": 0.0, "name": name})

    def join(k):
        x = ops[-k:]; del ops[-k:]
        ops.append(dict(x[0], kind="many", args=x, rd=[a for o in x for a in o["rd"]], wr=[a for o in x for a in o["wr"]], cost={q: sum(o["cost"][q] for o in x) for q in x[0]["cost"]}))

    def vc(out, ins, c):
        n = out["cnt"]
        if "off" in out: return 60 + n * SCA
        if "off" in ins[0]: return 60 + n * GAT
        return 30 + max(64, n * c) * CY

    def cp(out, a, eng="v", scale=None, bias=None):
        c = {}
        if "v" in eng: c["v"] = vc(out, [a], 0.5 if two(out, a) else 1)
        if "a" in eng: c["a"] = 70 + out["cnt"] * (GAT if "off" in a else CY)
        if "g" in eng: c["g"] = 200 + 2 * out["cnt"] * CY
        add(eng, "cp", (out, a, scale, bias), [a, bias], [out], c)

    def ts(out, a, s1, op0, s2=None, op1=None):
        add("v", "ts", (out, a, s1, s2, op0, op1), [a, s1, s2], [out], {"v": vc(out, [a], 0.5 if two(out, a) else 1)})

    def tt(out, a, b, op):
        add("v", "tt", (out, a, b, op), [a, b], [out], {"v": vc(out, [a], 1 if psum(a) or psum(b) else 2)})

    def scan(out, d0, d1, init, op0, op1):
        add("v", "scan", (out, d0, d1, init, op0, op1), [d0, d1], [out], {"v": vc(out, [d0], 0.5 if two(out, d0, d1) else 1)})

    def tr(out, a):
        add("v", "tr", (out, a), [a], [out], {"v": vc(out, [a], 0.5 if two(out, a) else 1)})

    def ms(out, val):
        add("v", "ms", (out, val), [], [out], {"v": vc(out, [out], 0.5 if two(out) else 1)})

    def act(out, a, func, scale=1.0):
        add("a", "act", (out, a, func, scale), [a], [out], {"a": 70 + out["cnt"] * CY})

    def step(out, a, eng="va"):
        add(eng, "step", (out, a), [a], [out], {"v": vc(out, [a], 1), "a": 70 + out["cnt"] * CY} if eng == "va" else {"a": 1400 * CY})

    def sign(out, a):
        add("va", "sign", (out, a), [a], [out], {"v": vc(out, [a], 0.5), "a": 70 + out["cnt"] * CY})

    def iota(out, pat, base=0, chm=0):
        add("g", "iota", (out, pat, base, chm), [], [out], {"g": 160 + 2 * out["cnt"] * CY})

    def sel(out, a, pat, op, fill, base=0, chm=0):
        add("g", "sel", (out, a, pat, op, fill, base, chm), [a], [out], {"g": 200 + 2 * out["cnt"] * CY})

    def mm(lst):
        c = sum(max(min(64, x[1]["cnt"]), x[2]["cnt"]) * (4 if SCRATCH[x[1]["n"]][2] == F else 1) * PECY for x in lst)
        add("t", "mm", lst, [x[1] for x in lst] + [x[2] for x in lst], [x[0] for x in lst], {"t": c}, 60)

    def hold(pairs):
        sides = [x[0] if isinstance(x[0], dict) else x[1] for x in pairs]
        return sum((a["p"][1] - a["p"][0]) * (a["cnt"] * SIZE[SCRATCH[a["n"]][2]] * 0.21 / 128 + a.get("runs", 1) * ROW / 16) for a in sides)

    def dma(q, pairs, after=None, kind="dma"):
        add(q, kind, pairs, [x[1] for x in pairs] + [after], [x[0] for x in pairs if isinstance(x[0], dict)], {q: (2.25 * MMI if q == "g" else 70) * len(pairs)}, DML)
        ops[-1]["hold"] = hold(pairs) * (2 if kind == "dadd" else 1)

    def send(pairs, first=False):
        add("g", "send", pairs, [x[1] for x in pairs], [x[0] for x in pairs], {"g": MMI}, RML + (FIRST if first else 0))
        ops[-1]["hold"] = hold(pairs)

    def sent():
        k = made.get("MARK", -1) + 1; add("g", "mark", None, [], [A("MARK", k, k + 1)], {"g": 40}); ops[-1]["soft"] = [len(ops) - 2]
        return A("MARK", k, k + 1)

    def lower(name, hi, lo, x):
        if name in LOW: cp(lo, x, "va", -1.0); cp(hi, x, "vag"); dma("g", [(lo, x)], None, "dadd")
        else: cp(hi, x, "va" if psum(x) else "vag"); tt(lo, x, hi, ALU.subtract)

    def fill(n, z, after, r0=0, rows=None):
        w = SCRATCH[n][1][2]; rows = rows or SCRATCH[n][1][1]; k = A(z)["cnt"] // w
        dma("s", [(A3(n, (r, min(rows, r + k))), A(z, 0, w * (min(rows, r + k) - r))) for r in range(r0, rows, k)], after)

    twin = lambda n, d: n + str(d if TWIN else 1)
    who = lambda s, j: "va" if j in ONV[s] else "av"
    H = lambda n, d, w=L: A(n, d * w, d * w + w)
    full = (slice(0, 128), slice(None))
    grp = lambda g: (16 * g, 16 * g + 16)
    quad = lambda q: (32 * q, 32 * q + 32)
    mask = lambda bank, n, left, p=(0, 128): (PB(bank, 0, n, p=p), A(left, p[0], p[1], 1, (0, 8)), A("COL", 0, n, 1, (0, 8)), True, False)
    OHT0, OKEY0, OSC = (H("S16", 1, 12), A("OT")), (H("S16", 2, 12), A("RKEY")), (H("OSC", 0, 12), A("ROSC"))
    ent = lambda s, d: H("NN", 2 * s + d)
    nn = lambda s, d: (ent(s, d), (("nh", "nt")[d], (slice(0, 128), slice(s * L, s * L + L))))
    dma("s", [(A("LL", 12 * j, 12 * j + 12), (n, full)) for j, n in enumerate(("tl", "rl"))])
    dma("a", [(A("LL", 24, 36), ("hl", full))])
    dma("a", [(A("XR", 0, 32), ("xr", full)), (A("XR", 32, 64), ("er", full))])
    dma("s", [nn(0, 1)])
    dma("s", [(A("X", 0, M), ("xe", full))])
    iota(A("IN"), [[0, 1]], 127, -1); ts(A("I1"), A("IN"), 15, ALU.bitwise_and); cp(A("K15"), A("I1"))
    ts(A("I2"), A("IN"), 31, ALU.bitwise_and, 1, ALU.arith_shift_right); cp(A("KB1"), A("I2")); cp(A("KB0"), A("KB1"), "va", 1.0, 16.0)
    iota(A("IP"), [[0, 1]], 0, 1)
    ms(A("ZERO", 0, 128), 0.0); ms(A("ZERO", 128, 768), 0.0); step(A("ONE"), A("ZERO", 0, 128), "a")
    iota(A("IOC"), [[0, 12], [-1, 16]], 15); iota(A("IOR"), [[1, 16]]); ts(A("MR"), A("IOR"), A("K15"), ALU.is_equal)
    if BROAD: cp(A("SELW"), A("ZERO", 0, 240), "vag"); ts(A("SELW", 112, 128), A("IOC", 0, 16), A("K15"), ALU.is_equal)
    ts(A("NMD"), A("IOC"), A("K15"), ALU.not_equal, 8192.0, ALU.mult)
    ts(A("NMD2"), A("NMD"), 8192.0, ALU.add)
    sel(A("IDB"), A("ONE"), [[-1, 128]], ALU.is_equal, 0.0, 0, 1); cp(A("ID32"), A("IDB"), "ag")
    sel(A("BO"), A("ONE"), [[-16, 8], [0, 16]], ALU.is_ge, 0.0, 0, 1); sel(A("BO"), A("BO"), [[16, 8], [0, 16]], ALU.is_ge, 0.0, 15, -1); cp(A("BO32"), A("BO"), "ag")
    cp(A("BO"), A("BO32"), "va", 8192.0)
    sel(A("TRI"), A("BO"), [[1, 128]], ALU.is_gt, 0.0, 0, -1); sel(A("TRI"), A("TRI"), [[1, 128]], ALU.not_equal, -8192.0, 0, -1)
    sel(A("RD"), A("ONE"), [[-32, 4], [-2, 32]], ALU.is_equal, 0.0, 0, 1); sel(A("RD"), A("RD"), [[-32, 4], [-2, 32]], ALU.not_equal, -1.0, -1, 1)
    iota(A("IOG"), [[-64, 4], [-1, 48]], 31); ts(A("I5"), A("IP"), 5, ALU.arith_shift_right); ts(A("KQ"), A("I5"), -64.0, ALU.mult, A("K15"), ALU.add)
    ts(A("I6"), A("IP"), 16, ALU.bitwise_and); ts(A("KQ2"), A("I6"), 64.0, ALU.mult, A("KQ"), ALU.add)
    ts(A("SEL"), A("IOG"), A("KQ"), ALU.is_equal); ts(A("SELQ"), A("IOG"), A("KQ2"), ALU.is_equal)
    for r in (0, 4) if min(EARLY[0][1], EARLY[1][1]) < 3 else (): cp(A3("UB1", (r, r + 4)), A("ZERO"), "va")
    cp(A("RS32"), A("ZERO", 0, 2 * L), "vag"); ms(A("RS32", 0, None, 32), -1e6); sel(A("RSB"), A("ZERO", 0, L), [[0, 12], [1, 16]], ALU.not_equal, 16384.0)
    iota(A("SC12"), [[16, 24]], 15)
    for n, base, k in (("DRC", NK, 12), ("DRX", M, 24)): cp(A(n), A("ZERO", 0, 16 * k), "vag"); ts(A(n, 0, None, 16), A("SC12", 0, k), A("K15"), ALU.subtract, float(base), ALU.add)
    ms(A("TIMES", 0, 72, 3), 0.0); ms(A("TIMES", 2, 36, 3), 37.0); ms(A("TIMES", 38, 72, 3), 1.0)
    for d in (1, 0):
        for c0 in range(0, 512 * NUA[d], 768): w = min(768, 512 * NUA[d] - c0); cp(A("UA%d" % d, c0, c0 + w), A("ZERO", 0, w), "va")
    ts(A("C1"), A("K15"), -8.0, ALU.mult, 120.0, ALU.add); ts(A("I3"), A("IP"), 1, ALU.bitwise_and); ts(A("C3"), A("I3"), -7.0, ALU.mult, A("C1"), ALU.add)
    ts(A("I4"), A("IP"), 4, ALU.arith_shift_right); ts(A("C4"), A("I4"), 2.0, ALU.mult, A("C3"), ALU.add)
    iota(A("SCB"), [[128, 12]], 0); ts(A("CBLK"), A("SCB"), A("C4"), ALU.add)
    if VEARLY and 0 in WIDE:
        ts(A("C5"), A("K15"), 7.5, ALU.is_lt, 56.0, ALU.mult); ts(A("C6"), A("K15"), -1.0, ALU.mult, A("C5"), ALU.add); ts(A("C7"), A("I4"), 8.0, ALU.mult, A("C6"), ALU.add)
        ts(A("CBLW"), A("SCB"), A("C7"), ALU.add, 15.0, ALU.add)
    send([(A("RL"), A("LL", 0, 24), 1)], True); dma("s", [(A("TC", 0, NK), ("tc", full))], sent())
    cp(A("S16", 0, 24), A("LL", 12, 36))
    cp(H("MX", 0), IND(A("XR", 0, 32), H("S16", 0, 12)), "va"); cp(H("ME", 0), IND(A("XR", 32, 64), H("S16", 0, 12)), "va", 0.125)
    send([(H("MX", 1), H("MX", 0), 1), (H("ME", 1), H("ME", 0), 1)])
    ts(A("KA"), A("LL", 12, 36), 37.0, ALU.mult); tt(A("KB"), A("KA"), A("LL", 0, 24), ALU.add); ts(A("KEY"), A("KB"), NK - 1, ALU.bitwise_and)
    cp(A("S16", 24, 48), A("KEY"))
    send([(A("RKEY"), H("S16", 3, 12), 1)])
    cp(OHT0[1], H("RL", 0, 12), "vg")
    dma("s", [nn(0, 0)], H("ME", 0))
    side = lambda n, d, c: A(n, 36 * d + c, 36 * d + 36, 3)
    cp(side("PLUS", 0, 1), A("LL", 24, 36), "vg"); cp(side("PLUS", 1, 1), H("RL", 0, 12), "vg")
    cp(side("PLUS", 0, 2), A("LL", 12, 24), "vg"); ts(side("PLUS", 1, 2), H("RL", 1, 12), 37.0, ALU.mult)
    swap = lambda land, src, w: [(H(land, 1, w), H(src, 0, w), 1), (H(land, 0, w), H(src, 1, w), -1)]
    pairs_of = lambda n, l: A(n, 8 * l, 8 * l + 16)

    def ublock(s, d):
        l0 = 64 * EARLY[s][d]
        if l0: cp(IND(A("UA%d" % d), A("CBLK", 0, l0 // 16)), A("U%d" % s, d * L, d * L + l0))
        if l0 == L: return
        dma("s", [(A3("UB%d" % d, g, (l0, L), grp(g)), A("U%d" % s, d * L + l0, d * L + L, 1, grp(g))) for g in range(8)])

    def vblock(s, d):
        v = H("V%d" % s, d)
        if s:
            l0 = 64 * d * VEARLY
            if l0: cp(IND(A("VA"), A("CBLW" if 0 in WIDE else "CBLK", 0, l0 // 16)), A("V1", L, L + l0))
            dma("s", [(A3("VF%d" % d, g, (l0, L), grp(g)), A("V1", d * L + l0, d * L + L, 1, grp(g))) for g in range(8)])
        else:
            lower("v%d" % d, H("VH", 2 * d), H("VH", 2 * d + 1), v)
            dma("s", [(A3(twin("VB", d), g, None, grp(g)), A("VH", 2 * d * L, (2 * d + 2) * L, 1, grp(g))) for g in range(8)])

    def lists(s, d):
        cand = IND(A(("HC", "TC")[d], 0, NK), H("OKEY1", d, 12) if s else OKEY0[d])
        cp(H("OFN", 2 * s + d), ent(s, d), "vg"); cp(H("OFC", 2 * s + d), cand, "v")
        tt(H("DD", d), cand, ent(s, d), ALU.subtract)

    def contest(d):
        scs, flat, j0 = "SCS%d" % d, "S1", 0
        bank = lambda j: (("PGA", "PGC", "PGD"), ("PGB", "PGC", "PGD"))[d][sum(x <= j for x in PARTS[d])]
        for l0 in range(0, L, 64):
            x0 = 32 * (d * L + l0)
            for part in (1, 0): cp(A("XG", x0 + part, x0 + 2048, 2), IND(A("X", 0, M), A(("OFC", "OFN")[part], d * L + l0, d * L + l0 + 64)), who(0, x0 // 1024 + part))
            lst = []
            for l in range(l0, l0 + 64):
                c, j16 = divmod(l, 16); j, q = divmod(c, 4)
                lst.append((PB(bank(j), 128 * j + j16, 1, 8, 16, quad(q)), A("XG", 32 * (d * L + l), 32 * (d * L + l) + 32),
                            A3("UB%d" % d, None, l) if l >= 64 * EARLY[0][d] else A("UA%d" % d, 16 * (l // 2) + l % 2, 16 * (l // 2) + 16, 2), True, True))
            mm(lst)
            j1 = l0 // 64 + 1
            if j1 not in PARTS[d]: continue
            a, b = 128 * j0, 128 * j1
            cp(A(scs, a, b), PB(bank(j0), a, b - a), "va", 32.0, A("KB%d" % d))
            mm([(PB(flat, 128 * j, 128), H(scs, j, 128), A("ID32"), True, True) for j in range(j0, j1)])
            mm([(PB("PZ%d" % d, a, b - a), A("RD"), A(scs, a, b), True, True)])
            scan(A(scs, a, b), A("RS32", 0, b - a), PB(flat, a, b - a), 0.0, ALU.add, ALU.max)
            step(A3("WN", (8 * j0, 8 * j1)), PB("PZ%d" % d, a, b - a)); j0 = j1
        cp(H("MI", d, 12), A(scs, 31, None, 32), "vg")
        send(swap("INS", "MI", 12)[d:d + 1])
        x = sent()
        for n in (("WB1", "WB0"), ("VB0",))[d] if TWIN else (("VF1", "VF0"), ("WB1",))[d]: fill(n, "ZERO32" if n[1] == "F" else "ZERO", x)
        mm([(PB("S0", L * d + 16 * q, 16, 3, 64, quad(g // 2)), A("SELQ", 48 * q + 16 - 16 * (g % 2), 48 * q + 48 - 16 * (g % 2)), A3("WN", (g, 24, 8)), g % 2 == 0, g % 2 == 1)
            for q in range(4) for g in range(8)])
        tt(PB("S0", L * d, L), PB("S0", L * d, L), H("DD", d), ALU.mult)
        tt(H("AF", d), PB("S0", L * d, L), ent(0, d), ALU.add)
        cp(H("OA", d), H("AF", d), "avg")

    def best(d):
        sc, flat = ("PGA", "PGB")[d], "S1"
        ts(H("KK", d, 12), H("MI", d, 12), 15, ALU.bitwise_and); cp(H("OKK", d, 12), H("KK", d, 12), "vg")
        tt(H("OAA", d), IND(A("MR"), H("OKK", d, 12)), H("AF", d), ALU.mult); mm([(PB(sc, 0, L), A("BO32"), H("OAA", d), True, True)])
        mm([(PB(flat, 0, L), A("IDB"), A("NMD"), True, False), (PB(flat, 0, L), A("BO32"), H("OAA", d), False, True)])
        cp(H("BR16", d), PB(sc, 0, L), "va")
        scan(H("BSC", d), A("RSB"), PB(flat, 0, L), 0.0, ALU.add, ALU.min)

    def duel(k):
        d, l0, w = DUELS[k]; o0 = d * L + l0; b = k % 2; n = w // 4; m = min(w, 64); f0 = 0 if k in BROAD else 256
        for l1 in range(l0, l0 + w, m):
            xc = 32 * d * L + 16 * l1; xn = xc + 16 * L; o1 = 2 * L + d * L + l1; j0 = (l1 - l0) // n; c = (d * 3 + l1 // 64 + 3) % 6
            cand = IND(A("X", 0, M), A("OFC", o1, o1 + m))
            cp(A("XG", xn, xn + 16 * m), IND(A("X", 0, M), A("OFN", o1, o1 + m)), who(1, (d * L + l1) // 32 + 1), -1.0)
            if c in DIFF: tt(A("XG", xc, xc + 16 * m), cand, A("XG", xn, xn + 16 * m), ALU.add)
            else: cp(A("XG", xc, xc + 16 * m), cand, who(1, (d * L + l1) // 32))
            for x0 in (xc,) if c in DIFF else (xn, xc):
                opens = x0 == xn or c in DIFF
                if k in BROAD:
                    mm([mask("S1", 8 * w, "OWN")] * opens + [(PB("S1", 64 * t, 64), A("XG", x0 + 128 * t, x0 + 128 * t + 128), A3("UB%d" % d, None, (l0 + 8 * t, l0 + 8 * t + 8)),
                                                              False, x0 == xc and t == w // 8 - 1) for t in range(w // 8)])
                    continue
                lst = [mask(DB[k], 2 * w, "HALF", (32 * j0, 32 * (j0 + m // n)))] * opens
                for l in range(l1, l1 + m, 2):
                    j, t = divmod(l - l0, n)
                    lst.append((PB(DB[k], 8 * t, 16, p=quad(j)), A("XG", x0 + 16 * (l - l1), x0 + 16 * (l - l1) + 32),
                                A3("UB%d" % d, None, (l, l + 2)) if l >= 64 * EARLY[1][d] else pairs_of("UA%d" % d, l), False, x0 == xc and t == n - 2))
                mm(lst)
        if k in BROAD:
            step(A3("AW", (0, w)), PB("S1", 0, 8 * w))
            mm([(PB("S1", 0, w), A("SELW", 112 - 16 * g, 240 - 16 * g), A3("AW", (g, w, 8)), g == 0, g == 7) for g in range(8)])
        else:
            step(A3("AM", (0, n // 2)), PB(DB[k], 0, 2 * w))
            mm([(PB(DB[k], 256 + n * j, n, p=quad(q)), A("SEL", 48 * j + 16 - 16 * h, 48 * j + 48 - 16 * h), A3("AM", (0, n // 2), (4 * q + 2 * h, 4 * q + 2 * h + 2)), h == 0, h == 1)
                for j in range(4) for q in range(4) for h in (0, 1)])
        tt(PB(DB[k], f0, w), PB(DB[k], f0, w), A("DD", o0, o0 + w), ALU.mult)
        tt(A("A64", 128 * b, 128 * b + w), PB(DB[k], f0, w), A("NN", 2 * L + o0, 2 * L + o0 + w), ALU.add)
        for l1 in range(0, w, m): cp(A("OA", o0 + l1, o0 + l1 + m), A("A64", 128 * b + l1, 128 * b + l1 + m), "gva")

    sums = lambda c: GB[c % len(GB)]
    gy = lambda c: "GY%d" % (c // 4)

    def readout(c):
        for j in range(4):
            cp(A3(gy(c), None, (2 * j, 2 * j + 2), quad(c % 4)), PB(sums(c), 128 * j, 128, p=quad(j)), RO)
            if c < 4 and j == 3: join(4)
            if c >= 4 and j % 2: join(2)

    def store(c):
        y, c0 = divmod(64 * c, L)
        pairs = [((("yt", "yh")[y], (slice(*grp(g)), slice(c0, c0 + 64))), A3(gy(c), (8 * g, 8 * g + 8), None, grp(2 * (c % 4) + g % 2))) for g in range(8)]
        if c == 5: dma("s", pairs[:4]); dma("a", pairs[4:])
        else: dma("s", pairs)

    def reals0(d):
        pz = "PZ%d" % d; at = lambda l: (l % 8 // 2, l // 8)
        for ch in range(3):
            c = 3 * d + ch; e0 = 1024 * (c % NEA)
            for l in range(0, 64, 64 // CUT[c]): cp(A("EA", e0 + 16 * l, e0 + 16 * l + 1024 // CUT[c]), IND(A("E"), A("OA", 64 * c + l, 64 * c + l + 64 // CUT[c])), "va")
            lst = [] if ch else [mask(pz, 2 * L, "HALF")]
            for l in range(64 * ch, 64 * ch + 64, 2):
                j, t = at(l); e = e0 + 16 * (l % 64)
                for part in (0, 1):
                    lst.append((PB(pz, 4 * t, 4, 4, 96, quad(j)), A("EA", e, e + 32), A3(twin("VB", d), None, (part * L + l, part * L + l + 2)), False, t == 23 and part == 1))
            for k in range(ZCUT): mm(lst[k * len(lst) // ZCUT:(k + 1) * len(lst) // ZCUT])
        z = PB(pz, 0, 2 * L); hi, lo = A3("WC", (8 * d, 8 * d + 4)), A3("WC", (8 * d + 4, 8 * d + 8)); w = A("SCS%d" % d) if "w%d" % d in LOW else z
        act(w, z, ACT.Sigmoid, 0.5); lower("w%d" % d, hi, lo, w)
        dma("s", [(A3(twin("WB", d), (4 * j + q, 32, 16), None, quad(q)), A3("WC", (8 * d + q, 8 * d + 8, 4), None, quad(j))) for j in range(4) for q in range(4)])

    def sums0(c):
        d, ch = divmod((c + 3) % 6, 3)
        tr(H("ET", 3 * d + ch, 1024), H("EA", 3 * d + ch, 1024))
        mm([(PB(sums(c), 2 * t, 2, 32, 16), H("ET", 24 * d + 8 * ch + t, 128), A3(twin("WB", d), (16 * part, 16 * part + 16), (32 * ch + 4 * t, 32 * ch + 4 * t + 4)), t == part == 0, False)
            for t in range(8) for part in (0, 1)])

    def reals1(c):
        d, ch = divmod((c + 3) % 6, 3); n = 8 - (NL if c == 5 else 0); wide = c in WIDE; pz = "PZ%d" % ZB[c]; o0 = d * L + 64 * ch
        e0, u0, r = 1024 * (c % NEF), 1024 * (c % NET), c % NW; vf = "VF%d" % d
        cp(A("EF", e0, e0 + 128 * n), IND(A("E32", 0, M), A("OA", o0, o0 + 8 * n)), "va")
        tr(A("EU", u0, u0 + 128 * n), A("EF", e0, e0 + 128 * n))
        ws = lambda j, q0, q1: A("WS", 128 * r + 32 * q0, 128 * r + 32 * q1, 1, quad(j))
        if wide:
            lst = [mask(pz, 512, "HALF")]
            if c in APART: mm(lst); lst = []
            lst += [(PB(pz, 8 * t, 8, 8, 64), A("EF", e0 + 128 * t, e0 + 128 * t + 128),
                     H("VA", 8 * c + t, 64) if c < VEARLY else A3(vf, None, (64 * ch + 8 * t, 64 * ch + 8 * t + 8)), False, t == n - 1) for t in range(n)]
            mm(lst)
            zq = lambda j, q0, q1: A3(pz, (16 * q0, 16 * q1), (2 * j, 2 * j + 2), quad(j))
            if c not in DIRECT:
                for j in range(4): act(ws(j, 0, 4), zq(j, 0, 4), ACT.Sigmoid, 0.5)
                join(4)
        else:
            lst = [mask(pz, 128, "HALF")]
            for j in range(4):
                for t in range(n):
                    l = 8 * t + 2 * j
                    lst.append((PB(pz, 2 * t, 2, 8, 16, quad(j)), A("EF", e0 + 16 * l, e0 + 16 * l + 32),
                                pairs_of("VA", 64 * ch + l) if c < VEARLY else A3(vf, None, (64 * ch + l, 64 * ch + l + 2)), False, t == n - 1))
            mm(lst)
            zq = lambda j, q0, q1: PB(pz, 32 * q0, 32 * (q1 - q0), p=quad(j))
            if c not in DIRECT: act(H("WS", r, 128), PB(pz, 0, 128), ACT.Sigmoid, 0.5)
        wf = lambda j, q: A3("WF", (32 * r + 8 * j + 2 * q, 32 * r + 8 * j + 2 * q + 2), None, quad(q))
        if c in DIRECT:
            for j in (3, 2, 1, 0):
                if (c, j) in SHARE: act(ws(j, 0, 4), zq(j, 0, 4), ACT.Sigmoid, 0.5)
                for q in range(4):
                    if (c, j) in SHARE: cp(wf(j, q), ws(j, q, q + 1), "va")
                    else: act(wf(j, q), zq(j, q, q + 1), ACT.Sigmoid, 0.5)
                join(4)
        else: dma("s", [(wf(j, q), ws(j, q, q + 1)) for j in range(4) for q in range(4)])
        mm([(PB(sums(c), 2 * t, 2, 32, 16), A("EU", u0 + 128 * t, u0 + 128 * t + 128), A3("WF", (32 * r, 32 * r + 32), (2 * t, 2 * t + 2)), False, t == n - 1) for t in range(n)])
        readout(c)

    def piece(k):
        n, t0 = LAST[k], sum(LAST[:k]); l0 = L - 8 * (NL - t0); e0, u0, w0 = 1024 * NEF + 128 * t0, 1024 * NET + 128 * t0, 64 * t0; pz = "PZ%d" % ((ZB[5] + 1 + k) % 2)
        cp(A("EF", e0, e0 + 128 * n), IND(A("E32", 0, M), A("OA", l0, l0 + 8 * n)), "va")
        tile = lambda t: A("EF", e0 + 128 * t, e0 + 128 * t + 128)
        mm([mask(pz, 64 * n, "OWN")] +
           [(PB(pz, 64 * t, 64), tile(t), A3("VF0", None, (l0 + 8 * t, l0 + 8 * t + 8)), False, t == n - 1) for t in range(n)])
        mm([(PB("S1", 128 * t, 128), tile(t), A("ID32"), True, True) for t in range(n)])
        act(A("WL", w0, w0 + 64 * n), PB(pz, 0, 64 * n), ACT.Sigmoid, 0.5)
        cp(A("EU", u0, u0 + 128 * n), PB("S1", 0, 128 * n), "va")
        mm([(PB(sums(k + 6), 64 * t + 16 * q, 16, p=quad(1)), A("EU", u0 + 128 * t + 32 * q, u0 + 128 * t + 32 * q + 32), A("WL", w0 + 64 * t + 16 * q, w0 + 64 * t + 16 * q + 16), t == q == 0, t == n - 1 and q == 3)
            for t in range(n) for q in range(4)])
        for t in range(n):
            y = A3(gy(5), (8 - NL + t0 + t, 64, 8), None, quad(1)); tt(y, PB(sums(k + 6), 64 * t, 64, p=quad(1)), y, ALU.add)
        join(n)

    def first(rep, col, live, sides, spare, num, out):
        lo, hi = min(sides), max(sides) + 1
        mm([(PB("S1", d * L, L), A("IDB"), A("NMD2"), d == sides[0], False) for d in sides] + [(PB("S1", lo * L, (hi - lo) * L), A("BO32"), A("OAA", lo * L, hi * L), False, False)] * (not num))
        for d in sides:
            r0 = 12 * d % NEQ; lst = []
            for c in range(12):
                n = L - 16 * c
                ts(A3("EQ", r0 + c, (0, n)), A(rep, d * L + 16 * c, d * L + L), col(12 * d + c), ALU.is_equal, live(12 * d + c), ALU.mult)
                if c in (4, 8, 11): join((5, 4, 3)[c // 4 - 1 + (c == 11)])
                if c < 11: lst.append((PB("S1", d * L + 16 * c + 16, n - 16), A("BO"), A3("EQ", r0 + c, (16, n)), False, False))
            lst.append((PB("S1", d * L, L), A("TRI"), A3("EQ", (r0, r0 + 12), (0, 16)), False, d == sides[-1]))
            mm(lst[:5]); mm(lst[5:9]); mm(lst[9:])
        scan(A("FS", lo * L, hi * L), A(spare), PB("S1", lo * L, (hi - lo) * L), 0.0, ALU.max, ALU.min)
        fs = A("FS", lo * L + 15, hi * L, 16)
        if num: tt(H("F1", lo, 12), fs, num, ALU.max); cp(out, H("F1", lo, 12), "gva")
        else: cp(out, fs, "vga")

    def keys(d):
        cp(H("KR16", d), IND(A("COUNT"), H("S16", 2 + d, 12)), "va")
        first("KR16", lambda c: A("KF", c, c + 1), lambda c: 1.0, (d,), "DRC", H("KF", d, 12), H("OSC", d, 12))

    def cache(d):
        cp(IND(A(("HC", "TC")[d]), OSC[d]), H("AF", d)); lists(1, d)

    pair = swap("U0", "UO0", L)
    half = lambda k: dma("g", [(A("E32", k * M // 2, (k + 1) * M // 2), ("ee", (slice(0, 128), slice(k * M // 2, (k + 1) * M // 2))))], sent())
    for d in (0, 1):
        tt(H("UO0", d), IND(A("X", 0, M), OHT0[d]), H("MX", d), ALU.mult); send(pair[d:d + 1])
        if d: half(0)
        else: x = sent(); dma("s", [(A("HC", 0, NK), ("hc", full))], x); dma("s", [(A("E"), ("ee", full))], x)
    for d in (0, 1):
        tt(H("VO0", d), IND(A("E"), OHT0[d]), H("ME", d), ALU.mult); send(swap("V0", "VO0", L)[d:d + 1])
        if d: half(1)
        else: x = sent(); fill("VB1", "ZERO", x); dma("s", [nn(1, 0), nn(1, 1)], x)
    iota(A("ZERO32"), [[0, 384]])
    for d in (0, 1): lists(0, d); ublock(0, d)
    sel(A("COL"), A("ZERO", 0, 512), [[0, 64], [1, 8]], ALU.not_equal, 1.0, 0, -1)
    sel(A("OWN"), A("ZERO", 0, 128), [[1, 8], [0, 16]], ALU.is_equal, -16384.0, 0, -1)
    iota(A("IH"), [[0, 4], [1, 2], [0, 16]], 0, 1); ts(A("IH"), A("IH"), 1, ALU.bitwise_and); ts(A("HALF"), A("IH"), -16384.0, ALU.mult)
    iota(A("COUNT"), [[1, NK]]); cp(A("KF"), A("KEY"), "vg")
    keys(1)
    if not KLATE: keys(0)
    send([(A("ROSC"), H("OSC", 1, 12), 1)])
    for d in (1, 0): contest(d)
    for d in (1, 0): best(d)
    if VEARLY: dma("s", [(H("VA", r, 256), A("ZERO32", 0, 256)) for r in range(2 * VEARLY)], H("AF", 0))
    vblock(0, 1); reals0(1); vblock(0, 0)
    BL = A("BSC", 15, None, 16)
    for d0, d1 in ((1, 2), (0, 1)) if SPLIT else ((0, 2),): cp(A("OB", 12 * d0, 12 * d1), A("BSC", d0 * L + 15, d1 * L, 16), "vag")
    tt(A("PLUS", 0, 72, 3), BL, A("PLUS", 1, 72, 3), ALU.subtract)
    for d in (0, 1): tt(side("TIMES", d, 1), H("MI", d, 12), H("INS", d, 12), ALU.is_gt)
    scan(A("NEW"), A("TIMES"), A("PLUS"), 0.0, ALU.mult, ALU.add)
    cp(A("Z2"), A("NEW", 2, 72, 3), "vg"); ts(A("EXK"), A("Z2"), NK - 1, ALU.bitwise_and); cp(A("EXU"), A("EXK"), "vg")
    send(swap("OKEY1", "EXU", 12)); x = sent(); fill("UB0", "ZERO", x)
    if TWIN: fill("VF1", "ZERO32", x)
    else: fill("WF", "ZERO32", x, 0, 72)
    cp(A("OHT1"), A("NEW", 1, 72, 3), "gva")
    S384 = PB("S0", 0, 2 * L)
    sign(A("SU"), A("U0"))
    for d0, d1 in ((1, 2), (0, 1)) if SPLIT else ((0, 2),):
        x = lambda n, w=L: A(n, d0 * w, d1 * w)
        tt(x("NX0"), IND(A("X", 0, M), x("OB", 12)), x("SU"), ALU.subtract); tt(x("PV"), IND(A("E"), x("OB", 12)), x("V0"), ALU.mult)
    ts(A("NX"), A("NX0"), -7.0, ALU.max, 7.0, ALU.min)
    mm([(S384, A("BO32"), A("PV"), True, True)])
    act(S384, S384, ACT.Sigmoid, 0.5); tt(A("WV"), S384, A("V0"), ALU.mult)
    cp(A("EB"), IND(A("E"), A("OB")), "va", 0.875)
    cache(1)
    first("BR16", lambda c: A("BSC", 16 * c + 15, 16 * c + 16), lambda c: A("TIMES", 3 * c + 1, 3 * c + 2), (0, 1), "DRX", None, A("OSX"))
    for d in (0, 1): cp(IND(A("X"), H("OSX", d, 12)), H("NX", d))
    for c in range(3): sums0(c)
    reals0(0)
    for c in range(3, len(GB)): sums0(c)
    for d in (0, 1): tt(IND(A("E32"), H("OSX", d, 12)), H("EB", d), H("WV", d), ALU.add)
    if SPLIT > 1:
        for d in (0, 1): tt(H("UO1", d), IND(A("X", 0, M), H("OHT1", d, 12)), H("MX", d), ALU.mult); send(swap("U1", "UO1", L)[d:d + 1])
    else: tt(A("UO1"), IND(A("X", 0, M), A("OHT1")), A("MX"), ALU.mult); send(swap("U1", "UO1", L))
    if TWIN: fill("VF0", "ZERO32", sent())
    if SPLIT > 2:
        for d in (0, 1): tt(H("VO1", d), IND(A("E32", 0, M), H("OHT1", d, 12)), H("ME", d), ALU.mult); send(swap("V1", "VO1", L)[d:d + 1])
    else: tt(A("VO1"), IND(A("E32", 0, M), A("OHT1")), A("ME"), ALU.mult); send(swap("V1", "VO1", L))
    fill("WF", "ZERO32", sent(), 0 if TWIN else 72)
    if KLATE: keys(0)
    cache(0)
    for d in (1, 0):
        ublock(1, d); vblock(1, d)
    for x in ORDER.split():
        c = int(x[1])
        if x[0] == "D": duel(c); continue
        reals1(c)
        if c + len(GB) < 6: sums0(c + len(GB))
        if c < 5: store(c)
    for k in range(len(LAST)): piece(k)
    store(5)
    long = [i for i, o in enumerate(ops) if o["kind"] in ("cp", "tt") and o["name"] in ("EA", "XG", "EF")][12:]
    for a, b in zip(long, long[AHEAD:]): ops[b]["soft"] = [a]
    nth = lambda n, k: [i for i, o in enumerate(ops) if o["name"] == n][k]
    for a, j, b, k in AFTER: ops[nth(a, j)].setdefault("soft", []).append(nth(b, k))
    seen = {}
    for o in ops:
        n = o["name"]; k = seen[n] = seen.get(n, -1) + 1; x = DUE.get(n, [])
        o["due"] = 1000.0 * (x[k] if k < len(x) and x[k] else END)
    return ops


def hazards(ops):
    hist = {}
    for i, o in enumerate(ops):
        deps = {}
        acc = [(a, False) for a in o["rd"]] + [(a, True) for a in o["wr"]]
        for a, w in acc:
            ps = psum(a)
            for j, lo, hi, w2, p, st in hist.get(a["n"], []):
                apart = st[1] < a["st"][0] or a["st"][1] < st[0] if isinstance(st, tuple) else st == a["st"] and (lo - a["lo"]) % st
                if p[0] < a["p"][1] and a["p"][0] < p[1] and (ps or (w or w2) and lo < a["hi"] and a["lo"] < hi and not apart):
                    deps[j] = deps.get(j, False) or w or w2
        for a, w in acc:
            h = hist.setdefault(a["n"], [])
            if psum(a): h[:] = [x for x in h if x[0] == i or (x[3] and not w) or x[4][0] < a["p"][0] or a["p"][1] < x[4][1]]
            elif w and a["cnt"] == a["hi"] - a["lo"] and "off" not in a:
                h[:] = [x for x in h if x[0] == i or not (a["lo"] <= x[1] and x[2] <= a["hi"] and a["p"][0] <= x[4][0] and x[4][1] <= a["p"][1])]
            x = (i, a["lo"], a["hi"], w, a["p"], a["st"])
            if x not in h: h.append(x)
        deps.pop(i, None)
        o["deps"] = deps


PLAN = {}
MOVES, SEED, PULL, LATE, FADE, LOAD, SHOW = 450000, 9, 0.3, 0.04, 1.05, 0.15, 0
QUEUES, STRIDE, SIDE = "vatgs", 24, dict(v=1.0, a=0.8)
HINGE = ("U1", "V1", "OKEY1")
STAGES = ((0.4, 1.0, 0.3, 0, 140.0), (0.85, 1.0, 0.0, 1, 140.0), (1.0, 1.0, 0.0, 0, 30.0), (1.25, 1.0, 0.0, 0, 40.0))
FAR, BYKEY, DROP = 0.25, 0, 2.5
MAIN = dict(EF=3.0, U1=5.0, V1=5.0, VA=8.0, WS=8.0, WB0=5.0, WB1=5.0)


def plan():
    if "seq" in PLAN: return PLAN
    three = [build(c) for c in CASES]; ops = three[0]; hazards(ops); n = len(ops)
    deps = [{**dict.fromkeys(o.get("soft", []), o["kind"] != "mark"), **o["deps"]} for o in ops]; above = []
    for i in range(n):
        x = 0
        for j in deps[i]: x |= above[j] | 1 << j
        above.append(x)
    pre = [[j for j in deps[i] if not any(above[k] >> j & 1 for k in deps[i])] for i in range(n)]; suc = [[] for _ in ops]
    for i in range(n):
        for j in pre[i]: suc[j].append(i)
    inline = lambda i, j: ops[i]["eng"] == ops[j]["eng"] and (ops[i]["eng"] == "t" or len(ops[i]["eng"]) == 1 and not deps[i][j])
    waits = [[j for j in pre[i] if not inline(i, j)] for i in range(n)]
    way = [o["lat"] + o["hold"] for o in ops]; eng = [o["eng"][0] for o in ops]; own = [o["cost"][o["eng"][0]] for o in ops]

    def gap(line, t, c):
        p = len(line)
        while p and line[p - 1][1] > t: p -= 1
        while p < len(line) and line[p][0] < t + c: t = line[p][1]; p += 1
        return t, p

    key = [0.0] * n
    for i in range(n - 1, -1, -1): key[i] = min([key[k] - (way[i] if i in waits[k] else 0.0) for k in suc[i]] + [ops[i]["due"], 1000.0 * END - way[i]]) - own[i]
    for i in range(n): key[i] = max([key[i]] + [key[j] + 1e-3 for j in pre[i]])
    busy = {q: [] for q in QUEUES + "d"}; at = [0.0] * n
    for i in sorted(range(n), key=lambda i: key[i]):
        c, h = own[i], ops[i]["hold"]; t, p = gap(busy[eng[i]], max([0.0] + [at[j] + own[j] + (way[j] if j in waits[i] else 0.0) for j in pre[i]]), c)
        while h:
            t2, p2 = gap(busy["d"], t + c, h)
            if t2 <= t + c + 1e-6: busy["d"].insert(p2, (t + c, t + c + h)); break
            t, p = gap(busy[eng[i]], t2 - c, c)
        at[i] = t; busy[eng[i]].insert(p, (t, t + c))
    seq = sorted(range(n), key=lambda i: ((key if BYKEY else at)[i], i)); PLAN["first"] = (list(at), list(key))

    figures = lambda three: [{q: (QUEUES.index(q),) + tuple(x[i]["cost"][q] for x in three) + tuple(x[i]["lat"] for x in three) + (waits[i], ops[i]["hold"] and tuple(x[i]["hold"] for x in three))
                              for q in ops[i]["cost"]} for i in range(n)]
    figs = figures(three)
    last = [i for i in range(n) if not ops[i]["wr"]]; flex = [i for i in range(n) if len(figs[i]) > 1]
    miles = [(i, ops[i]["due"] + way[i], MAIN.get(ops[i]["name"], 1.0)) for i in range(n) if ops[i]["due"] < 1000.0 * END]
    aims = [x for x in miles for _ in range(int(x[2]))]
    hinge = [i for i in range(n) if ops[i]["name"] in HINGE]; stage = list(STAGES[0])
    load = [{q: c * SIDE.get(q, 0.0) for q, c in o["cost"].items()} for o in ops]; W0, W1, W2 = WEIGHTS

    def times(seq, fig, p0, marks, done, past=10 ** 6, cut=0.0):
        p0 -= p0 % STRIDE
        if p0: m = marks[:p0 // STRIDE]; f0, f1, f2 = map(list, marks[p0 // STRIDE]); d0, d1, d2 = done[0][:], done[1][:], done[2][:]
        else: m = []; f0, f1, f2 = [0.0] * 6, [0.0] * 6, [0.0] * 6; d0, d1, d2 = [0.0] * n, [0.0] * n, [0.0] * n
        for p in range(p0, n, STRIDE):
            if p > past:
                a, b, c = marks[p // STRIDE]
                if W0 * (sum(f0[:3]) - sum(a[:3])) + W1 * (sum(f1[:3]) - sum(b[:3])) + W2 * (sum(f2[:3]) - sum(c[:3])) > cut: return None, None
            m.append((tuple(f0), tuple(f1), tuple(f2)))
            for i in seq[p:p + STRIDE]:
                q, c0, c1, c2, l0, l1, l2, before, h = fig[i]; t0 = f0[q]; t1 = f1[q]; t2 = f2[q]
                for j in before:
                    if d0[j] > t0: t0 = d0[j]
                    if d1[j] > t1: t1 = d1[j]
                    if d2[j] > t2: t2 = d2[j]
                t0 += c0; t1 += c1; t2 += c2; f0[q] = t0; f1[q] = t1; f2[q] = t2
                if h: t0 = f0[5] = max(t0, f0[5]) + h[0]; t1 = f1[5] = max(t1, f1[5]) + h[1]; t2 = f2[5] = max(t2, f2[5]) + h[2]
                d0[i] = t0 + l0; d1[i] = t1 + l1; d2[i] = t2 + l2
        return m, (d0, d1, d2)

    def worth(done, late):
        d0, d1, d2 = done; e = W0 * max([d0[i] for i in last]) + W1 * max([d1[i] for i in last]) + W2 * max([d2[i] for i in last])
        v = stage[1] * e + PULL * sum(d0) / n + stage[2] * sum([W0 * d0[i] + W1 * d1[i] + W2 * d2[i] for i in hinge]) / len(hinge)
        if late:
            for i, m, w in miles:
                if d0[i] > m: v += late * w * (d0[i] - m)
        return v, e

    def chain(seq, fig, case, to):
        free = [(0.0, -1)] * 6; d = [0.0] * n; why = [None] * n
        for i in seq:
            x = fig[i]; t, k = free[x[0]]; queue = True
            for j in x[7]:
                if d[j] > t: t, k, queue = d[j], j, False
            t += x[1 + case]; free[x[0]] = (t, i)
            if x[8]:
                if free[5][0] > t: (t, k), queue = free[5], True
                t += x[8][case]; free[5] = (t, i)
            why[i] = (k, queue); d[i] = t + x[4 + case]
        i = d.index(max(d)) if to is None else to; out = []
        while i >= 0:
            k, queue = why[i]
            if queue and k >= 0: out.append((i, k))
            i = k
        return out or chain(seq, fig, case, None)

    def in_time(seq, fig, done, case):
        at = [0.0] * n; free = [0.0] * 5; prev = [0.0] * 5
        for i in seq:
            x = fig[i]; t = max([free[x[0]]] + [done[j] for j in x[7]]); free[x[0]] = t + x[1 + case]
            at[i] = prev[x[0]] = max([free[x[0]] if x[8] else t, prev[x[0]]] + [at[j] for j in pre[i]]) + 1e-6
        return sorted(seq, key=lambda i: at[i])

    fig = [figs[i][eng[i]] for i in range(n)]; busy = sum(load[i][eng[i]] for i in range(n)); best = arcs = more = None
    ends = lambda done: sum(w * max([d[i] for i in last]) for w, d in zip(WLATER, done))
    marks, done = times(seq, fig, 0, None, None); pres, sucs = [set(x) for x in pre], [set(x) for x in suc]
    for it, (r0, r1, r2, r3, r4) in enumerate(np.random.default_rng(SEED).random((int(MOVES * STAGES[-1][0]), 5)).tolist()):
        if it % 250 == 0:
            if it >= MOVES and any(it == int(MOVES * s[0]) // 250 * 250 for s in STAGES):
                e, seq, eng = best
                if it == MOVES: more = figures([build(c) for c in LATER]); W0, W1, W2 = WSECOND; best = None
                fig = [figs[i][eng[i]] for i in range(n)]; busy = sum(load[i][eng[i]] for i in range(n)); marks, done = times(seq, fig, 0, None, None)
            x = it / MOVES; k = [s[0] > x for s in STAGES].index(True); stage[:] = STAGES[k]; x0 = STAGES[k - 1][0] if k else 0.0
            late = LATE * max(0.0, 1.0 - FADE * x); heat = stage[4] * (stage[0] - x) / (stage[0] - x0) + 5.0
            fixed = max(seq.index(i) for i in hinge) + 1 if stage[3] else 0
            seq = seq[:fixed] + in_time(seq, fig, done[0], 0)[fixed:] if fixed and set(seq[:fixed]) == set(in_time(seq, fig, done[0], 0)[:fixed]) else in_time(seq, fig, done[0], 0); marks, done = times(seq, fig, 0, None, None); cur, e = worth(done, late); cur += LOAD * busy; arcs = None
            if more: fig2 = [more[i][eng[i]] for i in range(n)]; marks2, done2 = times(seq, fig2, 0, None, None); end2 = ends(done2); e += end2
            if best is None or e < best[0]: best = (e, seq, eng)
        if arcs is None:
            to = aims[int(r2 * len(aims))]
            if more and r3 < 0.5: arcs = chain(seq, fig2, int(r4 * 3), None)
            elif r3 < 0.3 and late and done[0][to[0]] > to[1]: arcs = chain(seq, fig, 0, to[0])
            else: arcs = chain(seq, fig, int(r4 * 3), hinge[int(r2 * len(hinge))] if r1 * (stage[1] + stage[2]) < stage[2] else None)
        s2, f2, b2, e2 = seq, fig, busy, eng
        i, k = arcs[int(r1 * len(arcs))]
        if r0 < 0.25:
            i = (i, k)[r2 < 0.5] if r0 < 0.15 else flex[int(r1 * len(flex))]
            other = [q for q in figs[i] if q != eng[i]]
            if not other: continue
            q = other[int(r4 * len(other))]; f2 = list(fig); e2 = list(eng); f2[i] = figs[i][q]; e2[i] = q; lo = seq.index(i); hi = lo + 20; b2 += load[i][q] - load[i][eng[i]]
            if 0.08 < r0 < 0.15 or r0 > 0.2:
                p = min(n - 1, max(0, lo + int(r2 * 41) - 20)); j = seq[p]
                if j != i and eng[j] == q and eng[i] in figs[j]: f2[j] = figs[j][eng[i]]; e2[j] = eng[i]; lo = min(lo, p); b2 += load[j][eng[i]] - load[j][q]
        elif r0 < 0.45:
            s2 = list(seq); p = int(r1 * n); i = s2.pop(p); lo, hi = p, p
            while lo > 0 and p - lo < 60 and s2[lo - 1] not in pres[i]: lo -= 1
            while hi < n - 1 and hi - p < 60 and s2[hi] not in sucs[i]: hi += 1
            x = lo + int(r2 * (hi - lo + 1)); s2.insert(x, i); lo, hi = min(x, p), max(x, p)
        else:
            if r4 > 1.0 - FAR:
                hi = lo = int(r1 * n); w = int(8 + 80 * r2 * r2)
                if r0 < 0.75: i = seq[hi]; k = -1; lo = max(0, lo - w)
                else: k = seq[lo]; i = -1; hi = min(n - 1, hi + w)
            else: hi = seq.index(i); lo = seq.index(k)
            if hi < lo: continue
            if r0 < 0.75:
                lo = max(0, lo - int(r2 * r2 * 30) * (k >= 0)); need = set(pre[i]); up, rest = [i], []
                for j in reversed(seq[lo:hi]):
                    if j in need: up.append(j); need.update(pre[j])
                    else: rest.append(j)
                if k in up: continue
                s2 = seq[:lo] + up[::-1] + rest[::-1] + seq[hi + 1:]
            else:
                hi = min(n - 1, hi + int(r2 * r2 * 30) * (i >= 0)); need = set(suc[k]); down, rest = [k], []
                for j in seq[lo + 1:hi + 1]:
                    if j in need: down.append(j); need.update(suc[j])
                    else: rest.append(j)
                if i in down: continue
                s2 = seq[:lo] + rest + down + seq[hi + 1:]
        if lo < fixed: continue
        m2, d2 = times(s2, f2, lo, marks, done, hi + STRIDE, DROP * (100.0 - heat * math.log(r3 + 1e-12)))
        if m2 is None: continue
        v, e = worth(d2, late); v += LOAD * b2
        if more and v <= cur - heat * math.log(r3 + 1e-12) + 300.0:
            g2 = fig2 if e2 is eng else [more[j][e2[j]] for j in range(n)]; m3, d3 = times(s2, g2, lo, marks2, done2); e3 = ends(d3); v += e3 - end2
        if v <= cur - heat * math.log(r3 + 1e-12):
            if more: v -= e3 - end2; fig2, marks2, done2, end2 = g2, m3, d3, e3
            cur, seq, fig, marks, done, busy, eng = v, s2, f2, m2, d2, b2, e2
            if r4 < 0.3: arcs = None
        elif r4 < 0.05: arcs = None
    e, seq, eng = best; fig = [figs[i][eng[i]] for i in range(n)]; done = times(seq, fig, 0, None, None)[1]
    free = [0.0] * 5; start = [0.0] * n
    for i in seq: start[i] = max([free[fig[i][0]]] + [done[SHOW][j] for j in waits[i]]); free[fig[i][0]] = start[i] + fig[i][1 + SHOW]
    PLAN.update(waits=waits, ops=ops, seq=seq, start=start, eng=eng, end=[max(d[i] for i in last) for d in done])
    return PLAN


def rank_program(g, core, T, topo):
    rank = T.rank_of(core)
    if rank is None:
        return
    P = plan(); ops, eng, start = P["ops"], P["eng"], P["start"]
    Q = {"v": g.vector, "a": g.scalar, "t": g.tensor, "g": g, "s": g.sync}
    peer = {1: T.cores[(rank + D) % NR], -1: T.cores[(rank - D) % NR]}
    back = {1: peer[-1], -1: peer[1]}

    def ap(a):
        if isinstance(a, tuple): return T[a[0]][a[1]]
        if not isinstance(a, dict): return a
        x = T[a["n"]][a["ix"]]
        return x.indirect(ap(a["off"])) if "off" in a else x

    def share(src, dst, k, n, few):
        e = topo.engines(src, dst)[::2 if few else 1]; m = len(e) // n
        return e[k * m:(k + 1) * m]

    seq = P["seq"]; issue = caller(ap)
    count = {q: 0 for q in "vatg"}; nd = [0, 0, 0]; token = {}; known = {q: {} for q in Q}; snap = {}; total = {}

    def wait(q, sem, val, src):
        if known[q].get(sem, 0) < val:
            Q[q].wait_ge(T.sem[sem], val); known[q][sem] = val
        for s2, v2 in snap.get(src, {}).items():
            if known[q].get(s2, 0) < v2: known[q][s2] = v2

    for i in seq:
        o, q = ops[i], eng[i]; e = Q[q]; k, x = o["kind"], o["args"]
        for j in sorted(o["deps"], key=lambda j: -start[j]):
            if eng[j] == q and ops[j]["kind"] not in ("dma", "dadd", "send") and (q == "t" or not o["deps"][j]): continue
            if ops[j]["kind"] == "send":
                for land, sem, val in token[j]:
                    if any(a["n"] == land["n"] and a["lo"] < land["hi"] and land["lo"] < a["hi"] for a in o["rd"]): wait(q, sem, val, None)
            else:
                wait(q, token[j][0], token[j][1], j)
        snap[i] = dict(known[q])
        if k == "send":
            trs, token[i] = [], []
            for n, (land, src, way) in enumerate(x):
                sem = "r%d" % nd[1]; nd[1] += 1
                few = False; mine = share(core, peer[way], n, len(x), few); rid, pid = topo.addr(peer[way])[:2]
                trs.append(RemoteDMATransfer(dst_ids=[DstId(rid=rid, pnc=pid)], dma_engine_mask=sum(1 << b for b in mine), remote_sem=T.sem[sem], src=ap(src), dst=ap(land)))
                nd[2] += len(mine); val = len(share(back[way], core, n, len(x), few)); token[i].append((land, sem, val)); total[sem] = val
            g.remote_dma_fused(trs, local_sem=T.sem.loc)
            continue
        if k == "mark":
            g.sem_inc(T.sem.mark, 1); total["mark"] = total.get("mark", 0) + 1; token[i] = ("mark", total["mark"]); snap[i] = {}
            continue
        if k in ("dma", "dadd"):
            sem = "d%d" % nd[0]; nd[0] += 1
            for out, src in x: (e.dma_start(ap(out), ap(src)) if k == "dma" else e.dma_start(ap(out), ap(src), accum_op=ALU.add)).then_inc(T.sem[sem], 16)
            token[i] = (sem, 16 * len(x)); total[sem] = 16 * len(x)
            continue
        for y in (x if k == "many" else [o]):
            issue(e, q, y["kind"], y["args"]).then_inc(T.sem["c" + q], 1); count[q] += 1
        token[i] = ("c" + q, count[q]); total["c" + q] = count[q]
    total["loc"] = nd[2]
    seen = {}
    for q in Q:
        for s2, v2 in known[q].items(): seen[s2] = max(seen.get(s2, 0), v2)
    for s2, v2 in total.items():
        if seen.get(s2, 0) < v2: g.sync.wait_ge(T.sem[s2], v2)


def caller(ap):
    def issue(e, q, k, x):
        if k == "cp":
            out, a, sc, bi = x
            if q == "g": r = e.affine_select(ap(out), ap(a), [[0, out["cnt"]]], ALU.is_ge, 0.0, 0, 0)
            elif q == "a":
                if bi is None: r = e.activation(ap(out), ap(a), ACT.Copy, scale=1.0 if sc is None else sc)
                else: r = e.activation(ap(out), ap(a), ACT.Identity, bias=ap(bi), scale=sc)
            elif sc is None: r = e.tensor_copy(ap(out), ap(a))
            elif bi is None: r = e.tensor_scalar(ap(out), ap(a), sc, None, ALU.mult)
            else: r = e.tensor_scalar(ap(out), ap(a), sc, ap(bi), ALU.mult, ALU.add)
        elif k == "ts":
            if x[5] is None: r = e.tensor_scalar(ap(x[0]), ap(x[1]), ap(x[2]), None, x[4])
            else: r = e.tensor_scalar(ap(x[0]), ap(x[1]), ap(x[2]), ap(x[3]), x[4], x[5])
        elif k == "tt": r = e.tensor_tensor(ap(x[0]), ap(x[1]), ap(x[2]), x[3])
        elif k == "scan": r = e.tensor_tensor_scan(ap(x[0]), ap(x[1]), ap(x[2]), x[3], x[4], x[5])
        elif k == "tr": r = e.transpose(ap(x[0]), ap(x[1]))
        elif k == "ms": r = e.memset(ap(x[0]), x[1])
        elif k == "act": r = e.activation(ap(x[0]), ap(x[1]), x[2], scale=x[3])
        elif k == "step":
            if q == "a": r = e.activation(ap(x[0]), ap(x[1]), ACT.Sigmoid, bias=64.0, scale=128.0)
            else: r = e.tensor_scalar(ap(x[0]), ap(x[1]), 0.0, None, ALU.is_ge)
        elif k == "sign":
            if q == "a": r = e.activation(ap(x[0]), ap(x[1]), ACT.Sign)
            else: r = e.tensor_scalar(ap(x[0]), ap(x[1]), -1.0, 1.0, ALU.max, ALU.min)
        elif k == "sel": r = e.affine_select(ap(x[0]), ap(x[1]), x[2], x[3], x[4], x[5], x[6])
        elif k == "iota":
            if SCRATCH[x[0]["n"]][2] == I: r = e.iota(ap(x[0]), x[1], x[2], x[3])
            else: r = e.iota(ap(x[0]), x[1], x[2], x[3], allow_small_or_imprecise_dtypes=True)
        else:
            for out, a, b, s0, s1 in x: r = e.matmul(ap(out), ap(a), ap(b), s0, s1)
        return r
    return issue
